import numpy as np, ml_dtypes
CORES = [40,64,80,88,96,104,120,144]
N = 8
BF = ml_dtypes.bfloat16
def gentries(a):
    return np.ascontiguousarray(a.reshape(8, 16, -1).transpose(0, 2, 1)).reshape(8, -1)
def gtable(e):
    e = np.asarray(e); return np.ascontiguousarray(e.reshape(8, -1, 16).transpose(0, 2, 1)).reshape(128, -1).astype(np.int32)
V, FN, C, S, TV = 3072, 3072, 256, 745, 4
def perms(rng, *shape):
    return np.argsort(rng.random(shape), axis=-1)
def marks(rng, cnt):
    return np.argsort(rng.random(cnt.shape[:-2] + (16, cnt.shape[-1])), axis=-2) < cnt
def lay(loc, xw, nw, pw):
    inv = np.argsort(loc, axis=-1)
    x = np.take_along_axis(xw, inv[:, :, None, :], 3); nm = np.take_along_axis(nw, inv, 2)
    p = np.where(pw >= 0, np.take_along_axis(loc, np.maximum(pw, 0), 2), -1)
    return x, nm, p, np.take_along_axis(np.roll(loc, -1, axis=0), inv, 2)
def two(rng):
    return rng.integers(0, 64, (N, 16, FN)) + 192 * (np.arange(FN) & 1)
def reads(rng, hi):
    m = marks(rng, hi); return rng.integers(0, 64, m.shape) + 192 * m
def loose(rng, share):
    w = perms(rng, N, 8, FN); return np.where((w < V) & (rng.random((N, 8, FN)) < share), w, -1)
def tradition(rng):
    base = np.where(rng.random((8, 16, FN)) < 0.3, rng.choice(np.array([0, 128, 255]), (8, 16, FN)), rng.integers(0, 256, (8, 16, FN)))
    fo = np.where(rng.random((N, 8, 16, FN)) < 0.25, rng.integers(0, 256, (N, 8, 16, FN)), base)
    com = rng.integers(0, FN, (8, FN // 16))
    z = np.where(rng.random((8, V)) < 0.4, np.take_along_axis(com, rng.integers(0, FN // 16, (8, V)), 1), perms(rng, 8, FN)[:, :V])
    zz = np.where(rng.random((N, 8, V)) < 0.1, rng.integers(0, FN, (N, 8, V)), z)
    xw = np.take_along_axis(base[None], zz[:, :, None, :], 3)
    xw = np.where(rng.random((N, 8, 16, V)) < 0.25, rng.integers(0, 256, (N, 8, 16, V)), xw)
    nw = np.where(rng.random((N, 8, V)) < 0.15, rng.integers(0, FN, (N, 8, V)), z)
    pw = np.full((N, 8, FN), -1, np.int64); m = V // 12
    for r in range(N):
        for g in range(8):
            a = pw[r, g]; o = rng.permutation(V); a[z[g, o]] = o; a[rng.random(FN) < 0.3] = -1
            h = np.zeros(V, bool); h[a[a >= 0]] = True
            a[rng.permutation(np.flatnonzero(a < 0))[:m]] = rng.permutation(np.flatnonzero(~h))[:m]
    x, nm, p, cc = lay(perms(rng, N, 8, V), xw, nw, pw)
    for q in range(N):
        for g in range(8):
            i = rng.permutation(V)[:V // 32]; cc[q, g, i] = cc[q, g, rng.permutation(i)]
    return x, fo, nm, p, cc
def pack(x, fo, nm, p, cc):
    return {"tx": np.ascontiguousarray(x.reshape(N, 128, V)).astype(np.float32).astype(BF), "fo": np.ascontiguousarray(fo.reshape(N, 128, FN)).astype(np.float32).astype(BF),
            "nm": np.ascontiguousarray(nm).astype(np.int32), "pl": np.stack([gtable(a) for a in p]), "cc": np.stack([gtable(a) for a in cc])}
def setup_inputs(rng):
    return pack(*tradition(rng))
def setup_inputs_spread(rng):
    x = np.minimum(np.floor(256 * rng.random((N, 8, 16, V)) ** np.exp2(rng.integers(-2, 3, (N, 8, 1, V)))), 255)
    fo = np.minimum(np.floor(256 * rng.random((N, 8, 16, FN)) ** np.exp2(rng.integers(-2, 3, (N, 8, 1, FN)))), 255)
    nm = np.minimum(np.floor(FN * rng.random((N, 8, V)) ** np.exp2(rng.integers(-1, 3, (N, 8, 1)))), FN - 1)
    return pack(x, fo, nm, loose(rng, rng.choice(np.array([0.1, 0.3, 0.6, 1.0]), (N, 8, 1))), perms(rng, N, 8, V))
def setup_inputs_ends(rng):
    u = rng.integers(0, 2, (8, 16, 1)); side = rng.integers(0, 2, (8, 1, FN)); side[:, :, 0] = 0; side[:, :, FN - 1] = 1
    fl = rng.integers(1, 4, (N, 8, 1, FN)) * (rng.random((N, 8, 1, FN)) < 0.5); fl[..., 0] = 0; fl[..., FN - 1] = 0
    fo = 255 * (u ^ side ^ marks(rng, fl).astype(np.int64))
    xs = rng.integers(0, 2, (N, 8, 1, V)); xf = rng.choice(np.array([0, 1, 4, 7, 7, 8, 8, 16]), (N, 8, 1, V))
    e = np.arange(N)[:, None] + np.arange(8)[None, :]; v = np.array([0, 7, 8, 16])
    xs[..., 0] = 1; xs[..., V - 1] = 1; xf[:, :, 0, V - 1] = v[e & 3]; xf[:, :, 0, 0] = v[(e + 1) & 3]
    x = 255 * (u ^ xs ^ marks(rng, xf).astype(np.int64))
    nm = np.where(rng.random((N, 8, V)) < 0.7, (FN - 1) * rng.integers(0, 2, (N, 8, V)), rng.integers(0, FN, (N, 8, V))); nm[..., 0] = 0; nm[..., V - 1] = 0
    p = loose(rng, 0.4); p[(p == 0) | (p == V - 1)] = -1
    cc = np.zeros((N, 8, V), np.int64); cc[..., 1:V - 1] = 1 + perms(rng, N, 8, V - 2)
    for g in range(8):
        a, b = ((0, V - 1), (V - 1, 0))[g & 1]
        p[:, g, 0] = a; p[:, g, FN - 1] = b; cc[:, g, 0] = a; cc[:, g, V - 1] = b
    return pack(x, fo, nm, p, cc)
def hang(rng, un0):
    last = (S * TV - 1) % V; o = rng.permutation(V); o = np.concatenate([np.array([last]), o[o != last]]); un, on = o[:un0], o[un0:]
    phi = rng.permutation(FN)[:len(on)]; odd = phi[(phi & 1) == 1]; j = np.flatnonzero((phi & 1) == 0)[0]
    name = np.zeros(V, np.int64); name[on] = phi; name[un] = rng.choice(odd, un0); name[last] = phi[j]
    nm = np.tile(name, (N, 1)); q = rng.integers(0, N); nm[q, on[j]] = rng.choice(odd)
    hi = rng.choice(np.array([7, 8, 9]), (N, 1, V)); hi[q, 0, on[j]] = 8
    p = np.full(FN, -1, np.int64); p[phi] = on
    return reads(rng, hi), two(rng), nm, np.tile(p, (N, 1)), np.tile(np.arange(V), (N, 1))
def setup_inputs_corners(rng):
    x, fo, nm, p, cc = tradition(rng); o = rng.permutation(8)
    p[:, o[0]] = -1
    w = perms(rng, N, FN); p[:, o[1]] = np.where(w < V, w, -1)
    for r in range(N):
        w = rng.permutation(FN); a = np.where(w < V, w, -1)
        if r & 1: a[rng.choice(np.flatnonzero(a >= 0))] = -1
        else:
            a[:] = -1; a[rng.integers(0, FN)] = (0, V - 1)[(r >> 1) & 1]
        p[r, o[2]] = a
    for i in (3, 4):
        g = o[i]; fo[:, g] = two(rng); x[:, g] = reads(rng, rng.choice(np.array([0, 7, 7, 8, 8, 9, 9, 16]), (N, 1, V))); nm[:, g] = rng.integers(0, FN, (N, V))
        w = perms(rng, N, FN); p[:, g] = np.where((w < V) & ((i == 4) | (rng.random((N, FN)) < 0.5)), w, -1)
    cc[:, o[3]] = (np.arange(V) + 1) % V; cc[:, o[4]] = V - 1 - np.arange(V)
    for i, n in ((5, C - 2), (6, C - 1), (7, C)): x[:, o[i]], fo[:, o[i]], nm[:, o[i]], p[:, o[i]], cc[:, o[i]] = hang(rng, n)
    return pack(x, fo, nm, p, cc)
def late(rng, un0, vis, pair):
    n = len(vis)
    if pair: w = np.stack([rng.permutation(S)[:n], S * TV + rng.permutation(V - S * TV)[:n]])
    else: w = rng.permutation(V)[None, :n]
    o = rng.permutation(V); o = np.concatenate([w.reshape(-1), o[~np.isin(o, w)]]); un, on = o[:un0], o[un0:]
    a = rng.permutation(FN); new, phi = a[:n], a[FN - len(on):]; odd = phi[(phi & 1) == 1]
    name = np.zeros(V, np.int64); name[on] = phi; name[un] = rng.choice(odd, un0)
    nm = np.tile(name, (N, 1)); fo = two(rng); fo[:, :, new] = 255
    for k in range(n):
        r = int(rng.integers(0, N)); nm[(r + vis[k]) % N, w[:, k]] = new[k]; fo[r, :, int(new[k])] = rng.integers(0, 64, 16)
    hi = rng.choice(np.array([7, 8, 9]), (N, 1, V)); hi[:, :, w.reshape(-1)] = 0
    p = np.full(FN, -1, np.int64); p[phi] = on; x = reads(rng, hi)
    if pair: return x, fo, nm, np.tile(p, (N, 1)), np.tile(np.arange(V), (N, 1))
    x, nm, p, cc = lay(perms(rng, N, 1, V), x[:, None], nm[:, None], np.tile(p, (N, 1, 1)))
    return x[:, 0], fo, nm[:, 0], p[:, 0], cc[:, 0]
def turn(rng):
    c = rng.permutation(FN)[:N + 2]; x = rng.integers(0, 64, (N, 16, V)); fo = two(rng); fo[:, :, c] = 255
    nm = np.tile(c[:N, None], (1, V)); i = (S * TV + C) % V; nm[:, i - 1] = c[N]; nm[:, i] = c[N + 1]
    for r in range(N):
        t = 2 + r % (TV - 1); fo[r, :, int(c[(r + t) % N])] = rng.integers(0, 64, 16)
    return x, fo, nm, np.full((N, FN), -1, np.int64), np.tile(np.arange(V), (N, 1))
def setup_inputs_crowd(rng):
    x, fo, nm, p, cc = tradition(rng); o = rng.permutation(8); c = rng.permutation(FN)[:6 + N * TV]; half = loose(rng, 0.5)
    nm[:, o[0]] = c[0]; p[:, o[0]] = -1
    nm[:, o[1]] = c[1]; p[:, o[1]] = -1
    for t in range(1, TV + 1): nm[:, o[1], (S * t + 5) % V] = c[6 + N * (t - 1):6 + N * t]
    nm[:, o[2]] = c[2]; p[:, o[2]] = half[:, o[2]]
    nm[:, o[3]] = rng.choice(np.array([0, FN - 1, c[3]]), (N, V)); p[:, o[3]] = half[:, o[3]]
    nm[:, o[4]] = np.where((np.arange(V) & 1) == 1, c[3], c[4]); p[:, o[4]] = -1; p[1::2, o[4]] = half[1::2, o[4]]
    nm[:, o[5]] = c[5]; p[:, o[5]] = -1; p[:, o[5], c[5]] = V - 1
    x[:, o[6]], fo[:, o[6]], nm[:, o[6]], p[:, o[6]], cc[:, o[6]] = turn(rng)
    x[:, o[7]], fo[:, o[7]], nm[:, o[7]], p[:, o[7]], cc[:, o[7]] = late(rng, C // 2, list(range(1, TV + 1)), True)
    return pack(x, fo, nm, p, cc)
def still(rng, k):
    n = max(k - 1, 0); o = rng.permutation(V); un, on = o[:n], o[n:]
    phi = rng.permutation(FN)[:len(on)]; odd = phi[(phi & 1) == 1]; ev = on[(phi & 1) == 0]
    name = np.zeros(V, np.int64); name[on] = phi; name[un] = rng.choice(odd, n)
    nm = np.tile(name, (N, 1)); hi = rng.choice(np.array([7, 8, 9]), (N, 1, V))
    for q in range(N):
        w = ev[9 * q:9 * q + 9]; nm[q, w[1:]] = rng.choice(odd, 8); hi[q, 0, w[1:]] = rng.choice(np.array([7, 7, 6, 0]), 8)
        if k > 0 and q % 2 == 0:
            nm[q, w[0]] = rng.choice(odd); hi[q, 0, w[0]] = rng.choice(np.array([8, 8, 16]))
    p = np.full(FN, -1, np.int64); p[phi] = on
    x, nm, p, cc = lay(perms(rng, N, 1, V), reads(rng, hi)[:, None], nm[:, None], np.tile(p, (N, 1, 1)))
    return x[:, 0], two(rng), nm[:, 0], p[:, 0], cc[:, 0]
def setup_inputs_calm(rng):
    x, fo, nm, p, cc = tradition(rng); o = rng.permutation(8)
    for k in range(4): x[:, o[k]], fo[:, o[k]], nm[:, o[k]], p[:, o[k]], cc[:, o[k]] = still(rng, k)
    for k, n, vis, pair in ((4, 1, [2], False), (5, 1, [3], False), (6, 2 * TV, list(range(1, TV + 1)), True)):
        x[:, o[k]], fo[:, o[k]], nm[:, o[k]], p[:, o[k]], cc[:, o[k]] = late(rng, n, vis, pair)
    return pack(x, fo, nm, p, cc)
def check_inputs(d):
    bad = []
    for k, lo, hi in (("tx", 0, 255), ("fo", 0, 255), ("nm", 0, FN - 1), ("pl", -1, V - 1), ("cc", 0, V - 1)):
        v = np.asarray(d[k]).astype(np.float64)
        if not np.all((v >= lo) & (v <= hi) & (np.floor(v) == v)): bad.append("range of " + k)
    e = np.sort(np.stack([gentries(np.asarray(a)) for a in d["pl"]]), axis=-1)
    if np.any((e[..., 1:] == e[..., :-1]) & (e[..., 1:] >= 0)): bad.append("pl lists a place twice")
    e = np.sort(np.stack([gentries(np.asarray(a)) for a in d["cc"]]), axis=-1)
    if np.any(e != np.arange(V)): bad.append("cc is no permutation")
    return bad
def reference(tx, fo, nm, pl, cc):
    X = tx.astype(np.float32).astype(np.int32).reshape(N, 8, 16, V); F = fo.astype(np.float32).astype(np.int32).reshape(N, 8, 16, FN)
    name = nm.astype(np.int64).reshape(N, 8, V); P = np.stack([gentries(a) for a in pl]).astype(np.int64); con = np.stack([gentries(a) for a in cc]).astype(np.int64)
    forms = np.arange(FN)[None, :]
    for t in range(1, TV + 1):
        order = (np.arange(V) + S * t) % V
        for r in range(N):
            q = (r + t) % N; left = (r + t - 1) % N
            full = P[r] >= 0; y = np.where(full, np.take_along_axis(con[left], np.maximum(P[r], 0), 1), 0)
            n = np.take_along_axis(name[q], y, 1); x = np.take_along_axis(X[q], y[:, None, :], 2)
            near = np.abs(x - F[r]) < np.abs(x - np.take_along_axis(F[r], n[:, None, :], 2))
            votes = np.add.reduce(near.astype(np.int64), axis=1)
            other = full & (n != forms); amend = other & (votes >= 9)
            g, f = np.nonzero(amend); name[q, g, y[g, f]] = f
            p = np.where(full & ((n == forms) | amend), y, -1)
            listed = np.zeros((8, V), bool); g, f = np.nonzero(p >= 0); listed[g, p[g, f]] = True
            free = ~listed[:, order]; taken = free & (np.add.accumulate(free.astype(np.int64), axis=1) <= C)
            g, i = np.nonzero(taken); place = order[i]
            low = np.full((8, FN), V, np.int64); np.minimum.at(low, (g, name[q][g, place]), place)
            P[r] = np.where((p < 0) & (low < V), low, p)
    return {"yn": name.astype(np.float32), "yp": np.stack([gtable(a) for a in P]).astype(np.float32)}

@@ -1,0 +1,593 @@
+import numpy as np
+from concourse.bass import DstId, RemoteDMATransfer
+from concourse.mybir import AluOpType as A, ActivationFunctionType as AF, AxisListType
+
+N, V, S, TV = 8, 3072, 745, 4
+f32, bf, i32, u16 = "float32", "bfloat16", "int32", "uint16"
+
+
+def _sb(n, d):
+    return ("sbuf", [128, n], d)
+
+
+SCRATCH = {
+    "sx": ("dram", [8, 128, 384], bf), "sf": ("dram", [8, 128, 384], bf), "ss": ("dram", [8, 128, 96], i32),
+    "rx": ("dram", [8, 128, 384], bf), "rf": ("dram", [8, 128, 384], bf), "rs": ("dram", [8, 128, 96], i32),
+    "hx": ("dram", [128, 384], bf), "hf": ("dram", [128, 384], bf), "hs": ("dram", [128, 96], i32),
+    "on": ("dram", [8, 128, 24], f32), "op": ("dram", [8, 128, 24], f32),
+    "rn": ("dram", [8, 128, 24], f32), "rp": ("dram", [8, 128, 24], f32),
+    "hn": ("dram", [128, 24], f32), "hp": ("dram", [128, 24], f32),
+    "X": _sb(V, bf), "F": _sb(V, bf), "G2": _sb(V, bf), "D": _sb(V, bf), "PR": _sb(V, bf), "NE": _sb(V, bf),
+    "W": _sb(3328, bf), "TR": _sb(3328, bf), "PG": _sb(3584, bf),
+    "RHO": _sb(V, f32), "FV": _sb(V, f32), "ICW": _sb(V, f32), "LW": _sb(6144, f32), "LX": _sb(6144, f32),
+    "E": ("sbuf", [128, 16, 256], bf),
+    "PK": _sb(4, i32), "CC": _sb(32, f32), "IOT": _sb(256, f32), "IG": _sb(128, f32), "IK": _sb(256, f32),
+    "JL": _sb(192, f32), "TMP": _sb(256, f32), "TM2": _sb(256, f32), "SG": _sb(128, f32),
+    "ME": _sb(144, bf), "ML": _sb(144, bf), "MC": _sb(144, bf), "MB": _sb(144, bf), "MX": _sb(144, bf), "MS": _sb(144, bf),
+    "Y1": _sb(192, bf), "Y2": _sb(128, bf), "YM": _sb(192, bf), "Y4": _sb(192, bf), "YE": _sb(128, bf),
+    "ONE": _sb(128, bf), "TRI": _sb(128, bf), "BCN": _sb(128, bf), "POW": _sb(128, bf), "TWO": _sb(128, bf), "OCC": _sb(128, bf),
+    "ZER": _sb(208, bf), "JB": _sb(256, bf), "JF": _sb(256, f32), "TAU": _sb(256, f32), "THR": _sb(256, f32),
+    "DU1": _sb(16, f32), "DU2": _sb(16, f32), "MF": _sb(144, bf), "DU3": _sb(192, f32), "MK": _sb(8, bf), "VH": _sb(192, bf), "VL": _sb(192, bf),
+    "CP": _sb(384, i32), "NI": _sb(192, i32), "IA": _sb(384, i32), "IB": _sb(384, i32), "FA": _sb(384, f32), "RF": _sb(384, f32),
+    "FB": _sb(192, f32), "FC": _sb(192, f32), "FD": _sb(192, f32),
+    "RRU": _sb(192, u16), "BH": _sb(384, bf), "BL": _sb(384, bf), "ICF": _sb(576, f32), "ICI": _sb(576, i32), "ICU": _sb(576, u16),
+    "NF": _sb(192, f32), "N4": _sb(192, f32), "NU": _sb(192, u16), "LU": _sb(192, u16), "PU": _sb(192, u16), "LO": _sb(192, u16),
+    "CA": _sb(192, f32), "EQ": _sb(192, bf), "ZJ": _sb(192, f32),
+    "HI": _sb(192, bf), "LW2": _sb(192, bf), "FR": _sb(192, bf), "FS": _sb(2, bf),
+    "U": _sb(200, f32), "DB": _sb(2, f32), "BC": _sb(208, bf), "CU": _sb(200, f32), "BS": _sb(16, f32),
+    "L1": _sb(256, bf), "L2": _sb(256, bf), "SE": _sb(256, bf), "AU": _sb(16, u16), "AB": _sb(16, bf), "KU": _sb(16, u16),
+    "KB": _sb(32, bf), "RT": _sb(16, f32), "RU": _sb(16, u16), "Z": _sb(256, bf), "O": _sb(256, bf),
+    "NB": _sb(256, u16), "NL": _sb(16, f32), "NLU": _sb(16, u16), "NPU": _sb(16, u16), "WI": _sb(256, bf),
+    "QU": _sb(16, u16), "YP": _sb(192, f32), "TN": _sb(256, f32),
+}
+for _b in range(8):
+    SCRATCH["P%d" % _b] = ("psum", [128, 512], f32)
+NDMA = 64
+SEMAPHORES = (["cv", "ca", "cp", "cg", "loc", "as", "an", "ap", "h0", "h1", "h2", "h3", "h4"]
+              + ["af%d" % s for s in range(8)] + ["ax%d" % s for s in range(8)] + ["d%d" % k for k in range(NDMA)])
+CH_HI, CH_LO, CH_FR, CH_FI, CH_BH, CH_BL, CH_CH, CH_CL = 0, 1, 2, 3, 4, 5, 6, 7
+CY, PEC = 1.04, 0.52
+
+
+def routes(T, topo):
+    C = T.cores
+    cls = [[d for d in range(N) if topo.may_write(C[s], C[d])] for s in range(N)]
+    idx = [cls[s].index(s) for s in range(N)]
+    via, vib = [[None] * N for _ in range(N)], [[None] * N for _ in range(N)]
+    for s in range(N):
+        mine = [c for c in topo.cores_of(C[s]) if c != C[s]]
+        far = [d for d in range(N) if d not in cls[s]]
+        port = [c for c in mine if topo.may_write(c, C[far[0]])]
+        dies = sorted(set(topo.die(c) for c in port))
+        free = {x: [c for c in port if topo.die(c) == x] for x in dies}
+        for d in far:
+            via[s][d] = vib[s][d] = free[dies[(idx[s] + idx[d]) % 2]].pop(0)
+        plain = [c for c in mine if c not in port and topo.die(c) != topo.die(C[s])]
+        for d in cls[s]:
+            if d != s and idx[d] != (idx[s] + 1) % len(cls[s]):
+                via[s][d] = plain.pop(0)
+    return via, vib
+
+
+def bits(l):
+    return sum(1 << e for e in l)
+
+
+def helper(g, core, T, topo, s, d, short):
+    rid, pid = topo.addr(T.cores[d], core)
+    m = topo.mask(core, T.cores[d])
+    n = len(topo.engines(core, T.cores[d]))
+    steps = [("h1", T.hf, T.rf, "af%d" % s), ("h2", T.hx, T.rx, "ax%d" % s)]
+    if short:
+        steps = [("h0", T.hs, T.rs, "as")] + steps + [("h3", T.hn, T.rn, "an"), ("h4", T.hp, T.rp, "ap")]
+    for sem, src, dst, rs in steps:
+        g.wait_ge(T.sem[sem], 2)
+        g.remote_dma(dst[s], src[:], T.sem[rs], T.sem.loc, pid, rid, m)
+    g.wait_ge(T.sem.loc, n * len(steps))
+
+
+def rank_program(g, core, T, topo):
+    via, vib = routes(T, topo)
+    rank = T.rank_of(core)
+    if rank is None:
+        for s in range(N):
+            for d in range(N):
+                if via[s][d] == core:
+                    helper(g, core, T, topo, s, d, vib[s][d] == core)
+        return
+    ops = build(g, core, rank, T, topo, via, vib)
+    emit(g, T, ops)
+
+
+PLAN = {}
+TRIES = 1500
+
+
+def schedule(ops, succ, noise, win):
+    n, LAT = len(ops), 150.0
+    pr = [0.0] * n
+    for i in range(n - 1, -1, -1):
+        pr[i] = ops[i]["c"] + ops[i]["lat"] + max([pr[j] + LAT for j in succ[i]] + [0.0])
+    pr = [float(pr[i] + noise[i]) for i in range(n)]
+    left = [len(o["dep"]) for o in ops]
+    fin, start, busy, order, est = [0.0] * n, [0.0] * n, {}, [], {}
+    ready = [i for i in range(n) if left[i] == 0]
+    for i in ready: est[i] = ops[i]["t0"]
+    while ready:
+        st = {i: max(est[i], busy.get(ops[i]["e"], 0.0)) for i in ready}
+        i0 = min(ready, key=lambda i: (st[i], -pr[i], i))
+        e, t = ops[i0]["e"], st[i0]
+        i = max([j for j in ready if ops[j]["e"] == e and st[j] <= t + min(win, ops[i0]["c"])], key=lambda j: (pr[j], -j))
+        busy[e] = st[i] + ops[i]["c"]
+        fin[i] = busy[e] + ops[i]["lat"]
+        start[i] = st[i]
+        order.append(i)
+        ready.remove(i)
+        for j in succ[i]:
+            left[j] -= 1
+            if left[j] == 0:
+                o = ops[j]
+                est[j] = max([o["t0"]] + [fin[d] + (0.0 if ops[d]["e"] == o["e"] and not ops[d]["dma"] else LAT) for d in o["dep"]])
+                ready.append(j)
+    return max(fin), order, start
+
+
+def emit(g, T, ops):
+    n = len(ops)
+    lastw, readers = {}, {}
+    for i, o in enumerate(ops):
+        dep = set()
+        for r in o["r"]:
+            if r in lastw: dep.add(lastw[r])
+        for w in o["w"]:
+            if w in lastw: dep.add(lastw[w])
+            dep.update(readers.get(w, []))
+        dep.discard(i)
+        for r in o["r"]: readers.setdefault(r, []).append(i)
+        for w in o["w"]:
+            lastw[w] = i
+            readers[w] = []
+        o["dep"] = sorted(dep)
+    succ = [[] for _ in ops]
+    for i, o in enumerate(ops):
+        for d in o["dep"]: succ[d].append(i)
+    if "order" not in PLAN:
+        rnd = np.random.default_rng(1)
+        kinds = {}
+        for i, o in enumerate(ops): kinds.setdefault(o["e"] + (o["w"] + o["r"][1:])[0], []).append(i)
+        kinds = [kinds[k] for k in sorted(kinds)]
+        noise, win = np.zeros(n), 400.0
+        best = schedule(ops, succ, noise, win)
+        for _ in range(TRIES):
+            x, w = noise.copy(), win
+            for _ in range(int(rnd.integers(1, 4))):
+                k = kinds[int(rnd.integers(len(kinds)))] if rnd.random() < 0.6 else [int(rnd.integers(n))]
+                x[k] += rnd.normal() * [500.0, 2000.0, 6000.0][int(rnd.integers(3))]
+            if rnd.random() < 0.03: w = float(rnd.integers(1, 10)) * 100.0
+            r = schedule(ops, succ, x, w)
+            if r[0] <= best[0]: best, noise, win = r, x, w
+        PLAN["order"] = best
+    order = PLAN["order"][1]
+    Q = {"v": g.vector, "a": g.scalar, "p": g.tensor, "g": g, "s": g.sync}
+    cnt = {"v": 0, "a": 0, "p": 0, "g": 0}
+    tok, seen, nd, alltok = {}, {}, 0, {}
+    for i in order:
+        o = ops[i]
+        q = Q[o["e"]]
+        need = {}
+        for d in o["dep"]:
+            if tok[d] is None or (o["e"] == "p" and ops[d]["e"] == "p"): continue
+            s, v = tok[d]
+            need[s] = max(need.get(s, 0), v)
+        for s, v in o["ext"]:
+            need[s] = max(need.get(s, 0), v)
+            alltok[s] = v
+        for s in sorted(need):
+            if seen.get((o["e"], s), 0) < need[s]:
+                q.wait_ge(T.sem[s], need[s])
+                seen[(o["e"], s)] = need[s]
+        ins = o["f"](q)
+        if o["rem"]:
+            tok[i] = None
+        elif o["dma"]:
+            s = "d%d" % nd
+            nd += 1
+            for x in ins: x.then_inc(T.sem[s], 16)
+            tok[i] = (s, 16 * len(ins))
+            alltok[s] = 16 * len(ins)
+        else:
+            cnt[o["e"]] += 1
+            ins.then_inc(T.sem["c" + o["e"]], 1)
+            tok[i] = ("c" + o["e"], cnt[o["e"]])
+            alltok["c" + o["e"]] = cnt[o["e"]]
+    for o in ops:
+        if o["rem"]: alltok["loc"] = alltok.get("loc", 0) + o["rem"]
+    for s in sorted(alltok):
+        if not any(seen.get((e, s), 0) >= alltok[s] for e in Q):
+            g.wait_ge(T.sem[s], alltok[s])
+    return order
+
+
+def build(g, core, rank, T, topo, via, vib):
+    ops = []
+
+    def names(l):
+        return [x for x in l.split() if x]
+
+    def op(e, c, r, w, f, dma=False, lat=0.0, ext=(), t0=0.0, rem=0):
+        r, w = names(r), names(w)
+        w = w + [x for x in r if x[0] == "P" and x[1:].isdigit()]
+        ops.append({"e": e, "c": c, "r": r, "w": w, "f": f, "dma": dma, "lat": lat, "ext": list(ext), "t0": t0, "rem": rem})
+
+    def cyc(n, k=1.0):
+        return 60.0 + max(64.0, n * k) * CY
+
+    def ts(out, in0, s1, s2, o0, o1, r, w, n, k=1.0):
+        if o1 is None: op("v", cyc(n, k), r, w, lambda q: q.tensor_scalar(out, in0, s1, None, o0))
+        else: op("v", cyc(n, k), r, w, lambda q: q.tensor_scalar(out, in0, s1, s2, o0, o1))
+
+    def tt(out, a, b, o, r, w, n, k=2.0):
+        op("v", cyc(n, k), r, w, lambda q: q.tensor_tensor(out, a, b, o))
+
+    def cp(out, a, r, w, n, k=1.0):
+        op("v", cyc(n, k), r, w, lambda q: q.tensor_copy(out, a))
+
+    def ms(out, val, w, n, k=1.0):
+        op("v", cyc(n, k), "", w, lambda q: q.memset(out, val))
+
+    def act(out, a, fn, r, w, n, k=1.0, bias=None, scale=None):
+        kw = {}
+        if bias is not None: kw["bias"] = bias
+        if scale is not None: kw["scale"] = scale
+        op("a", cyc(n, k), r, w, lambda q: q.activation(out, a, fn, **kw))
+
+    def gat(e, out, win, r, w, n):
+        if e == "a": act(out, win, AF.Copy, r, w, n, 1.56)
+        else: cp(out, win, r, w, n, 1.56)
+
+    def mm(l, r, w, start=True, stop=True, each=False):
+        def f(q):
+            for j, (o, a, b, _) in enumerate(l):
+                x = q.matmul(o, a, b, each or (start and j == 0), each or (stop and j == len(l) - 1))
+            return x
+        op("p", sum(max(64, x[3]) for x in l) * PEC + 30.0, r, w, f, lat=60.0)
+
+    def group(bank, n, parts):
+        mm([(P[bank][:, 0:n], T.ZER[:, 0:128], T.JB[:, 0:n], n)], "ZER JB", "P%d A%d" % (bank, bank), True, False)
+        left = [len(parts)]
+
+        def one(l):
+            def f(q):
+                left[0] -= 1
+                for j, (o, a, b, _) in enumerate(l):
+                    x = q.matmul(o, a, b, False, left[0] == 0 and j == len(l) - 1)
+                return x
+            return f
+        return [lambda l=l, r=r: op("p", sum(max(64, x[3]) for x in l) * PEC + 30.0, r + " A%d" % bank, "", one(l), lat=60.0) for l, r in parts]
+
+    def dma(e, l, r, w, lat=2000.0, ext=(), t0=0.0):
+        op(e, 100.0 * len(l), r, w, lambda q: [q.dma_start(o, a) for o, a in l], dma=True, lat=lat, ext=ext, t0=t0)
+
+    def iota(out, pat, base, cm, w, n, fl=True):
+        if fl: op("g", 160 + 2 * n * CY, "", w, lambda q: q.iota(out, pat, base, cm, allow_small_or_imprecise_dtypes=True))
+        else: op("g", 160 + 2 * n * CY, "", w, lambda q: q.iota(out, pat, base, cm))
+
+    def strip(M, k):
+        return M[:, 15 - k:143 - k]
+
+    def ext16(out, M, src, lo, n):
+        return [(out, strip(M, k), src[:, lo + k:lo + 16 * n:16], n) for k in range(16)]
+
+    C = T.cores
+    others = [d for d in range(N) if d != rank]
+    P = [T["P%d" % b] for b in range(8)]
+
+    def send(src, land, hand, route, asem, hsem, wide, r):
+        off = topo.engines(core, C[[d for d in others if route[rank][d] is None][0]])
+        rest = [e for e in topo.engines(core, [c for c in topo.cores_of(core) if c != core][0]) if e not in off]
+        nd = 4 if wide else 2
+        pool = off + rest
+        tr, tot = [], 0
+        for d in [d for d in others if route[rank][d] is None]:
+            rid, pid = topo.addr(C[d], core)
+            tr.append(RemoteDMATransfer(dst_ids=[DstId(rid=rid, pnc=pid)], dma_engine_mask=bits(pool[:nd]), remote_sem=T.sem[asem], src=src[d], dst=land[rank]))
+            pool = pool[nd:]
+            tot += nd
+        for d in [d for d in others if route[rank][d] is not None]:
+            rid, pid = topo.addr(route[rank][d], core)
+            tr.append(RemoteDMATransfer(dst_ids=[DstId(rid=rid, pnc=pid)], dma_engine_mask=bits(pool[-2:]), remote_sem=T.sem[hsem], src=src[d], dst=hand[:]))
+            pool = pool[:-2]
+            tot += 2
+        op("g", 500.0, r + " gq", "gq", lambda q: q.remote_dma_fused(tr, local_sem=T.sem.loc), rem=tot)
+
+    def arrivals(route, s, wide):
+        return (4 if wide else 2) if route[s][rank] is None else len(topo.engines(route[s][rank], core))
+
+    short_all = sum(arrivals(vib, s, False) for s in others)
+    dma("s", [(T.ss[:, 0:32, :], T.nm[:]), (T.ss[:, 32:64, :], T.pl[:]), (T.ss[:, 64:96, :], T.cc[:]), (T.ss[:, 96:128, :], T.nm[:])], "", "ss q1")
+    dma("a", [(T.sf[:], T.fo[:])], "", "sf q2", lat=4000.0)
+    dma("s", [(T.sx[:], T.tx[:])], "", "sx", lat=6000.0, t0=250.0)
+    own = slice(16 * rank, 16 * rank + 16)
+    dma("s", [(T.rs[rank, 0:32, :], T.nm[rank:rank + 1, :]), (T.rs[rank, 32:64, :], T.pl[own, :]), (T.rs[rank, 64:96, :], T.cc[own, :])], "", "rso", t0=700.0)
+    dma("a", [(T.F[own, :], T.fo[own, :]), (T.X[own, :], T.tx[own, :])], "", "F%d X%d" % (rank, rank), t0=300.0)
+
+    PI = T.PK[:, 2:3]
+    iota(PI, [[0, 1]], 0, 1, "PI", 1, False)
+    iota(T.IOT[:], [[1, 256]], 0, 0, "IOT", 256)
+    iota(T.IG[:], [[1, 8], [0, 16]], 0, 0, "IG", 128)
+    iota(T.IK[:], [[0, 16], [1, 16]], 0, 0, "IK", 256)
+    send(T.ss, T.rs, T.hs, vib, "as", "h0", False, "ss PI IOT IG IK")
+    send(T.sf, T.rf, T.hf, via, "af%d" % rank, "h1", True, "sf")
+    send(T.sx, T.rx, T.hx, via, "ax%d" % rank, "h2", True, "sx")
+    op("g", 160 + 2 * V * CY, "gq", "RHO", lambda q: q.iota(T.RHO[:], [[1, 192], [192, 16]], 32, 0, allow_small_or_imprecise_dtypes=True))
+    op("g", 160 + 2 * V * CY, "RHO", "FV", lambda q: q.iota(T.FV[:], [[1, V]], 4096, 0, allow_small_or_imprecise_dtypes=True))
+    col = lambda j: T.CC[:, j:j + 1]
+    cP, cK, cG, cY, cS = 0, 1, 2, 3, 4
+    ts(T.PK[:, 0:1], PI, 15, None, A.bitwise_and, None, "PI", "PK", 1)
+    ts(T.PK[:, 1:2], PI, 4, None, A.arith_shift_right, None, "PI PK", "PK", 1)
+    cp(col(cP), PI, "PI", "c0", 1)
+    cp(T.CC[:, 1:3], T.PK[:, 0:2], "PK", "c1", 1)
+    ts(col(cY), col(cG), 16.0, 15.0, A.mult, A.add, "c1", "c3", 1)
+    ts(col(cS), col(cK), 192.0, -4096.0, A.mult, A.add, "c1", "c4", 1)
+    OH = T.TM2[:, 0:16]
+    ts(OH, T.IK[:, 0:16], col(cK), None, A.is_equal, None, "IK c1", "OH", 16)
+
+    def wcol(j, wts):
+        first = True
+        for ch, x in wts:
+            if first: ts(col(j), T.TM2[:, ch:ch + 1], float(x), None, A.mult, None, "OH", "c%d" % j, 1)
+            else: ts(col(j), T.TM2[:, ch:ch + 1], float(x), col(j), A.mult, A.add, "OH c%d" % j, "c%d" % j, 1)
+            first = False
+    wcol(5, [(CH_HI, 1), (CH_LO, 1)])
+    ts(col(6), T.TM2[:, CH_FR:CH_FR + 1], 4096.0, col(5), A.mult, A.add, "OH c5", "c6", 1)
+    ts(col(7), T.TM2[:, CH_FR:CH_FR + 1], -8192.0, col(5), A.mult, A.add, "OH c5", "c7", 1)
+    ts(col(7), T.TM2[:, CH_FI:CH_FI + 1], 12288.0, col(7), A.mult, A.add, "OH c7", "c7", 1)
+    wcol(8, [(CH_BH, 1), (CH_BL, 1), (CH_FR, 8192), (CH_FI, -8192)])
+    wcol(9, [(CH_FR, -2)])
+    wcol(10, [(CH_LO, 1), (CH_BL, 1), (CH_CL, 1)])
+    wcol(13, [(CH_CH, 1), (CH_CL, 1)])
+    wcol(11, [(CH_HI, 3072), (CH_BH, 3072), (CH_CH, 3072), (CH_FR, 1)])
+    wcol(12, [(CH_FI, 1)])
+    wcol(15, [(CH_FR, -524288), (CH_FI, 524288)])
+    ts(T.ME[:], T.IOT[:, 0:144], col(cY), 8192.0, A.is_equal, A.mult, "IOT c3", "ME", 144)
+    for M, nm_, j in ((T.ML, "ML", 6), (T.MC, "MC", 7), (T.MB, "MB", 8), (T.MX, "MX", 13), (T.MF, "MF", 15), (T.MS, "MS", cS)):
+        ts(M[:], T.IOT[:, 0:144], col(cY), col(j), A.is_equal, A.mult, "IOT c3 c%d" % j, nm_, 144)
+    ts(T.Y1[:, 0:128], T.IOT[:, 0:128], col(cP), None, A.is_equal, None, "IOT c0", "Y1a", 128)
+    cp(T.Y1[:, 128:192], T.Y1[:, 0:64], "Y1a", "Y1", 64)
+    ts(T.Y2[:], T.Y1[:, 0:128], 2.0, None, A.mult, None, "Y1a", "Y2", 128, 0.5)
+    ts(T.YE[:], T.Y1[:, 0:128], 262144.0, None, A.mult, None, "Y1a", "YE", 128, 0.5)
+    ts(T.YM[:], T.Y1[:], -2.0, None, A.mult, None, "Y1a Y1", "YM", 192, 0.5)
+    ts(T.Y4[:], T.Y1[:], 4096.0, None, A.mult, None, "Y1a Y1", "Y4", 192, 0.5)
+    ts(T.SG[:], T.IG[:], col(cG), None, A.is_equal, None, "IG c1", "SG", 128)
+    cp(T.ONE[:], T.SG[:], "SG", "ONE", 128)
+    ts(T.TWO[:], T.SG[:], 2.0, None, A.mult, None, "SG", "TWO", 128)
+    ts(T.BCN[:], T.SG[:], col(5), None, A.mult, None, "SG c5", "BCN", 128)
+    ts(T.OCC[:], T.SG[:], col(9), None, A.mult, None, "SG c9", "OCC", 128)
+    ts(T.TMP[:, 0:128], T.IK[:, 0:128], col(cK), -1.0, A.is_lt, A.mult, "IK c1", "TMP", 128)
+    tt(T.TMP[:, 0:128], T.TMP[:, 0:128], T.SG[:], A.mult, "TMP SG", "TMP", 128)
+    ts(T.TMP[:, 128:256], T.Y1[:, 0:128], 512.0, None, A.mult, None, "Y1a TMP", "TMP", 128)
+    tt(T.TRI[:], T.TMP[:, 0:128], T.TMP[:, 128:256], A.add, "TMP", "TRI", 128)
+    ms(T.ZER[:], 0.0, "ZER", 208, 0.5)
+    ts(T.TMP[:], T.IK[:], 0.0, 0.5, A.not_equal, A.mult, "IK TMP", "TMP", 256)
+    ts(T.TAU[:], T.IK[:], 0.0, None, A.is_equal, None, "IK", "TAU", 256)
+    op("v", cyc(256), "TMP TAU", "THR", lambda q: q.tensor_tensor_scan(T.THR[:], T.TMP[:], T.TAU[:], 0.0, A.mult, A.add))
+    tt(T.TM2[:, 16:32], T.THR[:, 0:16], OH, A.mult, "THR OH", "PW", 16)
+    op("v", cyc(16), "PW ZER", "PW2", lambda q: q.tensor_tensor_scan(T.TM2[:, 32:48], T.TM2[:, 16:32], T.ZER[:, 0:16], 0.0, A.add, A.add))
+    ts(T.POW[:], T.SG[:], T.TM2[:, 47:48], None, A.mult, None, "SG PW2", "POW", 128)
+    ts(T.THR[:], T.THR[:], 2.0, 2.0, A.mult, A.add, "THR", "THR", 256)
+    ts(T.THR[:], T.THR[:], col(12), -4.0, A.mult, A.add, "THR c12", "THR", 256)
+    ts(T.JB[:], T.IOT[:], -256.0, None, A.add, None, "IOT", "JB", 256)
+    ts(T.JF[:], T.IOT[:], -256.0, None, A.add, None, "IOT", "JF", 256)
+    ts(T.TAU[:], T.IOT[:], 257.0, None, A.add, None, "IOT TAU", "TAU", 256)
+    ts(T.JL[:], T.IOT[:, 0:192], 16.0, col(cK), A.mult, A.add, "IOT c1", "JL", 192)
+    ts(T.DU1[:], T.JL[:, 0:16], -1024.0, None, A.add, None, "JL", "DU1", 16)
+    ts(T.DU2[:], T.JL[:, 0:16], 3840.0, None, A.add, None, "JL", "DU2", 16)
+    ts(T.DU3[:], T.JL[:], 3072.0, None, A.add, None, "JL", "DU3", 192)
+    ts(T.VH[:], T.JL[:], -1.0, None, A.mult, None, "JL", "VH", 192)
+    ts(T.FD[:], T.JL[:], -1.0, None, A.mult, None, "JL", "FD", 192)
+    tt(T.VL[:], T.FD[:], T.VH[:], A.subtract, "FD VH", "VL", 192)
+    for t in range(1, TV + 1):
+        ks = (S * t % V) % 16
+        ts(T.MK[:, 2 * t - 2:2 * t - 1], col(cK), float(ks), None, A.is_lt, None, "c1", "MK%d" % t, 1)
+        ts(T.MK[:, 2 * t - 1:2 * t], col(cK), float(ks), None, A.is_ge, None, "c1 MK%d" % t, "MK%d" % t, 1)
+    ms(T.W[:, 0:V], 0.0, "Wd Wb", V, 0.5)
+    ts(T.W[:, V:3328], T.IOT[:], col(10), col(11), A.mult, A.add, "IOT c10 c11", "Wt", 256)
+    ms(T.PG[:, 3328:3584], 0.0, "PGt", 256, 0.5)
+    ms(T.BC[:], 0.0, "BCa BCb", 208, 0.5)
+    ms(T.BS[:], 0.0, "BS", 16)
+    ms(T.ZJ[:], -8192.0, "ZJ", 192)
+    dma("s", [(T.LW[0:128:16, 0:V], T.ZJ[:]), (T.LX[0:128:16, 0:V], T.ZJ[:])], "ZJ", "LW LX", t0=1500.0)
+
+    TS_ = 8000.0
+    dma("s", [(T.CP[:, 0:192], T.rs[:, 64:96, :]), (T.CP[:, 192:384], T.rs[:, 32:64, :]),
+              (T.NI[0:112, :], T.rs[1:8, 0:32, :]), (T.NI[112:128, :], T.rs[0, 0:32, :])], "rso", "CP NI", ext=[("as", short_all)], t0=TS_)
+    for k, s in enumerate(others):
+        sl = slice(16 * s, 16 * s + 16)
+        dma("s", [(T.F[sl, :], T.rf[s])], "CP", "F%d" % s, ext=[("af%d" % s, arrivals(via, s, True))], t0=16000.0)
+    for k, s in enumerate(others):
+        sl = slice(16 * s, 16 * s + 16)
+        dma("s", [(T.X[sl, :], T.rx[s])], "CP", "X%d" % s, ext=[("ax%d" % s, arrivals(via, s, True))], t0=22000.0)
+    Fall = " ".join("F%d" % s for s in range(N)) + " "
+    Xall = " ".join("X%d" % s for s in range(N)) + " "
+    ts(T.IA[:], T.CP[:], 15, None, A.bitwise_and, None, "CP", "IA", 384)
+    ts(T.IB[:], T.CP[:], 4, None, A.arith_shift_right, None, "CP", "IB", 384)
+    ts(T.FA[:], T.IA[:], 192.0, None, A.mult, None, "IA", "FA", 384)
+    tt(T.RF[:], T.FA[:], T.IB[:], A.add, "FA IB", "RF", 384)
+    cp(T.RRU[:], T.RF[:, 0:192], "RF", "RRU", 192)
+    act(T.BH[:, 0:192], T.RF[:, 0:192], AF.Copy, "RF", "BH", 192)
+    tt(T.BL[:, 0:192], T.RF[:, 0:192], T.BH[:, 0:192], A.subtract, "RF BH", "BL", 192)
+    cp(T.BH[:, 192:384], T.CP[:, 0:192], "CP", "CH", 192)
+    tt(T.BL[:, 192:384], T.CP[:, 0:192], T.BH[:, 192:384], A.subtract, "CP CH", "CL", 192)
+    ts(T.FB[:], T.CP[:, 192:384], 0.0, 8192.0, A.is_lt, A.mult, "CP", "FB", 192)
+    tt(T.FB[:], T.FB[:], T.RF[:, 192:384], A.add, "FB RF", "FB", 192)
+    ts(T.PU[:], T.FB[:], 3072.0, None, A.min, None, "FB", "PU", 192)
+
+    def rows(ch, src, t, o=0):
+        if t == 0: return [(T.W[ch:128:16, 0:V], src[:, o:o + 192])]
+        return [(T.W[ch:128 - 16 * t:16, 0:V], src[16 * t:128, o:o + 192]), (T.W[128 - 16 * t + ch:128:16, 0:V], src[0:16 * t, o:o + 192])]
+    dma("a", rows(CH_BH, T.BH, 0) + rows(CH_BL, T.BL, 0), "BH BL", "Wb")
+    cp(T.FC[:], T.NI[:], "NI", "FC", 192)
+    act(T.HI[:], T.FC[:], AF.Copy, "FC", "HI", 192)
+    tt(T.LW2[:], T.FC[:], T.HI[:], A.subtract, "FC HI", "LO2", 192)
+    dma("a", rows(CH_HI, T.HI, 0) + rows(CH_LO, T.LW2, 0), "HI LO2", "Wd")
+    mm(ext16(P[3][:, 0:192], T.ML, T.W, 0, 192), "Wd Wb ML", "P3")
+    act(T.NF[:], P[3][:, 0:192], AF.Copy, "P3", "NF", 192)
+    ts(T.NU[:], P[3][:, 0:192], 0.0, None, A.add, None, "P3", "NU", 192)
+    act(T.N4[:], T.NF[:], AF.Identity, "NF", "N4", 192, bias=4096.0)
+
+    def pgather(eng):
+        for j in range(6):
+            gat(eng[j], T.PG[:, 256 + 512 * j:768 + 512 * j], T.W[:, 0:3328].indirect(T.PU[:, 32 * j:32 * j + 32]), "Wd Wb Wt PU", "PG%d" % j, 512)
+    PGall, TRall = " PG0 PG1 PG2 PG3 PG4 PG5 ", " TR0 TR1 TR2 TR3 TR4 TR5 "
+    pgather(ENG["P0"])
+    for j in range(6):
+        act(T.ICW[:, 0:V].indirect(T.RRU[:, 32 * j:32 * j + 32]), T.RHO[:, 512 * j:512 * j + 512], AF.Silu, "RHO RRU", "ICW", 512, 3.8)
+    l = []
+    for t in range(1, TV):
+        l += [(T.ICF[0:128 - 16 * t, 192 * t - 192:192 * t], T.ICW[16 * t:128:16, :]), (T.ICF[128 - 16 * t:128, 192 * t - 192:192 * t], T.ICW[0:16 * t:16, :])]
+    dma("a", l, "ICW", "ICF")
+    cp(T.ICI[:], T.ICF[:], "ICF", "ICI", 576)
+    ts(T.ICU[:], T.ICI[:], -32.0, None, A.add, None, "ICI", "ICU", 576)
+    mm(ext16(P[4][:, 0:192], T.MB, T.PG, 256, 192), PGall + "MB", "P4")
+    tt(T.FC[:], P[4][:, 0:192], T.DU3[:], A.min, "P4 DU3 FC", "FC", 192, 1.0)
+    cp(T.LO[:], T.FC[:], "FC", "LO", 192)
+    ts(T.PU[:], P[4][:, 0:192], 3072.0, None, A.min, None, "P4", "PU", 192)
+    for j in range(3):
+        cp(T.LW[:, 0:6144].indirect(T.LO[:, 32 * j:32 * j + 32]), T.FV[:, 512 * j:512 * j + 512], "FV LO", "LW", 512, 3.8)
+        j += 3
+        act(T.LX[:, 0:6144].indirect(T.LO[:, 32 * j:32 * j + 32]), T.FV[:, 512 * j:512 * j + 512], AF.Silu, "FV LO", "LX", 512, 3.8)
+    dma("s", [(T.FA[:, 0:192], T.LW[0:128:16, 0:V]), (T.FA[:, 192:384], T.LX[0:128:16, 0:V])], "LW LX", "FA")
+    tt(T.FB[:], T.FA[:, 0:192], T.FA[:, 192:384], A.max, "FA", "FB", 192)
+    cp(T.NI[:], T.FB[:], "FB", "NI", 192)
+    ts(T.LU[:], T.NI[:], -4096.0, 0.0, A.add, A.max, "NI", "LU0 LU1 LU2", 192)
+    cp(T.CA[:], T.NI[:], "NI", "CA", 192)
+
+    for t in range(1, TV + 1):
+        s0 = S * t % V
+        cs = s0 // 16
+        last = t == TV
+        if last: dma("s", rows(CH_BH, T.VH, 0) + rows(CH_BL, T.VL, 0), "VH VL", "Wb")
+        else: dma("s", rows(CH_BH, T.BH, t) + rows(CH_BL, T.BL, t) + rows(CH_CH, T.BH, t, 192) + rows(CH_CL, T.BL, t, 192), "BH BL CH CL", "Wb")
+        for j in range(6):
+            gat(ENG["G%d" % t][j], T.G2[:, 512 * j:512 * j + 512], T.F[:, 0:V].indirect(T.NU[:, 32 * j:32 * j + 32]), Fall + "NU", "G%d" % j, 512)
+        parts = [(ext16(P[2][:, 64 * h:64 * h + 64], T.ME, T.NE, 1024 * h, 64), "ME NE%d NE%d" % (2 * h, 2 * h + 1)) for h in range(3)]
+        parts.append(([(P[2][:, 0:192], T.YE[:], T.EQ[:], 192)], "YE EQ"))
+        if t > 1: parts.append((ext16(P[2][:, 0:192], T.MF, T.TR, 0, 192), "MF" + TRall))
+        parts = group(2, 192, parts)
+        for j in range(6):
+            c = slice(512 * j, 512 * j + 512)
+            b = j % 2
+            tt(T.D[:, c], T.F[:, 0:V].indirect(T.LU[:, 32 * j:32 * j + 32]), T.G2[:, c], A.subtract, Fall + "LU%d G%d" % (j // 2, j), "D%d" % j, 512, 1.56)
+            mm([(P[b][:], T.YM[:, 16 * t:16 * t + 128], T.X[:, c], 512), (P[b][:], T.Y2[:], T.G2[:, c], 512), (P[b][:], T.Y1[:, 0:128], T.D[:, c], 512)],
+               Xall + "YM Y2 Y1a G%d D%d" % (j, j), "P%d" % b)
+            tt(T.PR[:, c], P[b][:], T.D[:, c], A.mult, "P%d D%d" % (b, j), "PR%d" % j, 512, 1.0)
+            if ENG["S%d" % t][j] == "v": ts(T.NE[:, c], T.PR[:, c], 0.0, 0.5, A.is_lt, A.subtract, "PR%d" % j, "NE%d" % j, 512, 0.5)
+            else: act(T.NE[:, c], T.PR[:, c], AF.Sign, "PR%d" % j, "NE%d" % j, 512, bias=-0.5, scale=-1.0)
+        if t == 1: tt(T.EQ[:], T.CA[:], T.N4[:], A.is_equal, "CA N4", "EQ", 192)
+        for x in parts: x()
+        tt(P[2][:, 256:448], P[2][:, 0:192], T.CA[:], A.min, "CA", "P2 A2", 192, 1.0)
+        tt(T.ZJ[:], P[2][:, 256:448], T.NF[:], A.max, "P2 NF", "ZJ", 192, 1.0)
+        act(T.HI[:], T.ZJ[:], AF.Copy, "ZJ", "HI", 192)
+        ts(T.FR[:], T.ZJ[:], 4096.0, None, A.is_lt, None, "ZJ", "FR", 192)
+        tt(T.LW2[:], T.ZJ[:], T.HI[:], A.subtract, "ZJ HI", "LO2", 192)
+        dma("s", rows(CH_FR, T.FR, 0) + rows(CH_HI, T.HI, 0) + rows(CH_LO, T.LW2, 0), "FR HI LO2", "Wd")
+        if not last:
+            mm([(P[3][:, 0:192], T.Y1[:, 16:144], T.HI[:], 192), (P[3][:, 0:192], T.Y1[:, 16:144], T.LW2[:], 192), (P[3][:, 0:192], T.Y4[:, 16:144], T.FR[:], 192)],
+               "Y1a Y1 Y4 HI LO2 FR", "P3")
+            ts(T.NU[:], P[3][:, 0:192], -4096.0, None, A.add, None, "P3", "NU", 192)
+            act(T.N4[:], P[3][:, 0:192], AF.Copy, "P3", "N4", 192)
+            act(T.NF[:], T.N4[:], AF.Identity, "N4", "NF", 192, bias=-4096.0)
+            for j in range(3):
+                for h in (2 * j, 2 * j + 1):
+                    o = 192 * t - 192 + 32 * h
+                    gat(ENG["T%d" % t][h], T.TR[:, 512 * h:512 * h + 512], T.W[:, 0:3328].indirect(T.ICU[:, o:o + 32]), "Wd Wb Wt ICU", "TR%d" % h, 512)
+                mm(ext16(P[4][:, 64 * j:64 * j + 64], T.ML, T.TR, 1024 * j, 64), "ML TR%d TR%d" % (2 * j, 2 * j + 1), "P4")
+                ts(T.LU[:, 64 * j:64 * j + 64], P[4][:, 64 * j:64 * j + 64], -4096.0, None, A.add, None, "P4", "LU%d" % j, 64)
+            tt(T.EQ[:], P[4][:, 0:192], T.N4[:], A.is_equal, "P4 N4", "EQ", 192, 1.0)
+            act(T.CA[:], P[4][:, 0:192], AF.Copy, "P4", "CA", 192)
+        else:
+            for q in range(N):
+                for b in range(2):
+                    o = P[0][0:96, 32 * q + 16 * b:32 * q + 16 * b + 16]
+                    y = slice(64 + 16 * q, 80 + 16 * q)
+                    mm([(o, T.HI[:, b:192:2], T.Y1[:, y], 16), (o, T.LW2[:, b:192:2], T.Y1[:, y], 16), (o, T.FR[:, b:192:2], T.Y4[:, y], 16)], "Y1a Y1 Y4 HI LO2 FR", "P0")
+            act(T.TN[0:96, :], P[0][0:96, 0:256], AF.Identity, "P0", "TN", 256, bias=-4096.0)
+            dma("s", [(T.on[q], T.TN[0:96, 32 * q:32 * q + 32]) for q in others], "TN", "on")
+            dma("s", [(T.yn[rank:rank + 1, :], T.TN[0:96, 32 * rank:32 * rank + 32])], "TN", "yno")
+            send(T.on, T.rn, T.hn, vib, "an", "h3", False, "on")
+        pgather(ENG["P%d" % t])
+        ts(T.FS[:], T.MK[:, 2 * t - 2:2 * t], T.FR[:, cs:cs + 1], None, A.mult, None, "MK%d FR" % t, "FS", 2)
+        for M, nm_, bk in ((T.ONE, "ONE", 5), (T.TRI, "TRI", 6)):
+            mm([(P[bk][:, a:b_], M[:], src, b_ - a) for a, b_, src in ((0, cs, T.FR[:, 0:cs]), (cs + 2, 193, T.FR[:, cs + 1:192]), (cs, cs + 2, T.FS[:]))],
+               nm_ + " FR FS", "P%d" % bk, each=True)
+        op("v", cyc(193), "P5 ZER", "U P5", lambda q: q.tensor_tensor_scan(T.U[:, 0:193], P[5][:, 0:193], T.ZER[:, 0:193], -256.0, A.add, A.add))
+        ts(T.DB[:, 0:1], T.U[:, cs:cs + 1], 256.0, T.U[:, 192:193], A.add, A.min, "U", "DB0", 1)
+        ts(T.DB[:, 1:2], T.U[:, cs:cs + 1], T.DB[:, 0:1], None, A.subtract, None, "U DB0", "DB1", 1)
+        ts(T.BC[:, cs + 1:193], T.U[:, cs + 1:193], T.DB[:, 0:1], None, A.subtract, None, "U DB0", "BCb", 192 - cs)
+        ts(T.BC[:, 0:cs + 1], T.U[:, 0:cs + 1], T.DB[:, 1:2], None, A.min, None, "U DB1", "BCa", cs + 1)
+        ts(T.U[:, cs + 1:193], T.U[:, cs + 1:193], T.DB[:, 0:1], None, A.subtract, None, "U DB0", "U", 192 - cs)
+        tt(T.CU[:, 0:193], P[6][:, 0:193], T.U[:, 0:193], A.add, "P6 U", "CU", 193, 1.0)
+        tt(T.TM2[:, 48:61], T.BC[:, 15:208:16], T.TM2[:, 0:13], A.mult, "BCa BCb OH", "TH", 13)
+        op("v", cyc(13), "TH", "c14", lambda q: q.tensor_reduce(col(14), T.TM2[:, 48:61], AxisListType.X, A.add))
+        mm(ext16(P[5][:, 0:13], T.ME, T.BC, 0, 13), "ME BCa BCb", "P5")
+        act(T.BS[:, 0:13], P[5][:, 0:13], AF.Copy, "P5", "BS", 13, scale=1.0 / 131072)
+        ts(T.L1[:], T.JB[:], col(14), None, A.is_ge, None, "JB c14", "L1", 256, 0.5)
+        mm(ext16(P[3][:, 256:272], T.ME, T.L1, 0, 16), "ME L1", "P3")
+        ts(T.AU[:], P[3][:, 256:272], 1.0 / 8192, None, A.mult, None, "P3", "AU", 16)
+        ts(T.AB[:], P[3][:, 256:272], 16.0, None, A.mult, None, "P3", "AB", 16)
+        tt(T.L2[:], T.BS[:, 0:16].indirect(T.AU[:]), T.JF[:], A.is_le, "BS AU JF", "L2", 256, 1.56)
+        mm([(P[6][:, 0:16], T.Y1[:, 0:128], T.AB[:], 16)] + ext16(P[6][:, 0:16], T.ME, T.L2, 0, 16), "ME Y1a AB L2", "P6")
+        ts(T.KU[:], P[6][:, 0:16], 1.0 / 8192, None, A.mult, None, "P6", "KU", 16)
+        ts(T.KB[:, 0:16], P[6][:, 0:16], 1.0 / 8192, None, A.mult, None, "P6", "KB", 16)
+        ts(T.KB[:, 16:32], P[6][:, 0:16], (cs + 0.5) * 8192, -1.0, A.is_gt, A.mult, "P6", "KC", 16)
+        tt(T.SE[:], T.CU[:, 0:193].indirect(T.KU[:]), T.TAU[:], A.is_equal, "CU KU TAU", "SE", 256, 1.56)
+        mm([(P[6][:, 0:16], T.Y1[:, 0:128], T.KB[:, 0:16], 16), (P[6][:, 0:16], T.Y1[:, 0:128], T.KB[:, 16:32], 16)] + ext16(P[6][:, 0:16], T.MS, T.SE, 0, 16), "MS Y1a KB KC SE", "P6")
+        tt(T.RT[:], P[6][:, 0:16], T.DU1[:], A.min, "P6 DU1", "RT", 16)
+        ts(T.RU[:], T.RT[:], 4096.0, None, A.add, None, "RT", "RU", 16)
+        gat("a", T.Z[:], T.W[:, 0:3328].indirect(T.RU[:]), "Wd Wb Wt RU", "Z", 256)
+        mm([(P[7][:, 0:256], T.BCN[:], T.Z[:], 256)], "BCN Z", "P7")
+        mm(ext16(P[6][:, 0:16], T.ML, T.Z, 0, 16), "ML Z", "P6")
+        cp(T.NB[:], P[7][:, 0:256], "P7", "NB", 256)
+        ts(T.NL[:], P[6][:, 0:16], -4096.0, None, A.add, None, "P6", "NL", 16)
+        ts(T.NLU[:], P[6][:, 0:16], -4096.0, None, A.add, None, "P6", "NLU", 16)
+        if not last:
+            mm(ext16(P[5][:, 0:16], T.MX, T.Z, 0, 16), "MX Z", "P5")
+            ts(T.NPU[:], P[5][:, 0:16], 0.0, None, A.add, None, "P5", "NPU", 16)
+        gat("a", T.O[:], T.PG[:, 256:3584].indirect(T.NLU[:]), PGall + "PGt NLU", "O", 256)
+        for m in range(16):
+            ts(T.E[:, m, 0:256 - 16 * m], T.NB[:, 16 * m:256], T.NL[:, m:m + 1], None, A.is_equal, None, "NB NL", "E%d" % m, 256 - 16 * m, 0.5)
+        parts = [([(P[7][:, 0:256], T.OCC[:], T.O[:], 256)], "OCC O")]
+        for h in range(5):
+            parts.append(([(P[7][:, 16 * m + 16:256], T.TWO[:], T.E[:, m, 16:256 - 16 * m], 240 - 16 * m) for m in range(3 * h, 3 * h + 3)],
+                          "TWO " + " ".join("E%d" % m for m in range(3 * h, 3 * h + 3))))
+        parts.append(([(P[7][:, 0:256], T.POW[:], T.E[:, :, 0:16], 256)], "POW " + " ".join("E%d" % m for m in range(16))))
+        for x in group(7, 256, parts): x()
+        tt(T.WI[:], P[7][:, 0:256], T.THR[:], A.is_lt, "THR", "WI P7 A7", 256, 1.0)
+        if not last:
+            tt(T.TR[:, 0:3328].indirect(T.NPU[:]), T.Z[:], T.WI[:], A.add, "Z WI NPU", TRall, 256, 3.8)
+        mm(ext16(P[6][:, 0:16], T.MC, T.Z, 0, 16), "MC Z", "P6", True, False)
+        mm(ext16(P[6][:, 0:16], T.MC, T.WI, 0, 16), "MC WI", "P6", False, True)
+        tt(T.RT[:], P[6][:, 0:16], T.DU2[:], A.max, "P6 DU2", "RT", 16)
+        ts(T.QU[:], T.RT[:], -3840.0, None, A.add, None, "RT", "QU", 16)
+        tt(T.PG[:, 0:3584].indirect(T.QU[:]), T.Z[:], T.WI[:], A.add, "Z WI QU", PGall + "PGt", 256, 3.8)
+        mm(ext16(P[7][:, 256:448], T.MB, T.PG, 256, 192), "MB" + PGall, "P7")
+        if not last: ts(T.PU[:], P[7][:, 256:448], 3072.0, None, A.min, None, "P7", "PU", 192)
+        else: ts(T.YP[:], P[7][:, 256:448], -1.0, -1.0, A.mult, A.max, "P7", "YP", 192)
+
+    dma("s", [(T.op[:], T.YP[:])], "YP", "op")
+    dma("a", [(T.yp[own, :], T.YP[own, :])], "YP", "ypo")
+    send(T.op, T.rp, T.hp, vib, "ap", "h4", False, "op")
+    ln, lp = [], []
+    if rank > 0:
+        ln.append((T.yn[0:rank, :], T.rn[0:rank]))
+        lp.append((T.yp[0:16 * rank, :], T.rp[0:rank]))
+    if rank < N - 1:
+        ln.append((T.yn[rank + 1:N, :], T.rn[rank + 1:N]))
+        lp.append((T.yp[16 * rank + 16:128, :], T.rp[rank + 1:N]))
+    dma("s", ln, "op yno", "yn", ext=[("an", short_all)])
+    dma("s", lp, "yn ypo", "yp", ext=[("ap", short_all)])
+    return ops
+
+
+ENG = {"P0": "avvavv", "G1": "aaaaaa", "G2": "aaaaaa", "G3": "aaaaaa", "G4": "aaaaaa", "S1": "aaaaav", "S2": "aaaaav", "S3": "aaaaav", "S4": "aaaaav",
+       "T1": "vavaaa", "T2": "vavaaa", "T3": "vavaaa", "P1": "aaaaaa", "P2": "aaaaaa", "P3": "aaaaaa", "P4": "avavav"}

@@ -1,6 +1,6 @@
 import numpy as np
 from concourse.bass import DstId, RemoteDMATransfer
-from concourse.mybir import AluOpType as A, ActivationFunctionType as AF, AxisListType
+from concourse.mybir import AluOpType as A, ActivationFunctionType as AF
 
 N, V, S, TV = 8, 3072, 745, 4
 f32, bf, i32, u16 = "float32", "bfloat16", "int32", "uint16"
@@ -10,43 +10,45 @@ def _sb(n, d):
     return ("sbuf", [128, n], d)
 
 
-SCRATCH = {
-    "sx": ("dram", [8, 128, 384], bf), "sf": ("dram", [8, 128, 384], bf), "ss": ("dram", [8, 128, 96], i32),
-    "rx": ("dram", [8, 128, 384], bf), "rf": ("dram", [8, 128, 384], bf), "rs": ("dram", [8, 128, 96], i32),
-    "hx": ("dram", [128, 384], bf), "hf": ("dram", [128, 384], bf), "hs": ("dram", [128, 96], i32),
-    "on": ("dram", [8, 128, 24], f32), "op": ("dram", [8, 128, 24], f32),
-    "rn": ("dram", [8, 128, 24], f32), "rp": ("dram", [8, 128, 24], f32),
-    "hn": ("dram", [128, 24], f32), "hp": ("dram", [128, 24], f32),
-    "X": _sb(V, bf), "F": _sb(V, bf), "G2": _sb(V, bf), "D": _sb(V, bf), "PR": _sb(V, bf), "NE": _sb(V, bf),
-    "W": _sb(3328, bf), "TR": _sb(3328, bf), "PG": _sb(3584, bf),
-    "RHO": _sb(V, f32), "FV": _sb(V, f32), "ICW": _sb(V, f32), "LW": _sb(6144, f32), "LX": _sb(6144, f32),
+MSG = {"f": (384, bf, True), "0": (96, bf, False), "x": (384, bf, True), "4": (96, bf, False), "2": (48, f32, False), "3": (24, f32, False),
+       "n": (24, f32, False), "p": (24, f32, False)}
+SCRATCH = {}
+for _m, (_n, _d, _w) in MSG.items():
+    SCRATCH["s" + _m] = ("dram", [8, 128, _n], _d)
+    SCRATCH["r" + _m] = ("dram", [8, 128, _n], _d)
+    SCRATCH["h" + _m] = ("dram", [128, _n], _d)
+SCRATCH.update({
+    "X": _sb(V, bf), "F": _sb(TV * V, bf), "G2": _sb(V, bf), "D": _sb(V, bf), "PR": _sb(V, bf), "NE": _sb(V, bf),
+    "W": _sb(3344, bf), "TR": _sb(3328, bf), "PG": _sb(2 * 3584, bf),
+    "RHO": _sb(V, f32), "FV": _sb(1536, f32), "ICW": _sb(V, f32), "LW": _sb(6144, f32), "LX": _sb(6144, f32),
     "E": ("sbuf", [128, 16, 256], bf),
-    "PK": _sb(4, i32), "CC": _sb(32, f32), "IOT": _sb(256, f32), "IG": _sb(128, f32), "IK": _sb(256, f32),
-    "JL": _sb(192, f32), "TMP": _sb(256, f32), "TM2": _sb(256, f32), "SG": _sb(128, f32),
-    "ME": _sb(144, bf), "ML": _sb(144, bf), "MC": _sb(144, bf), "MB": _sb(144, bf), "MX": _sb(144, bf), "MS": _sb(144, bf),
-    "Y1": _sb(192, bf), "Y2": _sb(128, bf), "YM": _sb(192, bf), "Y4": _sb(192, bf), "YE": _sb(128, bf),
-    "ONE": _sb(128, bf), "TRI": _sb(128, bf), "BCN": _sb(128, bf), "POW": _sb(128, bf), "TWO": _sb(128, bf), "OCC": _sb(128, bf),
+    "PK": _sb(24, i32), "CC": _sb(32, f32), "IOT": _sb(512, f32), "IG": _sb(128, f32), "IK": _sb(256, f32),
+    "JL": _sb(192, f32), "TMP": _sb(256, f32), "TM2": _sb(64, f32), "SG": _sb(128, bf), "MM": _sb(11 * 144, bf),
+    "Y1": _sb(128, bf), "Y2": _sb(128, bf), "YM": _sb(128, bf), "YE": _sb(128, bf), "YH": _sb(128, bf), "YR": _sb(128, bf),
+    "TRI": _sb(128, bf), "BCN": _sb(128, bf), "POW": _sb(128, bf), "TWO": _sb(128, bf), "OCC": _sb(128, bf),
     "ZER": _sb(208, bf), "JB": _sb(256, bf), "JF": _sb(256, f32), "TAU": _sb(256, f32), "THR": _sb(256, f32),
-    "DU1": _sb(16, f32), "DU2": _sb(16, f32), "MF": _sb(144, bf), "DU3": _sb(192, f32), "MK": _sb(8, bf), "VH": _sb(192, bf), "VL": _sb(192, bf),
-    "CP": _sb(384, i32), "NI": _sb(192, i32), "IA": _sb(384, i32), "IB": _sb(384, i32), "FA": _sb(384, f32), "RF": _sb(384, f32),
-    "FB": _sb(192, f32), "FC": _sb(192, f32), "FD": _sb(192, f32),
-    "RRU": _sb(192, u16), "BH": _sb(384, bf), "BL": _sb(384, bf), "ICF": _sb(576, f32), "ICI": _sb(576, i32), "ICU": _sb(576, u16),
-    "NF": _sb(192, f32), "N4": _sb(192, f32), "NU": _sb(192, u16), "LU": _sb(192, u16), "PU": _sb(192, u16), "LO": _sb(192, u16),
-    "CA": _sb(192, f32), "EQ": _sb(192, bf), "ZJ": _sb(192, f32),
+    "DU1": _sb(16, f32), "DU2": _sb(16, f32), "DU3": _sb(192, f32), "MK": _sb(8, bf), "VK": _sb(384, bf),
+    "CP": _sb(576, i32), "IA": _sb(768, i32), "KA": _sb(768, bf), "NH": _sb(384, bf), "RP": _sb(384, u16),
+    "FA": _sb(384, f32), "FC": _sb(192, f32), "NI": _sb(192, i32), "EM": _sb(192, bf),
+    "ICF": _sb(192, f32), "ICU": _sb(192, u16),
+    "NF": _sb(192, f32), "NU": _sb(192, u16), "LU": _sb(192, u16), "LO": _sb(192, u16),
+    "EQ": _sb(192, bf), "O1": _sb(256, bf), "OU": _sb(16, u16),
     "HI": _sb(192, bf), "LW2": _sb(192, bf), "FR": _sb(192, bf), "FS": _sb(2, bf),
-    "U": _sb(200, f32), "DB": _sb(2, f32), "BC": _sb(208, bf), "CU": _sb(200, f32), "BS": _sb(16, f32),
+    "U": _sb(200, f32), "DB": _sb(2, f32), "BC": _sb(210, bf), "CU": _sb(200, f32), "BS": _sb(16, f32),
     "L1": _sb(256, bf), "L2": _sb(256, bf), "SE": _sb(256, bf), "AU": _sb(16, u16), "AB": _sb(16, bf), "KU": _sb(16, u16),
     "KB": _sb(32, bf), "RT": _sb(16, f32), "RU": _sb(16, u16), "Z": _sb(256, bf), "O": _sb(256, bf),
-    "NB": _sb(256, u16), "NL": _sb(16, f32), "NLU": _sb(16, u16), "NPU": _sb(16, u16), "WI": _sb(256, bf),
+    "NB": _sb(256, u16), "NLU": _sb(32, u16), "WI": _sb(256, bf),
     "QU": _sb(16, u16), "YP": _sb(192, f32), "TN": _sb(256, f32),
-}
+})
 for _b in range(8):
     SCRATCH["P%d" % _b] = ("psum", [128, 512], f32)
-NDMA = 64
-SEMAPHORES = (["cv", "ca", "cp", "cg", "loc", "as", "an", "ap", "h0", "h1", "h2", "h3", "h4"]
+NDMA = 72
+SEMAPHORES = (["cv", "ca", "cp", "cg", "loc"] + ["h" + m for m in MSG] + ["a" + m for m in MSG if not MSG[m][2]]
               + ["af%d" % s for s in range(8)] + ["ax%d" % s for s in range(8)] + ["d%d" % k for k in range(NDMA)])
-CH_HI, CH_LO, CH_FR, CH_FI, CH_BH, CH_BL, CH_CH, CH_CL = 0, 1, 2, 3, 4, 5, 6, 7
-CY, PEC = 1.04, 0.52
+CH_HI, CH_LO, CH_FR, CH_FI, CH_K, CH_A = 0, 1, 2, 3, 4, 5
+STRIPS = ["ME", "MA", "MB", "MC", "MF", "ML", "MN", "MO", "MS", "MX", "MY"]
+FREE = 3328
+CY, PEC, FIX = 0.9, 0.45, 55.0
 
 
 def routes(T, topo):
@@ -73,17 +75,18 @@ def bits(l):
     return sum(1 << e for e in l)
 
 
+def arrival(m, s):
+    return "a%s%d" % (m, s) if MSG[m][2] else "a" + m
+
+
 def helper(g, core, T, topo, s, d, short):
     rid, pid = topo.addr(T.cores[d], core)
-    m = topo.mask(core, T.cores[d])
-    n = len(topo.engines(core, T.cores[d]))
-    steps = [("h1", T.hf, T.rf, "af%d" % s), ("h2", T.hx, T.rx, "ax%d" % s)]
-    if short:
-        steps = [("h0", T.hs, T.rs, "as")] + steps + [("h3", T.hn, T.rn, "an"), ("h4", T.hp, T.rp, "ap")]
-    for sem, src, dst, rs in steps:
-        g.wait_ge(T.sem[sem], 2)
-        g.remote_dma(dst[s], src[:], T.sem[rs], T.sem.loc, pid, rid, m)
-    g.wait_ge(T.sem.loc, n * len(steps))
+    mask = topo.mask(core, T.cores[d])
+    steps = [m for m in MSG if short or MSG[m][2]]
+    for m in steps:
+        g.wait_ge(T.sem["h" + m], 2)
+        g.remote_dma(T["r" + m][s], T["h" + m][:], T.sem[arrival(m, s)], T.sem.loc, pid, rid, mask)
+    g.wait_ge(T.sem.loc, len(topo.engines(core, T.cores[d])) * len(steps))
 
 
 def rank_program(g, core, T, topo):
@@ -100,35 +103,40 @@ def rank_program(g, core, T, topo):
 
 
 PLAN = {}
-TRIES = 1500
+TRIES = 3000
 
 
 def schedule(ops, succ, noise, win):
-    n, LAT = len(ops), 150.0
+    n, LAT = len(ops), 110.0
     pr = [0.0] * n
     for i in range(n - 1, -1, -1):
-        pr[i] = ops[i]["c"] + ops[i]["lat"] + max([pr[j] + LAT for j in succ[i]] + [0.0])
+        pr[i] = ops[i]["c"] + max([pr[j] + LAT + (0.0 if ops[i]["rem"] and ops[j]["e"] == "g" else ops[i]["lat"]) for j in succ[i]] + [0.0])
     pr = [float(pr[i] + noise[i]) for i in range(n)]
     left = [len(o["dep"]) for o in ops]
     fin, start, busy, order, est = [0.0] * n, [0.0] * n, {}, [], {}
-    ready = [i for i in range(n) if left[i] == 0]
-    for i in ready: est[i] = ops[i]["t0"]
-    while ready:
-        st = {i: max(est[i], busy.get(ops[i]["e"], 0.0)) for i in ready}
-        i0 = min(ready, key=lambda i: (st[i], -pr[i], i))
-        e, t = ops[i0]["e"], st[i0]
-        i = max([j for j in ready if ops[j]["e"] == e and st[j] <= t + min(win, ops[i0]["c"])], key=lambda j: (pr[j], -j))
-        busy[e] = st[i] + ops[i]["c"]
+    ready = {e: [] for e in "vapgs"}
+    for i in range(n):
+        if left[i] == 0:
+            ready[ops[i]["e"]].append(i)
+            est[i] = ops[i]["t0"]
+    busy = {e: 0.0 for e in ready}
+    for _ in range(n):
+        t, e = min((max(min(est[i] for i in l), busy[x]), x) for x, l in ready.items() if l)
+        l = ready[e]
+        i0 = max((j for j in l if est[j] <= t), key=lambda j: (pr[j], -j))
+        lim = t + min(win, ops[i0]["c"])
+        i = max((j for j in l if est[j] <= lim), key=lambda j: (pr[j], -j))
+        start[i] = max(est[i], t)
+        busy[e] = start[i] + ops[i]["c"]
         fin[i] = busy[e] + ops[i]["lat"]
-        start[i] = st[i]
         order.append(i)
-        ready.remove(i)
+        l.remove(i)
         for j in succ[i]:
             left[j] -= 1
             if left[j] == 0:
                 o = ops[j]
-                est[j] = max([o["t0"]] + [fin[d] + (0.0 if ops[d]["e"] == o["e"] and not ops[d]["dma"] else LAT) for d in o["dep"]])
-                ready.append(j)
+                est[j] = max([o["t0"]] + [fin[d] + LAT - (ops[d]["lat"] if ops[d]["rem"] and o["e"] == "g" else 0.0) for d in o["dep"]])
+                ready[o["e"]].append(j)
     return max(fin), order, start
 
 
@@ -154,19 +162,31 @@ def emit(g, T, ops):
     if "order" not in PLAN:
         rnd = np.random.default_rng(1)
         kinds = {}
-        for i, o in enumerate(ops): kinds.setdefault(o["e"] + (o["w"] + o["r"][1:])[0], []).append(i)
+        for i, o in enumerate(ops): kinds.setdefault(o["e"] + (o["w"] + o["r"][1:] + ["-"])[0], []).append(i)
         kinds = [kinds[k] for k in sorted(kinds)]
         noise, win = np.zeros(n), 400.0
         best = schedule(ops, succ, noise, win)
+        free = [i for i, o in enumerate(ops) if "alt" in o]
+
+        def flip(l):
+            for i in l:
+                ops[i]["e"] = "a" if ops[i]["e"] == "v" else "v"
+                ops[i]["c"] = ops[i]["alt"][ops[i]["e"]][0]
         for _ in range(TRIES):
-            x, w = noise.copy(), win
-            for _ in range(int(rnd.integers(1, 4))):
-                k = kinds[int(rnd.integers(len(kinds)))] if rnd.random() < 0.6 else [int(rnd.integers(n))]
-                x[k] += rnd.normal() * [500.0, 2000.0, 6000.0][int(rnd.integers(3))]
+            x, w, fl = noise.copy(), win, []
+            if rnd.random() < 0.4: fl = [free[int(k)] for k in rnd.choice(len(free), int(rnd.integers(1, 3)), replace=False)]
+            for _ in range(int(rnd.integers(0 if fl else 1, 3))):
+                k = kinds[int(rnd.integers(len(kinds)))] if rnd.random() < 0.4 else [int(rnd.integers(n))]
+                x[k] += rnd.normal() * [300.0, 1500.0, 5000.0][int(rnd.integers(3))]
             if rnd.random() < 0.03: w = float(rnd.integers(1, 10)) * 100.0
+            flip(fl)
             r = schedule(ops, succ, x, w)
             if r[0] <= best[0]: best, noise, win = r, x, w
+            else: flip(fl)
         PLAN["order"] = best
+        PLAN["on"] = {i: ops[i]["e"] for i in free}
+    for i, e in PLAN["on"].items():
+        ops[i]["e"], ops[i]["f"] = e, ops[i]["alt"][e][1]
     order = PLAN["order"][1]
     Q = {"v": g.vector, "a": g.scalar, "p": g.tensor, "g": g, "s": g.sync}
     cnt = {"v": 0, "a": 0, "p": 0, "g": 0}
@@ -220,7 +240,7 @@ def build(g, core, rank, T, topo, via, vib):
         ops.append({"e": e, "c": c, "r": r, "w": w, "f": f, "dma": dma, "lat": lat, "ext": list(ext), "t0": t0, "rem": rem})
 
     def cyc(n, k=1.0):
-        return 60.0 + max(64.0, n * k) * CY
+        return FIX + max(64.0, n * k) * CY
 
     def ts(out, in0, s1, s2, o0, o1, r, w, n, k=1.0):
         if o1 is None: op("v", cyc(n, k), r, w, lambda q: q.tensor_scalar(out, in0, s1, None, o0))
@@ -241,16 +261,29 @@ def build(g, core, rank, T, topo, via, vib):
         if scale is not None: kw["scale"] = scale
         op("a", cyc(n, k), r, w, lambda q: q.activation(out, a, fn, **kw))
 
+    def lin(out, a, scale, bias, r, w, n):
+        act(out, a, AF.Identity, r, w, n, scale=scale, bias=bias)
+
+    def either(e):
+        a, v = ops.pop(), ops.pop()
+        ops.append(dict(a if e == "a" else v, alt={"a": (a["c"], a["f"]), "v": (v["c"], v["f"])}))
+
     def gat(e, out, win, r, w, n):
-        if e == "a": act(out, win, AF.Copy, r, w, n, 1.56)
-        else: cp(out, win, r, w, n, 1.56)
+        cp(out, win, r, w, n, 1.56)
+        act(out, win, AF.Copy, r, w, n, 1.56)
+        either(e)
+
+    def scl(out, a, x, r, w, n):
+        ts(out, a, x, None, A.mult, None, r, w, n)
+        act(out, a, AF.Copy, r, w, n, scale=x)
+        either("a")
 
     def mm(l, r, w, start=True, stop=True, each=False):
         def f(q):
             for j, (o, a, b, _) in enumerate(l):
                 x = q.matmul(o, a, b, each or (start and j == 0), each or (stop and j == len(l) - 1))
             return x
-        op("p", sum(max(64, x[3]) for x in l) * PEC + 30.0, r, w, f, lat=60.0)
+        op("p", sum(max(64, x[3]) for x in l) * PEC + 30.0, r, w, f, lat=40.0)
 
     def group(bank, n, parts):
         mm([(P[bank][:, 0:n], T.ZER[:, 0:128], T.JB[:, 0:n], n)], "ZER JB", "P%d A%d" % (bank, bank), True, False)
@@ -263,17 +296,18 @@ def build(g, core, rank, T, topo, via, vib):
                     x = q.matmul(o, a, b, False, left[0] == 0 and j == len(l) - 1)
                 return x
             return f
-        return [lambda l=l, r=r: op("p", sum(max(64, x[3]) for x in l) * PEC + 30.0, r + " A%d" % bank, "", one(l), lat=60.0) for l, r in parts]
+        return [lambda l=l, r=r: op("p", sum(max(64, x[3]) for x in l) * PEC + 30.0, r + " A%d" % bank, "", one(l), lat=40.0) for l, r in parts]
 
-    def dma(e, l, r, w, lat=2000.0, ext=(), t0=0.0):
-        op(e, 100.0 * len(l), r, w, lambda q: [q.dma_start(o, a) for o, a in l], dma=True, lat=lat, ext=ext, t0=t0)
+    def dma(e, l, r, w, lat=1800.0, ext=(), t0=0.0):
+        op(e, 70.0 * len(l), r, w, lambda q: [q.dma_start(o, a) for o, a in l], dma=True, lat=lat, ext=ext, t0=t0)
 
-    def iota(out, pat, base, cm, w, n, fl=True):
-        if fl: op("g", 160 + 2 * n * CY, "", w, lambda q: q.iota(out, pat, base, cm, allow_small_or_imprecise_dtypes=True))
-        else: op("g", 160 + 2 * n * CY, "", w, lambda q: q.iota(out, pat, base, cm))
+    def iota(out, pat, base, cm, r, w, n, fl=True):
+        if fl: op("g", 140 + 2 * n * CY, r, w, lambda q: q.iota(out, pat, base, cm, allow_small_or_imprecise_dtypes=True))
+        else: op("g", 140 + 2 * n * CY, r, w, lambda q: q.iota(out, pat, base, cm))
 
     def strip(M, k):
-        return M[:, 15 - k:143 - k]
+        o = 144 * STRIPS.index(M)
+        return T.MM[:, o + 15 - k:o + 143 - k]
 
     def ext16(out, M, src, lo, n):
         return [(out, strip(M, k), src[:, lo + k:lo + 16 * n:16], n) for k in range(16)]
@@ -282,7 +316,9 @@ def build(g, core, rank, T, topo, via, vib):
     others = [d for d in range(N) if d != rank]
     P = [T["P%d" % b] for b in range(8)]
 
-    def send(src, land, hand, route, asem, hsem, wide, r):
+    def send(m, lat, r=""):
+        wide = MSG[m][2]
+        route = via if wide else vib
         off = topo.engines(core, C[[d for d in others if route[rank][d] is None][0]])
         rest = [e for e in topo.engines(core, [c for c in topo.cores_of(core) if c != core][0]) if e not in off]
         nd = 4 if wide else 2
@@ -290,293 +326,315 @@ def build(g, core, rank, T, topo, via, vib):
         tr, tot = [], 0
         for d in [d for d in others if route[rank][d] is None]:
             rid, pid = topo.addr(C[d], core)
-            tr.append(RemoteDMATransfer(dst_ids=[DstId(rid=rid, pnc=pid)], dma_engine_mask=bits(pool[:nd]), remote_sem=T.sem[asem], src=src[d], dst=land[rank]))
+            tr.append(RemoteDMATransfer(dst_ids=[DstId(rid=rid, pnc=pid)], dma_engine_mask=bits(pool[:nd]), remote_sem=T.sem[arrival(m, rank)],
+                                        src=T["s" + m][d], dst=T["r" + m][rank]))
             pool = pool[nd:]
             tot += nd
         for d in [d for d in others if route[rank][d] is not None]:
             rid, pid = topo.addr(route[rank][d], core)
-            tr.append(RemoteDMATransfer(dst_ids=[DstId(rid=rid, pnc=pid)], dma_engine_mask=bits(pool[-2:]), remote_sem=T.sem[hsem], src=src[d], dst=hand[:]))
+            tr.append(RemoteDMATransfer(dst_ids=[DstId(rid=rid, pnc=pid)], dma_engine_mask=bits(pool[-2:]), remote_sem=T.sem["h" + m],
+                                        src=T["s" + m][d], dst=T["h" + m][:]))
             pool = pool[:-2]
             tot += 2
-        op("g", 500.0, r + " gq", "gq", lambda q: q.remote_dma_fused(tr, local_sem=T.sem.loc), rem=tot)
+        op("g", 500.0, "s%s gq" % m + r, "gq m" + m, lambda q: q.remote_dma_fused(tr, local_sem=T.sem.loc), rem=tot, lat=lat)
 
     def arrivals(route, s, wide):
         return (4 if wide else 2) if route[s][rank] is None else len(topo.engines(route[s][rank], core))
 
     short_all = sum(arrivals(vib, s, False) for s in others)
-    dma("s", [(T.ss[:, 0:32, :], T.nm[:]), (T.ss[:, 32:64, :], T.pl[:]), (T.ss[:, 64:96, :], T.cc[:]), (T.ss[:, 96:128, :], T.nm[:])], "", "ss q1")
-    dma("a", [(T.sf[:], T.fo[:])], "", "sf q2", lat=4000.0)
-    dma("s", [(T.sx[:], T.tx[:])], "", "sx", lat=6000.0, t0=250.0)
     own = slice(16 * rank, 16 * rank + 16)
-    dma("s", [(T.rs[rank, 0:32, :], T.nm[rank:rank + 1, :]), (T.rs[rank, 32:64, :], T.pl[own, :]), (T.rs[rank, 64:96, :], T.cc[own, :])], "", "rso", t0=700.0)
-    dma("a", [(T.F[own, :], T.fo[own, :]), (T.X[own, :], T.tx[own, :])], "", "F%d X%d" % (rank, rank), t0=300.0)
 
-    PI = T.PK[:, 2:3]
-    iota(PI, [[0, 1]], 0, 1, "PI", 1, False)
-    iota(T.IOT[:], [[1, 256]], 0, 0, "IOT", 256)
-    iota(T.IG[:], [[1, 8], [0, 16]], 0, 0, "IG", 128)
-    iota(T.IK[:], [[0, 16], [1, 16]], 0, 0, "IK", 256)
-    send(T.ss, T.rs, T.hs, vib, "as", "h0", False, "ss PI IOT IG IK")
-    send(T.sf, T.rf, T.hf, via, "af%d" % rank, "h1", True, "sf")
-    send(T.sx, T.rx, T.hx, via, "ax%d" % rank, "h2", True, "sx")
-    op("g", 160 + 2 * V * CY, "gq", "RHO", lambda q: q.iota(T.RHO[:], [[1, 192], [192, 16]], 32, 0, allow_small_or_imprecise_dtypes=True))
-    op("g", 160 + 2 * V * CY, "RHO", "FV", lambda q: q.iota(T.FV[:], [[1, V]], 4096, 0, allow_small_or_imprecise_dtypes=True))
+    dma("s", [(T.CP[:, 0:192], T.cc[:])], "", "CPc")
+    dma("a", [(T.CP[:, 192:384], T.pl[:]), (T.CP[:, 384:576], T.nm[:])], "", "CPp")
+    dma("a", [(T.sf[:], T.fo[:])], "", "sf", lat=3500.0, t0=150.0)
+
+    iota(T.PK[:, 1:9], [[16, 8]], 0, 1, "", "PI", 8, False)
+    iota(T.IOT[:], [[1, 512]], 0, 0, "", "IOT", 512)
+    iota(T.IK[:], [[0, 16], [1, 16]], 0, 0, "", "IK", 256)
+    iota(T.IG[:], [[16, 8], [0, 16]], 15, 0, "", "IG", 128)
     col = lambda j: T.CC[:, j:j + 1]
-    cP, cK, cG, cY, cS = 0, 1, 2, 3, 4
-    ts(T.PK[:, 0:1], PI, 15, None, A.bitwise_and, None, "PI", "PK", 1)
-    ts(T.PK[:, 1:2], PI, 4, None, A.arith_shift_right, None, "PI PK", "PK", 1)
-    cp(col(cP), PI, "PI", "c0", 1)
-    cp(T.CC[:, 1:3], T.PK[:, 0:2], "PK", "c1", 1)
-    ts(col(cY), col(cG), 16.0, 15.0, A.mult, A.add, "c1", "c3", 1)
-    ts(col(cS), col(cK), 192.0, -4096.0, A.mult, A.add, "c1", "c4", 1)
+    cK, cP, cS, cY = 0, 1, 4, 24
+    ts(T.PK[:, 0:1], T.PK[:, 1:2], 15, None, A.bitwise_and, None, "PI", "PK0", 1)
+    ts(T.PK[:, 16:24], T.PK[:, 1:9], 112, None, A.bitwise_and, None, "PI", "PK1", 8)
+    cp(T.CC[:, 0:2], T.PK[:, 0:2], "PK0 PI", "c0 c1", 2)
+    ts(T.CC[:, cY:cY + 8], T.PK[:, 16:24], 15.0, None, A.add, None, "PK1", "c3", 8)
+    lin(col(cS), col(cK), 192.0, -4096.0, "c1", "c4", 1)
     OH = T.TM2[:, 0:16]
     ts(OH, T.IK[:, 0:16], col(cK), None, A.is_equal, None, "IK c1", "OH", 16)
 
-    def wcol(j, wts):
-        first = True
+    def wcol(j, wts, start=None):
         for ch, x in wts:
-            if first: ts(col(j), T.TM2[:, ch:ch + 1], float(x), None, A.mult, None, "OH", "c%d" % j, 1)
-            else: ts(col(j), T.TM2[:, ch:ch + 1], float(x), col(j), A.mult, A.add, "OH c%d" % j, "c%d" % j, 1)
-            first = False
+            if start is None: lin(col(j), T.TM2[:, ch:ch + 1], float(x), 0.0, "OH", "c%d" % j, 1)
+            else: lin(col(j), T.TM2[:, ch:ch + 1], float(x), col(start), "OH c%d" % start, "c%d" % j, 1)
+            start = j
     wcol(5, [(CH_HI, 1), (CH_LO, 1)])
-    ts(col(6), T.TM2[:, CH_FR:CH_FR + 1], 4096.0, col(5), A.mult, A.add, "OH c5", "c6", 1)
-    ts(col(7), T.TM2[:, CH_FR:CH_FR + 1], -8192.0, col(5), A.mult, A.add, "OH c5", "c7", 1)
-    ts(col(7), T.TM2[:, CH_FI:CH_FI + 1], 12288.0, col(7), A.mult, A.add, "OH c7", "c7", 1)
-    wcol(8, [(CH_BH, 1), (CH_BL, 1), (CH_FR, 8192), (CH_FI, -8192)])
+    wcol(7, [(CH_FR, -8192), (CH_FI, 12288)], 5)
+    wcol(6, [(CH_K, 16)])
+    wcol(15, [(CH_FR, -8192), (CH_FI, 8192)])
+    wcol(16, [(CH_K, 192), (CH_A, 1)])
+    lin(col(8), col(15), -1.0, col(16), "c15 c16", "c8", 1)
+    wcol(13, [(CH_K, 1), (CH_A, 16)])
+    lin(col(14), col(15), 1.0, col(13), "c15 c13", "c14", 1)
     wcol(9, [(CH_FR, -2)])
-    wcol(10, [(CH_LO, 1), (CH_BL, 1), (CH_CL, 1)])
-    wcol(13, [(CH_CH, 1), (CH_CL, 1)])
-    wcol(11, [(CH_HI, 3072), (CH_BH, 3072), (CH_CH, 3072), (CH_FR, 1)])
-    wcol(12, [(CH_FI, 1)])
-    wcol(15, [(CH_FR, -524288), (CH_FI, 524288)])
-    ts(T.ME[:], T.IOT[:, 0:144], col(cY), 8192.0, A.is_equal, A.mult, "IOT c3", "ME", 144)
-    for M, nm_, j in ((T.ML, "ML", 6), (T.MC, "MC", 7), (T.MB, "MB", 8), (T.MX, "MX", 13), (T.MF, "MF", 15), (T.MS, "MS", cS)):
-        ts(M[:], T.IOT[:, 0:144], col(cY), col(j), A.is_equal, A.mult, "IOT c3 c%d" % j, nm_, 144)
-    ts(T.Y1[:, 0:128], T.IOT[:, 0:128], col(cP), None, A.is_equal, None, "IOT c0", "Y1a", 128)
-    cp(T.Y1[:, 128:192], T.Y1[:, 0:64], "Y1a", "Y1", 64)
-    ts(T.Y2[:], T.Y1[:, 0:128], 2.0, None, A.mult, None, "Y1a", "Y2", 128, 0.5)
-    ts(T.YE[:], T.Y1[:, 0:128], 262144.0, None, A.mult, None, "Y1a", "YE", 128, 0.5)
-    ts(T.YM[:], T.Y1[:], -2.0, None, A.mult, None, "Y1a Y1", "YM", 192, 0.5)
-    ts(T.Y4[:], T.Y1[:], 4096.0, None, A.mult, None, "Y1a Y1", "Y4", 192, 0.5)
-    ts(T.SG[:], T.IG[:], col(cG), None, A.is_equal, None, "IG c1", "SG", 128)
-    cp(T.ONE[:], T.SG[:], "SG", "ONE", 128)
-    ts(T.TWO[:], T.SG[:], 2.0, None, A.mult, None, "SG", "TWO", 128)
-    ts(T.BCN[:], T.SG[:], col(5), None, A.mult, None, "SG c5", "BCN", 128)
-    ts(T.OCC[:], T.SG[:], col(9), None, A.mult, None, "SG c9", "OCC", 128)
-    ts(T.TMP[:, 0:128], T.IK[:, 0:128], col(cK), -1.0, A.is_lt, A.mult, "IK c1", "TMP", 128)
-    tt(T.TMP[:, 0:128], T.TMP[:, 0:128], T.SG[:], A.mult, "TMP SG", "TMP", 128)
-    ts(T.TMP[:, 128:256], T.Y1[:, 0:128], 512.0, None, A.mult, None, "Y1a TMP", "TMP", 128)
-    tt(T.TRI[:], T.TMP[:, 0:128], T.TMP[:, 128:256], A.add, "TMP", "TRI", 128)
+    wcol(10, [(CH_LO, 1), (CH_K, 1)])
+    wcol(11, [(CH_HI, 3072), (CH_A, 192)])
+    lin(col(17), col(15), 64.0, 0.0, "c15", "c17", 1)
+    for M, j, d in (("ME", None, 0), ("MA", 8, 0), ("MB", 8, 1), ("MC", 7, 0), ("MF", 17, 1), ("ML", 5, 1), ("MN", 5, 0), ("MO", 5, 7),
+                    ("MS", cS, 0), ("MX", 13, 0), ("MY", 14, 4)):
+        o = 144 * STRIPS.index(M)
+        ts(T.MM[:, o:o + 144], T.IOT[:, 0:144], col(cY + d), 8192.0 if j is None else col(j), A.is_equal, A.mult, "IOT c3 c%d" % (j or 3), M, 144)
+    ts(T.Y1[:], T.IOT[:, 0:128], col(cP), None, A.is_equal, None, "IOT c0", "Y1a", 128)
+    for M, nm_, x in ((T.Y2, "Y2", 2.0), (T.YE, "YE", 262144.0), (T.YH, "YH", -0.5), (T.YR, "YR", 192.0), (T.YM, "YM", -2.0)):
+        lin(M[:], T.Y1[:], x, 0.0, "Y1a", nm_, 128)
+    ts(T.SG[:], T.IG[:], col(cY), None, A.is_equal, None, "IG c3", "SG", 128)
+    lin(T.TWO[:], T.SG[:], 2.0, 0.0, "SG", "TWO", 128)
+    lin(T.BCN[:], T.SG[:], col(5), 0.0, "SG c5", "BCN", 128)
+    lin(T.OCC[:], T.SG[:], col(9), 0.0, "SG c9", "OCC", 128)
+    ts(T.TMP[:, 0:128], T.IK[:, 0:128], col(cK), None, A.is_gt, None, "IK c1", "TMPa", 128)
+    tt(T.TMP[:, 0:128], T.TMP[:, 0:128], T.SG[:], A.mult, "TMPa SG", "TMPa", 128)
+    lin(T.TMP[:, 128:256], T.Y1[:, 0:128], 512.0, 0.0, "Y1a", "TMPb", 128)
+    tt(T.TRI[:], T.TMP[:, 0:128], T.TMP[:, 128:256], A.add, "TMPa TMPb", "TRI", 128)
     ms(T.ZER[:], 0.0, "ZER", 208, 0.5)
-    ts(T.TMP[:], T.IK[:], 0.0, 0.5, A.not_equal, A.mult, "IK TMP", "TMP", 256)
+    ts(T.TMP[:], T.IK[:], 0.0, 0.5, A.not_equal, A.mult, "IK", "TMPa TMPb", 256)
     ts(T.TAU[:], T.IK[:], 0.0, None, A.is_equal, None, "IK", "TAU", 256)
-    op("v", cyc(256), "TMP TAU", "THR", lambda q: q.tensor_tensor_scan(T.THR[:], T.TMP[:], T.TAU[:], 0.0, A.mult, A.add))
+    op("v", cyc(256), "TMPa TMPb TAU", "THR", lambda q: q.tensor_tensor_scan(T.THR[:], T.TMP[:], T.TAU[:], 0.0, A.mult, A.add))
     tt(T.TM2[:, 16:32], T.THR[:, 0:16], OH, A.mult, "THR OH", "PW", 16)
     op("v", cyc(16), "PW ZER", "PW2", lambda q: q.tensor_tensor_scan(T.TM2[:, 32:48], T.TM2[:, 16:32], T.ZER[:, 0:16], 0.0, A.add, A.add))
-    ts(T.POW[:], T.SG[:], T.TM2[:, 47:48], None, A.mult, None, "SG PW2", "POW", 128)
-    ts(T.THR[:], T.THR[:], 2.0, 2.0, A.mult, A.add, "THR", "THR", 256)
-    ts(T.THR[:], T.THR[:], col(12), -4.0, A.mult, A.add, "THR c12", "THR", 256)
-    ts(T.JB[:], T.IOT[:], -256.0, None, A.add, None, "IOT", "JB", 256)
-    ts(T.JF[:], T.IOT[:], -256.0, None, A.add, None, "IOT", "JF", 256)
-    ts(T.TAU[:], T.IOT[:], 257.0, None, A.add, None, "IOT TAU", "TAU", 256)
-    ts(T.JL[:], T.IOT[:, 0:192], 16.0, col(cK), A.mult, A.add, "IOT c1", "JL", 192)
-    ts(T.DU1[:], T.JL[:, 0:16], -1024.0, None, A.add, None, "JL", "DU1", 16)
-    ts(T.DU2[:], T.JL[:, 0:16], 3840.0, None, A.add, None, "JL", "DU2", 16)
-    ts(T.DU3[:], T.JL[:], 3072.0, None, A.add, None, "JL", "DU3", 192)
-    ts(T.VH[:], T.JL[:], -1.0, None, A.mult, None, "JL", "VH", 192)
-    ts(T.FD[:], T.JL[:], -1.0, None, A.mult, None, "JL", "FD", 192)
-    tt(T.VL[:], T.FD[:], T.VH[:], A.subtract, "FD VH", "VL", 192)
+    lin(T.POW[:], T.SG[:], T.TM2[:, 47:48], 0.0, "SG PW2", "POW", 128)
+    lin(T.THR[:], T.THR[:], 2.0, 2.0, "THR", "THR", 256)
+    lin(T.THR[:], T.THR[:], T.TM2[:, CH_FI:CH_FI + 1], -4.0, "THR OH", "THR", 256)
+    lin(T.JB[:], T.IOT[:, 0:256], 131072.0, -256.0 * 131072, "IOT", "JB", 256)
+    lin(T.JF[:], T.IOT[:, 0:256], 1.0, -256.0, "IOT", "JF", 256)
+    lin(T.TAU[:], T.IOT[:, 0:256], 1.0, 256.0, "IOT", "TAU", 256)
+    lin(T.JL[:], T.IOT[:, 0:192], 16.0, col(cK), "IOT c1", "JL", 192)
+    lin(T.DU1[:], T.JL[:, 0:16], 1.0, -1023.5, "JL", "DU1", 16)
+    lin(T.DU2[:], T.JL[:, 0:16], 1.0, 3840.0, "JL", "DU2", 16)
+    lin(T.DU3[:], T.JL[:], 1.0, 3072.0, "JL", "DU3", 192)
+    lin(T.VK[:, 0:192], T.IOT[:, 0:192], 0.0, col(cK), "IOT c1", "VK", 192)
+    lin(T.VK[:, 192:384], T.IOT[:, 0:192], 1.0, 0.0, "IOT", "VA", 192)
     for t in range(1, TV + 1):
         ks = (S * t % V) % 16
         ts(T.MK[:, 2 * t - 2:2 * t - 1], col(cK), float(ks), None, A.is_lt, None, "c1", "MK%d" % t, 1)
-        ts(T.MK[:, 2 * t - 1:2 * t], col(cK), float(ks), None, A.is_ge, None, "c1 MK%d" % t, "MK%d" % t, 1)
-    ms(T.W[:, 0:V], 0.0, "Wd Wb", V, 0.5)
-    ts(T.W[:, V:3328], T.IOT[:], col(10), col(11), A.mult, A.add, "IOT c10 c11", "Wt", 256)
-    ms(T.PG[:, 3328:3584], 0.0, "PGt", 256, 0.5)
-    ms(T.BC[:], 0.0, "BCa BCb", 208, 0.5)
+        ts(T.MK[:, 2 * t - 1:2 * t], col(cK), float(ks), None, A.is_ge, None, "c1", "ML%d" % t, 1)
+    ms(T.W[:, 0:V], 0.0, "Wd Wb Wf", V, 0.5)
+    lin(T.W[:, V:3328], T.IOT[:, 0:256], col(10), col(11), "IOT c10 c11", "Wt", 256)
+    lin(T.W[:, FREE:3344], T.IOT[:, 0:16], 0.0, T.TM2[:, CH_FR:CH_FR + 1], "IOT OH", "Wu", 16)
+    for b in range(2): lin(T.PG[:, 3584 * b + 3328:3584 * b + 3584], T.IOT[:, 0:256], 0.0, col(6), "IOT c6", "PGt%d" % b, 256)
+    ms(T.BC[:], 0.0, "BCa BCb", 210, 0.5)
+    ms(T.BC[:, 0:1], -256.0, "BCa", 1)
     ms(T.BS[:], 0.0, "BS", 16)
-    ms(T.ZJ[:], -8192.0, "ZJ", 192)
-    dma("s", [(T.LW[0:128:16, 0:V], T.ZJ[:]), (T.LX[0:128:16, 0:V], T.ZJ[:])], "ZJ", "LW LX", t0=1500.0)
+    ms(T.CU[:], 0.0, "CU", 200)
+    ms(T.YP[:], -8192.0, "YP", 192)
+    for j in range(3): lin(T.FV[:, 512 * j:512 * j + 512], T.IOT[:], 1.0, 4096.0 + 1024 * j, "IOT", "FV%d" % j, 512)
 
-    TS_ = 8000.0
-    dma("s", [(T.CP[:, 0:192], T.rs[:, 64:96, :]), (T.CP[:, 192:384], T.rs[:, 32:64, :]),
-              (T.NI[0:112, :], T.rs[1:8, 0:32, :]), (T.NI[112:128, :], T.rs[0, 0:32, :])], "rso", "CP NI", ext=[("as", short_all)], t0=TS_)
-    for k, s in enumerate(others):
-        sl = slice(16 * s, 16 * s + 16)
-        dma("s", [(T.F[sl, :], T.rf[s])], "CP", "F%d" % s, ext=[("af%d" % s, arrivals(via, s, True))], t0=16000.0)
-    for k, s in enumerate(others):
-        sl = slice(16 * s, 16 * s + 16)
-        dma("s", [(T.X[sl, :], T.rx[s])], "CP", "X%d" % s, ext=[("ax%d" % s, arrivals(via, s, True))], t0=22000.0)
+    ts(T.IA[:, 0:192], T.CP[:, 0:192], 15, None, A.bitwise_and, None, "CPc", "IA0", 192)
+    ts(T.IA[:, 192:384], T.CP[:, 0:192], 4, None, A.logical_shift_right, None, "CPc", "IA1", 192)
+    cp(T.KA[:, 0:384], T.IA[:, 0:384], "IA0 IA1", "KAc", 384)
+
+    def rows(ch, src):
+        return [(T.W[ch:128:16, 0:V], src)]
+    dma("s", rows(CH_K, T.KA[:, 0:192]) + rows(CH_A, T.KA[:, 192:384]), "KAc", "Wb")
+    dma("s", [(T.LW[0:128:16, 0:V], T.YP[:]), (T.LX[0:128:16, 0:V], T.YP[:])], "YP KAc", "LW LX")
+    ts(T.IA[:, 384:576], T.CP[:, 192:384], 15, None, A.bitwise_and, None, "CPp", "IA2", 192)
+    ts(T.IA[:, 576:768], T.CP[:, 192:384], 4, None, A.logical_shift_right, None, "CPp", "IA3", 192)
+    cp(T.KA[:, 384:768], T.IA[:, 384:768], "IA2 IA3", "KAp", 384)
+    for h in range(2):
+        mm([(P[3][:, 192 * h:192 * h + 192], T.YR[:], T.KA[:, 384 * h:384 * h + 192], 192),
+            (P[3][:, 192 * h:192 * h + 192], T.Y1[:, 0:128], T.KA[:, 384 * h + 192:384 * h + 384], 192)], "YR Y1a KAc KAp", "P3")
+    ts(T.RP[:], P[3][:, 0:384], float(FREE), None, A.min, None, "P3", "RP PU", 384)
+    cp(T.NH[:, 0:192], T.CP[:, 384:576], "CPp", "NH0", 192)
+    tt(T.NH[:, 192:384], T.CP[:, 384:576], T.NH[:, 0:192], A.subtract, "CPp NH0", "NH1", 192)
+    l = []
+    for ch, src, o in ((0, T.KA, 0), (1, T.KA, 192), (2, T.NH, 0), (3, T.NH, 192)):
+        l += [(T.s0[:, 32 * ch:32 * ch + 32, :], src[:, o:o + 192]), (T.r0[rank, 32 * ch:32 * ch + 32, :], src[own, o:o + 192])]
+    dma("s", l, "KAc NH0 NH1", "s0 r0")
+    dma("s", [(T.sx[:], T.tx[:])], "NH1", "sx", lat=3500.0)
+    def slot(q):
+        return slice(16 * (q % N), 16 * (q % N) + 16)
+    dma("s", [(T.F[slot(rank + 1), 0:V], T.fo[own, :]), (T.X[own, :], T.tx[own, :]), (T.rf[rank], T.fo[own, :])], "sx", "F%d X%d" % (rank, rank))
+    send("f", 9000.0, " PI IOT IK IG")
+    send("0", 6000.0)
+    send("x", 9000.0)
+    iota(T.RHO[:], [[1, 192], [192, 16]], 32, 0, "gq", "RHO", V)
+
+    PU = T.RP[:, 192:384]
+    WA = "Wd Wb Wt Wu Wf "
+
+    def pgather(t):
+        o = 3584 * (t % 2) + 256
+        for j in range(6):
+            gat(ENG["P%d" % t][j], T.PG[:, o + 512 * j:o + 512 * j + 512], T.W[:, 0:3344].indirect(T.RP[:, 192 + 32 * j:224 + 32 * j]), WA + "PU",
+                "PG%d%d" % (t % 2, j), 512)
+    PGall = [" ".join("PG%d%d" % (b, j) for j in range(6)) + " PGt%d " % b for b in range(2)]
+    TRall = " TR0 TR1 TR2 TR3 TR4 TR5 "
+    pgather(0)
+    chans = (CH_K, CH_A, CH_FR, CH_FI)
+    dma("s", [x for k, ch in enumerate(chans) for x in ((T.s4[:, 32 * k:32 * k + 32, :], T.PG[ch:128:16, 256:3328]),
+                                                        (T.r4[rank, 32 * k:32 * k + 32, :], T.PG[16 * rank + ch:16 * rank + ch + 1, 256:3328]))], PGall[0], "s4 r4")
+    send("4", 5000.0)
+    for j in range(3):
+        c = slice(64 * j, 64 * j + 64)
+        b = 4 + j % 2
+        mm(ext16(P[b][:, c], "MA", T.PG, 256 + 1024 * j, 64), "PG0%d PG0%d MA" % (2 * j, 2 * j + 1), "P%d" % b)
+        tt(T.FC[:, c], P[b][:, c], T.DU3[:, c], A.min, "P%d DU3" % b, "FC%d" % j, 64, 1.0)
+        cp(T.LO[:, c], T.FC[:, c], "FC%d" % j, "LO%d" % j, 64)
+    for j in range(3):
+        h = 2 * j + 1
+        ts(T.LW[:, 0:6144].indirect(T.LO[:, 32 * h:32 * h + 32]), T.IOT[:], 1.0, 4096.0 + 512 * h, A.mult, A.add, "IOT LO%d" % j, "LW", 512, 3.8)
+        h = 2 * j
+        act(T.LX[:, 0:6144].indirect(T.LO[:, 32 * h:32 * h + 32]), T.FV[:, 512 * j:512 * j + 512], AF.Silu, "FV%d LO%d" % (j, j), "LX", 512, 3.8)
+    g0 = slice(16 * rank, 16 * rank + 1)
+    dma("a", [(T.s2[:, 0:64, :], T.LW[0:128:16, 0:V]), (T.s2[:, 64:128, :], T.LX[0:128:16, 0:V]),
+              (T.r2[rank, 0:64, :], T.LW[g0, 0:V]), (T.r2[rank, 64:128, :], T.LX[g0, 0:V])], "LW LX", "s2 r2")
+    send("2", 5000.0)
+    for j in range(6):
+        act(T.ICW[:, 0:V].indirect(T.RP[:, 32 * j:32 * j + 32]), T.RHO[:, 512 * j:512 * j + 512], AF.Silu, "RHO RP", "ICW", 512, 3.8)
+    dma("a", [(T.s3[:], T.ICW[0:128:16, :]), (T.r3[rank], T.ICW[g0, :])], "ICW", "s3 r3")
+    send("3", 5000.0)
+
+    dma("s", [(T.W[ch:128:16, 0:V], T.r0[:, 32 * k:32 * k + 32, :]) for k, ch in enumerate((CH_K, CH_A, CH_HI, CH_LO))], "r0 m0", "Wd Wb", ext=[("a0", short_all)])
+    for s in others:
+        dma("s", [(T.F[slot(s + 1), 0:V], T.rf[s])], "mf", "F%d" % s, ext=[("af%d" % s, arrivals(via, s, True))])
+    for s in others:
+        dma("s", [(T.X[slot(s), :], T.rx[s])], "mx", "X%d" % s, ext=[("ax%d" % s, arrivals(via, s, True))])
     Fall = " ".join("F%d" % s for s in range(N)) + " "
     Xall = " ".join("X%d" % s for s in range(N)) + " "
-    ts(T.IA[:], T.CP[:], 15, None, A.bitwise_and, None, "CP", "IA", 384)
-    ts(T.IB[:], T.CP[:], 4, None, A.arith_shift_right, None, "CP", "IB", 384)
-    ts(T.FA[:], T.IA[:], 192.0, None, A.mult, None, "IA", "FA", 384)
-    tt(T.RF[:], T.FA[:], T.IB[:], A.add, "FA IB", "RF", 384)
-    cp(T.RRU[:], T.RF[:, 0:192], "RF", "RRU", 192)
-    act(T.BH[:, 0:192], T.RF[:, 0:192], AF.Copy, "RF", "BH", 192)
-    tt(T.BL[:, 0:192], T.RF[:, 0:192], T.BH[:, 0:192], A.subtract, "RF BH", "BL", 192)
-    cp(T.BH[:, 192:384], T.CP[:, 0:192], "CP", "CH", 192)
-    tt(T.BL[:, 192:384], T.CP[:, 0:192], T.BH[:, 192:384], A.subtract, "CP CH", "CL", 192)
-    ts(T.FB[:], T.CP[:, 192:384], 0.0, 8192.0, A.is_lt, A.mult, "CP", "FB", 192)
-    tt(T.FB[:], T.FB[:], T.RF[:, 192:384], A.add, "FB RF", "FB", 192)
-    ts(T.PU[:], T.FB[:], 3072.0, None, A.min, None, "FB", "PU", 192)
-
-    def rows(ch, src, t, o=0):
-        if t == 0: return [(T.W[ch:128:16, 0:V], src[:, o:o + 192])]
-        return [(T.W[ch:128 - 16 * t:16, 0:V], src[16 * t:128, o:o + 192]), (T.W[128 - 16 * t + ch:128:16, 0:V], src[0:16 * t, o:o + 192])]
-    dma("a", rows(CH_BH, T.BH, 0) + rows(CH_BL, T.BL, 0), "BH BL", "Wb")
-    cp(T.FC[:], T.NI[:], "NI", "FC", 192)
-    act(T.HI[:], T.FC[:], AF.Copy, "FC", "HI", 192)
-    tt(T.LW2[:], T.FC[:], T.HI[:], A.subtract, "FC HI", "LO2", 192)
-    dma("a", rows(CH_HI, T.HI, 0) + rows(CH_LO, T.LW2, 0), "HI LO2", "Wd")
-    mm(ext16(P[3][:, 0:192], T.ML, T.W, 0, 192), "Wd Wb ML", "P3")
-    act(T.NF[:], P[3][:, 0:192], AF.Copy, "P3", "NF", 192)
+    mm(ext16(P[3][:, 0:192], "MN", T.W, 0, 192), "Wd Wb Wf MN", "P3")
     ts(T.NU[:], P[3][:, 0:192], 0.0, None, A.add, None, "P3", "NU", 192)
-    act(T.N4[:], T.NF[:], AF.Identity, "NF", "N4", 192, bias=4096.0)
-
-    def pgather(eng):
-        for j in range(6):
-            gat(eng[j], T.PG[:, 256 + 512 * j:768 + 512 * j], T.W[:, 0:3328].indirect(T.PU[:, 32 * j:32 * j + 32]), "Wd Wb Wt PU", "PG%d" % j, 512)
-    PGall, TRall = " PG0 PG1 PG2 PG3 PG4 PG5 ", " TR0 TR1 TR2 TR3 TR4 TR5 "
-    pgather(ENG["P0"])
-    for j in range(6):
-        act(T.ICW[:, 0:V].indirect(T.RRU[:, 32 * j:32 * j + 32]), T.RHO[:, 512 * j:512 * j + 512], AF.Silu, "RHO RRU", "ICW", 512, 3.8)
-    l = []
-    for t in range(1, TV):
-        l += [(T.ICF[0:128 - 16 * t, 192 * t - 192:192 * t], T.ICW[16 * t:128:16, :]), (T.ICF[128 - 16 * t:128, 192 * t - 192:192 * t], T.ICW[0:16 * t:16, :])]
-    dma("a", l, "ICW", "ICF")
-    cp(T.ICI[:], T.ICF[:], "ICF", "ICI", 576)
-    ts(T.ICU[:], T.ICI[:], -32.0, None, A.add, None, "ICI", "ICU", 576)
-    mm(ext16(P[4][:, 0:192], T.MB, T.PG, 256, 192), PGall + "MB", "P4")
-    tt(T.FC[:], P[4][:, 0:192], T.DU3[:], A.min, "P4 DU3 FC", "FC", 192, 1.0)
-    cp(T.LO[:], T.FC[:], "FC", "LO", 192)
-    ts(T.PU[:], P[4][:, 0:192], 3072.0, None, A.min, None, "P4", "PU", 192)
-    for j in range(3):
-        cp(T.LW[:, 0:6144].indirect(T.LO[:, 32 * j:32 * j + 32]), T.FV[:, 512 * j:512 * j + 512], "FV LO", "LW", 512, 3.8)
-        j += 3
-        act(T.LX[:, 0:6144].indirect(T.LO[:, 32 * j:32 * j + 32]), T.FV[:, 512 * j:512 * j + 512], AF.Silu, "FV LO", "LX", 512, 3.8)
-    dma("s", [(T.FA[:, 0:192], T.LW[0:128:16, 0:V]), (T.FA[:, 192:384], T.LX[0:128:16, 0:V])], "LW LX", "FA")
-    tt(T.FB[:], T.FA[:, 0:192], T.FA[:, 192:384], A.max, "FA", "FB", 192)
-    cp(T.NI[:], T.FB[:], "FB", "NI", 192)
+    act(T.NF[:], P[3][:, 0:192], AF.Copy, "P3 ICW", "NF", 192)
+    dma("s", [(T.PG[ch:128:16, 256:3328], T.r4[:, 32 * k:32 * k + 32, :]) for k, ch in enumerate(chans[:3])], "r4 m4", PGall[0], ext=[("a4", short_all)])
+    mm(ext16(P[7][:, 256:448], "MB", T.PG, 256, 192), "MB " + PGall[0], "P7")
+    ts(PU, P[7][:, 256:448], float(FREE), None, A.min, None, "P7", "PU", 192)
+    dma("s", [(T.FA[p, 192 * h:192 * h + 192], T.r2[r, 64 * h:64 * h + 64, :]) for h in range(2) for p, r in ((slice(16, 128), slice(0, 7)), (slice(0, 16), 7))],
+        "r2 m2", "FA", ext=[("a2", short_all)])
+    tt(T.NI[:], T.FA[:, 0:192], T.FA[:, 192:384], A.max, "FA", "NI", 192)
     ts(T.LU[:], T.NI[:], -4096.0, 0.0, A.add, A.max, "NI", "LU0 LU1 LU2", 192)
-    cp(T.CA[:], T.NI[:], "NI", "CA", 192)
+    ts(P[4][:, 0:192], T.NI[:], -4096.0, None, A.add, None, "NI", "P4", 192)
+    ts(T.EM[:], T.NI[:], 0.0, -2.0, A.is_lt, A.mult, "NI", "EM", 192)
+    dma("s", [(T.ICF[:], T.r3[:])], "r3 m3", "ICF", ext=[("a3", short_all)])
+    ts(T.ICU[:], T.ICF[:], -31.75, None, A.add, None, "ICF", "ICU", 192)
 
     for t in range(1, TV + 1):
         s0 = S * t % V
         cs = s0 // 16
         last = t == TV
-        if last: dma("s", rows(CH_BH, T.VH, 0) + rows(CH_BL, T.VL, 0), "VH VL", "Wb")
-        else: dma("s", rows(CH_BH, T.BH, t) + rows(CH_BL, T.BL, t) + rows(CH_CH, T.BH, t, 192) + rows(CH_CL, T.BL, t, 192), "BH BL CH CL", "Wb")
+        Ft = T.F[:, V * t - V:V * t]
+        if t > 1: Fall = "Ft%d " % t
+        if last: dma("s", rows(CH_K, T.VK[:, 0:192]) + rows(CH_A, T.VK[:, 192:384]), "VK VA", "Wb")
         for j in range(6):
-            gat(ENG["G%d" % t][j], T.G2[:, 512 * j:512 * j + 512], T.F[:, 0:V].indirect(T.NU[:, 32 * j:32 * j + 32]), Fall + "NU", "G%d" % j, 512)
-        parts = [(ext16(P[2][:, 64 * h:64 * h + 64], T.ME, T.NE, 1024 * h, 64), "ME NE%d NE%d" % (2 * h, 2 * h + 1)) for h in range(3)]
+            gat(ENG["G%d" % t][j], T.G2[:, 512 * j:512 * j + 512], Ft.indirect(T.NU[:, 32 * j:32 * j + 32]), Fall + "NU", "G%d" % j, 512)
+        if not last:
+            dma("s", [(T.F[16 * t + 16:128, V * t:V * t + V], T.rf[0:7 - t]), (T.F[0:16 * t + 16, V * t:V * t + V], T.rf[7 - t:8])],
+                Fall + Xall + ("FA" if t == 1 else "G5"), "Ft%d" % (t + 1), lat=3500.0)
+        tt(P[3][:, 0:192], P[4][:, 0:192], T.NF[:], A.subtract, "P4 NF", "P3", 192, 1.0)
+        ts(T.EQ[:], P[3][:, 0:192], 0.0, None, A.is_equal, None, "P3", "EQ", 192)
+        parts = [(ext16(P[2][:, 64 * h:64 * h + 64], "ME", T.NE, 1024 * h, 64), "ME NE%d NE%d" % (2 * h, 2 * h + 1)) for h in range(3)]
         parts.append(([(P[2][:, 0:192], T.YE[:], T.EQ[:], 192)], "YE EQ"))
-        if t > 1: parts.append((ext16(P[2][:, 0:192], T.MF, T.TR, 0, 192), "MF" + TRall))
+        if t > 1: parts += [(ext16(P[2][:, 64 * h:64 * h + 64], "MF", T.TR, 1024 * h, 64), "MF" + TRall) for h in range(3)]
+        else: parts.append(([(P[2][:, 0:192], T.YE[:], T.EM[:], 192)], "YE EM"))
         parts = group(2, 192, parts)
         for j in range(6):
             c = slice(512 * j, 512 * j + 512)
             b = j % 2
-            tt(T.D[:, c], T.F[:, 0:V].indirect(T.LU[:, 32 * j:32 * j + 32]), T.G2[:, c], A.subtract, Fall + "LU%d G%d" % (j // 2, j), "D%d" % j, 512, 1.56)
-            mm([(P[b][:], T.YM[:, 16 * t:16 * t + 128], T.X[:, c], 512), (P[b][:], T.Y2[:], T.G2[:, c], 512), (P[b][:], T.Y1[:, 0:128], T.D[:, c], 512)],
-               Xall + "YM Y2 Y1a G%d D%d" % (j, j), "P%d" % b)
+            tt(T.D[:, c], Ft.indirect(T.LU[:, 32 * j:32 * j + 32]), T.G2[:, c], A.subtract, Fall + "LU%d G%d" % (j // 2, j), "D%d" % j, 512, 1.56)
+            mm([(P[b][:], T.YM[:], T.X[:, c], 512), (P[b][:], T.Y2[:], T.G2[:, c], 512)], Xall + "YM Y2 G%d" % j, "P%d" % b, True, False)
+            mm([(P[b][:], T.Y1[:, 0:128], T.D[:, c], 512)], "Y1a D%d" % j, "P%d" % b, False, True)
             tt(T.PR[:, c], P[b][:], T.D[:, c], A.mult, "P%d D%d" % (b, j), "PR%d" % j, 512, 1.0)
-            if ENG["S%d" % t][j] == "v": ts(T.NE[:, c], T.PR[:, c], 0.0, 0.5, A.is_lt, A.subtract, "PR%d" % j, "NE%d" % j, 512, 0.5)
-            else: act(T.NE[:, c], T.PR[:, c], AF.Sign, "PR%d" % j, "NE%d" % j, 512, bias=-0.5, scale=-1.0)
-        if t == 1: tt(T.EQ[:], T.CA[:], T.N4[:], A.is_equal, "CA N4", "EQ", 192)
+            ts(T.NE[:, c], T.PR[:, c], 0.0, 0.5, A.is_lt, A.subtract, "PR%d" % j, "NE%d" % j, 512, 0.5)
+            act(T.NE[:, c], T.PR[:, c], AF.Sign, "PR%d" % j, "NE%d" % j, 512, bias=-0.5, scale=-1.0)
+            either(ENG["S%d" % t][j])
         for x in parts: x()
-        tt(P[2][:, 256:448], P[2][:, 0:192], T.CA[:], A.min, "CA", "P2 A2", 192, 1.0)
-        tt(T.ZJ[:], P[2][:, 256:448], T.NF[:], A.max, "P2 NF", "ZJ", 192, 1.0)
-        act(T.HI[:], T.ZJ[:], AF.Copy, "ZJ", "HI", 192)
-        ts(T.FR[:], T.ZJ[:], 4096.0, None, A.is_lt, None, "ZJ", "FR", 192)
-        tt(T.LW2[:], T.ZJ[:], T.HI[:], A.subtract, "ZJ HI", "LO2", 192)
-        dma("s", rows(CH_FR, T.FR, 0) + rows(CH_HI, T.HI, 0) + rows(CH_LO, T.LW2, 0), "FR HI LO2", "Wd")
+        ts(T.FR[:], P[2][:, 0:192], 4096.0, None, A.is_lt, None, "", "FR P2 A2", 192)
+        dma("s", rows(CH_FR, T.FR[:]), "FR", "Wf")
+        tt(T.FC[:], P[3][:, 0:192], T.FR[:], A.mult, "P3 FR", "FC0 FC1 FC2", 192, 1.0)
+        tt(T.NF[:], P[4][:, 0:192], T.FC[:], A.subtract, "P4 FC0 FC1 FC2", "NF", 192, 1.0)
+        scl(T.HI[:], T.NF[:], 1.0, "NF", "HI", 192)
+        tt(T.LW2[:], T.NF[:], T.HI[:], A.subtract, "NF HI", "LO2", 192)
+        dma("s", rows(CH_HI, T.HI[:]) + rows(CH_LO, T.LW2[:]), "HI LO2", "Wd")
         if not last:
-            mm([(P[3][:, 0:192], T.Y1[:, 16:144], T.HI[:], 192), (P[3][:, 0:192], T.Y1[:, 16:144], T.LW2[:], 192), (P[3][:, 0:192], T.Y4[:, 16:144], T.FR[:], 192)],
-               "Y1a Y1 Y4 HI LO2 FR", "P3")
-            ts(T.NU[:], P[3][:, 0:192], -4096.0, None, A.add, None, "P3", "NU", 192)
-            act(T.N4[:], P[3][:, 0:192], AF.Copy, "P3", "N4", 192)
-            act(T.NF[:], T.N4[:], AF.Identity, "N4", "NF", 192, bias=-4096.0)
+            cp(T.NU[:], T.NF[:], "NF", "NU", 192)
             for j in range(3):
                 for h in (2 * j, 2 * j + 1):
-                    o = 192 * t - 192 + 32 * h
-                    gat(ENG["T%d" % t][h], T.TR[:, 512 * h:512 * h + 512], T.W[:, 0:3328].indirect(T.ICU[:, o:o + 32]), "Wd Wb Wt ICU", "TR%d" % h, 512)
-                mm(ext16(P[4][:, 64 * j:64 * j + 64], T.ML, T.TR, 1024 * j, 64), "ML TR%d TR%d" % (2 * j, 2 * j + 1), "P4")
-                ts(T.LU[:, 64 * j:64 * j + 64], P[4][:, 64 * j:64 * j + 64], -4096.0, None, A.add, None, "P4", "LU%d" % j, 64)
-            tt(T.EQ[:], P[4][:, 0:192], T.N4[:], A.is_equal, "P4 N4", "EQ", 192, 1.0)
-            act(T.CA[:], P[4][:, 0:192], AF.Copy, "P4", "CA", 192)
+                    gat(ENG["T%d" % t][h], T.TR[:, 512 * h:512 * h + 512], T.W[:, 0:3344].indirect(T.ICU[:, 32 * h:32 * h + 32]), WA + "ICU", "TR%d" % h, 512)
+                mm(ext16(P[4][:, 64 * j:64 * j + 64], "ML", T.TR, 1024 * j, 64), "ML TR%d TR%d" % (2 * j, 2 * j + 1), "P4")
+                cp(T.LU[:, 64 * j:64 * j + 64], P[4][:, 64 * j:64 * j + 64], "P4", "LU%d" % j, 64)
         else:
             for q in range(N):
                 for b in range(2):
                     o = P[0][0:96, 32 * q + 16 * b:32 * q + 16 * b + 16]
-                    y = slice(64 + 16 * q, 80 + 16 * q)
-                    mm([(o, T.HI[:, b:192:2], T.Y1[:, y], 16), (o, T.LW2[:, b:192:2], T.Y1[:, y], 16), (o, T.FR[:, b:192:2], T.Y4[:, y], 16)], "Y1a Y1 Y4 HI LO2 FR", "P0")
-            act(T.TN[0:96, :], P[0][0:96, 0:256], AF.Identity, "P0", "TN", 256, bias=-4096.0)
-            dma("s", [(T.on[q], T.TN[0:96, 32 * q:32 * q + 32]) for q in others], "TN", "on")
+                    mm([(o, T.HI[:, b:192:2], T.Y1[:, slot(q)], 16), (o, T.LW2[:, b:192:2], T.Y1[:, slot(q)], 16)], "Y1a HI LO2", "P0")
+            act(T.TN[0:96, :], P[0][0:96, 0:256], AF.Copy, "P0", "TN", 256)
+            dma("s", [(T.sn[q], T.TN[0:96, 32 * q:32 * q + 32]) for q in others], "TN", "sn")
             dma("s", [(T.yn[rank:rank + 1, :], T.TN[0:96, 32 * rank:32 * rank + 32])], "TN", "yno")
-            send(T.on, T.rn, T.hn, vib, "an", "h3", False, "on")
-        pgather(ENG["P%d" % t])
-        ts(T.FS[:], T.MK[:, 2 * t - 2:2 * t], T.FR[:, cs:cs + 1], None, A.mult, None, "MK%d FR" % t, "FS", 2)
-        for M, nm_, bk in ((T.ONE, "ONE", 5), (T.TRI, "TRI", 6)):
-            mm([(P[bk][:, a:b_], M[:], src, b_ - a) for a, b_, src in ((0, cs, T.FR[:, 0:cs]), (cs + 2, 193, T.FR[:, cs + 1:192]), (cs, cs + 2, T.FS[:]))],
-               nm_ + " FR FS", "P%d" % bk, each=True)
+            send("n", 5000.0)
+        pgather(t)
+        po, pn = 3584 * ((t - 1) % 2), 3584 * (t % 2)
+        ts(T.FS[:], T.MK[:, 2 * t - 2:2 * t], T.FR[:, cs:cs + 1], None, A.mult, None, "MK%d ML%d FR" % (t, t), "FS", 2)
+        cols = ((0, cs, T.FR[:, 0:cs]), (cs + 2, 193, T.FR[:, cs + 1:192]), (cs, cs + 2, T.FS[:]))
+        mm([(P[5][:, a:b_], T.SG[:], src, b_ - a) for a, b_, src in cols], "SG FR FS", "P5", each=True)
         op("v", cyc(193), "P5 ZER", "U P5", lambda q: q.tensor_tensor_scan(T.U[:, 0:193], P[5][:, 0:193], T.ZER[:, 0:193], -256.0, A.add, A.add))
-        ts(T.DB[:, 0:1], T.U[:, cs:cs + 1], 256.0, T.U[:, 192:193], A.add, A.min, "U", "DB0", 1)
-        ts(T.DB[:, 1:2], T.U[:, cs:cs + 1], T.DB[:, 0:1], None, A.subtract, None, "U DB0", "DB1", 1)
-        ts(T.BC[:, cs + 1:193], T.U[:, cs + 1:193], T.DB[:, 0:1], None, A.subtract, None, "U DB0", "BCb", 192 - cs)
-        ts(T.BC[:, 0:cs + 1], T.U[:, 0:cs + 1], T.DB[:, 1:2], None, A.min, None, "U DB1", "BCa", cs + 1)
-        ts(T.U[:, cs + 1:193], T.U[:, cs + 1:193], T.DB[:, 0:1], None, A.subtract, None, "U DB0", "U", 192 - cs)
-        tt(T.CU[:, 0:193], P[6][:, 0:193], T.U[:, 0:193], A.add, "P6 U", "CU", 193, 1.0)
-        tt(T.TM2[:, 48:61], T.BC[:, 15:208:16], T.TM2[:, 0:13], A.mult, "BCa BCb OH", "TH", 13)
-        op("v", cyc(13), "TH", "c14", lambda q: q.tensor_reduce(col(14), T.TM2[:, 48:61], AxisListType.X, A.add))
-        mm(ext16(P[5][:, 0:13], T.ME, T.BC, 0, 13), "ME BCa BCb", "P5")
-        act(T.BS[:, 0:13], P[5][:, 0:13], AF.Copy, "P5", "BS", 13, scale=1.0 / 131072)
-        ts(T.L1[:], T.JB[:], col(14), None, A.is_ge, None, "JB c14", "L1", 256, 0.5)
-        mm(ext16(P[3][:, 256:272], T.ME, T.L1, 0, 16), "ME L1", "P3")
-        ts(T.AU[:], P[3][:, 256:272], 1.0 / 8192, None, A.mult, None, "P3", "AU", 16)
-        ts(T.AB[:], P[3][:, 256:272], 16.0, None, A.mult, None, "P3", "AB", 16)
+        Uc = T.U[:, cs:cs + 1]
+        ts(T.DB[:, 0:1], Uc, T.U[:, 192:193], -256.0, A.subtract, A.max, "U", "DB0", 1)
+        ts(T.BC[:, 1:cs + 2], T.U[:, 0:cs + 1], T.DB[:, 0:1], None, A.min, None, "U DB0", "BCa", cs + 1)
+        ts(T.DB[:, 1:2], T.DB[:, 0:1], Uc, Uc, A.min, A.subtract, "U DB0", "DB1", 1)
+        ts(T.BC[:, cs + 2:194], T.U[:, cs + 1:193], T.DB[:, 1:2], None, A.add, None, "U DB1", "BCb", 192 - cs)
+        for x in group(6, 193, [([(P[6][:, a:b_], T.TRI[:], src, b_ - a) for a, b_, src in cols], "TRI FR FS"),
+                                ([(P[6][:, 0:193], T.Y1[:, 0:128], T.BC[:, 0:193], 193)], "Y1a BCa BCb")]): x()
+        scl(T.CU[:, 0:193], P[6][:, 0:193], 1.0, "", "CU P6 A6", 193)
+        mm([(P[5][:, 200:201], strip("ME", k), T.BC[:, 16 * k + 16:16 * k + 17], 1) for k in range(12)], "ME BCa BCb", "P5")
+        mm(ext16(P[7][:, 448:461], "ME", T.BC, 1, 13), "ME BCa BCb", "P7")
+        scl(T.BS[:, 0:13], P[7][:, 448:461], 1.0 / 131072, "P7", "BS", 13)
+        ts(T.L1[:], T.JB[:], P[5][:, 200:201], None, A.is_ge, None, "JB P5", "L1", 256, 0.5)
+        mm(ext16(P[5][:, 256:272], "ME", T.L1, 0, 16), "ME L1", "P5")
+        ts(T.AU[:], P[5][:, 256:272], 1.0 / 8192, None, A.mult, None, "P5", "AU", 16)
+        scl(T.AB[:], P[5][:, 256:272], 16.0, "P5 AU", "AB", 16)
         tt(T.L2[:], T.BS[:, 0:16].indirect(T.AU[:]), T.JF[:], A.is_le, "BS AU JF", "L2", 256, 1.56)
-        mm([(P[6][:, 0:16], T.Y1[:, 0:128], T.AB[:], 16)] + ext16(P[6][:, 0:16], T.ME, T.L2, 0, 16), "ME Y1a AB L2", "P6")
+        mm(ext16(P[6][:, 0:16], "ME", T.L2, 0, 16) + [(P[6][:, 0:16], T.Y1[:, 0:128], T.AB[:], 16)], "ME Y1a AB L2", "P6")
         ts(T.KU[:], P[6][:, 0:16], 1.0 / 8192, None, A.mult, None, "P6", "KU", 16)
-        ts(T.KB[:, 0:16], P[6][:, 0:16], 1.0 / 8192, None, A.mult, None, "P6", "KB", 16)
-        ts(T.KB[:, 16:32], P[6][:, 0:16], (cs + 0.5) * 8192, -1.0, A.is_gt, A.mult, "P6", "KC", 16)
-        tt(T.SE[:], T.CU[:, 0:193].indirect(T.KU[:]), T.TAU[:], A.is_equal, "CU KU TAU", "SE", 256, 1.56)
-        mm([(P[6][:, 0:16], T.Y1[:, 0:128], T.KB[:, 0:16], 16), (P[6][:, 0:16], T.Y1[:, 0:128], T.KB[:, 16:32], 16)] + ext16(P[6][:, 0:16], T.MS, T.SE, 0, 16), "MS Y1a KB KC SE", "P6")
-        tt(T.RT[:], P[6][:, 0:16], T.DU1[:], A.min, "P6 DU1", "RT", 16)
-        ts(T.RU[:], T.RT[:], 4096.0, None, A.add, None, "RT", "RU", 16)
-        gat("a", T.Z[:], T.W[:, 0:3328].indirect(T.RU[:]), "Wd Wb Wt RU", "Z", 256)
+        scl(T.KB[:, 0:16], P[6][:, 0:16], 1.0 / 8192, "P6 KU", "KB", 16)
+        act(T.KB[:, 16:32], T.KB[:, 0:16], AF.Sign, "KB", "KC", 16, bias=-(cs + 0.5))
+        tt(T.SE[:], T.CU[:, 0:194].indirect(T.KU[:]), T.TAU[:], A.is_equal, "CU KU TAU", "SE", 256, 1.56)
+        mm(ext16(P[5][:, 0:16], "MS", T.SE, 0, 16) + [(P[5][:, 0:16], T.Y1[:, 0:128], T.KB[:, 0:16], 16), (P[5][:, 0:16], T.YH[:], T.KB[:, 16:32], 16)],
+           "MS Y1a YH KB KC SE", "P5")
+        tt(T.RT[:], P[5][:, 0:16], T.DU1[:], A.min, "P5 DU1", "RT", 16, 1.0)
+        ts(T.RU[:], T.RT[:], 4095.5, None, A.add, None, "RT", "RU", 16)
+        gat(ENG["Z"][t - 1], T.Z[:], T.W[:, 0:3344].indirect(T.RU[:]), WA + "RU", "Z", 256)
         mm([(P[7][:, 0:256], T.BCN[:], T.Z[:], 256)], "BCN Z", "P7")
-        mm(ext16(P[6][:, 0:16], T.ML, T.Z, 0, 16), "ML Z", "P6")
+        mm(ext16(P[5][:, 0:16], "MN", T.Z, 0, 16), "MN Z", "P5 NL")
         cp(T.NB[:], P[7][:, 0:256], "P7", "NB", 256)
-        ts(T.NL[:], P[6][:, 0:16], -4096.0, None, A.add, None, "P6", "NL", 16)
-        ts(T.NLU[:], P[6][:, 0:16], -4096.0, None, A.add, None, "P6", "NLU", 16)
+        mm(ext16(P[6][:, 0:16], "MO", T.Z, 0, 16), "MO Z", "P6")
+        cp(T.NLU[:, 0:16], P[6][:, 0:16], "P6", "NLU", 16)
+        gat(ENG["O"][t - 1], T.O1[:], T.PG[:, po + 256:po + 3584].indirect(T.NLU[:, 0:16]), PGall[(t - 1) % 2] + "NLU", "O1", 256)
         if not last:
-            mm(ext16(P[5][:, 0:16], T.MX, T.Z, 0, 16), "MX Z", "P5")
-            ts(T.NPU[:], P[5][:, 0:16], 0.0, None, A.add, None, "P5", "NPU", 16)
-        gat("a", T.O[:], T.PG[:, 256:3584].indirect(T.NLU[:]), PGall + "PGt NLU", "O", 256)
+            mm(ext16(P[6][:, 16:32], "MX", T.Z, 0, 16), "MX Z", "P6")
+            cp(T.NLU[:, 16:32], P[6][:, 16:32], "P6", "NPU", 16)
+        mm(ext16(P[6][:, 0:16], "MB", T.O1, 0, 16), "MB O1", "P6")
+        ts(T.OU[:], P[6][:, 0:16], float(FREE), None, A.min, None, "P6", "OU", 16)
+        gat(ENG["O"][t - 1], T.O[:], T.W[:, 0:3344].indirect(T.OU[:]), WA + "OU", "O", 256)
         for m in range(16):
-            ts(T.E[:, m, 0:256 - 16 * m], T.NB[:, 16 * m:256], T.NL[:, m:m + 1], None, A.is_equal, None, "NB NL", "E%d" % m, 256 - 16 * m, 0.5)
+            ts(T.E[:, m, 0:256 - 16 * m], T.NB[:, 16 * m:256], P[5][:, m:m + 1], None, A.is_equal, None, "NB NL", "E%d" % m, 256 - 16 * m, 0.5)
         parts = [([(P[7][:, 0:256], T.OCC[:], T.O[:], 256)], "OCC O")]
         for h in range(5):
             parts.append(([(P[7][:, 16 * m + 16:256], T.TWO[:], T.E[:, m, 16:256 - 16 * m], 240 - 16 * m) for m in range(3 * h, 3 * h + 3)],
                           "TWO " + " ".join("E%d" % m for m in range(3 * h, 3 * h + 3))))
         parts.append(([(P[7][:, 0:256], T.POW[:], T.E[:, :, 0:16], 256)], "POW " + " ".join("E%d" % m for m in range(16))))
         for x in group(7, 256, parts): x()
-        tt(T.WI[:], P[7][:, 0:256], T.THR[:], A.is_lt, "THR", "WI P7 A7", 256, 1.0)
+        tt(T.WI[:], P[7][:, 0:256], T.THR[:], A.is_lt, "THR", "WI P7 A7 P5", 256, 1.0)
         if not last:
-            tt(T.TR[:, 0:3328].indirect(T.NPU[:]), T.Z[:], T.WI[:], A.add, "Z WI NPU", TRall, 256, 3.8)
-        mm(ext16(P[6][:, 0:16], T.MC, T.Z, 0, 16), "MC Z", "P6", True, False)
-        mm(ext16(P[6][:, 0:16], T.MC, T.WI, 0, 16), "MC WI", "P6", False, True)
-        tt(T.RT[:], P[6][:, 0:16], T.DU2[:], A.max, "P6 DU2", "RT", 16)
+            tt(T.TR[:, 0:3328].indirect(T.NLU[:, 16:32]), T.Z[:], T.WI[:], A.add, "Z WI NPU", TRall, 256, 3.8)
+        mm(ext16(P[6][:, 0:16], "MC", T.Z, 0, 16), "MC Z", "P6", True, False)
+        mm(ext16(P[6][:, 0:16], "MC", T.WI, 0, 16), "MC WI", "P6", False, True)
+        tt(T.RT[:], P[6][:, 0:16], T.DU2[:], A.max, "P6 DU2", "RT", 16, 1.0)
         ts(T.QU[:], T.RT[:], -3840.0, None, A.add, None, "RT", "QU", 16)
-        tt(T.PG[:, 0:3584].indirect(T.QU[:]), T.Z[:], T.WI[:], A.add, "Z WI QU", PGall + "PGt", 256, 3.8)
-        mm(ext16(P[7][:, 256:448], T.MB, T.PG, 256, 192), "MB" + PGall, "P7")
-        if not last: ts(T.PU[:], P[7][:, 256:448], 3072.0, None, A.min, None, "P7", "PU", 192)
-        else: ts(T.YP[:], P[7][:, 256:448], -1.0, -1.0, A.mult, A.max, "P7", "YP", 192)
+        tt(T.PG[:, pn:pn + 3584].indirect(T.QU[:]), T.Z[:], T.WI[:], A.add, "Z WI QU", PGall[t % 2], 256, 3.8)
+        for h in range(3):
+            mm(ext16(P[7][:, 256 + 64 * h:320 + 64 * h], "MY" if last else "MB", T.PG, pn + 256 + 1024 * h, 64), "MB MY " + PGall[t % 2], "P7")
+        if not last: ts(PU, P[7][:, 256:448], float(FREE), None, A.min, None, "P7", "PU", 192)
+        else: ts(T.YP[:], P[7][:, 256:448], -1.0, None, A.max, None, "P7", "YP", 192)
 
-    dma("s", [(T.op[:], T.YP[:])], "YP", "op")
+    dma("s", [(T.sp[:], T.YP[:])], "YP", "sp")
     dma("a", [(T.yp[own, :], T.YP[own, :])], "YP", "ypo")
-    send(T.op, T.rp, T.hp, vib, "ap", "h4", False, "op")
+    send("p", 5000.0)
     ln, lp = [], []
     if rank > 0:
         ln.append((T.yn[0:rank, :], T.rn[0:rank]))
@@ -584,10 +642,10 @@ def build(g, core, rank, T, topo, via, vib):
     if rank < N - 1:
         ln.append((T.yn[rank + 1:N, :], T.rn[rank + 1:N]))
         lp.append((T.yp[16 * rank + 16:128, :], T.rp[rank + 1:N]))
-    dma("s", ln, "op yno", "yn", ext=[("an", short_all)])
-    dma("s", lp, "yn ypo", "yp", ext=[("ap", short_all)])
+    dma("s", ln, "sp mn yno", "yn", ext=[("an", short_all)])
+    dma("s", lp, "yn mp ypo", "yp", ext=[("ap", short_all)])
     return ops
 
 
-ENG = {"P0": "avvavv", "G1": "aaaaaa", "G2": "aaaaaa", "G3": "aaaaaa", "G4": "aaaaaa", "S1": "aaaaav", "S2": "aaaaav", "S3": "aaaaav", "S4": "aaaaav",
-       "T1": "vavaaa", "T2": "vavaaa", "T3": "vavaaa", "P1": "aaaaaa", "P2": "aaaaaa", "P3": "aaaaaa", "P4": "avavav"}
+ENG = {"P0": "avavav", "G1": "vvvvvv", "G2": "aaaaaa", "G3": "aaaaaa", "G4": "aaaaaa", "S1": "aaaaav", "S2": "aaaaav", "S3": "aaaaav", "S4": "aaaaav",
+       "T1": "vaaaaa", "T2": "vaaaaa", "T3": "vaaaaa", "P1": "aaaaaa", "P2": "aaaaaa", "P3": "aaaaaa", "P4": "avavav", "Z": "aaaa", "O": "aaaa"}

@@ -1,3 +1,4 @@
+import math
 import numpy as np
 from concourse.bass import DstId, RemoteDMATransfer
 from concourse.mybir import AluOpType as A, ActivationFunctionType as AF
@@ -10,7 +11,8 @@ def _sb(n, d):
     return ("sbuf", [128, n], d)
 
 
-MSG = {"f": (384, bf, True), "0": (96, bf, False), "x": (384, bf, True), "4": (96, bf, False), "2": (48, f32, False), "3": (24, f32, False),
+LATE = {"0": 8500.0, "f": 8500.0, "x": 11000.0, "2": 4300.0, "4": 5000.0, "3": 4300.0}
+MSG = {"0": (24, i32, False), "f": (384, bf, True), "x": (384, bf, True), "2": (48, f32, False), "4": (96, bf, False), "3": (48, f32, False),
        "n": (24, f32, False), "p": (24, f32, False)}
 SCRATCH = {}
 for _m, (_n, _d, _w) in MSG.items():
@@ -19,18 +21,18 @@ for _m, (_n, _d, _w) in MSG.items():
     SCRATCH["h" + _m] = ("dram", [128, _n], _d)
 SCRATCH.update({
     "X": _sb(V, bf), "F": _sb(TV * V, bf), "G2": _sb(V, bf), "D": _sb(V, bf), "PR": _sb(V, bf), "NE": _sb(V, bf),
-    "W": _sb(3344, bf), "TR": _sb(3328, bf), "PG": _sb(2 * 3584, bf),
-    "RHO": _sb(V, f32), "FV": _sb(1536, f32), "ICW": _sb(V, f32), "LW": _sb(6144, f32), "LX": _sb(6144, f32),
+    "W": _sb(2 * 3344, bf), "TR": _sb(3328, bf), "PG": _sb(2 * 3584, bf),
+    "RHO": _sb(2560, f32), "FV": _sb(1536, f32), "LW": _sb(6144, f32), "LX": _sb(6144, f32),
     "E": ("sbuf", [128, 16, 256], bf),
     "PK": _sb(24, i32), "CC": _sb(32, f32), "IOT": _sb(512, f32), "IG": _sb(128, f32), "IK": _sb(256, f32),
-    "JL": _sb(192, f32), "TMP": _sb(256, f32), "TM2": _sb(64, f32), "SG": _sb(128, bf), "MM": _sb(11 * 144, bf),
+    "JL": _sb(192, f32), "TM2": _sb(64, f32), "SG": _sb(128, bf), "MM": _sb(11 * 144, bf),
     "Y1": _sb(128, bf), "Y2": _sb(128, bf), "YM": _sb(128, bf), "YE": _sb(128, bf), "YH": _sb(128, bf), "YR": _sb(128, bf),
     "TRI": _sb(128, bf), "BCN": _sb(128, bf), "POW": _sb(128, bf), "TWO": _sb(128, bf), "OCC": _sb(128, bf),
     "ZER": _sb(208, bf), "JB": _sb(256, bf), "JF": _sb(256, f32), "TAU": _sb(256, f32), "THR": _sb(256, f32),
-    "DU1": _sb(16, f32), "DU2": _sb(16, f32), "DU3": _sb(192, f32), "MK": _sb(8, bf), "VK": _sb(384, bf),
+    "DU1": _sb(16, f32), "DU2": _sb(16, f32), "DU3": _sb(192, f32), "MK": _sb(32, bf), "MU": _sb(288, bf), "VK": _sb(384, bf),
     "CP": _sb(576, i32), "IA": _sb(768, i32), "KA": _sb(768, bf), "NH": _sb(384, bf), "RP": _sb(384, u16),
     "FA": _sb(384, f32), "FC": _sb(192, f32), "NI": _sb(192, i32), "EM": _sb(192, bf),
-    "ICF": _sb(192, f32), "ICU": _sb(192, u16),
+    "ICF": _sb(384, f32), "ICU": _sb(192, u16),
     "NF": _sb(192, f32), "NU": _sb(192, u16), "LU": _sb(192, u16), "LO": _sb(192, u16),
     "EQ": _sb(192, bf), "O1": _sb(256, bf), "OU": _sb(16, u16),
     "HI": _sb(192, bf), "LW2": _sb(192, bf), "FR": _sb(192, bf), "FS": _sb(2, bf),
@@ -47,7 +49,7 @@ SEMAPHORES = (["cv", "ca", "cp", "cg", "loc"] + ["h" + m for m in MSG] + ["a" + 
               + ["af%d" % s for s in range(8)] + ["ax%d" % s for s in range(8)] + ["d%d" % k for k in range(NDMA)])
 CH_HI, CH_LO, CH_FR, CH_FI, CH_K, CH_A = 0, 1, 2, 3, 4, 5
 STRIPS = ["ME", "MA", "MB", "MC", "MF", "ML", "MN", "MO", "MS", "MX", "MY"]
-FREE = 3328
+FREE = 3088
 CY, PEC, FIX = 0.9, 0.45, 55.0
 
 
@@ -79,65 +81,181 @@ def arrival(m, s):
     return "a%s%d" % (m, s) if MSG[m][2] else "a" + m
 
 
-def helper(g, core, T, topo, s, d, short):
-    rid, pid = topo.addr(T.cores[d], core)
-    mask = topo.mask(core, T.cores[d])
-    steps = [m for m in MSG if short or MSG[m][2]]
-    for m in steps:
-        g.wait_ge(T.sem["h" + m], 2)
-        g.remote_dma(T["r" + m][s], T["h" + m][:], T.sem[arrival(m, s)], T.sem.loc, pid, rid, mask)
-    g.wait_ge(T.sem.loc, len(topo.engines(core, T.cores[d])) * len(steps))
+def helper(g, core, T, topo, via, vib):
+    sent = 0
+    for m in MSG:
+        for s, d in [(s, d) for s in range(N) for d in range(N) if (via if MSG[m][2] else vib)[s][d] == core]:
+            rid, pid = topo.addr(T.cores[d], core)
+            g.wait_ge(T.sem["h" + m], 2)
+            g.remote_dma(T["r" + m][s], T["h" + m][:], T.sem[arrival(m, s)], T.sem.loc, pid, rid, topo.mask(core, T.cores[d]))
+            sent += len(topo.engines(core, T.cores[d]))
+    if sent: g.wait_ge(T.sem.loc, sent)
 
 
 def rank_program(g, core, T, topo):
     via, vib = routes(T, topo)
     rank = T.rank_of(core)
     if rank is None:
-        for s in range(N):
-            for d in range(N):
-                if via[s][d] == core:
-                    helper(g, core, T, topo, s, d, vib[s][d] == core)
+        helper(g, core, T, topo, via, vib)
         return
     ops = build(g, core, rank, T, topo, via, vib)
     emit(g, T, ops)
 
 
 PLAN = {}
-TRIES = 3000
+TRIES, HEAT, BIAS, NEAR, TIE = 55000, 50.0, 500.0, 50.0, 0.5
+CASES = [{"far": 1.0, "wide": 1.0, "dma": 1.0, "wake": 1.0},
+         {"gather": 1.3, "scatter": 1.55, "far": 0.8, "wide": 0.8, "dma": 0.8, "wake": 1.0},
+         {"gather": 0.7, "scatter": 0.5, "tensor": 1.2, "far": 1.3, "wide": 1.4, "dma": 1.2, "wake": 2.5}]
+EARLY, AFTER, NA = 6, "PR5", 3
+FIRST = ""
+SIGN = [(1, 3), (), (), ()]
+BANK = [(0, 1, 5, 6, 3, 7), (0, 1, 0, 1, 0, 1)]
 
 
-def schedule(ops, succ, noise, win):
+def schedule(ops):
     n, LAT = len(ops), 110.0
-    pr = [0.0] * n
-    for i in range(n - 1, -1, -1):
-        pr[i] = ops[i]["c"] + max([pr[j] + LAT + (0.0 if ops[i]["rem"] and ops[j]["e"] == "g" else ops[i]["lat"]) for j in succ[i]] + [0.0])
-    pr = [float(pr[i] + noise[i]) for i in range(n)]
-    left = [len(o["dep"]) for o in ops]
-    fin, start, busy, order, est = [0.0] * n, [0.0] * n, {}, [], {}
-    ready = {e: [] for e in "vapgs"}
+    alt = [[(e, o["alt"][e][0]) for e in "av"] if "alt" in o else [(o["e"], o["c"])] for o in ops]
+    pre = [[(d, (0.0 if ops[d]["e"] == o["e"] == "p" else LAT) + (0.0 if ops[d]["rem"] and o["e"] == "g" or d == o["soft"] else ops[d]["lat"])) for d in o["dep"]] for o in ops]
+    post = [[] for _ in ops]
     for i in range(n):
-        if left[i] == 0:
-            ready[ops[i]["e"]].append(i)
-            est[i] = ops[i]["t0"]
-    busy = {e: 0.0 for e in ready}
-    for _ in range(n):
-        t, e = min((max(min(est[i] for i in l), busy[x]), x) for x, l in ready.items() if l)
-        l = ready[e]
-        i0 = max((j for j in l if est[j] <= t), key=lambda j: (pr[j], -j))
-        lim = t + min(win, ops[i0]["c"])
-        i = max((j for j in l if est[j] <= lim), key=lambda j: (pr[j], -j))
-        start[i] = max(est[i], t)
-        busy[e] = start[i] + ops[i]["c"]
-        fin[i] = busy[e] + ops[i]["lat"]
-        order.append(i)
-        l.remove(i)
-        for j in succ[i]:
-            left[j] -= 1
-            if left[j] == 0:
-                o = ops[j]
-                est[j] = max([o["t0"]] + [fin[d] + LAT - (ops[d]["lat"] if ops[d]["rem"] and o["e"] == "g" else 0.0) for d in o["dep"]])
-                ready[o["e"]].append(j)
-    return max(fin), order, start
+        for d, x in pre[i]: post[d].append((i, x))
+    head, tail = [o["t0"] for o in ops], [o["lat"] for o in ops]
+
+    def place(seq, before, first, last, on, bias):
+        start, fin, used = [0.0] * n, [0.0] * n, {e: ([], []) for e in "vapgs"}
+        eng = [None] * n
+        for i in seq:
+            t0 = first[i]
+            for d, x in before[i]:
+                if fin[d] + x > t0: t0 = fin[d] + x
+            best = None
+            for e, c in alt[i]:
+                if on and on[i] != e: continue
+                a, b = used[e]
+                k, t = len(a), t0
+                while k and b[k - 1] > t0: k -= 1
+                while k < len(a) and a[k] < t + c:
+                    t = max(t, b[k])
+                    k += 1
+                v = t + c + (bias[i] if e == "v" else 0.0)
+                if best is None or v < best[0]: best = (v, t, c, e, k)
+            _, t, c, e, k = best
+            used[e][0].insert(k, t)
+            used[e][1].insert(k, t + c)
+            start[i], fin[i], eng[i] = t, t + c, e
+        return max(fin[i] + last[i] for i in range(n)), start, fin, eng
+
+    def topo_order(key):
+        key = list(key)
+        for i in range(n):
+            for d, _ in pre[i]:
+                if key[i] >= key[d]: key[i] = key[d] - 1e-3
+        return sorted(range(n), key=lambda i: -key[i])
+
+    def polish(key, bias):
+        r = place(topo_order(key), pre, head, tail, None, bias)
+        for _ in range(2):
+            b = place(sorted(range(n), key=lambda i: -r[2][i]), post, tail, head, r[3], bias)
+            x = place(sorted(range(n), key=lambda i: -b[2][i]), pre, head, tail, None, bias)
+            if x[0] >= r[0]: break
+            r = x
+        return r
+    key = [0.0] * n
+    for i in range(n - 1, -1, -1): key[i] = ops[i]["c"] + max([key[j] + x for j, x in post[i]] + [tail[i]])
+    first = polish(key, [BIAS] * n)
+    eng = list(first[3])
+    cost = [dict(alt[i])[eng[i]] for i in range(n)]
+    seq = {e: sorted((i for i in range(n) if eng[i] == e), key=lambda i: first[1][i]) for e in "vapgs"}
+    direct = [set(d for d, _ in pre[i]) for i in range(n)]
+    same = {}
+    for i, o in enumerate(ops): same.setdefault(o["k"], {})[o["t"]] = i
+    twin = [same[o["k"]] if o["t"] and same[o["k"]][o["t"]] == i else {o["t"]: i} for i, o in enumerate(ops)]
+
+    def times():
+        up, down = [-1] * n, [-1] * n
+        for l in seq.values():
+            for a, b in zip(l, l[1:]): up[b], down[a] = a, b
+        left = [len(pre[i]) + (up[i] >= 0) for i in range(n)]
+        order = [i for i in range(n) if not left[i]]
+        for i in order:
+            for j, _ in post[i]:
+                left[j] -= 1
+                if not left[j]: order.append(j)
+            j = down[i]
+            if j >= 0:
+                left[j] -= 1
+                if not left[j]: order.append(j)
+        if len(order) < n: return None
+        runs = []
+        for mul, before in cases:
+            r, fin = [0.0] * n, [0.0] * (n + 1)
+            for i in order:
+                t = fin[up[i]]
+                if head[i] > t: t = head[i]
+                for d, x in before[i]:
+                    if fin[d] + x > t: t = fin[d] + x
+                r[i], fin[i] = t, t + cost[i] * mul[i]
+            runs.append((max(fin[i] + tail[i] for i in ends), r, fin))
+        return sum(x[0] / w for x, w in zip(runs, norm)) / len(runs), runs, order, up, down
+
+    def longest(now, s):
+        (end, r, fin), (mul, before) = now[1][s], cases[s]
+        q, qp = [0.0] * (n + 1), list(tail)
+        for i in reversed(now[2]):
+            q[i] = t = fin[i] - r[i] + max(qp[i], q[now[4][i]])
+            for j, x in before[i]:
+                if t + x > qp[j]: qp[j] = t + x
+        rp = [max([head[i]] + [fin[d] + x for d, x in before[i]]) for i in range(n)]
+        return [v for v in range(n) if r[v] + q[v] > end - NEAR and (len(alt[v]) > 1 or r[v] > rp[v] + 1.0 or q[v] > fin[v] - r[v] + qp[v] + 1.0)], fin, rp
+    cases = [([c.get(o["g"], 1.0) for o in ops],
+              [[(d, x * (c["wide"] if "mx" in ops[d]["w"] or "mf" in ops[d]["w"] else c["far"] if ops[d]["rem"] else c["dma"] if ops[d]["dma"] else c["wake"])) for d, x in pre[i]] for i in range(n)]) for c in CASES]
+    ends, norm = [i for i in range(n) if not post[i]], [1.0] * len(cases)
+    rnd = np.random.default_rng(1)
+    now = times()
+    norm = [x[0] / now[1][0][0] for x in now[1]]
+    now = times()
+    best, crit = (now[0], now[1][0][1], list(eng)), None
+    for it in range(TRIES):
+        end = now[0]
+        if crit is None or rnd.random() < 0.05: crit, fin, rp = longest(now, int(rnd.integers(len(cases))))
+        v = crit[int(rnd.integers(len(crit)))]
+        o = e = eng[v]
+        p = seq[o].index(v)
+        if len(alt[v]) > 1 and rnd.random() < 0.5:
+            e = "av"[o == "a"]
+            k = 0
+            while k < len(seq[e]) and fin[seq[e][k]] <= rp[v]: k += 1
+            k = min(k + int(rnd.integers(4)), len(seq[e]))
+        else:
+            k = p + (1 + int(rnd.geometric(0.5)) - 1) * (1 if rnd.random() < 0.5 else -1)
+            if k < 0 or k >= len(seq[o]): continue
+            lo, hi = min(p, k), max(p, k)
+            if any(w in direct[v] or v in direct[w] for w in seq[o][lo:hi + 1]): continue
+        done = [(v, o, p)]
+        seq[o].pop(p)
+        seq[e].insert(k, v)
+        eng[v], cost[v] = e, dict(alt[v])[e]
+        if k + 1 < len(seq[e]) and rnd.random() < TIE:
+            a, b = twin[v], twin[seq[e][k + 1]]
+            for t in a:
+                if a[t] != v and t + ops[seq[e][k + 1]]["t"] - ops[v]["t"] in b:
+                    y, z = a[t], b[t + ops[seq[e][k + 1]]["t"] - ops[v]["t"]]
+                    if eng[z] == e and y != z:
+                        done.append((y, eng[y], seq[eng[y]].index(y)))
+                        seq[eng[y]].remove(y)
+                        seq[e].insert(seq[e].index(z), y)
+                        eng[y], cost[y] = e, dict(alt[y])[e]
+        x = times()
+        if x and x[0] - end <= -HEAT * (1.02 - it / TRIES) * math.log(1.0 - rnd.random()):
+            now, crit = x, None
+            if x[0] < best[0]: best = (x[0], x[1][0][1], list(eng))
+        else:
+            for y, o, p in reversed(done):
+                seq[e].remove(y)
+                seq[o].insert(p, y)
+                eng[y], cost[y] = o, dict(alt[y])[o]
+    return best[0], sorted(range(n), key=lambda i: (best[1][i], i)), best[2]
 
 
 def emit(g, T, ops):
@@ -151,6 +269,7 @@ def emit(g, T, ops):
             if w in lastw: dep.add(lastw[w])
             dep.update(readers.get(w, []))
         dep.discard(i)
+        o["soft"] = lastw.get("~" + o["e"]) if "~" + o["e"] in o["r"] else None
         for r in o["r"]: readers.setdefault(r, []).append(i)
         for w in o["w"]:
             lastw[w] = i
@@ -160,33 +279,9 @@ def emit(g, T, ops):
     for i, o in enumerate(ops):
         for d in o["dep"]: succ[d].append(i)
     if "order" not in PLAN:
-        rnd = np.random.default_rng(1)
-        kinds = {}
-        for i, o in enumerate(ops): kinds.setdefault(o["e"] + (o["w"] + o["r"][1:] + ["-"])[0], []).append(i)
-        kinds = [kinds[k] for k in sorted(kinds)]
-        noise, win = np.zeros(n), 400.0
-        best = schedule(ops, succ, noise, win)
-        free = [i for i, o in enumerate(ops) if "alt" in o]
-
-        def flip(l):
-            for i in l:
-                ops[i]["e"] = "a" if ops[i]["e"] == "v" else "v"
-                ops[i]["c"] = ops[i]["alt"][ops[i]["e"]][0]
-        for _ in range(TRIES):
-            x, w, fl = noise.copy(), win, []
-            if rnd.random() < 0.4: fl = [free[int(k)] for k in rnd.choice(len(free), int(rnd.integers(1, 3)), replace=False)]
-            for _ in range(int(rnd.integers(0 if fl else 1, 3))):
-                k = kinds[int(rnd.integers(len(kinds)))] if rnd.random() < 0.4 else [int(rnd.integers(n))]
-                x[k] += rnd.normal() * [300.0, 1500.0, 5000.0][int(rnd.integers(3))]
-            if rnd.random() < 0.03: w = float(rnd.integers(1, 10)) * 100.0
-            flip(fl)
-            r = schedule(ops, succ, x, w)
-            if r[0] <= best[0]: best, noise, win = r, x, w
-            else: flip(fl)
-        PLAN["order"] = best
-        PLAN["on"] = {i: ops[i]["e"] for i in free}
-    for i, e in PLAN["on"].items():
-        ops[i]["e"], ops[i]["f"] = e, ops[i]["alt"][e][1]
+        PLAN["order"] = schedule(ops)
+    for i, e in enumerate(PLAN["order"][2]):
+        if "alt" in ops[i]: ops[i]["e"], ops[i]["f"] = e, ops[i]["alt"][e][1]
     order = PLAN["order"][1]
     Q = {"v": g.vector, "a": g.scalar, "p": g.tensor, "g": g, "s": g.sync}
     cnt = {"v": 0, "a": 0, "p": 0, "g": 0}
@@ -196,7 +291,7 @@ def emit(g, T, ops):
         q = Q[o["e"]]
         need = {}
         for d in o["dep"]:
-            if tok[d] is None or (o["e"] == "p" and ops[d]["e"] == "p"): continue
+            if tok[d] is None or d == o["soft"] or (o["e"] == "p" and ops[d]["e"] == "p"): continue
             s, v = tok[d]
             need[s] = max(need.get(s, 0), v)
         for s, v in o["ext"]:
@@ -229,7 +324,7 @@ def emit(g, T, ops):
 
 
 def build(g, core, rank, T, topo, via, vib):
-    ops = []
+    ops, visit, kind = [], [0], [""]
 
     def names(l):
         return [x for x in l.split() if x]
@@ -237,9 +332,12 @@ def build(g, core, rank, T, topo, via, vib):
     def op(e, c, r, w, f, dma=False, lat=0.0, ext=(), t0=0.0, rem=0):
         r, w = names(r), names(w)
         w = w + [x for x in r if x[0] == "P" and x[1:].isdigit()]
-        ops.append({"e": e, "c": c, "r": r, "w": w, "f": f, "dma": dma, "lat": lat, "ext": list(ext), "t0": t0, "rem": rem})
+        k = " ".join(x[:2] + x[3:] if x[:2] == "PG" else x for x in w + ["|"] + r if x[0] not in "WF" or x in ("WI", "FR", "FS"))
+        ops.append({"g": "tensor" if e == "p" else kind[0] if e in "va" and not dma else "", "e": e, "c": c, "r": r, "w": w, "f": f, "dma": dma, "lat": lat, "ext": list(ext), "t0": t0, "rem": rem,
+                    "t": visit[0], "k": k + " %d" % sum(o["t"] == visit[0] and o["k"].rsplit(" ", 1)[0] == k and o["e"] == e for o in ops)})
 
     def cyc(n, k=1.0):
+        kind[0] = {1.56: "gather", 3.8: "scatter"}.get(k, "")
         return FIX + max(64.0, n * k) * CY
 
     def ts(out, in0, s1, s2, o0, o1, r, w, n, k=1.0):
@@ -261,12 +359,14 @@ def build(g, core, rank, T, topo, via, vib):
         if scale is not None: kw["scale"] = scale
         op("a", cyc(n, k), r, w, lambda q: q.activation(out, a, fn, **kw))
 
-    def lin(out, a, scale, bias, r, w, n):
-        act(out, a, AF.Identity, r, w, n, scale=scale, bias=bias)
-
     def either(e):
         a, v = ops.pop(), ops.pop()
         ops.append(dict(a if e == "a" else v, alt={"a": (a["c"], a["f"]), "v": (v["c"], v["f"])}))
+
+    def lin(out, a, scale, bias, r, w, n, k=1.0):
+        ts(out, a, scale, bias, A.mult, A.add, r, w, n, k)
+        act(out, a, AF.Identity, r, w, n, scale=scale, bias=bias)
+        either("a")
 
     def gat(e, out, win, r, w, n):
         cp(out, win, r, w, n, 1.56)
@@ -305,7 +405,11 @@ def build(g, core, rank, T, topo, via, vib):
         if fl: op("g", 140 + 2 * n * CY, r, w, lambda q: q.iota(out, pat, base, cm, allow_small_or_imprecise_dtypes=True))
         else: op("g", 140 + 2 * n * CY, r, w, lambda q: q.iota(out, pat, base, cm))
 
+    def sel(out, a, pat, cmp, fill, base, cm, r, w, n):
+        op("g", 180 + 2 * n * CY, r, w, lambda q: q.affine_select(out, a, pat, cmp, fill, base, cm))
+
     def strip(M, k):
+        if M == "MU": return T.MU[:, 15 - k:143 - k]
         o = 144 * STRIPS.index(M)
         return T.MM[:, o + 15 - k:o + 143 - k]
 
@@ -316,7 +420,7 @@ def build(g, core, rank, T, topo, via, vib):
     others = [d for d in range(N) if d != rank]
     P = [T["P%d" % b] for b in range(8)]
 
-    def send(m, lat, r=""):
+    def send(m, lat, r="", c=500.0):
         wide = MSG[m][2]
         route = via if wide else vib
         off = topo.engines(core, C[[d for d in others if route[rank][d] is None][0]])
@@ -336,7 +440,7 @@ def build(g, core, rank, T, topo, via, vib):
                                         src=T["s" + m][d], dst=T["h" + m][:]))
             pool = pool[:-2]
             tot += 2
-        op("g", 500.0, "s%s gq" % m + r, "gq m" + m, lambda q: q.remote_dma_fused(tr, local_sem=T.sem.loc), rem=tot, lat=lat)
+        op("g", c, "s%s gq" % m + r, "gq m" + m, lambda q: q.remote_dma_fused(tr, local_sem=T.sem.loc), rem=tot, lat=lat + 500.0 - c)
 
     def arrivals(route, s, wide):
         return (4 if wide else 2) if route[s][rank] is None else len(topo.engines(route[s][rank], core))
@@ -345,13 +449,19 @@ def build(g, core, rank, T, topo, via, vib):
     own = slice(16 * rank, 16 * rank + 16)
 
     dma("s", [(T.CP[:, 0:192], T.cc[:])], "", "CPc")
-    dma("a", [(T.CP[:, 192:384], T.pl[:]), (T.CP[:, 384:576], T.nm[:])], "", "CPp")
-    dma("a", [(T.sf[:], T.fo[:])], "", "sf", lat=3500.0, t0=150.0)
+    dma("a", [(T.s0[:], T.nm[:]), (T.CP[:, 192:384], T.pl[:]), (T.r0[rank], T.nm[rank:rank + 1, :])], "", "s0 r0 CPp ~a")
+    def staged(dst, src):
+        return [(dst[a:b], src[16 * a:16 * b, :]) for a, b in ((0, rank), (rank + 1, N)) if b > a]
+    dma("a", staged(T.sf, T.fo), "~a", "sf", lat=3500.0, t0=250.0)
 
     iota(T.PK[:, 1:9], [[16, 8]], 0, 1, "", "PI", 8, False)
     iota(T.IOT[:], [[1, 512]], 0, 0, "", "IOT", 512)
     iota(T.IK[:], [[0, 16], [1, 16]], 0, 0, "", "IK", 256)
     iota(T.IG[:], [[16, 8], [0, 16]], 15, 0, "", "IG", 128)
+    dma("s", staged(T.sx, T.tx), "", "sx", lat=3500.0, t0=4200.0)
+    send("0", LATE["0"], " PI IOT IK", 2500.0)
+    send("f", LATE["f"])
+    send("x", LATE["x"])
     col = lambda j: T.CC[:, j:j + 1]
     cK, cP, cS, cY = 0, 1, 4, 24
     ts(T.PK[:, 0:1], T.PK[:, 1:2], 15, None, A.bitwise_and, None, "PI", "PK0", 1)
@@ -375,55 +485,55 @@ def build(g, core, rank, T, topo, via, vib):
     lin(col(8), col(15), -1.0, col(16), "c15 c16", "c8", 1)
     wcol(13, [(CH_K, 1), (CH_A, 16)])
     lin(col(14), col(15), 1.0, col(13), "c15 c13", "c14", 1)
-    wcol(9, [(CH_FR, -2)])
-    wcol(10, [(CH_LO, 1), (CH_K, 1)])
-    wcol(11, [(CH_HI, 3072), (CH_A, 192)])
+    wcol(9, [(CH_FR, -4)])
+    wcol(11, [(CH_HI, 3072), (CH_A, 255)])
     lin(col(17), col(15), 64.0, 0.0, "c15", "c17", 1)
+    for d in range(2): ts(T.MU[:, 144 * d:144 * d + 144], T.IOT[:, 0:144], col(cY + d), None, A.is_equal, None, "IOT c3", "MU%d" % d, 144)
     for M, j, d in (("ME", None, 0), ("MA", 8, 0), ("MB", 8, 1), ("MC", 7, 0), ("MF", 17, 1), ("ML", 5, 1), ("MN", 5, 0), ("MO", 5, 7),
                     ("MS", cS, 0), ("MX", 13, 0), ("MY", 14, 4)):
-        o = 144 * STRIPS.index(M)
-        ts(T.MM[:, o:o + 144], T.IOT[:, 0:144], col(cY + d), 8192.0 if j is None else col(j), A.is_equal, A.mult, "IOT c3 c%d" % (j or 3), M, 144)
+        o, x = 144 * STRIPS.index(M), 8192.0 if j is None else col(j)
+        if d > 1: ts(T.MM[:, o:o + 144], T.IOT[:, 0:144], col(cY + d), x, A.is_equal, A.mult, "IOT c3 c%d" % j, M, 144)
+        else: lin(T.MM[:, o:o + 144], T.MU[:, 144 * d:144 * d + 144], x, 0.0, "MU%d c%d" % (d, j or 3), M, 144, 0.5)
     ts(T.Y1[:], T.IOT[:, 0:128], col(cP), None, A.is_equal, None, "IOT c0", "Y1a", 128)
-    for M, nm_, x in ((T.Y2, "Y2", 2.0), (T.YE, "YE", 262144.0), (T.YH, "YH", -0.5), (T.YR, "YR", 192.0), (T.YM, "YM", -2.0)):
-        lin(M[:], T.Y1[:], x, 0.0, "Y1a", nm_, 128)
-    ts(T.SG[:], T.IG[:], col(cY), None, A.is_equal, None, "IG c3", "SG", 128)
-    lin(T.TWO[:], T.SG[:], 2.0, 0.0, "SG", "TWO", 128)
-    lin(T.BCN[:], T.SG[:], col(5), 0.0, "SG c5", "BCN", 128)
+    lin(T.YR[:], T.Y1[:], 192.0, 0.0, "Y1a", "YR", 128, 0.5)
+    iota(T.ZER[:], [[0, 208]], 0, 0, "mx", "ZER", 208)
+    for M, nm_, x in ((T.Y2, "Y2", 2.0), (T.YE, "YE", 262144.0), (T.YM, "YM", -2.0), (T.YH, "YH", -0.5)):
+        sel(M[:], T.ZER[:, 0:128], [[1, 128]], A.not_equal, x, 0, -1, "ZER", nm_, 128)
+    iota(T.SG[:], [[0, 128]], 1, 0, "mx", "SG", 128)
+    sel(T.SG[:], T.SG[:], [[-16, 8], [0, 16]], A.is_ge, 0.0, 0, 1, "SG", "SG", 128)
+    sel(T.SG[:], T.SG[:], [[16, 8], [0, 16]], A.is_ge, 0.0, 15, -1, "SG", "SG", 128)
+    ts(T.TWO[:], T.IG[:], col(cY + 1), 2.0, A.is_equal, A.mult, "IG c3", "TWO", 128)
+    ts(T.BCN[:], T.IG[:], col(cY + 7), col(5), A.is_equal, A.mult, "IG c3 c5", "BCN", 128)
     lin(T.OCC[:], T.SG[:], col(9), 0.0, "SG c9", "OCC", 128)
-    ts(T.TMP[:, 0:128], T.IK[:, 0:128], col(cK), None, A.is_gt, None, "IK c1", "TMPa", 128)
-    tt(T.TMP[:, 0:128], T.TMP[:, 0:128], T.SG[:], A.mult, "TMPa SG", "TMPa", 128)
-    lin(T.TMP[:, 128:256], T.Y1[:, 0:128], 512.0, 0.0, "Y1a", "TMPb", 128)
-    tt(T.TRI[:], T.TMP[:, 0:128], T.TMP[:, 128:256], A.add, "TMPa TMPb", "TRI", 128)
-    ms(T.ZER[:], 0.0, "ZER", 208, 0.5)
-    ts(T.TMP[:], T.IK[:], 0.0, 0.5, A.not_equal, A.mult, "IK", "TMPa TMPb", 256)
-    ts(T.TAU[:], T.IK[:], 0.0, None, A.is_equal, None, "IK", "TAU", 256)
-    op("v", cyc(256), "TMPa TMPb TAU", "THR", lambda q: q.tensor_tensor_scan(T.THR[:], T.TMP[:], T.TAU[:], 0.0, A.mult, A.add))
-    tt(T.TM2[:, 16:32], T.THR[:, 0:16], OH, A.mult, "THR OH", "PW", 16)
+    sel(T.TRI[:], T.SG[:], [[1, 128]], A.is_gt, 0.0, 0, -1, "SG", "TRI", 128)
+    sel(T.TRI[:], T.TRI[:], [[1, 128]], A.not_equal, 512.0, 0, -1, "TRI", "TRI", 128)
+    ms(T.TM2[:, 16:32], 0.5, "PW", 16)
+    op("v", cyc(16), "PW ZER", "PV", lambda q: q.tensor_tensor_scan(T.TM2[:, 48:64], T.TM2[:, 16:32], T.ZER[:, 0:16], 2.0, A.mult, A.add))
+    tt(T.TM2[:, 16:32], T.TM2[:, 48:64], OH, A.mult, "PV OH", "PW", 16)
     op("v", cyc(16), "PW ZER", "PW2", lambda q: q.tensor_tensor_scan(T.TM2[:, 32:48], T.TM2[:, 16:32], T.ZER[:, 0:16], 0.0, A.add, A.add))
-    lin(T.POW[:], T.SG[:], T.TM2[:, 47:48], 0.0, "SG PW2", "POW", 128)
-    lin(T.THR[:], T.THR[:], 2.0, 2.0, "THR", "THR", 256)
-    lin(T.THR[:], T.THR[:], T.TM2[:, CH_FI:CH_FI + 1], -4.0, "THR OH", "THR", 256)
-    lin(T.JB[:], T.IOT[:, 0:256], 131072.0, -256.0 * 131072, "IOT", "JB", 256)
-    lin(T.JF[:], T.IOT[:, 0:256], 1.0, -256.0, "IOT", "JF", 256)
-    lin(T.TAU[:], T.IOT[:, 0:256], 1.0, 256.0, "IOT", "TAU", 256)
+    lin(T.POW[:], T.TWO[:], T.TM2[:, 47:48], 0.0, "TWO PW2", "POW", 128)
+    wcol(18, [(CH_FI, 4)])
+    lin(T.THR[:, 0:16], T.TM2[:, 48:64], col(18), -4.0, "PV c18", "THR", 16)
+    for n in (16, 32, 64, 128): lin(T.THR[:, n:2 * n], T.THR[:, 0:n], 1.0, 0.0, "THR", "THR", n)
+    iota(T.JB[:], [[16, 256]], -4096, 0, "mx", "JB", 256)
+    iota(T.JF[:], [[1, 256]], -256, 0, "mx", "JF", 256)
+    iota(T.TAU[:], [[1, 256]], 256, 0, "mx", "TAU", 256)
     lin(T.JL[:], T.IOT[:, 0:192], 16.0, col(cK), "IOT c1", "JL", 192)
-    lin(T.DU1[:], T.JL[:, 0:16], 1.0, -1023.5, "JL", "DU1", 16)
     lin(T.DU2[:], T.JL[:, 0:16], 1.0, 3840.0, "JL", "DU2", 16)
     lin(T.DU3[:], T.JL[:], 1.0, 3072.0, "JL", "DU3", 192)
     lin(T.VK[:, 0:192], T.IOT[:, 0:192], 0.0, col(cK), "IOT c1", "VK", 192)
-    lin(T.VK[:, 192:384], T.IOT[:, 0:192], 1.0, 0.0, "IOT", "VA", 192)
-    for t in range(1, TV + 1):
-        ks = (S * t % V) % 16
-        ts(T.MK[:, 2 * t - 2:2 * t - 1], col(cK), float(ks), None, A.is_lt, None, "c1", "MK%d" % t, 1)
-        ts(T.MK[:, 2 * t - 1:2 * t], col(cK), float(ks), None, A.is_ge, None, "c1", "ML%d" % t, 1)
-    ms(T.W[:, 0:V], 0.0, "Wd Wb Wf", V, 0.5)
-    lin(T.W[:, V:3328], T.IOT[:, 0:256], col(10), col(11), "IOT c10 c11", "Wt", 256)
-    lin(T.W[:, FREE:3344], T.IOT[:, 0:16], 0.0, T.TM2[:, CH_FR:CH_FR + 1], "IOT OH", "Wu", 16)
-    for b in range(2): lin(T.PG[:, 3584 * b + 3328:3584 * b + 3584], T.IOT[:, 0:256], 0.0, col(6), "IOT c6", "PGt%d" % b, 256)
-    ms(T.BC[:], 0.0, "BCa BCb", 210, 0.5)
-    ms(T.BC[:, 0:1], -256.0, "BCa", 1)
-    ms(T.BS[:], 0.0, "BS", 16)
-    ms(T.CU[:], 0.0, "CU", 200)
+    iota(T.VK[:, 192:384], [[1, 192]], 0, 0, "mx", "VA", 192)
+    ts(T.MK[:, 0:16], T.IK[:, 0:16], col(cK), None, A.is_gt, None, "IK c1", "MK0", 16)
+    lin(T.MK[:, 16:32], T.MK[:, 0:16], -1.0, 1.0, "MK0", "MK1", 16)
+    ms(T.W[:, 0:V], 0.0, "Wd0 Wb0 Wf0", V, 0.5)
+    lin(T.W[:, V:FREE], T.IOT[:, 0:16], 0.0, col(11), "IOT c11", "Wt0", 16)
+    lin(col(12), col(6), 4.0, T.TM2[:, CH_FR:CH_FR + 1], "c6 OH", "c12", 1)
+    lin(T.W[:, FREE:FREE + 16], T.IOT[:, 0:16], 0.0, col(12), "IOT c12", "Wu0", 16)
+    for b in range(2): lin(T.PG[:, 3584 * b + 3328:3584 * b + 3344], T.IOT[:, 0:16], 0.0, col(6), "IOT c6", "PGt%d" % b, 16)
+    iota(T.BC[:, 192:210], [[0, 18]], 0, 0, "mx", "BCb", 18)
+    iota(T.BC[:, 0:1], [[0, 1]], -256, 0, "mx", "BCa", 1)
+    iota(T.BS[:], [[0, 16]], 0, 0, "mx", "BS", 16)
+    iota(T.CU[:, 192:200], [[0, 8]], 0, 0, "mx", "CU", 8)
     ms(T.YP[:], -8192.0, "YP", 192)
     for j in range(3): lin(T.FV[:, 512 * j:512 * j + 512], T.IOT[:], 1.0, 4096.0 + 1024 * j, "IOT", "FV%d" % j, 512)
 
@@ -431,9 +541,9 @@ def build(g, core, rank, T, topo, via, vib):
     ts(T.IA[:, 192:384], T.CP[:, 0:192], 4, None, A.logical_shift_right, None, "CPc", "IA1", 192)
     cp(T.KA[:, 0:384], T.IA[:, 0:384], "IA0 IA1", "KAc", 384)
 
-    def rows(ch, src):
-        return [(T.W[ch:128:16, 0:V], src)]
-    dma("s", rows(CH_K, T.KA[:, 0:192]) + rows(CH_A, T.KA[:, 192:384]), "KAc", "Wb")
+    def rows(ch, src, b=0):
+        return [(T.W[ch:128:16, 3344 * b:3344 * b + V], src)]
+    dma("s", rows(CH_K, T.KA[:, 0:192]) + rows(CH_A, T.KA[:, 192:384]), "KAc", "Wb0")
     dma("s", [(T.LW[0:128:16, 0:V], T.YP[:]), (T.LX[0:128:16, 0:V], T.YP[:])], "YP KAc", "LW LX")
     ts(T.IA[:, 384:576], T.CP[:, 192:384], 15, None, A.bitwise_and, None, "CPp", "IA2", 192)
     ts(T.IA[:, 576:768], T.CP[:, 192:384], 4, None, A.logical_shift_right, None, "CPp", "IA3", 192)
@@ -442,36 +552,39 @@ def build(g, core, rank, T, topo, via, vib):
         mm([(P[3][:, 192 * h:192 * h + 192], T.YR[:], T.KA[:, 384 * h:384 * h + 192], 192),
             (P[3][:, 192 * h:192 * h + 192], T.Y1[:, 0:128], T.KA[:, 384 * h + 192:384 * h + 384], 192)], "YR Y1a KAc KAp", "P3")
     ts(T.RP[:], P[3][:, 0:384], float(FREE), None, A.min, None, "P3", "RP PU", 384)
-    cp(T.NH[:, 0:192], T.CP[:, 384:576], "CPp", "NH0", 192)
-    tt(T.NH[:, 192:384], T.CP[:, 384:576], T.NH[:, 0:192], A.subtract, "CPp NH0", "NH1", 192)
-    l = []
-    for ch, src, o in ((0, T.KA, 0), (1, T.KA, 192), (2, T.NH, 0), (3, T.NH, 192)):
-        l += [(T.s0[:, 32 * ch:32 * ch + 32, :], src[:, o:o + 192]), (T.r0[rank, 32 * ch:32 * ch + 32, :], src[own, o:o + 192])]
-    dma("s", l, "KAc NH0 NH1", "s0 r0")
-    dma("s", [(T.sx[:], T.tx[:])], "NH1", "sx", lat=3500.0)
+
     def slot(q):
         return slice(16 * (q % N), 16 * (q % N) + 16)
-    dma("s", [(T.F[slot(rank + 1), 0:V], T.fo[own, :]), (T.X[own, :], T.tx[own, :]), (T.rf[rank], T.fo[own, :])], "sx", "F%d X%d" % (rank, rank))
-    send("f", 9000.0, " PI IOT IK IG")
-    send("0", 6000.0)
-    send("x", 9000.0)
-    iota(T.RHO[:], [[1, 192], [192, 16]], 32, 0, "gq", "RHO", V)
+    dma("s", [(T.F[slot(rank + 1), 0:V], T.fo[own, :]), (T.X[own, :], T.tx[own, :])], "sx", "F%d X%d" % (rank, rank), t0=9000.0)
+    iota(T.RHO[:, 0:512 * NA], [[1, 32 * NA], [192, 16]], 8192, 0, "mx", "RHO", 512 * NA)
 
     PU = T.RP[:, 192:384]
-    WA = "Wd Wb Wt Wu Wf "
+    WW = [T.W[:, 3344 * b:3344 * b + FREE + 16] for b in range(2)]
+    WR = ["Wd%d Wb%d Wt%d Wu%d Wf%d " % (b, b, b, b, b) for b in range(2)]
 
-    def pgather(t):
+    def pgather(t, js=range(6), after=""):
         o = 3584 * (t % 2) + 256
-        for j in range(6):
-            gat(ENG["P%d" % t][j], T.PG[:, o + 512 * j:o + 512 * j + 512], T.W[:, 0:3344].indirect(T.RP[:, 192 + 32 * j:224 + 32 * j]), WA + "PU",
+        for j in js:
+            gat(ENG["P%d" % t][j], T.PG[:, o + 512 * j:o + 512 * j + 512], WW[t % 2].indirect(T.RP[:, 192 + 32 * j:224 + 32 * j]), WR[t % 2] + "PU" + after,
                 "PG%d%d" % (t % 2, j), 512)
+
+    def enter(t):
+        pn, last = 3584 * (t % 2), t == TV
+        tt(T.PG[:, pn:pn + 3328].indirect(T.QU[:]), T.Z[:], T.WI[:], A.add, "Z WI QU", PGall[t % 2], 256, 3.8)
+        for h in range(3):
+            mm(ext16(P[3][:, 256 + 64 * h:320 + 64 * h], "MY" if last else "MB", T.PG, pn + 256 + 1024 * h, 64), "MB MY " + PGall[t % 2], "P3")
+        if not last: ts(PU, P[3][:, 256:448], float(FREE), None, A.min, None, "P3", "PU", 192)
+        else: ts(T.YP[:], P[3][:, 256:448], -1.0, None, A.max, None, "P3", "YP", 192)
     PGall = [" ".join("PG%d%d" % (b, j) for j in range(6)) + " PGt%d " % b for b in range(2)]
     TRall = " TR0 TR1 TR2 TR3 TR4 TR5 "
     pgather(0)
-    chans = (CH_K, CH_A, CH_FR, CH_FI)
-    dma("s", [x for k, ch in enumerate(chans) for x in ((T.s4[:, 32 * k:32 * k + 32, :], T.PG[ch:128:16, 256:3328]),
-                                                        (T.r4[rank, 32 * k:32 * k + 32, :], T.PG[16 * rank + ch:16 * rank + ch + 1, 256:3328]))], PGall[0], "s4 r4")
-    send("4", 5000.0)
+    for h in range(2):
+        c = slice(3344 + 1536 * h, 3344 + 1536 * h + 1536)
+        ms(T.W[:, c], 0.0, "Wd1 Wb1 Wf1", 1536, 0.5)
+        act(T.W[:, c], T.FV[:], AF.Copy, "", "Wd1 Wb1 Wf1", 1536, scale=0.0)
+        either("v")
+        ops[-1]["r"] += ["FV0", "FV1", "FV2"]
+    lin(T.W[:, 3344 + V:3344 + FREE + 16], T.W[:, V:FREE + 16], 1.0, 0.0, "Wt0 Wu0", "Wt1 Wu1", 32, 0.5)
     for j in range(3):
         c = slice(64 * j, 64 * j + 64)
         b = 4 + j % 2
@@ -486,23 +599,35 @@ def build(g, core, rank, T, topo, via, vib):
     g0 = slice(16 * rank, 16 * rank + 1)
     dma("a", [(T.s2[:, 0:64, :], T.LW[0:128:16, 0:V]), (T.s2[:, 64:128, :], T.LX[0:128:16, 0:V]),
               (T.r2[rank, 0:64, :], T.LW[g0, 0:V]), (T.r2[rank, 64:128, :], T.LX[g0, 0:V])], "LW LX", "s2 r2")
-    send("2", 5000.0)
+    send("2", LATE["2"])
+    dma("s", [(T.s4[:, 32 * k:32 * k + 32, :], T.PG[ch:128:16, 256:3328]) for k, ch in enumerate((CH_K, CH_A))]
+        + [(T.s4[:, 64 + 32 * k:96 + 32 * k, :], T.KA[:, 192 * k:192 * k + 192]) for k in range(2)], PGall[0] + "KAc LO2", "s4")
+    dma("s", [(T.r4[rank], T.s4[rank]), (T.rf[rank], T.fo[own, :])], "s4", "r4")
+    send("4", LATE["4"])
     for j in range(6):
-        act(T.ICW[:, 0:V].indirect(T.RP[:, 32 * j:32 * j + 32]), T.RHO[:, 512 * j:512 * j + 512], AF.Silu, "RHO RP", "ICW", 512, 3.8)
-    dma("a", [(T.s3[:], T.ICW[0:128:16, :]), (T.r3[rank], T.ICW[g0, :])], "ICW", "s3 r3")
-    send("3", 5000.0)
+        if j < NA: act(T.LX[:, 0:V].indirect(T.RP[:, 32 * j:32 * j + 32]), T.RHO[:, 512 * j:512 * j + 512], AF.Silu, "RHO RP", "LX", 512, 3.8)
+        else: ts(T.LW[:, 0:V].indirect(T.RP[:, 32 * j:32 * j + 32]), T.RHO[:, 0:512], 1.0, 32.0 * j, A.mult, A.add, "RHO RP", "LW", 512, 3.8)
+    dma("a", [(T.s3[:, 0:64, :], T.LW[0:128:16, 0:V]), (T.s3[:, 64:128, :], T.LX[0:128:16, 0:V]),
+              (T.r3[rank, 0:64, :], T.LW[g0, 0:V]), (T.r3[rank, 64:128, :], T.LX[g0, 0:V])], "LW LX", "s3 r3")
+    send("3", LATE["3"])
 
-    dma("s", [(T.W[ch:128:16, 0:V], T.r0[:, 32 * k:32 * k + 32, :]) for k, ch in enumerate((CH_K, CH_A, CH_HI, CH_LO))], "r0 m0", "Wd Wb", ext=[("a0", short_all)])
+    dma("s", [(T.CP[:, 384:576], T.r0[:])], "r0 m0", "CPn", ext=[("a0", short_all)])
+    cp(T.NH[:, 0:192], T.CP[:, 384:576], "CPn", "NH0", 192)
+    tt(T.NH[:, 192:384], T.CP[:, 384:576], T.NH[:, 0:192], A.subtract, "CPn NH0", "NH1", 192)
+    dma("s", rows(CH_HI, T.NH[:, 0:192]) + rows(CH_LO, T.NH[:, 192:384]), "NH0 NH1", "Wd0")
     for s in others:
-        dma("s", [(T.F[slot(s + 1), 0:V], T.rf[s])], "mf", "F%d" % s, ext=[("af%d" % s, arrivals(via, s, True))])
+        dma("s", [(T.F[slot(s + 1), 0:V], T.rf[s])], "mf NH1 ~s", "F%d ~s" % s, ext=[("af%d" % s, arrivals(via, s, True))])
     for s in others:
-        dma("s", [(T.X[slot(s), :], T.rx[s])], "mx", "X%d" % s, ext=[("ax%d" % s, arrivals(via, s, True))])
+        dma("s", [(T.X[slot(s), :], T.rx[s])], "mx ~s", "X%d ~s" % s, ext=[("ax%d" % s, arrivals(via, s, True))])
     Fall = " ".join("F%d" % s for s in range(N)) + " "
     Xall = " ".join("X%d" % s for s in range(N)) + " "
-    mm(ext16(P[3][:, 0:192], "MN", T.W, 0, 192), "Wd Wb Wf MN", "P3")
+    mm(ext16(P[3][:, 0:192], "MN", T.W, 0, 192), "Wd0 Wb0 Wf0 MN", "P3")
     ts(T.NU[:], P[3][:, 0:192], 0.0, None, A.add, None, "P3", "NU", 192)
-    act(T.NF[:], P[3][:, 0:192], AF.Copy, "P3 ICW", "NF", 192)
-    dma("s", [(T.PG[ch:128:16, 256:3328], T.r4[:, 32 * k:32 * k + 32, :]) for k, ch in enumerate(chans[:3])], "r4 m4", PGall[0], ext=[("a4", short_all)])
+    scl(T.NF[:], P[3][:, 0:192], 1.0, "P3", "NF", 192)
+    dma("s", [(T.PG[ch:128:16, 256:3328], T.r4[:, 32 * k:32 * k + 32, :]) for k, ch in enumerate((CH_K, CH_A))]
+        + [(T.PG[CH_FR:128:16, 256:3328], T.PG[CH_FI:128:16, 256:3328])]
+        + [x for b in range(2) for x in rows(CH_K, T.r4[:, 64:96, :], b) + rows(CH_A, T.r4[:, 96:128, :], b)],
+        Xall + "r4 m4 m2", PGall[0] + "Wb0 Wb1", ext=[("a4", short_all)])
     mm(ext16(P[7][:, 256:448], "MB", T.PG, 256, 192), "MB " + PGall[0], "P7")
     ts(PU, P[7][:, 256:448], float(FREE), None, A.min, None, "P7", "PU", 192)
     dma("s", [(T.FA[p, 192 * h:192 * h + 192], T.r2[r, 64 * h:64 * h + 64, :]) for h in range(2) for p, r in ((slice(16, 128), slice(0, 7)), (slice(0, 16), 7))],
@@ -510,52 +635,71 @@ def build(g, core, rank, T, topo, via, vib):
     tt(T.NI[:], T.FA[:, 0:192], T.FA[:, 192:384], A.max, "FA", "NI", 192)
     ts(T.LU[:], T.NI[:], -4096.0, 0.0, A.add, A.max, "NI", "LU0 LU1 LU2", 192)
     ts(P[4][:, 0:192], T.NI[:], -4096.0, None, A.add, None, "NI", "P4", 192)
-    ts(T.EM[:], T.NI[:], 0.0, -2.0, A.is_lt, A.mult, "NI", "EM", 192)
-    dma("s", [(T.ICF[:], T.r3[:])], "r3 m3", "ICF", ext=[("a3", short_all)])
-    ts(T.ICU[:], T.ICF[:], -31.75, None, A.add, None, "ICF", "ICU", 192)
+    act(T.EM[:], P[4][:, 0:192], AF.Relu, "P4", "EM", 192, scale=-64.0)
+    dma("s", [(T.ICF[:, 192 * h:192 * h + 192], T.r3[:, 64 * h:64 * h + 64, :]) for h in range(2)], "r3 m3", "ICF", ext=[("a3", short_all)])
+    tt(T.ICF[:, 0:192], T.ICF[:, 0:192], T.ICF[:, 192:384], A.max, "ICF", "ICF", 192)
+    ts(T.ICU[:], T.ICF[:, 0:192], -8191.75, None, A.add, None, "ICF", "ICU", 192)
 
     for t in range(1, TV + 1):
+        visit[0] = t
         s0 = S * t % V
         cs = s0 // 16
         last = t == TV
         Ft = T.F[:, V * t - V:V * t]
         if t > 1: Fall = "Ft%d " % t
-        if last: dma("s", rows(CH_K, T.VK[:, 0:192]) + rows(CH_A, T.VK[:, 192:384]), "VK VA", "Wb")
+        if last: dma("s", rows(CH_K, T.VK[:, 0:192]) + rows(CH_A, T.VK[:, 192:384]), "VK VA", "Wb0")
+        wb = t % 2
+        Wt, WA = WW[wb], WR[wb]
         for j in range(6):
             gat(ENG["G%d" % t][j], T.G2[:, 512 * j:512 * j + 512], Ft.indirect(T.NU[:, 32 * j:32 * j + 32]), Fall + "NU", "G%d" % j, 512)
         if not last:
             dma("s", [(T.F[16 * t + 16:128, V * t:V * t + V], T.rf[0:7 - t]), (T.F[0:16 * t + 16, V * t:V * t + V], T.rf[7 - t:8])],
-                Fall + Xall + ("FA" if t == 1 else "G5"), "Ft%d" % (t + 1), lat=3500.0)
-        tt(P[3][:, 0:192], P[4][:, 0:192], T.NF[:], A.subtract, "P4 NF", "P3", 192, 1.0)
-        ts(T.EQ[:], P[3][:, 0:192], 0.0, None, A.is_equal, None, "P3", "EQ", 192)
+                Fall + Xall + ("FA r4" if t == 1 else "G5"), "Ft%d" % (t + 1), lat=3500.0)
+        tt(P[4][:, 256:448], P[4][:, 0:192], T.NF[:], A.subtract, "P4 NF", "P4", 192, 1.0)
+        ts(T.EQ[:], P[4][:, 256:448], 0.0, None, A.is_equal, None, "P4", "EQ", 192)
         parts = [(ext16(P[2][:, 64 * h:64 * h + 64], "ME", T.NE, 1024 * h, 64), "ME NE%d NE%d" % (2 * h, 2 * h + 1)) for h in range(3)]
         parts.append(([(P[2][:, 0:192], T.YE[:], T.EQ[:], 192)], "YE EQ"))
         if t > 1: parts += [(ext16(P[2][:, 64 * h:64 * h + 64], "MF", T.TR, 1024 * h, 64), "MF" + TRall) for h in range(3)]
-        else: parts.append(([(P[2][:, 0:192], T.YE[:], T.EM[:], 192)], "YE EM"))
+        else: parts.append(([(P[2][:, 0:192], T.YM[:], T.EM[:], 192)], "YM EM"))
         parts = group(2, 192, parts)
         for j in range(6):
             c = slice(512 * j, 512 * j + 512)
-            b = j % 2
-            tt(T.D[:, c], Ft.indirect(T.LU[:, 32 * j:32 * j + 32]), T.G2[:, c], A.subtract, Fall + "LU%d G%d" % (j // 2, j), "D%d" % j, 512, 1.56)
-            mm([(P[b][:], T.YM[:], T.X[:, c], 512), (P[b][:], T.Y2[:], T.G2[:, c], 512)], Xall + "YM Y2 G%d" % j, "P%d" % b, True, False)
-            mm([(P[b][:], T.Y1[:, 0:128], T.D[:, c], 512)], "Y1a D%d" % j, "P%d" % b, False, True)
-            tt(T.PR[:, c], P[b][:], T.D[:, c], A.mult, "P%d D%d" % (b, j), "PR%d" % j, 512, 1.0)
+            b = BANK[t > 1][j]
+            if j in SIGN[t - 1]:
+                act(T.PR[:, c], Ft.indirect(T.LU[:, 32 * j:32 * j + 32]), AF.Copy, Fall + "LU%d" % (j // 2), "PR%d" % j, 512, 1.56)
+                mm([(P[b][:], T.YM[:], T.G2[:, c], 512), (P[b][:], T.Y2[:], T.PR[:, c], 512)], "YM Y2 G%d PR%d" % (j, j), "P%d" % b)
+                act(T.D[:, c], P[b][:], AF.Sign, "P%d" % b, "D%d" % j, 512)
+            else:
+                tt(T.D[:, c], Ft.indirect(T.LU[:, 32 * j:32 * j + 32]), T.G2[:, c], A.subtract, Fall + "LU%d G%d" % (j // 2, j), "D%d" % j, 512, 1.56)
+        for j in range(6):
+            c = slice(512 * j, 512 * j + 512)
+            b = BANK[t > 1][j]
+            x, a = ([(P[b][:], T.YM[:], T.X[:, c], 512)], Xall + "YM"), ([(P[b][:], T.Y1[:], T.D[:, c], 512)], "Y1a D%d" % j)
+            n = ([(P[b][:], T.Y2[:], T.G2[:, c], 512)], "Y2 G%d" % j)
+            if j in SIGN[t - 1]: a, n = ([(P[b][:], T.Y1[:], T.PR[:, c], 512)], "Y1a PR%d" % j), ([(P[b][:], T.Y1[:], T.G2[:, c], 512)], "Y1a G%d" % j)
+            one, two, three = (n, a, x) if t == 1 else (x, n, a)
+            mm(one[0] + two[0], one[1] + " " + two[1], "P%d" % b, True, False)
+            mm(three[0], three[1], "P%d" % b, False, True)
+            tt(T.PR[:, c], P[b][:], T.D[:, c], A.mult, "P%d D%d " % (b, j) + (FIRST if t == 1 else ""), "PR%d" % j, 512, 1.0)
             ts(T.NE[:, c], T.PR[:, c], 0.0, 0.5, A.is_lt, A.subtract, "PR%d" % j, "NE%d" % j, 512, 0.5)
             act(T.NE[:, c], T.PR[:, c], AF.Sign, "PR%d" % j, "NE%d" % j, 512, bias=-0.5, scale=-1.0)
             either(ENG["S%d" % t][j])
+        if t > 1:
+            pgather(t - 1, range(EARLY, 6), " " + AFTER)
+            enter(t - 1)
         for x in parts: x()
         ts(T.FR[:], P[2][:, 0:192], 4096.0, None, A.is_lt, None, "", "FR P2 A2", 192)
-        dma("s", rows(CH_FR, T.FR[:]), "FR", "Wf")
-        tt(T.FC[:], P[3][:, 0:192], T.FR[:], A.mult, "P3 FR", "FC0 FC1 FC2", 192, 1.0)
+        dma("s", rows(CH_FR, T.FR[:], wb), "FR", "Wf%d" % wb)
+        tt(T.FC[:], P[4][:, 256:448], T.FR[:], A.mult, "P4 FR", "FC0 FC1 FC2", 192, 1.0)
         tt(T.NF[:], P[4][:, 0:192], T.FC[:], A.subtract, "P4 FC0 FC1 FC2", "NF", 192, 1.0)
         scl(T.HI[:], T.NF[:], 1.0, "NF", "HI", 192)
         tt(T.LW2[:], T.NF[:], T.HI[:], A.subtract, "NF HI", "LO2", 192)
-        dma("s", rows(CH_HI, T.HI[:]) + rows(CH_LO, T.LW2[:]), "HI LO2", "Wd")
+        dma("s", rows(CH_HI, T.HI[:], wb) + rows(CH_LO, T.LW2[:], wb), "HI LO2", "Wd%d" % wb)
         if not last:
             cp(T.NU[:], T.NF[:], "NF", "NU", 192)
             for j in range(3):
                 for h in (2 * j, 2 * j + 1):
-                    gat(ENG["T%d" % t][h], T.TR[:, 512 * h:512 * h + 512], T.W[:, 0:3344].indirect(T.ICU[:, 32 * h:32 * h + 32]), WA + "ICU", "TR%d" % h, 512)
+                    gat(ENG["T%d" % t][h], T.TR[:, 512 * h:512 * h + 512], Wt.indirect(T.ICU[:, 32 * h:32 * h + 32]), WA + "ICU", "TR%d" % h, 512)
                 mm(ext16(P[4][:, 64 * j:64 * j + 64], "ML", T.TR, 1024 * j, 64), "ML TR%d TR%d" % (2 * j, 2 * j + 1), "P4")
                 cp(T.LU[:, 64 * j:64 * j + 64], P[4][:, 64 * j:64 * j + 64], "P4", "LU%d" % j, 64)
         else:
@@ -567,21 +711,21 @@ def build(g, core, rank, T, topo, via, vib):
             dma("s", [(T.sn[q], T.TN[0:96, 32 * q:32 * q + 32]) for q in others], "TN", "sn")
             dma("s", [(T.yn[rank:rank + 1, :], T.TN[0:96, 32 * rank:32 * rank + 32])], "TN", "yno")
             send("n", 5000.0)
-        pgather(t)
-        po, pn = 3584 * ((t - 1) % 2), 3584 * (t % 2)
-        ts(T.FS[:], T.MK[:, 2 * t - 2:2 * t], T.FR[:, cs:cs + 1], None, A.mult, None, "MK%d ML%d FR" % (t, t), "FS", 2)
+        pgather(t, range(6 if last else EARLY))
+        po = 3584 * ((t - 1) % 2)
+        ts(T.FS[:], T.MK[:, s0 % 16:32:16], T.FR[:, cs:cs + 1], None, A.mult, None, "MK0 MK1 FR", "FS", 2)
         cols = ((0, cs, T.FR[:, 0:cs]), (cs + 2, 193, T.FR[:, cs + 1:192]), (cs, cs + 2, T.FS[:]))
         mm([(P[5][:, a:b_], T.SG[:], src, b_ - a) for a, b_, src in cols], "SG FR FS", "P5", each=True)
         op("v", cyc(193), "P5 ZER", "U P5", lambda q: q.tensor_tensor_scan(T.U[:, 0:193], P[5][:, 0:193], T.ZER[:, 0:193], -256.0, A.add, A.add))
         Uc = T.U[:, cs:cs + 1]
         ts(T.DB[:, 0:1], Uc, T.U[:, 192:193], -256.0, A.subtract, A.max, "U", "DB0", 1)
-        ts(T.BC[:, 1:cs + 2], T.U[:, 0:cs + 1], T.DB[:, 0:1], None, A.min, None, "U DB0", "BCa", cs + 1)
-        ts(T.DB[:, 1:2], T.DB[:, 0:1], Uc, Uc, A.min, A.subtract, "U DB0", "DB1", 1)
-        ts(T.BC[:, cs + 2:194], T.U[:, cs + 1:193], T.DB[:, 1:2], None, A.add, None, "U DB1", "BCb", 192 - cs)
+        ts(T.DB[:, 1:2], Uc, 256.0, T.U[:, 192:193], A.add, A.min, "U", "DB1", 1)
+        ts(T.BC[:, 1:cs + 1], T.U[:, 0:cs], T.DB[:, 0:1], None, A.min, None, "U DB0", "BCa", cs)
+        ts(T.BC[:, cs + 1:194], T.U[:, cs:193], T.DB[:, 1:2], None, A.subtract, None, "U DB1", "BCb", 193 - cs)
         for x in group(6, 193, [([(P[6][:, a:b_], T.TRI[:], src, b_ - a) for a, b_, src in cols], "TRI FR FS"),
                                 ([(P[6][:, 0:193], T.Y1[:, 0:128], T.BC[:, 0:193], 193)], "Y1a BCa BCb")]): x()
         scl(T.CU[:, 0:193], P[6][:, 0:193], 1.0, "", "CU P6 A6", 193)
-        mm([(P[5][:, 200:201], strip("ME", k), T.BC[:, 16 * k + 16:16 * k + 17], 1) for k in range(12)], "ME BCa BCb", "P5")
+        mm([(P[5][:, 200:201], strip("MU", k), T.BC[:, 16 * k + 16:16 * k + 17], 1) for k in range(12)], "MU0 BCa BCb", "P5")
         mm(ext16(P[7][:, 448:461], "ME", T.BC, 1, 13), "ME BCa BCb", "P7")
         scl(T.BS[:, 0:13], P[7][:, 448:461], 1.0 / 131072, "P7", "BS", 13)
         ts(T.L1[:], T.JB[:], P[5][:, 200:201], None, A.is_ge, None, "JB P5", "L1", 256, 0.5)
@@ -596,21 +740,20 @@ def build(g, core, rank, T, topo, via, vib):
         tt(T.SE[:], T.CU[:, 0:194].indirect(T.KU[:]), T.TAU[:], A.is_equal, "CU KU TAU", "SE", 256, 1.56)
         mm(ext16(P[5][:, 0:16], "MS", T.SE, 0, 16) + [(P[5][:, 0:16], T.Y1[:, 0:128], T.KB[:, 0:16], 16), (P[5][:, 0:16], T.YH[:], T.KB[:, 16:32], 16)],
            "MS Y1a YH KB KC SE", "P5")
-        tt(T.RT[:], P[5][:, 0:16], T.DU1[:], A.min, "P5 DU1", "RT", 16, 1.0)
-        ts(T.RU[:], T.RT[:], 4095.5, None, A.add, None, "RT", "RU", 16)
-        gat(ENG["Z"][t - 1], T.Z[:], T.W[:, 0:3344].indirect(T.RU[:]), WA + "RU", "Z", 256)
+        ts(T.RU[:], P[5][:, 0:16], 4095.5, float(V), A.add, A.min, "P5", "RU", 16)
+        gat(ENG["Z"][t - 1], T.Z[:], Wt.indirect(T.RU[:]), WA + "RU", "Z", 256)
         mm([(P[7][:, 0:256], T.BCN[:], T.Z[:], 256)], "BCN Z", "P7")
-        mm(ext16(P[5][:, 0:16], "MN", T.Z, 0, 16), "MN Z", "P5 NL")
+        mm(ext16(P[5][:, 0:16], "MO", T.Z, 0, 16), "MO Z", "P5 NL")
         cp(T.NB[:], P[7][:, 0:256], "P7", "NB", 256)
-        mm(ext16(P[6][:, 0:16], "MO", T.Z, 0, 16), "MO Z", "P6")
-        cp(T.NLU[:, 0:16], P[6][:, 0:16], "P6", "NLU", 16)
-        gat(ENG["O"][t - 1], T.O1[:], T.PG[:, po + 256:po + 3584].indirect(T.NLU[:, 0:16]), PGall[(t - 1) % 2] + "NLU", "O1", 256)
+        cp(T.NLU[:, 0:16], P[5][:, 0:16], "NL", "NLU", 16)
+        gat(ENG["O"][t - 1], T.O1[:], T.PG[:, po + 256:po + 3344].indirect(T.NLU[:, 0:16]), PGall[(t - 1) % 2] + "NLU", "O1", 256)
         if not last:
-            mm(ext16(P[6][:, 16:32], "MX", T.Z, 0, 16), "MX Z", "P6")
-            cp(T.NLU[:, 16:32], P[6][:, 16:32], "P6", "NPU", 16)
+            mm(ext16(P[3][:, 16:32], "MX", T.Z, 0, 16), "MX Z", "P3")
+            tt(T.RT[:], P[3][:, 16:32], T.DU3[:, 0:16], A.min, "P3 DU3", "RT", 16, 1.0)
+            cp(T.NLU[:, 16:32], T.RT[:], "RT", "NPU", 16)
         mm(ext16(P[6][:, 0:16], "MB", T.O1, 0, 16), "MB O1", "P6")
         ts(T.OU[:], P[6][:, 0:16], float(FREE), None, A.min, None, "P6", "OU", 16)
-        gat(ENG["O"][t - 1], T.O[:], T.W[:, 0:3344].indirect(T.OU[:]), WA + "OU", "O", 256)
+        gat(ENG["O"][t - 1], T.O[:], Wt.indirect(T.OU[:]), WA + "OU", "O", 256)
         for m in range(16):
             ts(T.E[:, m, 0:256 - 16 * m], T.NB[:, 16 * m:256], P[5][:, m:m + 1], None, A.is_equal, None, "NB NL", "E%d" % m, 256 - 16 * m, 0.5)
         parts = [([(P[7][:, 0:256], T.OCC[:], T.O[:], 256)], "OCC O")]
@@ -626,11 +769,7 @@ def build(g, core, rank, T, topo, via, vib):
         mm(ext16(P[6][:, 0:16], "MC", T.WI, 0, 16), "MC WI", "P6", False, True)
         tt(T.RT[:], P[6][:, 0:16], T.DU2[:], A.max, "P6 DU2", "RT", 16, 1.0)
         ts(T.QU[:], T.RT[:], -3840.0, None, A.add, None, "RT", "QU", 16)
-        tt(T.PG[:, pn:pn + 3584].indirect(T.QU[:]), T.Z[:], T.WI[:], A.add, "Z WI QU", PGall[t % 2], 256, 3.8)
-        for h in range(3):
-            mm(ext16(P[7][:, 256 + 64 * h:320 + 64 * h], "MY" if last else "MB", T.PG, pn + 256 + 1024 * h, 64), "MB MY " + PGall[t % 2], "P7")
-        if not last: ts(PU, P[7][:, 256:448], float(FREE), None, A.min, None, "P7", "PU", 192)
-        else: ts(T.YP[:], P[7][:, 256:448], -1.0, None, A.max, None, "P7", "YP", 192)
+    enter(TV)
 
     dma("s", [(T.sp[:], T.YP[:])], "YP", "sp")
     dma("a", [(T.yp[own, :], T.YP[own, :])], "YP", "ypo")

@@ -1,9 +1,11 @@
 import math
 import numpy as np
 from concourse.bass import DstId, RemoteDMATransfer
-from concourse.mybir import AluOpType as A, ActivationFunctionType as AF
+from concourse.mybir import AluOpType as A, ActivationFunctionType as AF, AxisListType as AX
 
 N, V, S, TV = 8, 3072, 745, 4
+FREE, SAME, NONE, TAB, LWN, BIG = 3088, 3264, 6336, 384, 5520, 524288
+HALF, MAG = 7.5, 1.5 * 2 ** 27
 f32, bf, i32, u16 = "float32", "bfloat16", "int32", "uint16"
 
 
@@ -19,27 +21,28 @@ for _m, (_n, _d, _w) in MSG.items():
     SCRATCH["s" + _m] = ("dram", [8, 128, _n], _d)
     SCRATCH["r" + _m] = ("dram", [8, 128, _n], _d)
     SCRATCH["h" + _m] = ("dram", [128, _n], _d)
+SCRATCH["sq"] = SCRATCH["sp"]
 SCRATCH.update({
     "X": _sb(V, bf), "F": _sb(TV * V, bf), "G2": _sb(V, bf), "D": _sb(V, bf), "PR": _sb(V, bf), "NE": _sb(V, bf),
-    "W": _sb(2 * 3344, bf), "TR": _sb(3328, bf), "PG": _sb(2 * 3584, bf),
-    "RHO": _sb(2560, f32), "FV": _sb(1536, f32), "LW": _sb(6144, f32), "LX": _sb(6144, f32),
+    "W": _sb(NONE + 16, bf), "TR": _sb(3440, bf), "PG": _sb(2 * 3584, bf),
+    "RHO": _sb(1536, f32), "FV": _sb(2048, f32), "LW": _sb(LWN, f32), "LX": _sb(LWN, f32), "LY": _sb(V, f32), "LZ": _sb(V, f32),
     "E": ("sbuf", [128, 16, 256], bf),
-    "PK": _sb(24, i32), "CC": _sb(32, f32), "IOT": _sb(512, f32), "IG": _sb(128, f32), "IK": _sb(256, f32),
-    "JL": _sb(192, f32), "TM2": _sb(64, f32), "SG": _sb(128, bf), "MM": _sb(11 * 144, bf),
-    "Y1": _sb(128, bf), "Y2": _sb(128, bf), "YM": _sb(128, bf), "YE": _sb(128, bf), "YH": _sb(128, bf), "YR": _sb(128, bf),
-    "TRI": _sb(128, bf), "BCN": _sb(128, bf), "POW": _sb(128, bf), "TWO": _sb(128, bf), "OCC": _sb(128, bf),
-    "ZER": _sb(208, bf), "JB": _sb(256, bf), "JF": _sb(256, f32), "TAU": _sb(256, f32), "THR": _sb(256, f32),
-    "DU1": _sb(16, f32), "DU2": _sb(16, f32), "DU3": _sb(192, f32), "MK": _sb(32, bf), "MU": _sb(288, bf), "VK": _sb(384, bf),
+    "PK": _sb(8, i32), "CC": _sb(8, f32), "CT": _sb(16, f32), "IOT": _sb(512, f32), "TM2": _sb(64, f32), "SG": _sb(128, bf), "MM": _sb(9 * 272, bf),
+    "Y1": _sb(128, bf), "Y2": _sb(128, bf), "YM": _sb(128, bf), "YE": _sb(128, bf), "YH": _sb(128, bf), "YR": _sb(128, bf), "YN": _sb(128, bf), "YS": _sb(128, bf),
+    "TRI": _sb(128, bf), "BCN": _sb(128, bf), "POW": _sb(128, bf), "TWO": _sb(128, bf),
+    "DO": _sb(128, bf), "DZ": _sb(128, bf), "DX": _sb(128, bf), "DL": _sb(128, bf), "BCV": _sb(128, bf),
+    "ZER": _sb(272, bf), "JB": _sb(256, bf), "JF": _sb(256, f32), "TAU": _sb(256, f32), "THR": _sb(256, bf),
+    "DU2": _sb(32, f32), "DU3": _sb(192, f32), "SH": _sb(1024, bf), "VK": _sb(576, bf),
     "CP": _sb(576, i32), "IA": _sb(768, i32), "KA": _sb(768, bf), "NH": _sb(384, bf), "RP": _sb(384, u16),
-    "FA": _sb(384, f32), "FC": _sb(192, f32), "NI": _sb(192, i32), "EM": _sb(192, bf),
+    "FA": _sb(384, f32), "FC": _sb(192, f32), "NI": _sb(192, i32), "EM": _sb(384, bf), "RF": _sb(192, f32),
     "ICF": _sb(384, f32), "ICU": _sb(192, u16),
     "NF": _sb(192, f32), "NU": _sb(192, u16), "LU": _sb(192, u16), "LO": _sb(192, u16),
     "EQ": _sb(192, bf), "O1": _sb(256, bf), "OU": _sb(16, u16),
-    "HI": _sb(192, bf), "LW2": _sb(192, bf), "FR": _sb(192, bf), "FS": _sb(2, bf),
-    "U": _sb(200, f32), "DB": _sb(2, f32), "BC": _sb(210, bf), "CU": _sb(200, f32), "BS": _sb(16, f32),
+    "HL": _sb(768, bf), "CD": _sb(384, bf), "FR": _sb(192, bf),
+    "U": _sb(200, f32), "BC": _sb(210, bf), "CU": _sb(200, f32), "BS": _sb(16, f32),
     "L1": _sb(256, bf), "L2": _sb(256, bf), "SE": _sb(256, bf), "AU": _sb(16, u16), "AB": _sb(16, bf), "KU": _sb(16, u16),
-    "KB": _sb(32, bf), "RT": _sb(16, f32), "RU": _sb(16, u16), "Z": _sb(256, bf), "O": _sb(256, bf),
-    "NB": _sb(256, u16), "NLU": _sb(32, u16), "WI": _sb(256, bf),
+    "KB": _sb(32, bf), "RT": _sb(32, f32), "RU": _sb(16, u16), "Z": _sb(256, bf), "O": _sb(256, bf),
+    "NB": _sb(256, u16), "NLU": _sb(32, u16), "WI": _sb(256, bf), "VAL": _sb(256, f32), "NL": _sb(16, f32),
     "QU": _sb(16, u16), "YP": _sb(192, f32), "TN": _sb(256, f32),
 })
 for _b in range(8):
@@ -47,10 +50,9 @@ for _b in range(8):
 NDMA = 72
 SEMAPHORES = (["cv", "ca", "cp", "cg", "loc"] + ["h" + m for m in MSG] + ["a" + m for m in MSG if not MSG[m][2]]
               + ["af%d" % s for s in range(8)] + ["ax%d" % s for s in range(8)] + ["d%d" % k for k in range(NDMA)])
-CH_HI, CH_LO, CH_FR, CH_FI, CH_K, CH_A = 0, 1, 2, 3, 4, 5
-STRIPS = ["ME", "MA", "MB", "MC", "MF", "ML", "MN", "MO", "MS", "MX", "MY"]
-FREE = 3088
-CY, PEC, FIX = 0.9, 0.45, 55.0
+CH_HI, CH_LO, CH_FR, CH_E, CH_K, CH_A, CH_D, CH_OK, CH_OA, CH_X, CH_Y, CH_C = 0, 1, 2, 3, 4, 5, 6, 8, 9, 10, 11, 12
+STRIPS = ["ME", "MU", "MA", "MP", "MF", "MN", "MS", "MX", "MR"]
+CY, PEC, FIX, LAT = 0.9, 0.45, 55.0, 110.0
 
 
 def routes(T, topo):
@@ -70,6 +72,7 @@ def routes(T, topo):
         for d in cls[s]:
             if d != s and idx[d] != (idx[s] + 1) % len(cls[s]):
                 via[s][d] = plain.pop(0)
+        vib[s][s] = [c for c in mine if c not in port][0]
     return via, vib
 
 
@@ -84,7 +87,7 @@ def arrival(m, s):
 def helper(g, core, T, topo, via, vib):
     sent = 0
     for m in MSG:
-        for s, d in [(s, d) for s in range(N) for d in range(N) if (via if MSG[m][2] else vib)[s][d] == core]:
+        for s, d in [(s, d) for s in range(N) for d in range(N) if (via if MSG[m][2] else vib)[s][d] == core and (s != d or m == "p")]:
             rid, pid = topo.addr(T.cores[d], core)
             g.wait_ge(T.sem["h" + m], 2)
             g.remote_dma(T["r" + m][s], T["h" + m][:], T.sem[arrival(m, s)], T.sem.loc, pid, rid, topo.mask(core, T.cores[d]))
@@ -103,163 +106,217 @@ def rank_program(g, core, T, topo):
 
 
 PLAN = {}
-TRIES, HEAT, BIAS, NEAR, TIE = 55000, 50.0, 500.0, 50.0, 0.5
 CASES = [{"far": 1.0, "wide": 1.0, "dma": 1.0, "wake": 1.0},
          {"gather": 1.3, "scatter": 1.55, "far": 0.8, "wide": 0.8, "dma": 0.8, "wake": 1.0},
          {"gather": 0.7, "scatter": 0.5, "tensor": 1.2, "far": 1.3, "wide": 1.4, "dma": 1.2, "wake": 2.5}]
-EARLY, AFTER, NA = 6, "PR5", 3
-FIRST = ""
-SIGN = [(1, 3), (), (), ()]
-BANK = [(0, 1, 5, 6, 3, 7), (0, 1, 0, 1, 0, 1)]
+ROUNDS = [(1, 520, 70.0), (3, 360, 35.0)]
+MOVES, WINDOW, NEAR, SOON = 1200, 100, 400.0, 0.05
+NA, VS = 3, 8
+SIGN = [(1, 3, 5), (5,), (5,), (5,)]
+BANK = [(0, 1, 5, 6, 3, 7), (0, 1, 3, 5, 0, 1), (0, 1, 3, 5, 0, 1), (0, 1, 3, 5, 0, 1)]
+FIRST = [{"v": "ZER Wd IA0 IA1 KAc IA2 IA3 KAp Wu YP PU Wt T0 T2 FC0 LO0 RP FC1 LW LO1 LW+ FC2 LO2 LW++ NH0 NH1 LY LY+ LY++ NU NF HI0 G2 LO4 G5 NI LU0 "
+               "D0 D2 P4 PR0 D4 PR2 PR3+ EQ PR1+ PR4 PR5+ HI1 NE5 LO5 FR",
+          "a": "MA MN FV0 FV1 FV2 MF ME MX MR MU MP MS T1 T3 T4 LX T5 LX+ LX++ LZ LZ+ LZ++ G1 G4 G3 G0 EM PR1 PR3 PR5 D3 D1 D5 NE2 NE3 NE0 NE1 NE4",
+          "p": "YR.Y1+ YR.Y1 T0.T1 T2.T3 T4.T5 Wd.Wc Y2.G4 YN.G1 Y2.G2 X0.X1+ YN.G3 Y2.G0 YN.G5 X0.X1++ Y1.PR1 Y1.D0 X0.X1 Y1.PR3 Y1.D2 Y1.PR5 "
+               "Y2.G3 Y2.G1 Y1.D4 YE.EQ Y2.G5 YE.EM ME.NE2 ME.NE0 ME.NE4 YN.HI0"},
+         {"v": "CH CL U BCb BCa NU NF L1 G0 AU AB L2 TR2 KU SE G1 LU0 RU D0 D1 NLU LU1 NB D2 E0 RX E1 E2 E3 LU2 PR0 E4 E5 OU E6 E7 E8 E9 E10 NPU "
+               "E11 E12 E13 PR1 OU+ E14 E15 D3 OU++ EQ NE0 D4 PR4 PR2 TR0+ RF PR3 PR5+ HI0 RT LO4 QU T0 FR",
+          "a": "G2 BS TR0 TR1 CU KB KC TR3 TR4 Z G3 NL TR5 O G4 O+ G5 O++ PR5 O+++ NE1 WI D5 NE4 NE2 NE3 NE5",
+          "p": "YN.HI0+- SG.FR CH.CL MU.BCa ME.BCa ME.L1 Y2.G0 TRI.Y1 L2.ME Y2.G2 TR0.TR1 MS.SE Y2.G1 TR2.TR3 MN.Z BCN.Z Y1.D0 Y2.G3 MX.Z TR4.TR5 O.MA "
+               "YH.THR Y1.D2 Y1.D1 Y2.G4 DZ.Z E0.E1 O.MA+ E3.E4 E6.E7 Y1.D4 O.MA++ E9.E10 E12.E13 POW.E0 YN.G5 DO.O Y1.PR5 YE.EQ Y1.D3 ME.NE0 "
+               "MF.WI Y2.G5 MF.TR0 MF.TR0+ MF.TR0++ ME.NE2 ME.NE4 YN.HI0"},
+         {"v": "U BCb BCa RF CH LO0 L1 LW CL AU L2 AB LW+ KU LW++ SE KC LW+++ LW++++ RU LW+++++ LW++++++ NB NL LW+++++++ E0 E1 E2 E3 E4 E5 E6 E7 E8 E9 "
+               "E10 E11 OU E12 E13 E14 E15 O VAL RT YP QU LW++++++++",
+          "a": "BS LX CU KB LX+ Z LX++ LX+++ O1 TN WI",
+          "p": "SG.FR YE.FR YN.HI0+- MU.BCa ME.BCa ME.L1 TRI.Y1 L2.ME MS.SE BCN.Z MN.Z MR.Z YH.THR BCV.Z DX.Z E0.E1 E3.E4 E6.E7 E9.E10 E12.E13 POW.E0 "
+               "DL.O DL.O1 Z.MR MF.WI"}]
+LISTED = "vap"
+
+
+def labels(ops):
+    out, seen, s = [], {}, 0
+    for o in ops:
+        w = "" if o["dma"] or o["e"] == "g" else ".".join(o["r"][:2]) if o["e"] == "p" else o["w"][0]
+        w = {"HI1": "HI0", "LO5": "LO4", "U0": "T0"}.get(w, w) if s else w
+        seen[(s, w)] = seen.get((s, w), -1) + 1
+        out.append((s, w + "+" * seen[(s, w)]))
+        s += w == "FR"
+    return out
+
+
+def first_order(ops, pre, post, alt):
+    n = len(ops)
+    q = [0.0] * n
+    for i in range(n - 1, -1, -1): q[i] = ops[i]["c"] + max([q[j] + x for j, x in post[i]] + [ops[i]["lat"]])
+    marks = [0.0] + [q[0] - q[i] for i, o in enumerate(ops) if o["w"][:1] == ["FR"]] + [q[0]]
+    key, eng = [q[0] - x for x in q], [o["e"] for o in ops]
+    for i, (s, w) in enumerate(labels(ops)):
+        for e, l in FIRST[(s > 0) + (s == TV)].items():
+            l = l.split()
+            if 0 < s < TV and w + "-" in l: w, s = w + "-", s + 1
+            if w in l and e in alt[i]:
+                key[i], eng[i] = marks[s] + (marks[s + 1] - marks[s]) * (l.index(w) + 1) / (len(l) + 1), e
+    qs = {e: sorted((i for i in range(n) if eng[i] == e), key=lambda i: key[i]) for e in LISTED}
+    fin, free, left = [0.0] * n, {e: 0.0 for e in "vapgs"}, [len(x) for x in pre]
+    ready, order = set(i for i in range(n) if not left[i]), []
+    while ready:
+        c = [i for i in ready if eng[i] not in qs or qs[eng[i]][0] == i] or [min(ready, key=lambda i: (key[i], i))]
+        t, _, i = min((max([free[eng[i]], ops[i]["t0"]] + [fin[d] + x for d, x in pre[i]]), -q[i], i) for i in c)
+        if eng[i] in qs: qs[eng[i]].remove(i)
+        fin[i] = free[eng[i]] = t + alt[i][eng[i]]
+        ready.discard(i)
+        order.append(i)
+        for j, _ in post[i]:
+            left[j] -= 1
+            if not left[j]: ready.add(j)
+    return order, eng
 
 
 def schedule(ops):
-    n, LAT = len(ops), 110.0
-    alt = [[(e, o["alt"][e][0]) for e in "av"] if "alt" in o else [(o["e"], o["c"])] for o in ops]
+    n = len(ops)
+    alt = [{e: o["alt"][e][0] for e in sorted(o["alt"])} if "alt" in o else {o["e"]: o["c"]} for o in ops]
     pre = [[(d, (0.0 if ops[d]["e"] == o["e"] == "p" else LAT) + (0.0 if ops[d]["rem"] and o["e"] == "g" or d == o["soft"] else ops[d]["lat"])) for d in o["dep"]] for o in ops]
     post = [[] for _ in ops]
     for i in range(n):
         for d, x in pre[i]: post[d].append((i, x))
     head, tail = [o["t0"] for o in ops], [o["lat"] for o in ops]
+    every = [([c.get(o["g"], 1.0) for o in ops],
+              [[(d, x * (c["wide"] if "mx" in ops[d]["w"] or "mf" in ops[d]["w"] else c["far"] if ops[d]["rem"] else c["dma"] if ops[d]["dma"] else c["wake"]))
+                for d, x in pre[i]] for i in range(n)]) for c in CASES]
+    order, eng = first_order(ops, pre, post, alt)
+    rnd = np.random.default_rng(1)
 
-    def place(seq, before, first, last, on, bias):
-        start, fin, used = [0.0] * n, [0.0] * n, {e: ([], []) for e in "vapgs"}
-        eng = [None] * n
-        for i in seq:
-            t0 = first[i]
-            for d, x in before[i]:
-                if fin[d] + x > t0: t0 = fin[d] + x
-            best = None
-            for e, c in alt[i]:
-                if on and on[i] != e: continue
-                a, b = used[e]
-                k, t = len(a), t0
-                while k and b[k - 1] > t0: k -= 1
-                while k < len(a) and a[k] < t + c:
-                    t = max(t, b[k])
-                    k += 1
-                v = t + c + (bias[i] if e == "v" else 0.0)
-                if best is None or v < best[0]: best = (v, t, c, e, k)
-            _, t, c, e, k = best
-            used[e][0].insert(k, t)
-            used[e][1].insert(k, t + c)
-            start[i], fin[i], eng[i] = t, t + c, e
-        return max(fin[i] + last[i] for i in range(n)), start, fin, eng
-
-    def topo_order(key):
-        key = list(key)
-        for i in range(n):
-            for d, _ in pre[i]:
-                if key[i] >= key[d]: key[i] = key[d] - 1e-3
-        return sorted(range(n), key=lambda i: -key[i])
-
-    def polish(key, bias):
-        r = place(topo_order(key), pre, head, tail, None, bias)
-        for _ in range(2):
-            b = place(sorted(range(n), key=lambda i: -r[2][i]), post, tail, head, r[3], bias)
-            x = place(sorted(range(n), key=lambda i: -b[2][i]), pre, head, tail, None, bias)
-            if x[0] >= r[0]: break
-            r = x
-        return r
-    key = [0.0] * n
-    for i in range(n - 1, -1, -1): key[i] = ops[i]["c"] + max([key[j] + x for j, x in post[i]] + [tail[i]])
-    first = polish(key, [BIAS] * n)
-    eng = list(first[3])
-    cost = [dict(alt[i])[eng[i]] for i in range(n)]
-    seq = {e: sorted((i for i in range(n) if eng[i] == e), key=lambda i: first[1][i]) for e in "vapgs"}
-    direct = [set(d for d, _ in pre[i]) for i in range(n)]
-    same = {}
-    for i, o in enumerate(ops): same.setdefault(o["k"], {})[o["t"]] = i
-    twin = [same[o["k"]] if o["t"] and same[o["k"]][o["t"]] == i else {o["t"]: i} for i, o in enumerate(ops)]
-
-    def times():
-        up, down = [-1] * n, [-1] * n
-        for l in seq.values():
-            for a, b in zip(l, l[1:]): up[b], down[a] = a, b
-        left = [len(pre[i]) + (up[i] >= 0) for i in range(n)]
-        order = [i for i in range(n) if not left[i]]
-        for i in order:
-            for j, _ in post[i]:
-                left[j] -= 1
-                if not left[j]: order.append(j)
-            j = down[i]
-            if j >= 0:
-                left[j] -= 1
-                if not left[j]: order.append(j)
-        if len(order) < n: return None
-        runs = []
+    def whole(cases):
+        res = []
         for mul, before in cases:
-            r, fin = [0.0] * n, [0.0] * (n + 1)
+            fin, q, last, up = [0.0] * n, list(tail), {}, [-1] * n
             for i in order:
-                t = fin[up[i]]
-                if head[i] > t: t = head[i]
+                t, u = head[i], last.get(eng[i], -1)
+                if u >= 0 and fin[u] > t: t = fin[u]
                 for d, x in before[i]:
                     if fin[d] + x > t: t = fin[d] + x
-                r[i], fin[i] = t, t + cost[i] * mul[i]
-            runs.append((max(fin[i] + tail[i] for i in ends), r, fin))
-        return sum(x[0] / w for x, w in zip(runs, norm)) / len(runs), runs, order, up, down
+                fin[i], last[eng[i]], up[i] = t + alt[i][eng[i]] * mul[i], i, u
+            for i in reversed(order):
+                t = q[i] + alt[i][eng[i]] * mul[i]
+                if up[i] >= 0 and t > q[up[i]]: q[up[i]] = t
+                for d, x in before[i]:
+                    if t + x > q[d]: q[d] = t + x
+            res.append((max(fin[i] + q[i] for i in range(n)), fin, q))
+        return res
 
-    def longest(now, s):
-        (end, r, fin), (mul, before) = now[1][s], cases[s]
-        q, qp = [0.0] * (n + 1), list(tail)
-        for i in reversed(now[2]):
-            q[i] = t = fin[i] - r[i] + max(qp[i], q[now[4][i]])
-            for j, x in before[i]:
-                if t + x > qp[j]: qp[j] = t + x
-        rp = [max([head[i]] + [fin[d] + x for d, x in before[i]]) for i in range(n)]
-        return [v for v in range(n) if r[v] + q[v] > end - NEAR and (len(alt[v]) > 1 or r[v] > rp[v] + 1.0 or q[v] > fin[v] - r[v] + qp[v] + 1.0)], fin, rp
-    cases = [([c.get(o["g"], 1.0) for o in ops],
-              [[(d, x * (c["wide"] if "mx" in ops[d]["w"] or "mf" in ops[d]["w"] else c["far"] if ops[d]["rem"] else c["dma"] if ops[d]["dma"] else c["wake"])) for d, x in pre[i]] for i in range(n)]) for c in CASES]
-    ends, norm = [i for i in range(n) if not post[i]], [1.0] * len(cases)
-    rnd = np.random.default_rng(1)
-    now = times()
-    norm = [x[0] / now[1][0][0] for x in now[1]]
-    now = times()
-    best, crit = (now[0], now[1][0][1], list(eng)), None
-    for it in range(TRIES):
-        end = now[0]
-        if crit is None or rnd.random() < 0.05: crit, fin, rp = longest(now, int(rnd.integers(len(cases))))
-        v = crit[int(rnd.integers(len(crit)))]
-        o = e = eng[v]
-        p = seq[o].index(v)
-        if len(alt[v]) > 1 and rnd.random() < 0.5:
-            e = "av"[o == "a"]
-            k = 0
-            while k < len(seq[e]) and fin[seq[e][k]] <= rp[v]: k += 1
-            k = min(k + int(rnd.integers(4)), len(seq[e]))
-        else:
-            k = p + (1 + int(rnd.geometric(0.5)) - 1) * (1 if rnd.random() < 0.5 else -1)
-            if k < 0 or k >= len(seq[o]): continue
-            lo, hi = min(p, k), max(p, k)
-            if any(w in direct[v] or v in direct[w] for w in seq[o][lo:hi + 1]): continue
-        done = [(v, o, p)]
-        seq[o].pop(p)
-        seq[e].insert(k, v)
-        eng[v], cost[v] = e, dict(alt[v])[e]
-        if k + 1 < len(seq[e]) and rnd.random() < TIE:
-            a, b = twin[v], twin[seq[e][k + 1]]
-            for t in a:
-                if a[t] != v and t + ops[seq[e][k + 1]]["t"] - ops[v]["t"] in b:
-                    y, z = a[t], b[t + ops[seq[e][k + 1]]["t"] - ops[v]["t"]]
-                    if eng[z] == e and y != z:
-                        done.append((y, eng[y], seq[eng[y]].index(y)))
-                        seq[eng[y]].remove(y)
-                        seq[e].insert(seq[e].index(z), y)
-                        eng[y], cost[y] = e, dict(alt[y])[e]
-        x = times()
-        if x and x[0] - end <= -HEAT * (1.02 - it / TRIES) * math.log(1.0 - rnd.random()):
-            now, crit = x, None
-            if x[0] < best[0]: best = (x[0], x[1][0][1], list(eng))
-        else:
-            for y, o, p in reversed(done):
-                seq[e].remove(y)
-                seq[o].insert(p, y)
-                eng[y], cost[y] = o, dict(alt[y])[o]
-    return best[0], sorted(range(n), key=lambda i: (best[1][i], i)), best[2]
+    def window(cases, norm, res, a, b, heat):
+        win = order[a:b]
+        m, loc, early, L = len(win), {i: k for k, i in enumerate(win)}, set(order[:a]), []
+        for (mul, before), (end, fin, q) in zip(cases, res):
+            h, tl = [max([head[i]] + [fin[d] + x for d, x in before[i] if d not in loc]) for i in win], [tail[i] for i in win]
+            e0, e1, by = {e: 0.0 for e in "vapgs"}, {e: 0.0 for e in "vapgs"}, 0.0
+            for i in order[:a]: e0[eng[i]] = fin[i]
+            for j in reversed(order[b:]):
+                e1[eng[j]] = t = q[j] + alt[j][eng[j]] * mul[j]
+                by = max(by, head[j] + t)
+                for d, x in before[j]:
+                    if d in loc: tl[loc[d]] = max(tl[loc[d]], t + x)
+                    elif d in early: by = max(by, fin[d] + x + t)
+            L.append((h, tl, e0, e1, by, [[(loc[d], x) for d, x in before[i] if d in loc] for i in win], [mul[i] for i in win]))
+        npre, direct = [len(x) for x in L[0][5]], [set(d for d, _ in x) for x in L[0][5]]
+        sc = [[loc[j] for j, _ in post[i] if j in loc] for i in win]
+        en, co = [eng[i] for i in win], [alt[i][eng[i]] for i in win]
+        seq = {e: [k for k in range(m) if en[k] == e] for e in "vapgs"}
+
+        def times():
+            up, down, left = [-1] * m, [-1] * m, list(npre)
+            for l in seq.values():
+                for x, y in zip(l, l[1:]):
+                    up[y], down[x] = x, y
+                    left[y] += 1
+            o = [k for k in range(m) if not left[k]]
+            for k in o:
+                for j in sc[k]:
+                    left[j] -= 1
+                    if not left[j]: o.append(j)
+                j = down[k]
+                if j >= 0:
+                    left[j] -= 1
+                    if not left[j]: o.append(j)
+            if len(o) < m: return None
+            tot, out = 0.0, []
+            for (h, tl, e0, e1, by, bf_, mul), z in zip(L, norm):
+                f, end = [0.0] * m, by
+                for k in o:
+                    u = up[k]
+                    t = f[u] if u >= 0 else e0[en[k]]
+                    if h[k] > t: t = h[k]
+                    for d, x in bf_[k]:
+                        if f[d] + x > t: t = f[d] + x
+                    f[k] = t = t + co[k] * mul[k]
+                    if t + tl[k] > end: end = t + tl[k]
+                for e, l in seq.items(): end = max(end, (f[l[-1]] if l else e0[e]) + e1[e])
+                tot += (end + SOON * sum(f) / m) / z
+                out.append((end, f))
+            return tot, out, o, up
+
+        def longest(x):
+            s = int(rnd.integers(len(L)))
+            h, tl, e0, e1, by, bf_, mul = L[s]
+            (end, f), q = x[1][s], list(tl)
+            for e, l in seq.items():
+                if l: q[l[-1]] = max(q[l[-1]], e1[e])
+            for k in reversed(x[2]):
+                t = q[k] + co[k] * mul[k]
+                if x[3][k] >= 0 and t > q[x[3][k]]: q[x[3][k]] = t
+                for d, y in bf_[k]:
+                    if t + y > q[d]: q[d] = t + y
+            return [k for k in range(m) if f[k] + q[k] > end - NEAR] or list(range(m)), f
+        now, cr = times(), None
+        for r in rnd.random((MOVES, 6)).tolist():
+            if cr is None or r[5] < 0.05: cr, f = longest(now)
+            v = cr[int(r[0] * len(cr))] if r[5] < 0.9 else int(r[0] * m)
+            o = e = en[v]
+            l, al = seq[o], alt[win[v]]
+            k = p = l.index(v)
+            if len(al) > 1 and r[1] < 0.4:
+                e = [x for x in al if x != o][int(r[1] * 2.5 * (len(al) - 1))]
+                k = sum(f[y] <= f[v] - co[v] for y in seq[e])
+                k = max(0, min(k + int(r[2] * 4) - 1, len(seq[e])))
+            elif r[1] > 0.7:
+                if r[3] < 0.5:
+                    while k > 0 and l[k - 1] not in direct[v]: k -= 1
+                else:
+                    while k + 1 < len(l) and v not in direct[l[k + 1]]: k += 1
+                k = p + int(round((k - p) * r[2] ** 2))
+                if k == p: continue
+            else:
+                k = p + (1 + int(-math.log(1 - r[2]) * 1.5)) * (1 if r[3] < 0.5 else -1)
+                if k < 0 or k >= len(l) or any(y in direct[v] or v in direct[y] for y in l[min(p, k):max(p, k) + 1]): continue
+            l.pop(p)
+            seq[e].insert(k, v)
+            en[v], co[v] = e, al[e]
+            x = times()
+            if x and x[0] - now[0] <= -heat * math.log(1.0 - r[4]): now, cr = x, None
+            else:
+                seq[e].pop(k)
+                l.insert(p, v)
+                en[v], co[v] = o, al[o]
+        order[a:b] = [win[k] for k in now[2]]
+        for k, i in enumerate(win): eng[i] = en[k]
+    for nc, rounds, heat in ROUNDS:
+        cases = every[:nc]
+        norm = [x[0] for x in whole(cases)]
+        norm = [x / norm[0] * nc for x in norm]
+        best = None
+        for sw in range(rounds + 1):
+            res = whole(cases)
+            tot = sum(x[0] / z for x, z in zip(res, norm))
+            if best is None or tot < best[0]: best = (tot, list(order), list(eng), res)
+            if sw == rounds: break
+            order.sort(key=lambda i: res[0][1][i] - alt[i][eng[i]])
+            a = int(rnd.integers(-WINDOW // 2, n - WINDOW // 2))
+            window(cases, norm, res, max(0, a), min(n, a + WINDOW), heat * (1.02 - sw / rounds))
+        order[:], eng[:] = best[1], best[2]
+    return best[3], order, eng
 
 
 def emit(g, T, ops):
-    n = len(ops)
     lastw, readers = {}, {}
     for i, o in enumerate(ops):
         dep = set()
@@ -275,9 +332,6 @@ def emit(g, T, ops):
             lastw[w] = i
             readers[w] = []
         o["dep"] = sorted(dep)
-    succ = [[] for _ in ops]
-    for i, o in enumerate(ops):
-        for d in o["dep"]: succ[d].append(i)
     if "order" not in PLAN:
         PLAN["order"] = schedule(ops)
     for i, e in enumerate(PLAN["order"][2]):
@@ -320,21 +374,16 @@ def emit(g, T, ops):
     for s in sorted(alltok):
         if not any(seen.get((e, s), 0) >= alltok[s] for e in Q):
             g.wait_ge(T.sem[s], alltok[s])
-    return order
 
 
 def build(g, core, rank, T, topo, via, vib):
-    ops, visit, kind = [], [0], [""]
-
-    def names(l):
-        return [x for x in l.split() if x]
+    ops, kind, gate = [], [""], [""]
 
     def op(e, c, r, w, f, dma=False, lat=0.0, ext=(), t0=0.0, rem=0):
-        r, w = names(r), names(w)
+        r, w = (r + (gate[0] if e == "g" and not rem else "")).split(), w.split()
         w = w + [x for x in r if x[0] == "P" and x[1:].isdigit()]
-        k = " ".join(x[:2] + x[3:] if x[:2] == "PG" else x for x in w + ["|"] + r if x[0] not in "WF" or x in ("WI", "FR", "FS"))
-        ops.append({"g": "tensor" if e == "p" else kind[0] if e in "va" and not dma else "", "e": e, "c": c, "r": r, "w": w, "f": f, "dma": dma, "lat": lat, "ext": list(ext), "t0": t0, "rem": rem,
-                    "t": visit[0], "k": k + " %d" % sum(o["t"] == visit[0] and o["k"].rsplit(" ", 1)[0] == k and o["e"] == e for o in ops)})
+        ops.append({"g": "tensor" if e == "p" else kind[0] if e in "va" and not dma else "", "e": e, "c": c, "r": r, "w": w, "f": f, "dma": dma,
+                    "lat": lat, "ext": list(ext), "t0": t0, "rem": rem})
 
     def cyc(n, k=1.0):
         kind[0] = {1.56: "gather", 3.8: "scatter"}.get(k, "")
@@ -353,15 +402,20 @@ def build(g, core, rank, T, topo, via, vib):
     def ms(out, val, w, n, k=1.0):
         op("v", cyc(n, k), "", w, lambda q: q.memset(out, val))
 
+    def red(out, a, o, r, w, n):
+        op("v", cyc(n), r, w, lambda q: q.tensor_reduce(out, a, AX.X, o))
+
     def act(out, a, fn, r, w, n, k=1.0, bias=None, scale=None):
         kw = {}
         if bias is not None: kw["bias"] = bias
         if scale is not None: kw["scale"] = scale
         op("a", cyc(n, k), r, w, lambda q: q.activation(out, a, fn, **kw))
 
-    def either(e):
-        a, v = ops.pop(), ops.pop()
-        ops.append(dict(a if e == "a" else v, alt={"a": (a["c"], a["f"]), "v": (v["c"], v["f"])}))
+    def either(e, n=2):
+        l = [ops.pop() for _ in range(n)]
+        o = dict([x for x in l if x["e"] == e][0], alt={x["e"]: (x["c"], x["f"]) for x in l})
+        o["r"] = sorted(set(y for x in l for y in x["r"] if y not in ("mf", "mx")))
+        ops.append(o)
 
     def lin(out, a, scale, bias, r, w, n, k=1.0):
         ts(out, a, scale, bias, A.mult, A.add, r, w, n, k)
@@ -378,15 +432,16 @@ def build(g, core, rank, T, topo, via, vib):
         act(out, a, AF.Copy, r, w, n, scale=x)
         either("a")
 
-    def mm(l, r, w, start=True, stop=True, each=False):
+    def mm(l, r, w, start=True, stop=True, pair=False):
         def f(q):
             for j, (o, a, b, _) in enumerate(l):
-                x = q.matmul(o, a, b, each or (start and j == 0), each or (stop and j == len(l) - 1))
+                x = q.matmul(o, a, b, j != 1 if pair else start and j == 0, j != 0 if pair else stop and j == len(l) - 1)
             return x
         op("p", sum(max(64, x[3]) for x in l) * PEC + 30.0, r, w, f, lat=40.0)
 
-    def group(bank, n, parts):
-        mm([(P[bank][:, 0:n], T.ZER[:, 0:128], T.JB[:, 0:n], n)], "ZER JB", "P%d A%d" % (bank, bank), True, False)
+    def group(bank, n, parts, first=None):
+        a, b, r = first or (T.ZER[:, 0:128], T.ZER[:, 0:n], "ZER")
+        mm([(P[bank][:, 0:n], a, b, n)], r, "P%d A%d" % (bank, bank), True, False)
         left = [len(parts)]
 
         def one(l):
@@ -408,13 +463,36 @@ def build(g, core, rank, T, topo, via, vib):
     def sel(out, a, pat, cmp, fill, base, cm, r, w, n):
         op("g", 180 + 2 * n * CY, r, w, lambda q: q.affine_select(out, a, pat, cmp, fill, base, cm))
 
-    def strip(M, k):
-        if M == "MU": return T.MU[:, 15 - k:143 - k]
-        o = 144 * STRIPS.index(M)
-        return T.MM[:, o + 15 - k:o + 143 - k]
+    def picks(out, wts, w, reps=1, wide=1):
+        pat = [p for p in ([0, reps], [16, 8], [0, wide]) if p[1] > 1]
+        for ch, x in wts: sel(out, out, pat, A.not_equal, float(x), ch, -1, w, w, 8 * reps * wide)
 
-    def ext16(out, M, src, lo, n):
-        return [(out, strip(M, k), src[:, lo + k:lo + 16 * n:16], n) for k in range(16)]
+    def inslot(out, w, reps=1, wide=1):
+        for s, b in ((-1, 0), (1, 15)):
+            sel(out, out, [p for p in ([0, reps], [16 * s, 8], [0, wide]) if p[1] > 1], A.is_ge, 0.0, b, -s, w, w, 8 * reps * wide)
+
+    def diag(l):
+        for M, x in l: sel(T[M][:], T.ZER[:, 0:128], [[1, 128]], A.not_equal, x, 0, -1, "ZER", M, 128)
+
+    def strip(M, k, d=0):
+        o = 272 * STRIPS.index(M) + 143 - k - 16 * (d % N)
+        return T.MM[:, o:o + 128]
+
+    def ext16(out, M, src, lo, n, d=0):
+        return [(out, strip(M, k, d), src[:, lo + k:lo + 16 * n:16], n) for k in range(16)]
+
+    def rows(ch, src, o=0):
+        return [(T.W[ch:128:16, o:o + V], src)]
+
+    def onward(dst, src):
+        return [(dst(1, N), src(0, N - 1)), (dst(0, 1), src(N - 1, N))]
+
+    def slot(q):
+        return slice(16 * (q % N), 16 * (q % N) + 16)
+
+    def parts2(b, src, r, k):
+        ts(T.HL[:, 384 * b:384 * b + 192], src, MAG, -MAG, A.add, A.add, r, "HI%d" % b, 192)
+        tt(T.HL[:, 384 * b + 192:384 * b + 384], src, T.HL[:, 384 * b:384 * b + 192], A.subtract, r + " HI%d" % b, "LO%d" % (b + 4), 192, k)
 
     C = T.cores
     others = [d for d in range(N) if d != rank]
@@ -428,16 +506,17 @@ def build(g, core, rank, T, topo, via, vib):
         nd = 4 if wide else 2
         pool = off + rest
         tr, tot = [], 0
+        src = lambda d: dict(srcs=[T.sp[d], T.sq[d]], alu_op=2) if m == "p" else dict(src=T["s" + m][d])
         for d in [d for d in others if route[rank][d] is None]:
             rid, pid = topo.addr(C[d], core)
             tr.append(RemoteDMATransfer(dst_ids=[DstId(rid=rid, pnc=pid)], dma_engine_mask=bits(pool[:nd]), remote_sem=T.sem[arrival(m, rank)],
-                                        src=T["s" + m][d], dst=T["r" + m][rank]))
+                                        dst=T["r" + m][rank], **src(d)))
             pool = pool[nd:]
             tot += nd
-        for d in [d for d in others if route[rank][d] is not None]:
+        for d in [d for d in others + [rank] * (m == "p") if route[rank][d] is not None]:
             rid, pid = topo.addr(route[rank][d], core)
             tr.append(RemoteDMATransfer(dst_ids=[DstId(rid=rid, pnc=pid)], dma_engine_mask=bits(pool[-2:]), remote_sem=T.sem["h" + m],
-                                        src=T["s" + m][d], dst=T["h" + m][:]))
+                                        dst=T["h" + m][:], **src(d)))
             pool = pool[:-2]
             tot += 2
         op("g", c, "s%s gq" % m + r, "gq m" + m, lambda q: q.remote_dma_fused(tr, local_sem=T.sem.loc), rem=tot, lat=lat + 500.0 - c)
@@ -450,341 +529,341 @@ def build(g, core, rank, T, topo, via, vib):
 
     dma("s", [(T.CP[:, 0:192], T.cc[:])], "", "CPc")
     dma("a", [(T.s0[:], T.nm[:]), (T.CP[:, 192:384], T.pl[:]), (T.r0[rank], T.nm[rank:rank + 1, :])], "", "s0 r0 CPp ~a")
+
     def staged(dst, src):
         return [(dst[a:b], src[16 * a:16 * b, :]) for a, b in ((0, rank), (rank + 1, N)) if b > a]
     dma("a", staged(T.sf, T.fo), "~a", "sf", lat=3500.0, t0=250.0)
-
-    iota(T.PK[:, 1:9], [[16, 8]], 0, 1, "", "PI", 8, False)
-    iota(T.IOT[:], [[1, 512]], 0, 0, "", "IOT", 512)
-    iota(T.IK[:], [[0, 16], [1, 16]], 0, 0, "", "IK", 256)
-    iota(T.IG[:], [[16, 8], [0, 16]], 15, 0, "", "IG", 128)
     dma("s", staged(T.sx, T.tx), "", "sx", lat=3500.0, t0=4200.0)
-    send("0", LATE["0"], " PI IOT IK", 2500.0)
+
+    col = lambda j: T.CC[:, j:j + 1]
+    ms(T.ZER[:], 0.0, "ZER", 272, 0.5)
+    ms(T.W[:, 0:V], 0.0, "Wd Wc Wb Wf Wo", V, 0.5)
+    ms(T.W[:, V:FREE], 255.0, "Wt", 16)
+    ms(T.W[:, FREE:FREE + 16], 64.0, "Wu", 16)
+    ms(T.YP[:], -8192.0, "YP", 192)
+    diag((("Y1", 1.0), ("YR", 192.0)))
+    iota(T.IOT[:], [[1, 512]], 0, 0, "", "IOT", 512)
+    send("0", LATE["0"], " Y1 YR IOT", 2500.0)
     send("f", LATE["f"])
     send("x", LATE["x"])
-    col = lambda j: T.CC[:, j:j + 1]
-    cK, cP, cS, cY = 0, 1, 4, 24
-    ts(T.PK[:, 0:1], T.PK[:, 1:2], 15, None, A.bitwise_and, None, "PI", "PK0", 1)
-    ts(T.PK[:, 16:24], T.PK[:, 1:9], 112, None, A.bitwise_and, None, "PI", "PK1", 8)
-    cp(T.CC[:, 0:2], T.PK[:, 0:2], "PK0 PI", "c0 c1", 2)
-    ts(T.CC[:, cY:cY + 8], T.PK[:, 16:24], 15.0, None, A.add, None, "PK1", "c3", 8)
-    lin(col(cS), col(cK), 192.0, -4096.0, "c1", "c4", 1)
-    OH = T.TM2[:, 0:16]
-    ts(OH, T.IK[:, 0:16], col(cK), None, A.is_equal, None, "IK c1", "OH", 16)
-
-    def wcol(j, wts, start=None):
-        for ch, x in wts:
-            if start is None: lin(col(j), T.TM2[:, ch:ch + 1], float(x), 0.0, "OH", "c%d" % j, 1)
-            else: lin(col(j), T.TM2[:, ch:ch + 1], float(x), col(start), "OH c%d" % start, "c%d" % j, 1)
-            start = j
-    wcol(5, [(CH_HI, 1), (CH_LO, 1)])
-    wcol(7, [(CH_FR, -8192), (CH_FI, 12288)], 5)
-    wcol(6, [(CH_K, 16)])
-    wcol(15, [(CH_FR, -8192), (CH_FI, 8192)])
-    wcol(16, [(CH_K, 192), (CH_A, 1)])
-    lin(col(8), col(15), -1.0, col(16), "c15 c16", "c8", 1)
-    wcol(13, [(CH_K, 1), (CH_A, 16)])
-    lin(col(14), col(15), 1.0, col(13), "c15 c13", "c14", 1)
-    wcol(9, [(CH_FR, -4)])
-    wcol(11, [(CH_HI, 3072), (CH_A, 255)])
-    lin(col(17), col(15), 64.0, 0.0, "c15", "c17", 1)
-    for d in range(2): ts(T.MU[:, 144 * d:144 * d + 144], T.IOT[:, 0:144], col(cY + d), None, A.is_equal, None, "IOT c3", "MU%d" % d, 144)
-    for M, j, d in (("ME", None, 0), ("MA", 8, 0), ("MB", 8, 1), ("MC", 7, 0), ("MF", 17, 1), ("ML", 5, 1), ("MN", 5, 0), ("MO", 5, 7),
-                    ("MS", cS, 0), ("MX", 13, 0), ("MY", 14, 4)):
-        o, x = 144 * STRIPS.index(M), 8192.0 if j is None else col(j)
-        if d > 1: ts(T.MM[:, o:o + 144], T.IOT[:, 0:144], col(cY + d), x, A.is_equal, A.mult, "IOT c3 c%d" % j, M, 144)
-        else: lin(T.MM[:, o:o + 144], T.MU[:, 144 * d:144 * d + 144], x, 0.0, "MU%d c%d" % (d, j or 3), M, 144, 0.5)
-    ts(T.Y1[:], T.IOT[:, 0:128], col(cP), None, A.is_equal, None, "IOT c0", "Y1a", 128)
-    lin(T.YR[:], T.Y1[:], 192.0, 0.0, "Y1a", "YR", 128, 0.5)
-    iota(T.ZER[:], [[0, 208]], 0, 0, "mx", "ZER", 208)
-    for M, nm_, x in ((T.Y2, "Y2", 2.0), (T.YE, "YE", 262144.0), (T.YM, "YM", -2.0), (T.YH, "YH", -0.5)):
-        sel(M[:], T.ZER[:, 0:128], [[1, 128]], A.not_equal, x, 0, -1, "ZER", nm_, 128)
-    iota(T.SG[:], [[0, 128]], 1, 0, "mx", "SG", 128)
-    sel(T.SG[:], T.SG[:], [[-16, 8], [0, 16]], A.is_ge, 0.0, 0, 1, "SG", "SG", 128)
-    sel(T.SG[:], T.SG[:], [[16, 8], [0, 16]], A.is_ge, 0.0, 15, -1, "SG", "SG", 128)
-    ts(T.TWO[:], T.IG[:], col(cY + 1), 2.0, A.is_equal, A.mult, "IG c3", "TWO", 128)
-    ts(T.BCN[:], T.IG[:], col(cY + 7), col(5), A.is_equal, A.mult, "IG c3 c5", "BCN", 128)
-    lin(T.OCC[:], T.SG[:], col(9), 0.0, "SG c9", "OCC", 128)
+    gate[0] = " mf"
+    iota(T.DU3[:], [[0, 6], [16, 32]], V, 1, "", "DU3", 192)
+    gate[0] = " mx"
+    iota(T.DU2[:], [[-int(192 * HALF), 2], [16, 16]], BIG - TAB, 1, "", "DU2", 32)
+    diag((("Y2", 2.0), ("YE", 262144.0), ("YM", -2.0), ("YH", -0.5), ("YN", -1.0), ("YS", 1.0 / 16)))
+    nms = ((CH_HI, 1), (CH_LO, 1), (CH_C, -1), (CH_C + 1, -1))
+    for j, h in enumerate((0, 2, 4, 5)):
+        c = T.FV[:, 512 * j:512 * j + 512]
+        if j: lin(c, T.IOT[:], 1.0, 4096.0 + 512 * h, "IOT", "FV%d" % j, 512)
+        else:
+            act(c, T.IOT[:], AF.Silu, "IOT", "FV0", 512, bias=4096.0)
+            ops[-1]["c"] += 1300.0
+    for M, wts in (("MA", ((CH_K, 192), (CH_A, 1))), ("MN", nms), ("MP", ((CH_OK, 192), (CH_OA, 1))),
+                   ("MF", ((CH_FR, -BIG), (CH_E, BIG // 2), (CH_D, BIG // 2), (CH_D + 1, BIG // 2), (CH_Y, 3 * BIG // 2))), ("MX", ((CH_K, 1), (CH_A, 16))),
+                   ("MR", ((CH_HI, 1.0 / 16), (CH_LO, 192), (CH_C, -1.0 / 16), (CH_C + 1, -192))), ("ME", 8192), ("MU", 1), ("MS", None)):
+        o = 272 * STRIPS.index(M)
+        gate[0] = " mf" if M == "MA" else " mx"
+        act(T.MM[:, o:o + 272], T.ZER[:], AF.Copy, "ZER", M, 272)
+        ops[-1]["t0"] = 350.0
+        c = T.MM[:, o + 15:o + 271:16]
+        if M == "MS": iota(c, [[0, 2], [-V, 8]], -4096, 192, M, M, 16)
+        elif M in ("ME", "MU"): iota(c, [[0, 16]], wts, 0, M, M, 16)
+        if M in ("ME", "MU", "MS"): inslot(c, M, 2)
+        else: picks(c, wts, M, 2)
+    for j, wts in enumerate((((CH_E, 8),), ((CH_FR, 8), (CH_Y, 8), (CH_D, -1), (CH_D + 1, -1)))):
+        c = T.CT[:, 8 * j:8 * j + 8]
+        iota(c, [[0, 8]], 0, 0, "", "CT%d" % j, 8)
+        picks(c, wts, "CT%d" % j)
+        red(col(2 + j), c, A.add, "CT%d" % j, "c%d" % (2 + j), 8)
+    iota(T.PK[:, 0:1], [[0, 1]], 0, 1, "", "PI", 1, False)
+    ts(T.PK[:, 1:2], T.PK[:, 0:1], 15, None, A.bitwise_and, None, "PI", "PK", 1)
+    cp(col(0), T.PK[:, 1:2], "PK", "c0", 1)
+    cK = col(0)
+    iota(T.SG[:], [[0, 128]], 1, 0, "", "SG", 128)
+    inslot(T.SG[:], "SG", 1, 16)
     sel(T.TRI[:], T.SG[:], [[1, 128]], A.is_gt, 0.0, 0, -1, "SG", "TRI", 128)
     sel(T.TRI[:], T.TRI[:], [[1, 128]], A.not_equal, 512.0, 0, -1, "TRI", "TRI", 128)
+    for M in ("BCN", "TWO", "POW", "DO", "DZ", "DX", "DL", "BCV"): iota(T[M][:], [[0, 128]], 0, 0, "", M, 128)
+    picks(T.BCN[:], nms, "BCN", 1, 16)
+    iota(T.TWO[:, CH_E:128:16], [[0, 8]], 2, 0, "TWO", "TWO", 8)
+    inslot(T.TWO[:, CH_E:128:16], "TWO")
+    o = 272 * STRIPS.index("MN")
+    for M, h in (("DO", 0), ("DZ", 1)):
+        sel(T[M][:, CH_D + h:128:16], T.MM[:, o + 15:o + 143:16], [[0, 8]], A.is_ge, 0.0, 0, 0, "MN " + M, M, 8)
+        if M == "DO": picks(T.DO[:, CH_D:128:16], ((CH_FR, 8192),), M)
+        lin(T[M][:, CH_D + 1 - h:128:16], T[M][:, CH_D + h:128:16], -1.0, 0.0, M, M, 8)
+    for M in ("DZ", "DX"): picks(T[M][:, CH_E:128:16], ((CH_X, 8),), M)
+    picks(T.DL[:, CH_D:128:16], ((0, 1),), "DL")
+    picks(T.BCV[:, 0:128:16], ((CH_OK, 1), (CH_OA, 16)), "BCV")
     ms(T.TM2[:, 16:32], 0.5, "PW", 16)
     op("v", cyc(16), "PW ZER", "PV", lambda q: q.tensor_tensor_scan(T.TM2[:, 48:64], T.TM2[:, 16:32], T.ZER[:, 0:16], 2.0, A.mult, A.add))
-    tt(T.TM2[:, 16:32], T.TM2[:, 48:64], OH, A.mult, "PV OH", "PW", 16)
-    op("v", cyc(16), "PW ZER", "PW2", lambda q: q.tensor_tensor_scan(T.TM2[:, 32:48], T.TM2[:, 16:32], T.ZER[:, 0:16], 0.0, A.add, A.add))
-    lin(T.POW[:], T.TWO[:], T.TM2[:, 47:48], 0.0, "TWO PW2", "POW", 128)
-    wcol(18, [(CH_FI, 4)])
-    lin(T.THR[:, 0:16], T.TM2[:, 48:64], col(18), -4.0, "PV c18", "THR", 16)
-    for n in (16, 32, 64, 128): lin(T.THR[:, n:2 * n], T.THR[:, 0:n], 1.0, 0.0, "THR", "THR", n)
-    iota(T.JB[:], [[16, 256]], -4096, 0, "mx", "JB", 256)
-    iota(T.JF[:], [[1, 256]], -256, 0, "mx", "JF", 256)
-    iota(T.TAU[:], [[1, 256]], 256, 0, "mx", "TAU", 256)
-    lin(T.JL[:], T.IOT[:, 0:192], 16.0, col(cK), "IOT c1", "JL", 192)
-    lin(T.DU2[:], T.JL[:, 0:16], 1.0, 3840.0, "JL", "DU2", 16)
-    lin(T.DU3[:], T.JL[:], 1.0, 3072.0, "JL", "DU3", 192)
-    lin(T.VK[:, 0:192], T.IOT[:, 0:192], 0.0, col(cK), "IOT c1", "VK", 192)
-    iota(T.VK[:, 192:384], [[1, 192]], 0, 0, "mx", "VA", 192)
-    ts(T.MK[:, 0:16], T.IK[:, 0:16], col(cK), None, A.is_gt, None, "IK c1", "MK0", 16)
-    lin(T.MK[:, 16:32], T.MK[:, 0:16], -1.0, 1.0, "MK0", "MK1", 16)
-    ms(T.W[:, 0:V], 0.0, "Wd0 Wb0 Wf0", V, 0.5)
-    lin(T.W[:, V:FREE], T.IOT[:, 0:16], 0.0, col(11), "IOT c11", "Wt0", 16)
-    lin(col(12), col(6), 4.0, T.TM2[:, CH_FR:CH_FR + 1], "c6 OH", "c12", 1)
-    lin(T.W[:, FREE:FREE + 16], T.IOT[:, 0:16], 0.0, col(12), "IOT c12", "Wu0", 16)
-    for b in range(2): lin(T.PG[:, 3584 * b + 3328:3584 * b + 3344], T.IOT[:, 0:16], 0.0, col(6), "IOT c6", "PGt%d" % b, 16)
-    iota(T.BC[:, 192:210], [[0, 18]], 0, 0, "mx", "BCb", 18)
-    iota(T.BC[:, 0:1], [[0, 1]], -256, 0, "mx", "BCa", 1)
-    iota(T.BS[:], [[0, 16]], 0, 0, "mx", "BS", 16)
-    iota(T.CU[:, 192:200], [[0, 8]], 0, 0, "mx", "CU", 8)
-    ms(T.YP[:], -8192.0, "YP", 192)
-    for j in range(3): lin(T.FV[:, 512 * j:512 * j + 512], T.IOT[:], 1.0, 4096.0 + 1024 * j, "IOT", "FV%d" % j, 512)
+    ts(T.TM2[:, 0:16], T.IOT[:, 0:16], cK, None, A.is_equal, None, "IOT c0", "OH", 16)
+    tt(T.TM2[:, 32:48], T.TM2[:, 48:64], T.TM2[:, 0:16], A.mult, "PV OH", "PW2", 16)
+    red(col(1), T.TM2[:, 32:48], A.max, "PW2", "c1", 16)
+    lin(T.POW[:, CH_E:128:16], T.TWO[:, CH_E:128:16], col(1), 0.0, "TWO POW c1", "POW", 8)
+    lin(T.THR[:, 0:16], T.TM2[:, 48:64], col(2), col(3), "PV c2 c3", "THR", 16)
+    for n in (16, 32, 64, 128): sel(T.THR[:, n:2 * n], T.THR[:, 0:n], [[0, n]], A.is_ge, 0.0, 0, 0, "THR", "THR", n)
+    iota(T.JB[:], [[16, 256]], -4096, 0, "", "JB", 256)
+    iota(T.JF[:], [[1, 256]], -256, 0, "", "JF", 256)
+    iota(T.TAU[:], [[1, 256]], 256, 0, "", "TAU", 256)
+    lin(T.VK[:, 0:192], T.IOT[:, 0:192], 0.0, cK, "IOT c0", "VK", 192)
+    lin(T.VK[:, 384:576], T.VK[:, 0:192], 1.0, float(SAME // 192), "VK", "VL", 192, 0.5)
+    iota(T.VK[:, 192:384], [[1, 192]], 0, 0, "", "VA", 192)
+    for t in range(1, TV + 1):
+        c = T.SH[:, 256 * t - 256:256 * t - 128]
+        sel(c, T.SG[:], [[16, 8], [0, 16]], A.is_gt, 0.0, S * t % 16, -1, "SG", "SH%d" % t, 128)
+        lin(T.SH[:, 256 * t - 128:256 * t], c, -1.0, 0.0, "SH%d" % t, "SH%d" % t, 128, 0.5)
+    iota(T.BC[:, 192:210], [[0, 18]], 0, 0, "", "BCb", 18)
+    iota(T.BC[:, 0:1], [[0, 1]], -256, 0, "", "BCa", 1)
+    iota(T.BS[:], [[0, 16]], 0, 0, "", "BS", 16)
+    iota(T.CU[:, 192:200], [[0, 8]], 0, 0, "", "CU", 8)
+    iota(T.PG[:, TAB + V:TAB + V + 16], [[0, 16]], 0, 0, "", "Tt", 16)
+    for j in range(NA): iota(T.RHO[:, 512 * j:512 * j + 512], [[1, 32], [192, 16]], 8192 + 32 * j, 0, "", "RHO%d" % j, 512)
 
     ts(T.IA[:, 0:192], T.CP[:, 0:192], 15, None, A.bitwise_and, None, "CPc", "IA0", 192)
     ts(T.IA[:, 192:384], T.CP[:, 0:192], 4, None, A.logical_shift_right, None, "CPc", "IA1", 192)
     cp(T.KA[:, 0:384], T.IA[:, 0:384], "IA0 IA1", "KAc", 384)
-
-    def rows(ch, src, b=0):
-        return [(T.W[ch:128:16, 3344 * b:3344 * b + V], src)]
-    dma("s", rows(CH_K, T.KA[:, 0:192]) + rows(CH_A, T.KA[:, 192:384]), "KAc", "Wb0")
+    dma("s", rows(CH_K, T.KA[:, 0:192]) + rows(CH_A, T.KA[:, 192:384]), "KAc", "Wb")
     dma("s", [(T.LW[0:128:16, 0:V], T.YP[:]), (T.LX[0:128:16, 0:V], T.YP[:])], "YP KAc", "LW LX")
+    dma("s", [(T.LY[0:128:16, 0:V], T.YP[:]), (T.LZ[0:128:16, 0:V], T.YP[:])], "YP sx", "LY LZ")
     ts(T.IA[:, 384:576], T.CP[:, 192:384], 15, None, A.bitwise_and, None, "CPp", "IA2", 192)
     ts(T.IA[:, 576:768], T.CP[:, 192:384], 4, None, A.logical_shift_right, None, "CPp", "IA3", 192)
     cp(T.KA[:, 384:768], T.IA[:, 384:768], "IA2 IA3", "KAp", 384)
-    for h in range(2):
-        mm([(P[3][:, 192 * h:192 * h + 192], T.YR[:], T.KA[:, 384 * h:384 * h + 192], 192),
-            (P[3][:, 192 * h:192 * h + 192], T.Y1[:, 0:128], T.KA[:, 384 * h + 192:384 * h + 384], 192)], "YR Y1a KAc KAp", "P3")
-    ts(T.RP[:], P[3][:, 0:384], float(FREE), None, A.min, None, "P3", "RP PU", 384)
-
-    def slot(q):
-        return slice(16 * (q % N), 16 * (q % N) + 16)
+    for h in (1, 0):
+        c = slice(192 * h, 192 * h + 192)
+        mm([(P[3 + h][:, c], T.YR[:], T.KA[:, 384 * h:384 * h + 192], 192),
+            (P[3 + h][:, c], T.Y1[:], T.KA[:, 384 * h + 192:384 * h + 384], 192)], "YR Y1 " + ("KAc", "KAp")[h], "P%d" % (3 + h))
+        ts(T.RP[:, c], P[3 + h][:, c], float(FREE), None, A.min, None, "P%d" % (3 + h), ("RP", "PU")[h], 192)
     dma("s", [(T.F[slot(rank + 1), 0:V], T.fo[own, :]), (T.X[own, :], T.tx[own, :])], "sx", "F%d X%d" % (rank, rank), t0=9000.0)
-    iota(T.RHO[:, 0:512 * NA], [[1, 32 * NA], [192, 16]], 8192, 0, "mx", "RHO", 512 * NA)
 
-    PU = T.RP[:, 192:384]
-    WW = [T.W[:, 3344 * b:3344 * b + FREE + 16] for b in range(2)]
-    WR = ["Wd%d Wb%d Wt%d Wu%d Wf%d " % (b, b, b, b, b) for b in range(2)]
-
-    def pgather(t, js=range(6), after=""):
-        o = 3584 * (t % 2) + 256
-        for j in js:
-            gat(ENG["P%d" % t][j], T.PG[:, o + 512 * j:o + 512 * j + 512], WW[t % 2].indirect(T.RP[:, 192 + 32 * j:224 + 32 * j]), WR[t % 2] + "PU" + after,
-                "PG%d%d" % (t % 2, j), 512)
-
-    def enter(t):
-        pn, last = 3584 * (t % 2), t == TV
-        tt(T.PG[:, pn:pn + 3328].indirect(T.QU[:]), T.Z[:], T.WI[:], A.add, "Z WI QU", PGall[t % 2], 256, 3.8)
-        for h in range(3):
-            mm(ext16(P[3][:, 256 + 64 * h:320 + 64 * h], "MY" if last else "MB", T.PG, pn + 256 + 1024 * h, 64), "MB MY " + PGall[t % 2], "P3")
-        if not last: ts(PU, P[3][:, 256:448], float(FREE), None, A.min, None, "P3", "PU", 192)
-        else: ts(T.YP[:], P[3][:, 256:448], -1.0, None, A.max, None, "P3", "YP", 192)
-    PGall = [" ".join("PG%d%d" % (b, j) for j in range(6)) + " PGt%d " % b for b in range(2)]
+    Wt, WA = T.W[:, 0:FREE + 16], "Wd Wc Wb Wf Wo Wt Wu "
+    Tall = " T0 T1 T2 T3 T4 T5 Tt "
     TRall = " TR0 TR1 TR2 TR3 TR4 TR5 "
-    pgather(0)
-    for h in range(2):
-        c = slice(3344 + 1536 * h, 3344 + 1536 * h + 1536)
-        ms(T.W[:, c], 0.0, "Wd1 Wb1 Wf1", 1536, 0.5)
-        act(T.W[:, c], T.FV[:], AF.Copy, "", "Wd1 Wb1 Wf1", 1536, scale=0.0)
-        either("v")
-        ops[-1]["r"] += ["FV0", "FV1", "FV2"]
-    lin(T.W[:, 3344 + V:3344 + FREE + 16], T.W[:, V:FREE + 16], 1.0, 0.0, "Wt0 Wu0", "Wt1 Wu1", 32, 0.5)
+    for j in range(6):
+        gat("av"[j % 2], T.PG[:, TAB + 512 * j:TAB + 512 * j + 512], Wt.indirect(T.RP[:, 192 + 32 * j:224 + 32 * j]), WA + "PU", "T%d" % j, 512)
     for j in range(3):
         c = slice(64 * j, 64 * j + 64)
-        b = 4 + j % 2
-        mm(ext16(P[b][:, c], "MA", T.PG, 256 + 1024 * j, 64), "PG0%d PG0%d MA" % (2 * j, 2 * j + 1), "P%d" % b)
+        b = 5 + j % 2
+        mm(ext16(P[b][:, c], "MA", T.PG, TAB + 1024 * j, 64), "T%d T%d MA" % (2 * j, 2 * j + 1), "P%d" % b)
         tt(T.FC[:, c], P[b][:, c], T.DU3[:, c], A.min, "P%d DU3" % b, "FC%d" % j, 64, 1.0)
         cp(T.LO[:, c], T.FC[:, c], "FC%d" % j, "LO%d" % j, 64)
     for j in range(3):
         h = 2 * j + 1
-        ts(T.LW[:, 0:6144].indirect(T.LO[:, 32 * h:32 * h + 32]), T.IOT[:], 1.0, 4096.0 + 512 * h, A.mult, A.add, "IOT LO%d" % j, "LW", 512, 3.8)
+        ts(T.LW[:].indirect(T.LO[:, 32 * h:32 * h + 32]), T.IOT[:], 1.0, 4096.0 + 512 * h, A.mult, A.add, "IOT LO%d" % j, "LW", 512, 3.8)
         h = 2 * j
-        act(T.LX[:, 0:6144].indirect(T.LO[:, 32 * h:32 * h + 32]), T.FV[:, 512 * j:512 * j + 512], AF.Silu, "FV%d LO%d" % (j, j), "LX", 512, 3.8)
+        act(T.LX[:].indirect(T.LO[:, 32 * h:32 * h + 32]), T.FV[:, 512 * j:512 * j + 512], AF.Silu, "FV%d LO%d" % (j, j), "LX", 512, 3.8)
     g0 = slice(16 * rank, 16 * rank + 1)
     dma("a", [(T.s2[:, 0:64, :], T.LW[0:128:16, 0:V]), (T.s2[:, 64:128, :], T.LX[0:128:16, 0:V]),
               (T.r2[rank, 0:64, :], T.LW[g0, 0:V]), (T.r2[rank, 64:128, :], T.LX[g0, 0:V])], "LW LX", "s2 r2")
     send("2", LATE["2"])
-    dma("s", [(T.s4[:, 32 * k:32 * k + 32, :], T.PG[ch:128:16, 256:3328]) for k, ch in enumerate((CH_K, CH_A))]
-        + [(T.s4[:, 64 + 32 * k:96 + 32 * k, :], T.KA[:, 192 * k:192 * k + 192]) for k in range(2)], PGall[0] + "KAc LO2", "s4")
+    dma("s", [(T.s4[:, 32 * k:32 * k + 32, :], T.PG[ch:128:16, TAB:TAB + V]) for k, ch in enumerate((CH_K, CH_A))]
+        + [(T.s4[:, 64 + 32 * k:96 + 32 * k, :], T.KA[:, 192 * k:192 * k + 192]) for k in range(2)], Tall + "KAc LO2", "s4")
     dma("s", [(T.r4[rank], T.s4[rank]), (T.rf[rank], T.fo[own, :])], "s4", "r4")
     send("4", LATE["4"])
     for j in range(6):
-        if j < NA: act(T.LX[:, 0:V].indirect(T.RP[:, 32 * j:32 * j + 32]), T.RHO[:, 512 * j:512 * j + 512], AF.Silu, "RHO RP", "LX", 512, 3.8)
-        else: ts(T.LW[:, 0:V].indirect(T.RP[:, 32 * j:32 * j + 32]), T.RHO[:, 0:512], 1.0, 32.0 * j, A.mult, A.add, "RHO RP", "LW", 512, 3.8)
-    dma("a", [(T.s3[:, 0:64, :], T.LW[0:128:16, 0:V]), (T.s3[:, 64:128, :], T.LX[0:128:16, 0:V]),
-              (T.r3[rank, 0:64, :], T.LW[g0, 0:V]), (T.r3[rank, 64:128, :], T.LX[g0, 0:V])], "LW LX", "s3 r3")
+        if j < NA: act(T.LZ[:].indirect(T.RP[:, 32 * j:32 * j + 32]), T.RHO[:, 512 * j:512 * j + 512], AF.Silu, "RHO%d RP" % j, "LZ", 512, 3.8)
+        else: ts(T.LY[:, 0:V].indirect(T.RP[:, 32 * j:32 * j + 32]), T.RHO[:, 0:512], 1.0, 32.0 * j, A.mult, A.add, "RHO0 RP", "LY", 512, 3.8)
+    dma("a", [(T.s3[:, 0:64, :], T.LY[0:128:16, 0:V]), (T.s3[:, 64:128, :], T.LZ[0:128:16, 0:V]),
+              (T.r3[rank, 0:64, :], T.LY[g0, 0:V]), (T.r3[rank, 64:128, :], T.LZ[g0, 0:V])], "LY LZ", "s3 r3")
     send("3", LATE["3"])
+    iota(T.PG[:, 3584 + TAB:3584 + TAB + V + 16], [[0, V + 16]], 0, 0, "m3", "U0", V + 16)
+    iota(T.W[:, FREE + 16:NONE + 16], [[0, NONE - FREE]], 64, 0, "m3", "Wi", NONE - FREE)
+    dma("s", rows(CH_K, T.VK[:, 0:192], SAME) + rows(CH_A, T.VK[:, 192:384], SAME), "VK VA", "Wi")
+    for M, x in (("LW", -1), ("LX", 0)): iota(T[M][:, TAB:TAB + V], [[0, V]], x, 0, "m3", M, V)
 
     dma("s", [(T.CP[:, 384:576], T.r0[:])], "r0 m0", "CPn", ext=[("a0", short_all)])
     cp(T.NH[:, 0:192], T.CP[:, 384:576], "CPn", "NH0", 192)
     tt(T.NH[:, 192:384], T.CP[:, 384:576], T.NH[:, 0:192], A.subtract, "CPn NH0", "NH1", 192)
-    dma("s", rows(CH_HI, T.NH[:, 0:192]) + rows(CH_LO, T.NH[:, 192:384]), "NH0 NH1", "Wd0")
+    dma("s", rows(CH_HI, T.NH[:, 0:192]) + rows(CH_LO, T.NH[:, 192:384]), "NH0 NH1", "Wd")
     for s in others:
-        dma("s", [(T.F[slot(s + 1), 0:V], T.rf[s])], "mf NH1 ~s", "F%d ~s" % s, ext=[("af%d" % s, arrivals(via, s, True))])
+        dma("s", [(T.F[slot(s + 1), 0:V], T.rf[s])], "mf NH1 s4 ~s", "F%d ~s" % s, ext=[("af%d" % s, arrivals(via, s, True))])
     for s in others:
         dma("s", [(T.X[slot(s), :], T.rx[s])], "mx ~s", "X%d ~s" % s, ext=[("ax%d" % s, arrivals(via, s, True))])
     Fall = " ".join("F%d" % s for s in range(N)) + " "
     Xall = " ".join("X%d" % s for s in range(N)) + " "
-    mm(ext16(P[3][:, 0:192], "MN", T.W, 0, 192), "Wd0 Wb0 Wf0 MN", "P3")
+    mm(ext16(P[3][:, 0:192], "MN", T.W, 0, 192), "Wd Wc Wb Wf Wo MN", "P3")
     ts(T.NU[:], P[3][:, 0:192], 0.0, None, A.add, None, "P3", "NU", 192)
-    scl(T.NF[:], P[3][:, 0:192], 1.0, "P3", "NF", 192)
-    dma("s", [(T.PG[ch:128:16, 256:3328], T.r4[:, 32 * k:32 * k + 32, :]) for k, ch in enumerate((CH_K, CH_A))]
-        + [(T.PG[CH_FR:128:16, 256:3328], T.PG[CH_FI:128:16, 256:3328])]
-        + [x for b in range(2) for x in rows(CH_K, T.r4[:, 64:96, :], b) + rows(CH_A, T.r4[:, 96:128, :], b)],
-        Xall + "r4 m4 m2", PGall[0] + "Wb0 Wb1", ext=[("a4", short_all)])
-    mm(ext16(P[7][:, 256:448], "MB", T.PG, 256, 192), "MB " + PGall[0], "P7")
-    ts(PU, P[7][:, 256:448], float(FREE), None, A.min, None, "P7", "PU", 192)
+    lin(T.NF[:], P[3][:, 0:192], 1.0, -HALF, "P3", "NF", 192)
+    parts2(0, T.NF[:], "NF", 2.0)
+    dma("s", [x for k, ch in enumerate((CH_OK, CH_OA))
+              for x in onward(lambda a, b: T.PG[16 * a + ch:16 * b:16, TAB:TAB + V], lambda a, b: T.r4[a:b, 32 * k:32 * k + 32, :])]
+        + rows(CH_K, T.r4[:, 64:96, :]) + rows(CH_A, T.r4[:, 96:128, :]) + rows(CH_OK, T.VK[:, 0:192]) + rows(CH_OA, T.VK[:, 192:384]),
+        Xall + "r4 m4 m2 VK VA", Tall + "Wb Wo", ext=[("a4", short_all)])
     dma("s", [(T.FA[p, 192 * h:192 * h + 192], T.r2[r, 64 * h:64 * h + 64, :]) for h in range(2) for p, r in ((slice(16, 128), slice(0, 7)), (slice(0, 16), 7))],
         "r2 m2", "FA", ext=[("a2", short_all)])
     tt(T.NI[:], T.FA[:, 0:192], T.FA[:, 192:384], A.max, "FA", "NI", 192)
     ts(T.LU[:], T.NI[:], -4096.0, 0.0, A.add, A.max, "NI", "LU0 LU1 LU2", 192)
-    ts(P[4][:, 0:192], T.NI[:], -4096.0, None, A.add, None, "NI", "P4", 192)
-    act(T.EM[:], P[4][:, 0:192], AF.Relu, "P4", "EM", 192, scale=-64.0)
+    ts(P[4][:, 0:192], T.NI[:], -4096.0 - HALF, -HALF, A.add, A.max, "NI", "P4", 192)
+    act(T.EM[:], T.FA[:], AF.Sign, "FA", "EM", 384)
     dma("s", [(T.ICF[:, 192 * h:192 * h + 192], T.r3[:, 64 * h:64 * h + 64, :]) for h in range(2)], "r3 m3", "ICF", ext=[("a3", short_all)])
     tt(T.ICF[:, 0:192], T.ICF[:, 0:192], T.ICF[:, 192:384], A.max, "ICF", "ICF", 192)
     ts(T.ICU[:], T.ICF[:, 0:192], -8191.75, None, A.add, None, "ICF", "ICU", 192)
 
     for t in range(1, TV + 1):
-        visit[0] = t
         s0 = S * t % V
         cs = s0 // 16
         last = t == TV
         Ft = T.F[:, V * t - V:V * t]
         if t > 1: Fall = "Ft%d " % t
-        if last: dma("s", rows(CH_K, T.VK[:, 0:192]) + rows(CH_A, T.VK[:, 192:384]), "VK VA", "Wb0")
-        wb = t % 2
-        Wt, WA = WW[wb], WR[wb]
+        b0, b1 = (t - 1) % 2, t % 2
+        HI, LO, CH, CL = T.HL[:, 384 * b1:384 * b1 + 192], T.HL[:, 384 * b1 + 192:384 * b1 + 384], T.CD[:, 0:192], T.CD[:, 192:384]
+        now = "HI%d LO%d " % (b1, b1 + 4)
         for j in range(6):
-            gat(ENG["G%d" % t][j], T.G2[:, 512 * j:512 * j + 512], Ft.indirect(T.NU[:, 32 * j:32 * j + 32]), Fall + "NU", "G%d" % j, 512)
+            gat("a", T.G2[:, 512 * j:512 * j + 512], Ft.indirect(T.NU[:, 32 * j:32 * j + 32]), Fall + "NU", "G%d" % j, 512)
         if not last:
             dma("s", [(T.F[16 * t + 16:128, V * t:V * t + V], T.rf[0:7 - t]), (T.F[0:16 * t + 16, V * t:V * t + V], T.rf[7 - t:8])],
                 Fall + Xall + ("FA r4" if t == 1 else "G5"), "Ft%d" % (t + 1), lat=3500.0)
-        tt(P[4][:, 256:448], P[4][:, 0:192], T.NF[:], A.subtract, "P4 NF", "P4", 192, 1.0)
-        ts(T.EQ[:], P[4][:, 256:448], 0.0, None, A.is_equal, None, "P4", "EQ", 192)
+        tt(T.EQ[:], P[4][:, 0:192], T.NF[:], A.is_equal, "P4 NF", "EQ", 192, 1.0)
+        parts2(b1, P[4][:, 0:192], "P4", 1.0)
+        if not last: dma("s", rows(CH_HI, HI) + rows(CH_LO, LO), now, "Wd")
+        for h in (0, 1):
+            o = P[4][:, 192 - 192 * h:384 - 192 * h]
+            mm([(o, T.Y1[:], (HI, LO)[h], 192), (o, T.YN[:], T.HL[:, 384 * b0 + 192 * h:384 * b0 + 192 * h + 192], 192)]
+               + ([(o, T.Y1[:], (CH, CL)[h], 192)] if t > 1 else []), "YN HI0 HI1 LO4 LO5 Y1 CH CL", "P4")
         parts = [(ext16(P[2][:, 64 * h:64 * h + 64], "ME", T.NE, 1024 * h, 64), "ME NE%d NE%d" % (2 * h, 2 * h + 1)) for h in range(3)]
-        parts.append(([(P[2][:, 0:192], T.YE[:], T.EQ[:], 192)], "YE EQ"))
-        if t > 1: parts += [(ext16(P[2][:, 64 * h:64 * h + 64], "MF", T.TR, 1024 * h, 64), "MF" + TRall) for h in range(3)]
-        else: parts.append(([(P[2][:, 0:192], T.YM[:], T.EM[:], 192)], "YM EM"))
-        parts = group(2, 192, parts)
+        if t > 1: parts += [(ext16(P[2][:, 64 * h:64 * h + 64], "MF", T.TR, 1024 * h, 64, 1), "MF" + TRall) for h in range(3)]
+        else: parts.append(([(P[2][:, 0:192], T.YE[:], T.EM[:, 192 * h:192 * h + 192], 192) for h in (0, 1)], "YE EM"))
+        parts = group(2, 192, parts, (T.YE[:], T.EQ[:], "YE EQ"))
         for j in range(6):
             c = slice(512 * j, 512 * j + 512)
-            b = BANK[t > 1][j]
+            b = BANK[t - 1][j]
             if j in SIGN[t - 1]:
                 act(T.PR[:, c], Ft.indirect(T.LU[:, 32 * j:32 * j + 32]), AF.Copy, Fall + "LU%d" % (j // 2), "PR%d" % j, 512, 1.56)
-                mm([(P[b][:], T.YM[:], T.G2[:, c], 512), (P[b][:], T.Y2[:], T.PR[:, c], 512)], "YM Y2 G%d PR%d" % (j, j), "P%d" % b)
+                mm([(P[b][:], T.YN[:], T.G2[:, c], 512)], "YN G%d" % j, "P%d" % b, True, False)
+                mm([(P[b][:], T.Y1[:], T.PR[:, c], 512)], "Y1 PR%d" % j, "P%d" % b, False, True)
                 act(T.D[:, c], P[b][:], AF.Sign, "P%d" % b, "D%d" % j, 512)
             else:
                 tt(T.D[:, c], Ft.indirect(T.LU[:, 32 * j:32 * j + 32]), T.G2[:, c], A.subtract, Fall + "LU%d G%d" % (j // 2, j), "D%d" % j, 512, 1.56)
-        for j in range(6):
-            c = slice(512 * j, 512 * j + 512)
-            b = BANK[t > 1][j]
-            x, a = ([(P[b][:], T.YM[:], T.X[:, c], 512)], Xall + "YM"), ([(P[b][:], T.Y1[:], T.D[:, c], 512)], "Y1a D%d" % j)
+            x, a = ([(P[b][:], T.YM[:], T.X[:, c], 512)], Xall + "YM"), ([(P[b][:], T.Y1[:], T.D[:, c], 512)], "Y1 D%d" % j)
             n = ([(P[b][:], T.Y2[:], T.G2[:, c], 512)], "Y2 G%d" % j)
-            if j in SIGN[t - 1]: a, n = ([(P[b][:], T.Y1[:], T.PR[:, c], 512)], "Y1a PR%d" % j), ([(P[b][:], T.Y1[:], T.G2[:, c], 512)], "Y1a G%d" % j)
-            one, two, three = (n, a, x) if t == 1 else (x, n, a)
-            mm(one[0] + two[0], one[1] + " " + two[1], "P%d" % b, True, False)
-            mm(three[0], three[1], "P%d" % b, False, True)
-            tt(T.PR[:, c], P[b][:], T.D[:, c], A.mult, "P%d D%d " % (b, j) + (FIRST if t == 1 else ""), "PR%d" % j, 512, 1.0)
+            if j in SIGN[t - 1]:
+                mm([(P[b][:], T.Y1[:], y[:, c], 512) for y in (T.G2, T.PR)] + x[0], "Y2 G%d Y1 PR%d " % (j, j) + x[1], "P%d" % b)
+            elif t == 1:
+                for y in group(b, 512, [x, a], n[0][0][1:3] + (n[1],)): y()
+            else:
+                mm(x[0] + n[0], n[1] + " " + x[1], "P%d" % b, True, False)
+                mm(a[0], a[1], "P%d" % b, False, True)
+            tt(T.PR[:, c], P[b][:], T.D[:, c], A.mult, "P%d D%d " % (b, j), "PR%d A%d" % (j, b), 512, 1.0)
             ts(T.NE[:, c], T.PR[:, c], 0.0, 0.5, A.is_lt, A.subtract, "PR%d" % j, "NE%d" % j, 512, 0.5)
             act(T.NE[:, c], T.PR[:, c], AF.Sign, "PR%d" % j, "NE%d" % j, 512, bias=-0.5, scale=-1.0)
-            either(ENG["S%d" % t][j])
-        if t > 1:
-            pgather(t - 1, range(EARLY, 6), " " + AFTER)
-            enter(t - 1)
+            either("a")
         for x in parts: x()
         ts(T.FR[:], P[2][:, 0:192], 4096.0, None, A.is_lt, None, "", "FR P2 A2", 192)
-        dma("s", rows(CH_FR, T.FR[:], wb), "FR", "Wf%d" % wb)
-        tt(T.FC[:], P[4][:, 256:448], T.FR[:], A.mult, "P4 FR", "FC0 FC1 FC2", 192, 1.0)
-        tt(T.NF[:], P[4][:, 0:192], T.FC[:], A.subtract, "P4 FC0 FC1 FC2", "NF", 192, 1.0)
-        scl(T.HI[:], T.NF[:], 1.0, "NF", "HI", 192)
-        tt(T.LW2[:], T.NF[:], T.HI[:], A.subtract, "NF HI", "LO2", 192)
-        dma("s", rows(CH_HI, T.HI[:], wb) + rows(CH_LO, T.LW2[:], wb), "HI LO2", "Wd%d" % wb)
+        if not last: dma("s", rows(CH_FR, T.FR[:]) + (rows(CH_OK, T.VK[:, 384:576]) if t == 2 else []), "FR VL", "Wf Wo")
+        tt(CH, P[4][:, 192:384], T.FR[:], A.mult, "P4 FR", "CH", 192, 1.0)
+        tt(CL, P[4][:, 0:192], T.FR[:], A.mult, "P4 FR", "CL", 192, 1.0)
+        four = ((HI, T.Y1), (LO, T.Y1), (CH, T.YN), (CL, T.YN))
         if not last:
-            cp(T.NU[:], T.NF[:], "NF", "NU", 192)
+            dma("s", rows(CH_C, CH) + rows(CH_C + 1, CL), "CH CL", "Wc")
+            mm([(P[2][:, 0:192], y[:], x, 192) for x, y in four], "CH CL Y1 YN " + now, "P2")
+            ts(T.NU[:], P[2][:, 0:192], HALF, None, A.add, None, "P2", "NU", 192)
+            scl(T.NF[:], P[2][:, 0:192], 1.0, "P2", "NF", 192)
             for j in range(3):
                 for h in (2 * j, 2 * j + 1):
-                    gat(ENG["T%d" % t][h], T.TR[:, 512 * h:512 * h + 512], Wt.indirect(T.ICU[:, 32 * h:32 * h + 32]), WA + "ICU", "TR%d" % h, 512)
-                mm(ext16(P[4][:, 64 * j:64 * j + 64], "ML", T.TR, 1024 * j, 64), "ML TR%d TR%d" % (2 * j, 2 * j + 1), "P4")
-                cp(T.LU[:, 64 * j:64 * j + 64], P[4][:, 64 * j:64 * j + 64], "P4", "LU%d" % j, 64)
+                    gat("a", T.TR[:, 512 * h:512 * h + 512], Wt.indirect(T.ICU[:, 32 * h:32 * h + 32]), WA + "ICU", "TR%d" % h, 512)
+                mm(ext16(P[4][:, 64 * j:64 * j + 64], "MN", T.TR, 1024 * j, 64, 1), "TR%d TR%d MN" % (2 * j, 2 * j + 1), "P4")
+                ts(T.LU[:, 64 * j:64 * j + 64], P[4][:, 64 * j:64 * j + 64], HALF, None, A.add, None, "P4", "LU%d" % j, 64)
         else:
+            mm([(P[2][:, 0:192], y[:], x, 192) for x, y in ((HI, T.YS), (LO, T.YR), (T.FR[:], T.YE))], "YE FR YS YR " + now, "P2")
+            tt(T.RF[:], P[2][:, 0:192], T.DU3[:], A.min, "DU3 P2", "RF", 192, 1.0)
+            ts(T.LO[:], T.RF[:], 192 * HALF + TAB, None, A.add, None, "RF", "LO0 LO1 LO2", 192)
+            for j, h in enumerate((0, 2, 4, 5)):
+                act(T.LX[:].indirect(T.LO[:, 32 * h:32 * h + 32]), T.FV[:, 512 * j:512 * j + 512], AF.Silu, "FV%d LO0" % j, "LX", 512, 3.8)
+            for h in [x for x in range(0, 192, VS) if x // 32 in (1, 3)]:
+                ts(T.LW[:].indirect(T.LO[:, h:h + VS]), T.IOT[:, 0:16 * VS], 1.0, 16.0 * h, A.mult, A.add, "IOT LO0", "LW", 16 * VS, 3.8)
+            dma("s", [(T.FA[:, 0:192], T.LX[0:128:16, TAB:TAB + V])], "LX", "FA")
+            ts(T.YP[:], T.FA[:, 0:192], MAG / 16 - 4096, -MAG / 16, A.add, A.add, "FA", "YP", 192)
+            dma("s", [(T.sq[0:N - TV], T.YP[16 * TV:128, :]), (T.sq[N - TV:N], T.YP[0:16 * TV, :])], "YP", "sq")
             for q in range(N):
                 for b in range(2):
                     o = P[0][0:96, 32 * q + 16 * b:32 * q + 16 * b + 16]
-                    mm([(o, T.HI[:, b:192:2], T.Y1[:, slot(q)], 16), (o, T.LW2[:, b:192:2], T.Y1[:, slot(q)], 16)], "Y1a HI LO2", "P0")
-            act(T.TN[0:96, :], P[0][0:96, 0:256], AF.Copy, "P0", "TN", 256)
+                    mm([(o, x[:, b:192:2], y[:, slot(q)], 16) for x, y in four], "Y1 YN CH CL " + now, "P0")
+            act(T.TN[0:96, :], P[0][0:96, 0:256], AF.Identity, "P0", "TN", 256, bias=HALF)
             dma("s", [(T.sn[q], T.TN[0:96, 32 * q:32 * q + 32]) for q in others], "TN", "sn")
             dma("s", [(T.yn[rank:rank + 1, :], T.TN[0:96, 32 * rank:32 * rank + 32])], "TN", "yno")
             send("n", 5000.0)
-        pgather(t, range(6 if last else EARLY))
-        po = 3584 * ((t - 1) % 2)
-        ts(T.FS[:], T.MK[:, s0 % 16:32:16], T.FR[:, cs:cs + 1], None, A.mult, None, "MK0 MK1 FR", "FS", 2)
-        cols = ((0, cs, T.FR[:, 0:cs]), (cs + 2, 193, T.FR[:, cs + 1:192]), (cs, cs + 2, T.FS[:]))
-        mm([(P[5][:, a:b_], T.SG[:], src, b_ - a) for a, b_, src in cols], "SG FR FS", "P5", each=True)
-        op("v", cyc(193), "P5 ZER", "U P5", lambda q: q.tensor_tensor_scan(T.U[:, 0:193], P[5][:, 0:193], T.ZER[:, 0:193], -256.0, A.add, A.add))
-        Uc = T.U[:, cs:cs + 1]
-        ts(T.DB[:, 0:1], Uc, T.U[:, 192:193], -256.0, A.subtract, A.max, "U", "DB0", 1)
-        ts(T.DB[:, 1:2], Uc, 256.0, T.U[:, 192:193], A.add, A.min, "U", "DB1", 1)
-        ts(T.BC[:, 1:cs + 1], T.U[:, 0:cs], T.DB[:, 0:1], None, A.min, None, "U DB0", "BCa", cs)
-        ts(T.BC[:, cs + 1:194], T.U[:, cs:193], T.DB[:, 1:2], None, A.subtract, None, "U DB1", "BCb", 193 - cs)
-        for x in group(6, 193, [([(P[6][:, a:b_], T.TRI[:], src, b_ - a) for a, b_, src in cols], "TRI FR FS"),
-                                ([(P[6][:, 0:193], T.Y1[:, 0:128], T.BC[:, 0:193], 193)], "Y1a BCa BCb")]): x()
-        scl(T.CU[:, 0:193], P[6][:, 0:193], 1.0, "", "CU P6 A6", 193)
-        mm([(P[5][:, 200:201], strip("MU", k), T.BC[:, 16 * k + 16:16 * k + 17], 1) for k in range(12)], "MU0 BCa BCb", "P5")
+        nt, Fc, HP, HM = 192 - cs, T.FR[:, cs:cs + 1], T.SH[:, 256 * t - 256:256 * t - 128], T.SH[:, 256 * t - 128:256 * t]
+        mm([(P[6][:, 0:nt], T.SG[:], T.FR[:, cs:192], nt), (P[6][:, 0:1], HM, Fc, 1), (P[6][:, nt:192], T.SG[:], T.FR[:, 0:cs], cs), (P[6][:, 192:193], HP, Fc, 1)],
+           "SG FR SH%d" % t, "P6", pair=True)
+        op("v", cyc(193), "P6 ZER", "U", lambda q: q.tensor_tensor_scan(T.U[:, 0:193], P[6][:, 0:193], T.ZER[:, 0:193], -256.0, A.add, A.min))
+        ts(T.BC[:, 1:cs + 2], T.U[:, nt:193], T.U[:, nt - 1:nt], -256.0, A.subtract, A.add, "U", "BCa", cs + 1)
+        ts(T.BC[:, cs + 2:194], T.U[:, 0:nt], T.U[:, 192:193], T.U[:, nt - 1:nt], A.add, A.subtract, "U", "BCb", nt)
+        mm([(P[6][:, 200:201], strip("MU", k), T.BC[:, 16 * k + 16:16 * k + 17], 1) for k in range(12)], "MU BCa BCb", "P6")
         mm(ext16(P[7][:, 448:461], "ME", T.BC, 1, 13), "ME BCa BCb", "P7")
         scl(T.BS[:, 0:13], P[7][:, 448:461], 1.0 / 131072, "P7", "BS", 13)
-        ts(T.L1[:], T.JB[:], P[5][:, 200:201], None, A.is_ge, None, "JB P5", "L1", 256, 0.5)
-        mm(ext16(P[5][:, 256:272], "ME", T.L1, 0, 16), "ME L1", "P5")
-        ts(T.AU[:], P[5][:, 256:272], 1.0 / 8192, None, A.mult, None, "P5", "AU", 16)
-        scl(T.AB[:], P[5][:, 256:272], 16.0, "P5 AU", "AB", 16)
+        mm([(P[7][:, 0:193], T.Y1[:], T.BC[:, 0:193], 193), (P[7][:, 0:cs + 1], T.TRI[:], T.FR[:, 0:cs + 1], cs + 1),
+            (P[7][:, cs + 1:193], T.TRI[:], T.FR[:, cs:192], nt), (P[7][:, cs + 1:cs + 2], HM, Fc, 1)], "TRI Y1 BCa BCb FR SH%d" % t, "P7")
+        scl(T.CU[:, 0:193], P[7][:, 0:193], 1.0, "P7", "CU", 193)
+        ts(T.L1[:], T.JB[:], P[6][:, 200:201], None, A.is_ge, None, "JB P6", "L1", 256, 0.5)
+        mm(ext16(P[6][:, 256:272], "ME", T.L1, 0, 16), "ME L1", "P6")
+        ts(T.AU[:], P[6][:, 256:272], 1.0 / 8192, None, A.mult, None, "P6", "AU", 16)
+        scl(T.AB[:], P[6][:, 256:272], 16.0, "P6 AU", "AB", 16)
         tt(T.L2[:], T.BS[:, 0:16].indirect(T.AU[:]), T.JF[:], A.is_le, "BS AU JF", "L2", 256, 1.56)
-        mm(ext16(P[6][:, 0:16], "ME", T.L2, 0, 16) + [(P[6][:, 0:16], T.Y1[:, 0:128], T.AB[:], 16)], "ME Y1a AB L2", "P6")
+        mm(ext16(P[6][:, 0:16], "ME", T.L2, 0, 16) + [(P[6][:, 0:16], T.Y1[:], T.AB[:], 16)], "L2 ME Y1 AB", "P6")
         ts(T.KU[:], P[6][:, 0:16], 1.0 / 8192, None, A.mult, None, "P6", "KU", 16)
         scl(T.KB[:, 0:16], P[6][:, 0:16], 1.0 / 8192, "P6 KU", "KB", 16)
-        act(T.KB[:, 16:32], T.KB[:, 0:16], AF.Sign, "KB", "KC", 16, bias=-(cs + 0.5))
+        if last: ts(T.KB[:, 16:32], T.KB[:, 0:16], cs + 0.5, 0.5, A.is_gt, A.subtract, "KB", "KC", 16)
+        else: act(T.KB[:, 16:32], T.KB[:, 0:16], AF.Sign, "KB", "KC", 16, bias=-(cs + 0.5))
         tt(T.SE[:], T.CU[:, 0:194].indirect(T.KU[:]), T.TAU[:], A.is_equal, "CU KU TAU", "SE", 256, 1.56)
-        mm(ext16(P[5][:, 0:16], "MS", T.SE, 0, 16) + [(P[5][:, 0:16], T.Y1[:, 0:128], T.KB[:, 0:16], 16), (P[5][:, 0:16], T.YH[:], T.KB[:, 16:32], 16)],
-           "MS Y1a YH KB KC SE", "P5")
-        ts(T.RU[:], P[5][:, 0:16], 4095.5, float(V), A.add, A.min, "P5", "RU", 16)
-        gat(ENG["Z"][t - 1], T.Z[:], Wt.indirect(T.RU[:]), WA + "RU", "Z", 256)
+        mm(ext16(P[6][:, 0:16], "MS", T.SE, 0, 16) + [(P[6][:, 0:16], T.Y1[:], T.KB[:, 0:16], 16), (P[6][:, 0:16], (T.YN if last else T.YH)[:], T.KB[:, 16:32], 16)],
+           "MS SE Y1 YH YN KB KC", "P6")
+        ts(T.RU[:], P[6][:, 0:16], 4095.5, float(V), A.add, A.min, "P6", "RU", 16)
+        gat("a", T.Z[:], Wt.indirect(T.RU[:]), WA + "RU", "Z", 256)
         mm([(P[7][:, 0:256], T.BCN[:], T.Z[:], 256)], "BCN Z", "P7")
-        mm(ext16(P[5][:, 0:16], "MO", T.Z, 0, 16), "MO Z", "P5 NL")
-        cp(T.NB[:], P[7][:, 0:256], "P7", "NB", 256)
-        cp(T.NLU[:, 0:16], P[5][:, 0:16], "NL", "NLU", 16)
-        gat(ENG["O"][t - 1], T.O1[:], T.PG[:, po + 256:po + 3344].indirect(T.NLU[:, 0:16]), PGall[(t - 1) % 2] + "NLU", "O1", 256)
+        mm(ext16(P[6][:, 0:16], "MN", T.Z, 0, 16), "MN Z", "P6")
+        if not last: ts(T.NLU[:, 0:16], P[6][:, 0:16], HALF, None, A.add, None, "P6", "NLU", 16)
+        lin(T.NL[:], P[6][:, 0:16], 1.0, HALF, "P6", "NL", 16)
+        ts(T.NB[:], P[7][:, 0:256], HALF, None, A.add, None, "P7", "NB", 256)
+        tb, TB = 3584 * ((t - 1) % 2), (Tall, " U0 ")[(t - 1) % 2]
         if not last:
-            mm(ext16(P[3][:, 16:32], "MX", T.Z, 0, 16), "MX Z", "P3")
-            tt(T.RT[:], P[3][:, 16:32], T.DU3[:, 0:16], A.min, "P3 DU3", "RT", 16, 1.0)
-            cp(T.NLU[:, 16:32], T.RT[:], "RT", "NPU", 16)
-        mm(ext16(P[6][:, 0:16], "MB", T.O1, 0, 16), "MB O1", "P6")
-        ts(T.OU[:], P[6][:, 0:16], float(FREE), None, A.min, None, "P6", "OU", 16)
-        gat(ENG["O"][t - 1], T.O[:], Wt.indirect(T.OU[:]), WA + "OU", "O", 256)
+            mm(ext16(P[6][:, 16:32], "MX", T.Z, 0, 16), "MX Z", "P6")
+            tt(T.RT[:, 16:32], P[6][:, 16:32], T.DU3[:, 0:16], A.min, "P6 DU3", "RX", 16, 1.0)
+            cp(T.NLU[:, 16:32], T.RT[:, 16:32], "RX", "NPU", 16)
+            gat("a", T.O[:], T.PG[:, tb + TAB:tb + TAB + V + 16].indirect(T.NLU[:, 0:16]), TB + "NLU", "O", 256)
+            for k in range(t):
+                wide = t == 3 and k == 0
+                mm(ext16(P[6][:, 0:16], "MA" if k else "MP", T.O, 0, 16, 1 if k else 1 - t), "O MA MP", "P6")
+                ts(T.OU[:], P[6][:, 0:16], float(NONE if wide else FREE), None, A.min, None, "P6", "OU", 16)
+                gat("a", T.O[:], (T.W[:, 0:NONE + 16] if wide else Wt).indirect(T.OU[:]), WA + "OU" + (" Wi" if wide else ""), "O", 256)
+            parts = [([(P[7][:, 0:256], T.DO[:], T.O[:], 256)], "DO O"), ([(P[7][:, 0:256], T.DZ[:], T.Z[:], 256)], "DZ Z")]
+        else:
+            mm(ext16(P[6][:, 0:16], "MR", T.Z, 0, 16), "MR Z", "P6")
+            ts(T.OU[:], P[6][:, 0:16], 192 * HALF, None, A.add, None, "P6", "OU", 16)
+            gat("a", T.O[:], T.LW[:, TAB:TAB + V].indirect(T.OU[:]), "LW OU", "O", 256)
+            gat("a", T.O1[:], T.LX[:, TAB:TAB + V].indirect(T.OU[:]), "LX OU", "O1", 256)
+            parts = [([(P[7][:, 0:256], T.DL[:], T.O[:], 256)], "DL O"), ([(P[7][:, 0:256], T.DL[:], T.O1[:], 256)], "DL O1"),
+                     ([(P[7][:, 0:256], T.DX[:], T.Z[:], 256)], "DX Z")]
+            mm([(P[3][:, 0:256], T.BCV[:], T.Z[:], 256)], "BCV Z", "P3")
+            lin(T.VAL[:], P[3][:, 0:256], 1.0, -float(SAME // 192), "P3", "VAL", 256)
         for m in range(16):
-            ts(T.E[:, m, 0:256 - 16 * m], T.NB[:, 16 * m:256], P[5][:, m:m + 1], None, A.is_equal, None, "NB NL", "E%d" % m, 256 - 16 * m, 0.5)
-        parts = [([(P[7][:, 0:256], T.OCC[:], T.O[:], 256)], "OCC O")]
+            ts(T.E[:, m, 0:256 - 16 * m], T.NB[:, 16 * m:256], T.NL[:, m:m + 1], None, A.is_equal, None, "NB NL", "E%d" % m, 256 - 16 * m, 0.5)
         for h in range(5):
             parts.append(([(P[7][:, 16 * m + 16:256], T.TWO[:], T.E[:, m, 16:256 - 16 * m], 240 - 16 * m) for m in range(3 * h, 3 * h + 3)],
-                          "TWO " + " ".join("E%d" % m for m in range(3 * h, 3 * h + 3))))
+                          " ".join("E%d" % m for m in range(3 * h, 3 * h + 3)) + " TWO"))
         parts.append(([(P[7][:, 0:256], T.POW[:], T.E[:, :, 0:16], 256)], "POW " + " ".join("E%d" % m for m in range(16))))
-        for x in group(7, 256, parts): x()
-        tt(T.WI[:], P[7][:, 0:256], T.THR[:], A.is_lt, "THR", "WI P7 A7 P5", 256, 1.0)
+        for x in group(7, 256, parts, (T.YH[:], T.THR[:], "YH THR")): x()
+        act(T.WI[:], P[7][:, 0:256], AF.Sign, "", "WI P7 A7", 256, scale=-1.0)
         if not last:
-            tt(T.TR[:, 0:3328].indirect(T.NLU[:, 16:32]), T.Z[:], T.WI[:], A.add, "Z WI NPU", TRall, 256, 3.8)
-        mm(ext16(P[6][:, 0:16], "MC", T.Z, 0, 16), "MC Z", "P6", True, False)
-        mm(ext16(P[6][:, 0:16], "MC", T.WI, 0, 16), "MC WI", "P6", False, True)
-        tt(T.RT[:], P[6][:, 0:16], T.DU2[:], A.max, "P6 DU2", "RT", 16, 1.0)
-        ts(T.QU[:], T.RT[:], -3840.0, None, A.add, None, "RT", "QU", 16)
-    enter(TV)
+            tt(T.TR[:, 0:3440].indirect(T.NLU[:, 16:32]), T.Z[:], T.WI[:], A.add, "Z WI NPU", TRall, 256, 3.8)
+        if last:
+            mm(ext16(P[6][:, 0:16], "MR", T.Z, 0, 16), "Z MR", "P6", True, False)
+            mm(ext16(P[6][:, 0:16], "MF", T.WI, 0, 16), "MF WI", "P6", False, True)
+            tt(T.RT[:, 0:16], P[6][:, 0:16], T.DU2[:, 16:32], A.max, "P6 DU2", "RT", 16, 1.0)
+            ts(T.QU[:], T.RT[:, 0:16], TAB - BIG + 192 * HALF, None, A.add, None, "RT", "QU", 16)
+        elif t < TV - 1:
+            mm(ext16(P[7][:, 0:16], "MF", T.WI, 0, 16), "MF WI", "P7")
+            tt(T.RF[:, 0:16], P[7][:, 0:16], T.NL[:], A.add, "P7 NL", "RF", 16, 1.0)
+            tt(T.RT[:, 0:16], T.RF[:, 0:16], T.DU2[:, 0:16], A.max, "RF DU2", "RT", 16)
+            ts(T.QU[:], T.RT[:, 0:16], float(TAB - BIG), None, A.add, None, "RT", "QU", 16)
+            cp(T.PG[:, tb:tb + TAB + V].indirect(T.QU[:]), T.Z[:], "Z QU", TB, 256, 3.8)
+            tn = 3584 - tb
+            dma("s", [x for ch in (CH_OK, CH_OA) for x in onward(lambda a, b: T.PG[16 * a + ch:16 * b:16, tn + TAB:tn + TAB + V],
+                                                                 lambda a, b: T.PG[16 * a + ch:16 * b:16, tb + TAB:tb + TAB + V])],
+                TB, (Tall, " U0 ")[t % 2])
 
-    dma("s", [(T.sp[:], T.YP[:])], "YP", "sp")
-    dma("a", [(T.yp[own, :], T.YP[own, :])], "YP", "ypo")
-    send("p", 5000.0)
-    ln, lp = [], []
-    if rank > 0:
-        ln.append((T.yn[0:rank, :], T.rn[0:rank]))
-        lp.append((T.yp[0:16 * rank, :], T.rp[0:rank]))
-    if rank < N - 1:
-        ln.append((T.yn[rank + 1:N, :], T.rn[rank + 1:N]))
-        lp.append((T.yp[16 * rank + 16:128, :], T.rp[rank + 1:N]))
-    dma("s", ln, "sp mn yno", "yn", ext=[("an", short_all)])
-    dma("s", lp, "yn mp ypo", "yp", ext=[("ap", short_all)])
+    cp(T.LW[:, 0:TAB + V].indirect(T.QU[:]), T.VAL[:], "VAL QU", "LW", 256, 3.8)
+    dma("s", [(T.sp[0:N - TV], T.LW[16 * TV:128:16, TAB:TAB + V]), (T.sp[N - TV:N], T.LW[0:16 * TV:16, TAB:TAB + V])], "LW", "sp")
+    send("p", 5000.0, " sq")
+    dma("s", [(T.yn[a:b, :], T.rn[a:b]) for a, b in ((0, rank), (rank + 1, N)) if b > a], "sp mn yno", "yn", ext=[("an", short_all)])
+    dma("s", [(T.yp[:], T.rp[:])], "yn mp", "yp", ext=[("ap", short_all + arrivals(vib, rank, False))])
     return ops
-
-
-ENG = {"P0": "avavav", "G1": "vvvvvv", "G2": "aaaaaa", "G3": "aaaaaa", "G4": "aaaaaa", "S1": "aaaaav", "S2": "aaaaav", "S3": "aaaaav", "S4": "aaaaav",
-       "T1": "vaaaaa", "T2": "vaaaaa", "T3": "vaaaaa", "P1": "aaaaaa", "P2": "aaaaaa", "P3": "aaaaaa", "P4": "avavav", "Z": "aaaa", "O": "aaaa"}

@@ -13,157 +13,176 @@ def _sb(n, d):
     return ("sbuf", [128, n], d)
 
 
-LATE = {"0": 8500.0, "f": 8500.0, "x": 11000.0, "2": 4300.0, "4": 5000.0, "3": 4300.0}
-MSG = {"0": (24, i32, False), "f": (384, bf, True), "x": (384, bf, True), "2": (48, f32, False), "4": (96, bf, False), "3": (48, f32, False),
-       "n": (24, f32, False), "p": (24, f32, False)}
-SCRATCH = {}
-for _m, (_n, _d, _w) in MSG.items():
-    SCRATCH["s" + _m] = ("dram", [8, 128, _n], _d)
-    SCRATCH["r" + _m] = ("dram", [8, 128, _n], _d)
-    SCRATCH["h" + _m] = ("dram", [128, _n], _d)
-SCRATCH["sq"] = SCRATCH["sp"]
+LATE = {"y": 0.0, "0": 8500.0, "x": 12000.0, "c": 7000.0, "i": 6200.0, "a": 6200.0, "e": 6200.0, "b": 6200.0, "n": 6500.0}
+PARTS = ((0, 64), (64, 192))
+SCRATCH = {"s0": ("dram", [4, 128, 48], i32), "h0": ("dram", [128, 48], i32), "sx": ("dram", [4, 128, V // 4], bf), "hx": ("dram", [128, V // 4], bf), "hy": ("dram", [128, V // 4], bf),
+           "hc": ("dram", [128, 384], bf), "hi": ("dram", [128, 192], u16), "ka": ("dram", [TV - 1, 128, 192], bf),
+           "ke": ("dram", [TV - 1, 128, PARTS[0][1]], bf), "kb": ("dram", [TV - 1, 128, 192 - PARTS[0][1]], bf), "hn": ("dram", [128, 48], f32), "rn": ("dram", [4, 128, 48], f32)}
+STRIPS = ["MP", "MN", "ME", "MU", "MV", "MA", "MF", "MS", "MX", "MR"]
+SQUARE = ["Y1", "YE", "YH", "YR", "YN", "YS", "SG", "SN", "TRI", "BCN", "POW", "TWO", "DO", "DZ", "DX", "DL", "BCV"]
+UB = max(192 - S * _t % V // 16 for _t in range(1, TV + 1)) - 1
 SCRATCH.update({
-    "X": _sb(V, bf), "F": _sb(TV * V, bf), "G2": _sb(V, bf), "D": _sb(V, bf), "PR": _sb(V, bf), "NE": _sb(V, bf),
-    "W": _sb(NONE + 16, bf), "TR": _sb(3440, bf), "PG": _sb(2 * 3584, bf),
-    "RHO": _sb(1536, f32), "FV": _sb(2048, f32), "LW": _sb(LWN, f32), "LX": _sb(LWN, f32), "LY": _sb(V, f32), "LZ": _sb(V, f32),
+    "X": _sb(TV * V, bf), "F": _sb(V, bf), "G2": _sb(V, bf), "D": _sb(V, bf), "PR": _sb(V, bf), "NE": _sb(V, bf),
+    "W": _sb(NONE + 16, bf), "TR": _sb(3440, bf), "PG": _sb(3584, bf),
+    "RHO": _sb(2048, f32), "FV": _sb(V, f32), "LW": _sb(LWN, f32), "LX": _sb(LWN, f32), "LY": _sb(V, f32), "LZ": _sb(V, f32),
     "E": ("sbuf", [128, 16, 256], bf),
-    "PK": _sb(8, i32), "CC": _sb(8, f32), "CT": _sb(16, f32), "IOT": _sb(512, f32), "TM2": _sb(64, f32), "SG": _sb(128, bf), "MM": _sb(9 * 272, bf),
-    "Y1": _sb(128, bf), "Y2": _sb(128, bf), "YM": _sb(128, bf), "YE": _sb(128, bf), "YH": _sb(128, bf), "YR": _sb(128, bf), "YN": _sb(128, bf), "YS": _sb(128, bf),
-    "TRI": _sb(128, bf), "BCN": _sb(128, bf), "POW": _sb(128, bf), "TWO": _sb(128, bf),
-    "DO": _sb(128, bf), "DZ": _sb(128, bf), "DX": _sb(128, bf), "DL": _sb(128, bf), "BCV": _sb(128, bf),
-    "ZER": _sb(272, bf), "JB": _sb(256, bf), "JF": _sb(256, f32), "TAU": _sb(256, f32), "THR": _sb(256, bf),
-    "DU2": _sb(32, f32), "DU3": _sb(192, f32), "SH": _sb(1024, bf), "VK": _sb(576, bf),
-    "CP": _sb(576, i32), "IA": _sb(768, i32), "KA": _sb(768, bf), "NH": _sb(384, bf), "RP": _sb(384, u16),
-    "FA": _sb(384, f32), "FC": _sb(192, f32), "NI": _sb(192, i32), "EM": _sb(384, bf), "RF": _sb(192, f32),
-    "ICF": _sb(384, f32), "ICU": _sb(192, u16),
+    "PK": _sb(8, i32), "CC": _sb(8, f32), "CT": _sb(16, f32), "IOT": _sb(512, f32), "TM2": _sb(64, f32), "MM": _sb(len(STRIPS) * 144, bf),
+    "YF": _sb(128, f32),
+    "ZER": _sb(720, bf), "JB": _sb(256, bf), "JF": _sb(256, f32), "TAU": _sb(256, f32), "THR": _sb(256, bf),
+    "DU2": _sb(32, f32), "DU3": _sb(192, f32), "SH": _sb(1024, bf), "SA": _sb(512, bf), "VK": _sb(592, bf),
+    "CP": _sb(384, i32), "N0": ("sbuf", [128, 4, 48], i32), "IA": _sb(768, i32), "KA": _sb(768, bf), "NH": _sb(192, f32), "RP": _sb(384, u16),
+    "FA": _sb(384, f32), "RF": _sb(192, f32),
+    "ICF": _sb(384, f32), "ICU": _sb(192 * TV, u16), "KC": _sb(384 * (TV - 1), bf), "HN": _sb(768 * TV, bf),
     "NF": _sb(192, f32), "NU": _sb(192, u16), "LU": _sb(192, u16), "LO": _sb(192, u16),
     "EQ": _sb(192, bf), "O1": _sb(256, bf), "OU": _sb(16, u16),
-    "HL": _sb(768, bf), "CD": _sb(384, bf), "FR": _sb(192, bf),
-    "U": _sb(200, f32), "BC": _sb(210, bf), "CU": _sb(200, f32), "BS": _sb(16, f32),
-    "L1": _sb(256, bf), "L2": _sb(256, bf), "SE": _sb(256, bf), "AU": _sb(16, u16), "AB": _sb(16, bf), "KU": _sb(16, u16),
-    "KB": _sb(32, bf), "RT": _sb(32, f32), "RU": _sb(16, u16), "Z": _sb(256, bf), "O": _sb(256, bf),
+    "HL": _sb(768 * TV, bf), "FR": _sb(192, bf), "MK": _sb(192, bf),
+    "U": _sb(UB + 215, bf), "CU": _sb(200, f32), "BS": _sb(16, f32),
+    "L1": _sb(256, bf), "L2": _sb(256, bf), "SE": _sb(256, bf), "AU": _sb(16, u16), "KU": _sb(16, u16), "KB": _sb(48, bf),
+    "RT": _sb(48, f32), "RU": _sb(16, u16), "Z": _sb(256, bf), "O": _sb(256, bf),
     "NB": _sb(256, u16), "NLU": _sb(32, u16), "WI": _sb(256, bf), "VAL": _sb(256, f32), "NL": _sb(16, f32),
-    "QU": _sb(16, u16), "YP": _sb(192, f32), "TN": _sb(256, f32),
+    "QU": _sb(16, u16), "YP": _sb(192, f32), "TN": ("sbuf", [128, 4, 48], f32),
 })
+for _m in SQUARE:
+    SCRATCH[_m] = _sb(128, bf)
 for _b in range(8):
     SCRATCH["P%d" % _b] = ("psum", [128, 512], f32)
 NDMA = 72
-SEMAPHORES = (["cv", "ca", "cp", "cg", "loc"] + ["h" + m for m in MSG] + ["a" + m for m in MSG if not MSG[m][2]]
-              + ["af%d" % s for s in range(8)] + ["ax%d" % s for s in range(8)] + ["d%d" % k for k in range(NDMA)])
-CH_HI, CH_LO, CH_FR, CH_E, CH_K, CH_A, CH_D, CH_OK, CH_OA, CH_X, CH_Y, CH_C = 0, 1, 2, 3, 4, 5, 6, 8, 9, 10, 11, 12
-STRIPS = ["ME", "MU", "MA", "MP", "MF", "MN", "MS", "MX", "MR"]
+LATER = range(1, TV)
+SEMAPHORES = (["cv", "ca", "cp", "cg", "loc", "h0", "hx", "hy", "hc", "hi", "hn", "a0", "an", "ax%d" % TV] + [m + str(t) for m in ("ha", "he", "hb", "ax", "ac", "ai", "av", "aw") for t in LATER]
+              + ["d%d" % k for k in range(NDMA)])
+CH_HI, CH_LO, CH_FR, CH_E, CH_K, CH_A, CH_D, CH_OK, CH_OA, CH_X, CH_Y, CH_C, CH_J = 0, 1, 2, 3, 4, 5, 6, 8, 9, 10, 11, 12, 14
 CY, PEC, FIX, LAT = 0.9, 0.45, 55.0, 110.0
 
 
 def routes(T, topo):
-    C = T.cores
-    cls = [[d for d in range(N) if topo.may_write(C[s], C[d])] for s in range(N)]
-    idx = [cls[s].index(s) for s in range(N)]
-    via, vib = [[None] * N for _ in range(N)], [[None] * N for _ in range(N)]
-    for s in range(N):
-        mine = [c for c in topo.cores_of(C[s]) if c != C[s]]
-        far = [d for d in range(N) if d not in cls[s]]
-        port = [c for c in mine if topo.may_write(c, C[far[0]])]
-        dies = sorted(set(topo.die(c) for c in port))
-        free = {x: [c for c in port if topo.die(c) == x] for x in dies}
-        for d in far:
-            via[s][d] = vib[s][d] = free[dies[(idx[s] + idx[d]) % 2]].pop(0)
-        plain = [c for c in mine if c not in port and topo.die(c) != topo.die(C[s])]
-        for d in cls[s]:
-            if d != s and idx[d] != (idx[s] + 1) % len(cls[s]):
-                via[s][d] = plain.pop(0)
-        vib[s][s] = [c for c in mine if c not in port][0]
-    return via, vib
+    out = []
+    for c in T.cores:
+        port = [x for x in topo.cores_of(c) if x != c and all(topo.may_write(x, d) for d in T.cores)]
+        by = [[x for x in port if topo.die(x) == y] for y in sorted(set(topo.die(x) for x in port))]
+        out.append([l[0] for l in by] + [l[1] for l in by])
+    return out
+
+
+def messages(T):
+    half = lambda k, t: (t, T.X[:, V * t - V + V // 4 * k:V * t - V + V // 4 * (k + 1)], "ax%d" % t)
+    l = {"0": [(k, T.s0[k], T.h0[:], [(1, T.N0[:, k, :], "a0")]) for k in range(4)],
+         "x": [(k, T.sx[k], T.hx[:], [half(k, 1), half(k, 2)]) for k in range(4)],
+         "c": [(3, T.KA[:, 0:384], T.hc[:], [(t, T.KC[:, 384 * t - 384:384 * t], "ac%d" % t) for t in LATER])],
+         "y": [(k, T.sx[2 + k], T.hy[:], []) for k in range(2)],
+         "i": [(2, T.ICU[:, 0:192], T.hi[:], [(t, T.ICU[:, 192 * t:192 * t + 192], "ai%d" % t) for t in LATER])]}
+    for t in LATER:
+        for m, first, o, (a, b), sem in (("a", 2, 0, (0, 192), "av"), ("e", 2, 384, PARTS[0], "av"), ("b", 0, 384, PARTS[1], "aw")):
+            c = [768 * t - 768 + o + 192 * k for k in range(2)]
+            l[m + str(t)] = [(first + k, T.HL[:, c[k] + a:c[k] + b], T["k" + m][t - 1], [(1, T.HN[:, c[k] + 768 + a:c[k] + 768 + b], sem + str(t))]) for k in range(2)]
+        if t + 2 <= TV: l["x%d" % t] = [(k % 2, None, T["hxhy"[k & 2:][:2]][:], [half(k, t + 2)]) for k in range(4)]
+    l["n"] = [(k, T.TN[:, k, :], T.hn[:], [(-TV, T.rn[k], "an")]) for k in range(4)]
+    return l
 
 
 def bits(l):
     return sum(1 << e for e in l)
 
 
-def arrival(m, s):
-    return "a%s%d" % (m, s) if MSG[m][2] else "a" + m
-
-
-def helper(g, core, T, topo, via, vib):
+def helper(g, core, T, topo, ports):
     sent = 0
-    for m in MSG:
-        for s, d in [(s, d) for s in range(N) for d in range(N) if (via if MSG[m][2] else vib)[s][d] == core and (s != d or m == "p")]:
-            rid, pid = topo.addr(T.cores[d], core)
-            g.wait_ge(T.sem["h" + m], 2)
-            g.remote_dma(T["r" + m][s], T["h" + m][:], T.sem[arrival(m, s)], T.sem.loc, pid, rid, topo.mask(core, T.cores[d]))
-            sent += len(topo.engines(core, T.cores[d]))
+    for s in [s for s in range(N) if core in ports[s]]:
+        for m, l in messages(T).items():
+            for k, src, here, to in l:
+                if ports[s][k] != core: continue
+                if src is not None: g.wait_ge(T.sem["h" + m], len(topo.engines(T.cores[s], core)) // len(l))
+                for back, dst, sem in to:
+                    d = T.cores[(s - back) % N]
+                    rid, pid = topo.addr(d, core)
+                    g.remote_dma(dst, here, T.sem[sem], T.sem.loc, pid, rid, topo.mask(core, d))
+                    sent += len(topo.engines(core, d))
     if sent: g.wait_ge(T.sem.loc, sent)
 
 
 def rank_program(g, core, T, topo):
-    via, vib = routes(T, topo)
+    ports = routes(T, topo)
     rank = T.rank_of(core)
     if rank is None:
-        helper(g, core, T, topo, via, vib)
+        helper(g, core, T, topo, ports)
         return
-    ops = build(g, core, rank, T, topo, via, vib)
+    ops = build(g, core, rank, T, topo, ports)
     emit(g, T, ops)
 
 
 PLAN = {}
-CASES = [{"far": 1.0, "wide": 1.0, "dma": 1.0, "wake": 1.0},
-         {"gather": 1.3, "scatter": 1.55, "far": 0.8, "wide": 0.8, "dma": 0.8, "wake": 1.0},
-         {"gather": 0.7, "scatter": 0.5, "tensor": 1.2, "far": 1.3, "wide": 1.4, "dma": 1.2, "wake": 2.5}]
-ROUNDS = [(1, 520, 70.0), (3, 360, 35.0)]
-MOVES, WINDOW, NEAR, SOON = 1200, 100, 400.0, 0.05
-NA, VS = 3, 8
-SIGN = [(1, 3, 5), (5,), (5,), (5,)]
+CASES = [{"far": 1.0, "wide": 1.0, "dma": 1.0, "wake": 1.0, "weight": 1.5},
+         {"gather": 1.3, "scatter": 1.55, "far": 0.75, "wide": 0.75, "dma": 0.75, "wake": 0.9, "weight": 1.5},
+         {"gather": 0.85, "scatter": 0.8, "tensor": 1.1, "far": 1.45, "wide": 1.4, "dma": 1.2, "wake": 2.5, "weight": 2.0},
+         {"gather": 1.1, "scatter": 0.7, "far": 1.8, "wide": 1.4, "dma": 1.0, "wake": 1.2, "weight": 2.0},
+         {"gather": 0.78, "scatter": 1.45, "far": 0.85, "wide": 0.9, "dma": 0.85, "wake": 1.2}]
+ROUNDS = [((0, 1, 2, 3, 4), 650, 18.0), ((0, 1, 2, 3, 4), 400, 7.0)]
+MOVES, WINDOW, NEAR, SOON, URGE = 1200, 70, 400.0, 0.05, 150.0
+NA, VS, VCH = 3, 16, ((1, 3, 5), (3, 5))
+SPAN = (0.0, 1.0)
+SIGN = [(3,), (), (), ()]
+SIZE = [(5,), (5,), (5,), (5,)]
 BANK = [(0, 1, 5, 6, 3, 7), (0, 1, 3, 5, 0, 1), (0, 1, 3, 5, 0, 1), (0, 1, 3, 5, 0, 1)]
-FIRST = [{"v": "ZER Wd IA0 IA1 KAc IA2 IA3 KAp Wu YP PU Wt T0 T2 FC0 LO0 RP FC1 LW LO1 LW+ FC2 LO2 LW++ NH0 NH1 LY LY+ LY++ NU NF HI0 G2 LO4 G5 NI LU0 "
-               "D0 D2 P4 PR0 D4 PR2 PR3+ EQ PR1+ PR4 PR5+ HI1 NE5 LO5 FR",
-          "a": "MA MN FV0 FV1 FV2 MF ME MX MR MU MP MS T1 T3 T4 LX T5 LX+ LX++ LZ LZ+ LZ++ G1 G4 G3 G0 EM PR1 PR3 PR5 D3 D1 D5 NE2 NE3 NE0 NE1 NE4",
-          "p": "YR.Y1+ YR.Y1 T0.T1 T2.T3 T4.T5 Wd.Wc Y2.G4 YN.G1 Y2.G2 X0.X1+ YN.G3 Y2.G0 YN.G5 X0.X1++ Y1.PR1 Y1.D0 X0.X1 Y1.PR3 Y1.D2 Y1.PR5 "
-               "Y2.G3 Y2.G1 Y1.D4 YE.EQ Y2.G5 YE.EM ME.NE2 ME.NE0 ME.NE4 YN.HI0"},
-         {"v": "CH CL U BCb BCa NU NF L1 G0 AU AB L2 TR2 KU SE G1 LU0 RU D0 D1 NLU LU1 NB D2 E0 RX E1 E2 E3 LU2 PR0 E4 E5 OU E6 E7 E8 E9 E10 NPU "
-               "E11 E12 E13 PR1 OU+ E14 E15 D3 OU++ EQ NE0 D4 PR4 PR2 TR0+ RF PR3 PR5+ HI0 RT LO4 QU T0 FR",
-          "a": "G2 BS TR0 TR1 CU KB KC TR3 TR4 Z G3 NL TR5 O G4 O+ G5 O++ PR5 O+++ NE1 WI D5 NE4 NE2 NE3 NE5",
-          "p": "YN.HI0+- SG.FR CH.CL MU.BCa ME.BCa ME.L1 Y2.G0 TRI.Y1 L2.ME Y2.G2 TR0.TR1 MS.SE Y2.G1 TR2.TR3 MN.Z BCN.Z Y1.D0 Y2.G3 MX.Z TR4.TR5 O.MA "
-               "YH.THR Y1.D2 Y1.D1 Y2.G4 DZ.Z E0.E1 O.MA+ E3.E4 E6.E7 Y1.D4 O.MA++ E9.E10 E12.E13 POW.E0 YN.G5 DO.O Y1.PR5 YE.EQ Y1.D3 ME.NE0 "
-               "MF.WI Y2.G5 MF.TR0 MF.TR0+ MF.TR0++ ME.NE2 ME.NE4 YN.HI0"},
-         {"v": "U BCb BCa RF CH LO0 L1 LW CL AU L2 AB LW+ KU LW++ SE KC LW+++ LW++++ RU LW+++++ LW++++++ NB NL LW+++++++ E0 E1 E2 E3 E4 E5 E6 E7 E8 E9 "
-               "E10 E11 OU E12 E13 E14 E15 O VAL RT YP QU LW++++++++",
-          "a": "BS LX CU KB LX+ Z LX++ LX+++ O1 TN WI",
-          "p": "SG.FR YE.FR YN.HI0+- MU.BCa ME.BCa ME.L1 TRI.Y1 L2.ME MS.SE BCN.Z MN.Z MR.Z YH.THR BCV.Z DX.Z E0.E1 E3.E4 E6.E7 E9.E10 E12.E13 POW.E0 "
-               "DL.O DL.O1 Z.MR MF.WI"}]
-LISTED = "vap"
+
+
+FIRST = [{"v": "ZER YP Wd IA0 IA1 PW KAc Wt Wu IA2 IA3 RP KAp FV2 PU LY T1 LY+ FC0 FC1 LO0 LO1 T4 LW FC2 LW+ LO2 PV LW++ NH LY++ NU0 OH G0 LU0 NF0 D0 D1 P4 "
+               "ICU HI1 HI0 LO5 LO4 EQ0 c2 D2 EQ1 PR0 PR1 D4 NE1 PR2 PR3+ PR4 FQ NE5 CH10 c4 CL10 c3 PW2 THR FR",
+          "a": "MP FV4 MA FV0 LZ T2 T3 T0 T5 LZ+ LX LX+ LX++ LZ++ G1 G2 G3 MK PR3 G5 G4 D3 D5 PR5 NE0 PR5+ NE2 NE3 NE4 DZ DO BCN",
+          "p": "YR.Y1+ YR.Y1 T2.T3 T0.T1 T4.T5 NH.YF NH.YF+ NH.YF++ NH.YF+++ NH.YF++++ NH.YF+++++ FA.YF G1.YN G0.YN G2.YN ICF.YF D0.YH YN.G3 D1.YH Y1.PR3 "
+               "ax1.YN ax1.Y1++ ax1.Y1 YN.Y1 Y1.G5 YN.Y1+ ax1.Y1+ G4.YN D2.YH YN.Y1++ ax1.Y1++++ YN.Y1+++ ax1.Y1+++ ax1.YN+ G3.YH Y1.PR5 PR3.YH YE.EQ0 D4.YH "
+               "ME.NE0 YN.D5 YN.MK Y1.PR5+ YE.EQ1 YN.MK+ ME.NE2 ME.NE4"},
+         {"v": "CH1 U CL1 Ua KC L1 T0- AU L2 TR0 KU SE TR4 LU0 RU Z LU1 NLU NB E3 E12 RX LU2 E6 E0 HI OU NPU NU0 LO D0 E15 EQ0 OU+ E9 D1 PR0 NU1 OU++ PR1 "
+               "EQ1 D4 D2 TR0+ D3 PR4 FQ RG CH0 RF0 PR2 CL0 LO0 PR3 NE3 RT QU FR",
+          "a": "BS CU AB TR1 TR2 KB TR3 TR5 G1 NL O G3 G0 O+ NF0 G2 O++ G5 G4 O+++ NF1 NE0 NE1 WI D5 PR5 PR5+ NE4 NE5 NE2",
+          "p": "ax.Y1+++ SG.FQ ax.Y1+ SG.U MU.U MU.U+ MV.L1 TRI.Y1 ax.Y1 ax.Y1++ L2.MU TR0.TR1 MS.SE TR2.TR3 MN.Z BCN.Z TR4.TR5 MX.Z YH.THR G1.YN E3.E4 O.MA "
+               "E6.E7 Y1.YN G3.YN G0.YN E0.E1 O.MA+ DZ.Z D0.YH YN.Y1 G2.YN YN.Y1+ E12.E13 Y1.YN+ O.MA++ D1.YH E9.E10 ax.Y1++++ G4.YN POW.E0 DO.O ax.YN YN.Y1++ "
+               "Y1.G5 YN.Y1+++ YE.EQ0 D4.YH ME.NE0 ax.YN+ MF.WI D2.YH Y1.PR5 YE.EQ1 MF.TR0 D3.YH YN.D5 Y1.PR5+ YE.YS MF.TR0++ MF.TR0+ ME.NE4 ME.NE2"},
+         {"v": "CH1 CL1 RF1 U LO1 Ua KC TN1 TN2 TN0 L1 LW BS AU L2 CU LW+ KU SE LW++ RU Z LW+++ NB E9 E0 OU E3 YP E6 E12 E15 RT QU LW++++",
+          "a": "LX LX+ AB LX++ KB LX+++ NL O1 O VAL WI",
+          "p": "YE.YS SG.FQ Y1.YN++ Y1.YN++++ Y1.YN+++ Y1.YN Y1.YN+++++ SG.U Y1.YN+ MU.U MU.U+ MV.L1 TRI.Y1 L2.MU MS.SE BCN.Z MN.Z BCV.Z YH.THR MR.Z DX.Z "
+               "E9.E10 E0.E1 E3.E4 DL.O1 E6.E7 DL.O E12.E13 POW.E0 Z.MR MF.WI"}]
 
 
 def labels(ops):
     out, seen, s = [], {}, 0
     for o in ops:
         w = "" if o["dma"] or o["e"] == "g" else ".".join(o["r"][:2]) if o["e"] == "p" else o["w"][0]
-        w = {"HI1": "HI0", "LO5": "LO4", "U0": "T0"}.get(w, w) if s else w
+        if s and (w[:2] in ("CH", "CL", "HI", "ax") or w[:2] == "LO" and int(w[2]) > 3): w = w[:2] + w[3:]
         seen[(s, w)] = seen.get((s, w), -1) + 1
         out.append((s, w + "+" * seen[(s, w)]))
         s += w == "FR"
     return out
 
 
+def listed(ops, alt):
+    out = {e: [] for e in "vap"}
+    for i, (s, w) in enumerate(labels(ops)):
+        for z, x in ((s + 1, w + "-"), (s, w))[s == 0:]:
+            hit = [(e, l.split().index(x)) for e, l in FIRST[(z > 0) + (z >= TV)].items() if e in alt[i] and x in l.split() and z <= TV]
+            if hit:
+                out[hit[0][0]].append((z, hit[0][1], i))
+                break
+    return {e: [x[2] for x in sorted(l)] for e, l in out.items()}
+
+
 def first_order(ops, pre, post, alt):
     n = len(ops)
-    q = [0.0] * n
-    for i in range(n - 1, -1, -1): q[i] = ops[i]["c"] + max([q[j] + x for j, x in post[i]] + [ops[i]["lat"]])
-    marks = [0.0] + [q[0] - q[i] for i, o in enumerate(ops) if o["w"][:1] == ["FR"]] + [q[0]]
-    key, eng = [q[0] - x for x in q], [o["e"] for o in ops]
-    for i, (s, w) in enumerate(labels(ops)):
-        for e, l in FIRST[(s > 0) + (s == TV)].items():
-            l = l.split()
-            if 0 < s < TV and w + "-" in l: w, s = w + "-", s + 1
-            if w in l and e in alt[i]:
-                key[i], eng[i] = marks[s] + (marks[s + 1] - marks[s]) * (l.index(w) + 1) / (len(l) + 1), e
-    qs = {e: sorted((i for i in range(n) if eng[i] == e), key=lambda i: key[i]) for e in LISTED}
+    eng, qs = [o["e"] for o in ops], listed(ops, alt)
+    home = {i: e for e in qs for i in qs[e]}
+    q, nxt = [0.0] * n, {x: y for l in qs.values() for x, y in zip(l, l[1:])}
+    for _ in range(60):
+        for i in range(n - 1, -1, -1):
+            q[i] = alt[i][home.get(i, eng[i])] + max([q[j] + x for j, x in post[i]] + [ops[i]["lat"], q[nxt[i]] if i in nxt else 0.0])
     fin, free, left = [0.0] * n, {e: 0.0 for e in "vapgs"}, [len(x) for x in pre]
     ready, order = set(i for i in range(n) if not left[i]), []
     while ready:
-        c = [i for i in ready if eng[i] not in qs or qs[eng[i]][0] == i] or [min(ready, key=lambda i: (key[i], i))]
-        t, _, i = min((max([free[eng[i]], ops[i]["t0"]] + [fin[d] + x for d, x in pre[i]]), -q[i], i) for i in c)
-        if eng[i] in qs: qs[eng[i]].remove(i)
-        fin[i] = free[eng[i]] = t + alt[i][eng[i]]
+        c = []
+        for i in [x for x in ready if x not in home or qs[home[x]][0] == x] or ready:
+            t = max([ops[i]["t0"]] + [fin[d] + x for d, x in pre[i]])
+            f, e = min((max(t, free[e]) + alt[i][e], e) for e in (home[i] if i in home else alt[i]))
+            c.append((f - alt[i][e], i, f, e))
+        t = min(c)[0] + URGE
+        _, i, f, eng[i] = max((q[x[1]],) + x[1:] for x in c if x[0] <= t)
+        if i in home: qs[home[i]].remove(i)
+        fin[i] = free[eng[i]] = f
         ready.discard(i)
         order.append(i)
         for j, _ in post[i]:
@@ -181,7 +200,7 @@ def schedule(ops):
         for d, x in pre[i]: post[d].append((i, x))
     head, tail = [o["t0"] for o in ops], [o["lat"] for o in ops]
     every = [([c.get(o["g"], 1.0) for o in ops],
-              [[(d, x * (c["wide"] if "mx" in ops[d]["w"] or "mf" in ops[d]["w"] else c["far"] if ops[d]["rem"] else c["dma"] if ops[d]["dma"] else c["wake"]))
+              [[(d, x * (c["wide"] if "mx" in ops[d]["w"] else c.get("early", 1.0) * c["far"] if ops[d]["rem"] and ops[d]["w"][1][:2] == "me" else c["far"] if ops[d]["rem"] else c["dma"] if ops[d]["dma"] else c["wake"]))
                 for d, x in pre[i]] for i in range(n)]) for c in CASES]
     order, eng = first_order(ops, pre, post, alt)
     rnd = np.random.default_rng(1)
@@ -299,18 +318,18 @@ def schedule(ops):
                 en[v], co[v] = o, al[o]
         order[a:b] = [win[k] for k in now[2]]
         for k, i in enumerate(win): eng[i] = en[k]
-    for nc, rounds, heat in ROUNDS:
-        cases = every[:nc]
+    for which, rounds, heat in ROUNDS:
+        cases, nc = [every[k] for k in which], len(which)
         norm = [x[0] for x in whole(cases)]
-        norm = [x / norm[0] * nc for x in norm]
+        norm = [x / norm[0] * sum(CASES[j].get("weight", 1.0) for j in which) / CASES[k].get("weight", 1.0) for x, k in zip(norm, which)]
         best = None
         for sw in range(rounds + 1):
             res = whole(cases)
             tot = sum(x[0] / z for x, z in zip(res, norm))
             if best is None or tot < best[0]: best = (tot, list(order), list(eng), res)
             if sw == rounds: break
-            order.sort(key=lambda i: res[0][1][i] - alt[i][eng[i]])
-            a = int(rnd.integers(-WINDOW // 2, n - WINDOW // 2))
+            order.sort(key=lambda i: res[0][1][i] - alt[i][eng[i]] * cases[0][0][i])
+            a = int(rnd.integers(int(SPAN[0] * n) - WINDOW // 2, int(SPAN[1] * n) - WINDOW // 2))
             window(cases, norm, res, max(0, a), min(n, a + WINDOW), heat * (1.02 - sw / rounds))
         order[:], eng[:] = best[1], best[2]
     return best[3], order, eng
@@ -365,8 +384,9 @@ def emit(g, T, ops):
             tok[i] = (s, 16 * len(ins))
             alltok[s] = 16 * len(ins)
         else:
-            cnt[o["e"]] += 1
-            ins.then_inc(T.sem["c" + o["e"]], 1)
+            for x in ins if isinstance(ins, list) else [ins]:
+                cnt[o["e"]] += 1
+                x.then_inc(T.sem["c" + o["e"]], 1)
             tok[i] = ("c" + o["e"], cnt[o["e"]])
             alltok["c" + o["e"]] = cnt[o["e"]]
     for o in ops:
@@ -376,14 +396,18 @@ def emit(g, T, ops):
             g.wait_ge(T.sem[s], alltok[s])
 
 
-def build(g, core, rank, T, topo, via, vib):
+def build(g, core, rank, T, topo, ports):
     ops, kind, gate = [], [""], [""]
+    MSG, landed = messages(T), {}
+    for l in MSG.values():
+        for k, _, _, to in l:
+            for back, _, sem in to: landed[sem] = landed.get(sem, 0) + len(topo.engines(ports[(rank + back) % N][k], core))
 
-    def op(e, c, r, w, f, dma=False, lat=0.0, ext=(), t0=0.0, rem=0):
+    def op(e, c, r, w, f, dma=False, lat=0.0, t0=0.0, rem=0):
         r, w = (r + (gate[0] if e == "g" and not rem else "")).split(), w.split()
         w = w + [x for x in r if x[0] == "P" and x[1:].isdigit()]
         ops.append({"g": "tensor" if e == "p" else kind[0] if e in "va" and not dma else "", "e": e, "c": c, "r": r, "w": w, "f": f, "dma": dma,
-                    "lat": lat, "ext": list(ext), "t0": t0, "rem": rem})
+                    "lat": lat, "ext": [] if rem else [(x, landed[x]) for x in r if x in landed], "t0": t0, "rem": rem})
 
     def cyc(n, k=1.0):
         kind[0] = {1.56: "gather", 3.8: "scatter"}.get(k, "")
@@ -414,7 +438,7 @@ def build(g, core, rank, T, topo, via, vib):
     def either(e, n=2):
         l = [ops.pop() for _ in range(n)]
         o = dict([x for x in l if x["e"] == e][0], alt={x["e"]: (x["c"], x["f"]) for x in l})
-        o["r"] = sorted(set(y for x in l for y in x["r"] if y not in ("mf", "mx")))
+        o["r"] = sorted(set(y for x in l for y in x["r"] if y not in ("m0", "mx")))
         ops.append(o)
 
     def lin(out, a, scale, bias, r, w, n, k=1.0):
@@ -439,9 +463,9 @@ def build(g, core, rank, T, topo, via, vib):
             return x
         op("p", sum(max(64, x[3]) for x in l) * PEC + 30.0, r, w, f, lat=40.0)
 
-    def group(bank, n, parts, first=None):
-        a, b, r = first or (T.ZER[:, 0:128], T.ZER[:, 0:n], "ZER")
-        mm([(P[bank][:, 0:n], a, b, n)], r, "P%d A%d" % (bank, bank), True, False)
+    def group(bank, n, parts, first, lo=0):
+        a, b, r = first
+        mm([(P[bank][:, lo:n], a, b, n - lo)], r, "P%d A%d" % (bank, bank), True, False)
         left = [len(parts)]
 
         def one(l):
@@ -453,8 +477,8 @@ def build(g, core, rank, T, topo, via, vib):
             return f
         return [lambda l=l, r=r: op("p", sum(max(64, x[3]) for x in l) * PEC + 30.0, r + " A%d" % bank, "", one(l), lat=40.0) for l, r in parts]
 
-    def dma(e, l, r, w, lat=1800.0, ext=(), t0=0.0):
-        op(e, 70.0 * len(l), r, w, lambda q: [q.dma_start(o, a) for o, a in l], dma=True, lat=lat, ext=ext, t0=t0)
+    def dma(e, l, r, w, lat=1800.0, t0=0.0):
+        op(e, 70.0 * len(l), r, w, lambda q: [q.dma_start(o, a) for o, a in l], dma=True, lat=lat, t0=t0)
 
     def iota(out, pat, base, cm, r, w, n, fl=True):
         if fl: op("g", 140 + 2 * n * CY, r, w, lambda q: q.iota(out, pat, base, cm, allow_small_or_imprecise_dtypes=True))
@@ -467,127 +491,107 @@ def build(g, core, rank, T, topo, via, vib):
         pat = [p for p in ([0, reps], [16, 8], [0, wide]) if p[1] > 1]
         for ch, x in wts: sel(out, out, pat, A.not_equal, float(x), ch, -1, w, w, 8 * reps * wide)
 
-    def inslot(out, w, reps=1, wide=1):
-        for s, b in ((-1, 0), (1, 15)):
+    def inslot(out, w, reps=1, wide=1, top=15):
+        for s, b in ((-1, 0), (1, top)):
             sel(out, out, [p for p in ([0, reps], [16 * s, 8], [0, wide]) if p[1] > 1], A.is_ge, 0.0, b, -s, w, w, 8 * reps * wide)
 
     def diag(l):
         for M, x in l: sel(T[M][:], T.ZER[:, 0:128], [[1, 128]], A.not_equal, x, 0, -1, "ZER", M, 128)
 
-    def strip(M, k, d=0):
-        o = 272 * STRIPS.index(M) + 143 - k - 16 * (d % N)
+    def strip(M, k):
+        o = 144 * STRIPS.index(M) + 15 - k
         return T.MM[:, o:o + 128]
 
-    def ext16(out, M, src, lo, n, d=0):
-        return [(out, strip(M, k, d), src[:, lo + k:lo + 16 * n:16], n) for k in range(16)]
+    def ext16(out, M, src, lo, n):
+        return [(out, strip(M, k), src[:, lo + k:lo + 16 * n:16], n) for k in range(16)]
 
     def rows(ch, src, o=0):
         return [(T.W[ch:128:16, o:o + V], src)]
 
-    def onward(dst, src):
-        return [(dst(1, N), src(0, N - 1)), (dst(0, 1), src(N - 1, N))]
-
     def slot(q):
         return slice(16 * (q % N), 16 * (q % N) + 16)
 
-    def parts2(b, src, r, k):
-        ts(T.HL[:, 384 * b:384 * b + 192], src, MAG, -MAG, A.add, A.add, r, "HI%d" % b, 192)
-        tt(T.HL[:, 384 * b + 192:384 * b + 384], src, T.HL[:, 384 * b:384 * b + 192], A.subtract, r + " HI%d" % b, "LO%d" % (b + 4), 192, k)
+    def parts2(hi, lo, b, src, r, k):
+        ts(hi, src, MAG, -MAG, A.add, A.add, r, "HI%d" % b, 192)
+        tt(lo, src, hi, A.subtract, r + " HI%d" % b, "LO%d" % (b + 4), 192, k)
 
-    C = T.cores
-    others = [d for d in range(N) if d != rank]
     P = [T["P%d" % b] for b in range(8)]
 
-    def send(m, lat, r="", c=500.0):
-        wide = MSG[m][2]
-        route = via if wide else vib
-        off = topo.engines(core, C[[d for d in others if route[rank][d] is None][0]])
-        rest = [e for e in topo.engines(core, [c for c in topo.cores_of(core) if c != core][0]) if e not in off]
-        nd = 4 if wide else 2
-        pool = off + rest
-        tr, tot = [], 0
-        src = lambda d: dict(srcs=[T.sp[d], T.sq[d]], alu_op=2) if m == "p" else dict(src=T["s" + m][d])
-        for d in [d for d in others if route[rank][d] is None]:
-            rid, pid = topo.addr(C[d], core)
-            tr.append(RemoteDMATransfer(dst_ids=[DstId(rid=rid, pnc=pid)], dma_engine_mask=bits(pool[:nd]), remote_sem=T.sem[arrival(m, rank)],
-                                        dst=T["r" + m][rank], **src(d)))
-            pool = pool[nd:]
-            tot += nd
-        for d in [d for d in others + [rank] * (m == "p") if route[rank][d] is not None]:
-            rid, pid = topo.addr(route[rank][d], core)
-            tr.append(RemoteDMATransfer(dst_ids=[DstId(rid=rid, pnc=pid)], dma_engine_mask=bits(pool[-2:]), remote_sem=T.sem["h" + m],
-                                        dst=T["h" + m][:], **src(d)))
-            pool = pool[:-2]
-            tot += 2
-        op("g", c, "s%s gq" % m + r, "gq m" + m, lambda q: q.remote_dma_fused(tr, local_sem=T.sem.loc), rem=tot, lat=lat + 500.0 - c)
-
-    def arrivals(route, s, wide):
-        return (4 if wide else 2) if route[s][rank] is None else len(topo.engines(route[s][rank], core))
-
-    short_all = sum(arrivals(vib, s, False) for s in others)
-    own = slice(16 * rank, 16 * rank + 16)
+    def send(m, r, c=500.0, also=""):
+        l, tr = MSG[m], []
+        mine = topo.engines(core, ports[rank][0])
+        n = len(mine) // len(l)
+        for j, (k, src, there, _) in enumerate(l):
+            rid, pid = topo.addr(ports[rank][k], core)
+            tr.append(RemoteDMATransfer(dst_ids=[DstId(rid=rid, pnc=pid)], dma_engine_mask=bits(mine[n * j:n * j + n]), remote_sem=T.sem["h" + m], dst=there, src=src))
+        op("g", c, r + " gq", "gq m%s %s " % (m, also) + " ".join(x[2] for x in l[0][3]), lambda q: q.remote_dma_fused(tr, local_sem=T.sem.loc),
+           rem=len(mine), lat=LATE[m[0]] + 500.0 - c)
 
     dma("s", [(T.CP[:, 0:192], T.cc[:])], "", "CPc")
-    dma("a", [(T.s0[:], T.nm[:]), (T.CP[:, 192:384], T.pl[:]), (T.r0[rank], T.nm[rank:rank + 1, :])], "", "s0 r0 CPp ~a")
-
-    def staged(dst, src):
-        return [(dst[a:b], src[16 * a:16 * b, :]) for a, b in ((0, rank), (rank + 1, N)) if b > a]
-    dma("a", staged(T.sf, T.fo), "~a", "sf", lat=3500.0, t0=250.0)
-    dma("s", staged(T.sx, T.tx), "", "sx", lat=3500.0, t0=4200.0)
+    dma("a", [(T.s0[:, 64 * h:64 * h + 64, :], T.nm[4 * h:4 * h + 4, :]) for h in range(2)] + [(T.CP[:, 192:384], T.pl[:])], "", "s0 CPp ~a")
+    dma("a", [(T.sx[k], T.tx[:, V // 4 * k:V // 4 * k + V // 4]) for k in range(4)], "~a", "sx", lat=3500.0, t0=250.0)
+    dma("s", [(T.F[:], T.fo[:])], "", "F", lat=3500.0, t0=5500.0)
 
     col = lambda j: T.CC[:, j:j + 1]
-    ms(T.ZER[:], 0.0, "ZER", 272, 0.5)
+    ms(T.ZER[:], 0.0, "ZER", 720, 0.5)
     ms(T.W[:, 0:V], 0.0, "Wd Wc Wb Wf Wo", V, 0.5)
     ms(T.W[:, V:FREE], 255.0, "Wt", 16)
     ms(T.W[:, FREE:FREE + 16], 64.0, "Wu", 16)
-    ms(T.YP[:], -8192.0, "YP", 192)
+    ms(T.YP[:], 0.0, "YP", 192)
     diag((("Y1", 1.0), ("YR", 192.0)))
     iota(T.IOT[:], [[1, 512]], 0, 0, "", "IOT", 512)
-    send("0", LATE["0"], " Y1 YR IOT", 2500.0)
-    send("f", LATE["f"])
-    send("x", LATE["x"])
-    gate[0] = " mf"
+    iota(T.RHO[:, 0:512], [[1, 32], [192, 16]], 8192, 0, "", "RHO0", 512)
+    send("0", "s0 Y1 YR IOT", 2500.0)
+    send("x", "sx")
+    ts(T.IA[:, 0:192], T.CP[:, 0:192], 15, None, A.bitwise_and, None, "CPc", "IA0", 192)
+    ts(T.IA[:, 192:384], T.CP[:, 0:192], 4, None, A.logical_shift_right, None, "CPc", "IA1", 192)
+    cp(T.KA[:, 0:384], T.IA[:, 0:384], "IA0 IA1", "KAc", 384)
+    send("c", "KAc", also="mx")
     iota(T.DU3[:], [[0, 6], [16, 32]], V, 1, "", "DU3", 192)
     gate[0] = " mx"
     iota(T.DU2[:], [[-int(192 * HALF), 2], [16, 16]], BIG - TAB, 1, "", "DU2", 32)
-    diag((("Y2", 2.0), ("YE", 262144.0), ("YM", -2.0), ("YH", -0.5), ("YN", -1.0), ("YS", 1.0 / 16)))
+    diag((("YE", 262144.0), ("YH", -0.5), ("YN", -1.0), ("YS", 1.0 / 16)))
+    sel(T.YF[:], T.YP[:, 0:128], [[1, 128]], A.not_equal, 1.0, 0, -1, "YP", "YF", 128)
     nms = ((CH_HI, 1), (CH_LO, 1), (CH_C, -1), (CH_C + 1, -1))
-    for j, h in enumerate((0, 2, 4, 5)):
-        c = T.FV[:, 512 * j:512 * j + 512]
-        if j: lin(c, T.IOT[:], 1.0, 4096.0 + 512 * h, "IOT", "FV%d" % j, 512)
+    for h in [x for x in range(6) if x not in VCH[0]]:
+        c = T.FV[:, 512 * h:512 * h + 512]
+        if h: lin(c, T.IOT[:], 1.0, 4096.0 + 512 * h, "IOT", "FV%d" % h, 512)
         else:
             act(c, T.IOT[:], AF.Silu, "IOT", "FV0", 512, bias=4096.0)
             ops[-1]["c"] += 1300.0
-    for M, wts in (("MA", ((CH_K, 192), (CH_A, 1))), ("MN", nms), ("MP", ((CH_OK, 192), (CH_OA, 1))),
+    for h in range(2): act(T.MM[:, 720 * h:720 * h + 720], T.ZER[:], AF.Copy, "ZER", " ".join(STRIPS[5 * h:5 * h + 5]), 720)
+    for M, wts in (("MA", ((CH_J, 192), (CH_J + 1, 1))), ("MN", nms), ("MP", ((CH_OK, 192), (CH_OA, 1))),
                    ("MF", ((CH_FR, -BIG), (CH_E, BIG // 2), (CH_D, BIG // 2), (CH_D + 1, BIG // 2), (CH_Y, 3 * BIG // 2))), ("MX", ((CH_K, 1), (CH_A, 16))),
-                   ("MR", ((CH_HI, 1.0 / 16), (CH_LO, 192), (CH_C, -1.0 / 16), (CH_C + 1, -192))), ("ME", 8192), ("MU", 1), ("MS", None)):
-        o = 272 * STRIPS.index(M)
-        gate[0] = " mf" if M == "MA" else " mx"
-        act(T.MM[:, o:o + 272], T.ZER[:], AF.Copy, "ZER", M, 272)
-        ops[-1]["t0"] = 350.0
-        c = T.MM[:, o + 15:o + 271:16]
-        if M == "MS": iota(c, [[0, 2], [-V, 8]], -4096, 192, M, M, 16)
-        elif M in ("ME", "MU"): iota(c, [[0, 16]], wts, 0, M, M, 16)
-        if M in ("ME", "MU", "MS"): inslot(c, M, 2)
-        else: picks(c, wts, M, 2)
+                   ("MR", ((CH_HI, 1.0 / 16), (CH_LO, 192), (CH_C, -1.0 / 16), (CH_C + 1, -192))),
+                   ("ME", 8192), ("MU", 1), ("MV", 1), ("MS", None)):
+        o = 144 * STRIPS.index(M)
+        gate[0] = "" if M == "MP" else " mx"
+        c = T.MM[:, o + 15:o + 143:16]
+        if M == "MS": iota(c, [[-V, 8]], -4096, 192, M, M, 8)
+        elif M in ("ME", "MU", "MV"): iota(c, [[0, 8]], wts, 0, M, M, 8)
+        if M in ("ME", "MU", "MV", "MS"): inslot(c, M, 1, 1, 11 if M == "MV" else 15)
+        else: picks(c, wts, M)
     for j, wts in enumerate((((CH_E, 8),), ((CH_FR, 8), (CH_Y, 8), (CH_D, -1), (CH_D + 1, -1)))):
         c = T.CT[:, 8 * j:8 * j + 8]
         iota(c, [[0, 8]], 0, 0, "", "CT%d" % j, 8)
         picks(c, wts, "CT%d" % j)
         red(col(2 + j), c, A.add, "CT%d" % j, "c%d" % (2 + j), 8)
-    iota(T.PK[:, 0:1], [[0, 1]], 0, 1, "", "PI", 1, False)
-    ts(T.PK[:, 1:2], T.PK[:, 0:1], 15, None, A.bitwise_and, None, "PI", "PK", 1)
-    cp(col(0), T.PK[:, 1:2], "PK", "c0", 1)
-    cK = col(0)
+    iota(T.VK[:, 0:384], [[SAME // 192, 2], [0, 192]], 0, 1, "", "VK", 384)
+    iota(T.VK[:, 384:400], [[16, 16]], 0, 1, "", "VJ", 16)
+    dma("s", [(T.VK[slot(q), 0:400], T.VK[slot(0), 0:400]) for q in range(1, N)], "VK VJ", "VK")
+    iota(T.VK[:, 400:592], [[1, 192]], 0, 0, "", "VA", 192)
+    cK = T.VK[:, 0:1]
     iota(T.SG[:], [[0, 128]], 1, 0, "", "SG", 128)
     inslot(T.SG[:], "SG", 1, 16)
     sel(T.TRI[:], T.SG[:], [[1, 128]], A.is_gt, 0.0, 0, -1, "SG", "TRI", 128)
     sel(T.TRI[:], T.TRI[:], [[1, 128]], A.not_equal, 512.0, 0, -1, "TRI", "TRI", 128)
-    for M in ("BCN", "TWO", "POW", "DO", "DZ", "DX", "DL", "BCV"): iota(T[M][:], [[0, 128]], 0, 0, "", M, 128)
-    picks(T.BCN[:], nms, "BCN", 1, 16)
+    for l in (("TWO", "POW", "DO", "DZ"), ("DX", "DL", "BCV")): dma("s", [(T[M][:], T.ZER[:, 0:128]) for M in l], "ZER F", " ".join(l))
+    o = 144 * STRIPS.index("MN")
+    red(col(4), T.MM[:, o + 15:o + 143:16], A.add, "MN", "c4", 8)
+    lin(T.BCN[:], T.SG[:], col(4), 0.0, "SG c4", "BCN", 128, 0.5)
     iota(T.TWO[:, CH_E:128:16], [[0, 8]], 2, 0, "TWO", "TWO", 8)
     inslot(T.TWO[:, CH_E:128:16], "TWO")
-    o = 272 * STRIPS.index("MN")
+    o = 144 * STRIPS.index("MN")
     for M, h in (("DO", 0), ("DZ", 1)):
         sel(T[M][:, CH_D + h:128:16], T.MM[:, o + 15:o + 143:16], [[0, 8]], A.is_ge, 0.0, 0, 0, "MN " + M, M, 8)
         if M == "DO": picks(T.DO[:, CH_D:128:16], ((CH_FR, 8192),), M)
@@ -597,35 +601,31 @@ def build(g, core, rank, T, topo, via, vib):
     picks(T.BCV[:, 0:128:16], ((CH_OK, 1), (CH_OA, 16)), "BCV")
     ms(T.TM2[:, 16:32], 0.5, "PW", 16)
     op("v", cyc(16), "PW ZER", "PV", lambda q: q.tensor_tensor_scan(T.TM2[:, 48:64], T.TM2[:, 16:32], T.ZER[:, 0:16], 2.0, A.mult, A.add))
-    ts(T.TM2[:, 0:16], T.IOT[:, 0:16], cK, None, A.is_equal, None, "IOT c0", "OH", 16)
+    ts(T.TM2[:, 0:16], T.IOT[:, 0:16], cK, None, A.is_equal, None, "IOT VK", "OH", 16)
     tt(T.TM2[:, 32:48], T.TM2[:, 48:64], T.TM2[:, 0:16], A.mult, "PV OH", "PW2", 16)
     red(col(1), T.TM2[:, 32:48], A.max, "PW2", "c1", 16)
     lin(T.POW[:, CH_E:128:16], T.TWO[:, CH_E:128:16], col(1), 0.0, "TWO POW c1", "POW", 8)
     lin(T.THR[:, 0:16], T.TM2[:, 48:64], col(2), col(3), "PV c2 c3", "THR", 16)
     for n in (16, 32, 64, 128): sel(T.THR[:, n:2 * n], T.THR[:, 0:n], [[0, n]], A.is_ge, 0.0, 0, 0, "THR", "THR", n)
-    iota(T.JB[:], [[16, 256]], -4096, 0, "", "JB", 256)
-    iota(T.JF[:], [[1, 256]], -256, 0, "", "JF", 256)
-    iota(T.TAU[:], [[1, 256]], 256, 0, "", "TAU", 256)
-    lin(T.VK[:, 0:192], T.IOT[:, 0:192], 0.0, cK, "IOT c0", "VK", 192)
-    lin(T.VK[:, 384:576], T.VK[:, 0:192], 1.0, float(SAME // 192), "VK", "VL", 192, 0.5)
-    iota(T.VK[:, 192:384], [[1, 192]], 0, 0, "", "VA", 192)
+    iota(T.JB[:], [[16, 256]], 0, 0, "", "JB", 256)
+    iota(T.JF[:], [[-1, 256]], 0, 0, "", "JF", 256)
+    iota(T.TAU[:], [[-1, 256]], -512, 0, "", "TAU", 256)
+    iota(T.SN[:], [[0, 128]], -1, 0, "", "SN", 128)
+    inslot(T.SN[:], "SN", 1, 16)
     for t in range(1, TV + 1):
-        c = T.SH[:, 256 * t - 256:256 * t - 128]
-        sel(c, T.SG[:], [[16, 8], [0, 16]], A.is_gt, 0.0, S * t % 16, -1, "SG", "SH%d" % t, 128)
-        lin(T.SH[:, 256 * t - 128:256 * t], c, -1.0, 0.0, "SH%d" % t, "SH%d" % t, 128, 0.5)
-    iota(T.BC[:, 192:210], [[0, 18]], 0, 0, "", "BCb", 18)
-    iota(T.BC[:, 0:1], [[0, 1]], -256, 0, "", "BCa", 1)
+        for h, M in enumerate(("SG", "SN")):
+            sel(T.SH[:, 256 * t - 256 + 128 * h:256 * t - 128 + 128 * h], T[M][:], [[16, 8], [0, 16]], A.is_gt, 0.0, S * t % 16, -1, M, "SH%d%d" % (t, h), 128)
+        sel(T.SA[:, 128 * t - 128:128 * t], T.SG[:], [[0, 8], [16, 16]], A.is_ge, 0.0, 14 - S * t % V // 16, 0, "SG", "SA%d" % t, 128)
+    iota(T.U[:, UB + 194:UB + 215], [[0, 21]], 256, 0, "", "Ue", 21)
     iota(T.BS[:], [[0, 16]], 0, 0, "", "BS", 16)
     iota(T.CU[:, 192:200], [[0, 8]], 0, 0, "", "CU", 8)
     iota(T.PG[:, TAB + V:TAB + V + 16], [[0, 16]], 0, 0, "", "Tt", 16)
-    for j in range(NA): iota(T.RHO[:, 512 * j:512 * j + 512], [[1, 32], [192, 16]], 8192 + 32 * j, 0, "", "RHO%d" % j, 512)
+    for j in range(1, NA): iota(T.RHO[:, 512 * j:512 * j + 512], [[1, 32], [192, 16]], 8192 + 32 * j, 0, "", "RHO%d" % j, 512)
 
-    ts(T.IA[:, 0:192], T.CP[:, 0:192], 15, None, A.bitwise_and, None, "CPc", "IA0", 192)
-    ts(T.IA[:, 192:384], T.CP[:, 0:192], 4, None, A.logical_shift_right, None, "CPc", "IA1", 192)
-    cp(T.KA[:, 0:384], T.IA[:, 0:384], "IA0 IA1", "KAc", 384)
-    dma("s", rows(CH_K, T.KA[:, 0:192]) + rows(CH_A, T.KA[:, 192:384]), "KAc", "Wb")
+    dma("s", rows(CH_OK, T.KA[:, 0:192]) + rows(CH_OA, T.KA[:, 192:384]), "KAc", "Wo")
+    dma("s", [(T.LZ[0:128:16, 0:V], T.YP[:])], "YP", "LZ")
     dma("s", [(T.LW[0:128:16, 0:V], T.YP[:]), (T.LX[0:128:16, 0:V], T.YP[:])], "YP KAc", "LW LX")
-    dma("s", [(T.LY[0:128:16, 0:V], T.YP[:]), (T.LZ[0:128:16, 0:V], T.YP[:])], "YP sx", "LY LZ")
+    dma("s", [(T.LY[0:128:16, 0:V], T.YP[:])], "YP KAc", "LY")
     ts(T.IA[:, 384:576], T.CP[:, 192:384], 15, None, A.bitwise_and, None, "CPp", "IA2", 192)
     ts(T.IA[:, 576:768], T.CP[:, 192:384], 4, None, A.logical_shift_right, None, "CPp", "IA3", 192)
     cp(T.KA[:, 384:768], T.IA[:, 384:768], "IA2 IA3", "KAp", 384)
@@ -634,7 +634,6 @@ def build(g, core, rank, T, topo, via, vib):
         mm([(P[3 + h][:, c], T.YR[:], T.KA[:, 384 * h:384 * h + 192], 192),
             (P[3 + h][:, c], T.Y1[:], T.KA[:, 384 * h + 192:384 * h + 384], 192)], "YR Y1 " + ("KAc", "KAp")[h], "P%d" % (3 + h))
         ts(T.RP[:, c], P[3 + h][:, c], float(FREE), None, A.min, None, "P%d" % (3 + h), ("RP", "PU")[h], 192)
-    dma("s", [(T.F[slot(rank + 1), 0:V], T.fo[own, :]), (T.X[own, :], T.tx[own, :])], "sx", "F%d X%d" % (rank, rank), t0=9000.0)
 
     Wt, WA = T.W[:, 0:FREE + 16], "Wd Wc Wb Wf Wo Wt Wu "
     Tall = " T0 T1 T2 T3 T4 T5 Tt "
@@ -644,185 +643,202 @@ def build(g, core, rank, T, topo, via, vib):
     for j in range(3):
         c = slice(64 * j, 64 * j + 64)
         b = 5 + j % 2
-        mm(ext16(P[b][:, c], "MA", T.PG, TAB + 1024 * j, 64), "T%d T%d MA" % (2 * j, 2 * j + 1), "P%d" % b)
-        tt(T.FC[:, c], P[b][:, c], T.DU3[:, c], A.min, "P%d DU3" % b, "FC%d" % j, 64, 1.0)
-        cp(T.LO[:, c], T.FC[:, c], "FC%d" % j, "LO%d" % j, 64)
-    for j in range(3):
-        h = 2 * j + 1
-        ts(T.LW[:].indirect(T.LO[:, 32 * h:32 * h + 32]), T.IOT[:], 1.0, 4096.0 + 512 * h, A.mult, A.add, "IOT LO%d" % j, "LW", 512, 3.8)
-        h = 2 * j
-        act(T.LX[:].indirect(T.LO[:, 32 * h:32 * h + 32]), T.FV[:, 512 * j:512 * j + 512], AF.Silu, "FV%d LO%d" % (j, j), "LX", 512, 3.8)
-    g0 = slice(16 * rank, 16 * rank + 1)
-    dma("a", [(T.s2[:, 0:64, :], T.LW[0:128:16, 0:V]), (T.s2[:, 64:128, :], T.LX[0:128:16, 0:V]),
-              (T.r2[rank, 0:64, :], T.LW[g0, 0:V]), (T.r2[rank, 64:128, :], T.LX[g0, 0:V])], "LW LX", "s2 r2")
-    send("2", LATE["2"])
-    dma("s", [(T.s4[:, 32 * k:32 * k + 32, :], T.PG[ch:128:16, TAB:TAB + V]) for k, ch in enumerate((CH_K, CH_A))]
-        + [(T.s4[:, 64 + 32 * k:96 + 32 * k, :], T.KA[:, 192 * k:192 * k + 192]) for k in range(2)], Tall + "KAc LO2", "s4")
-    dma("s", [(T.r4[rank], T.s4[rank]), (T.rf[rank], T.fo[own, :])], "s4", "r4")
-    send("4", LATE["4"])
+        mm(ext16(P[b][:, c], "MP", T.PG, TAB + 1024 * j, 64), "T%d T%d MP" % (2 * j, 2 * j + 1), "P%d" % b)
+        tt(T.RF[:, c], P[b][:, c], T.DU3[:, c], A.min, "P%d DU3" % b, "FC%d" % j, 64, 1.0)
+        cp(T.LO[:, c], T.RF[:, c], "FC%d" % j, "LO%d" % j, 64)
+    for h in range(6):
+        if h in VCH[0]: ts(T.LW[:].indirect(T.LO[:, 32 * h:32 * h + 32]), T.IOT[:], 1.0, 4096.0 + 512 * h, A.mult, A.add, "IOT LO%d" % (h // 2), "LW", 512, 3.8)
+        else: act(T.LX[:].indirect(T.LO[:, 32 * h:32 * h + 32]), T.FV[:, 512 * h:512 * h + 512], AF.Silu, "FV%d LO%d" % (h, h // 2), "LX", 512, 3.8)
+
+    def join(out, dst, a, b, lo, w, bank):
+        dma("s", [(dst[:, 192 * h:192 * h + 192], T[x][0:128:16, lo:lo + V]) for h, x in enumerate((a, b))], a + " " + b, w)
+        mm([(out, T.YF[:], dst[:, 192 * h:192 * h + 192], 4 * 192) for h in range(2)], w + " YF", bank)
+    send("y", "F")
+    join(P[4][:, 192:384], T.FA, "LW", "LX", 0, "FA", "P4")
+    ops[-2]["r"].append("my")
+    ts(T.LU[:], P[4][:, 192:384], -4095.75, 0.0, A.add, A.max, "P4", "LU0 LU1 LU2", 192)
+    act(T.MK[:], P[4][:, 192:384], AF.Relu, "P4", "MK", 192, scale=-256.0, bias=float(BIG))
+    ts(P[4][:, 0:192], T.LU[:], -HALF, None, A.add, None, "LU0 LU1 LU2", "P4", 192)
     for j in range(6):
         if j < NA: act(T.LZ[:].indirect(T.RP[:, 32 * j:32 * j + 32]), T.RHO[:, 512 * j:512 * j + 512], AF.Silu, "RHO%d RP" % j, "LZ", 512, 3.8)
         else: ts(T.LY[:, 0:V].indirect(T.RP[:, 32 * j:32 * j + 32]), T.RHO[:, 0:512], 1.0, 32.0 * j, A.mult, A.add, "RHO0 RP", "LY", 512, 3.8)
-    dma("a", [(T.s3[:, 0:64, :], T.LY[0:128:16, 0:V]), (T.s3[:, 64:128, :], T.LZ[0:128:16, 0:V]),
-              (T.r3[rank, 0:64, :], T.LY[g0, 0:V]), (T.r3[rank, 64:128, :], T.LZ[g0, 0:V])], "LY LZ", "s3 r3")
-    send("3", LATE["3"])
-    iota(T.PG[:, 3584 + TAB:3584 + TAB + V + 16], [[0, V + 16]], 0, 0, "m3", "U0", V + 16)
-    iota(T.W[:, FREE + 16:NONE + 16], [[0, NONE - FREE]], 64, 0, "m3", "Wi", NONE - FREE)
-    dma("s", rows(CH_K, T.VK[:, 0:192], SAME) + rows(CH_A, T.VK[:, 192:384], SAME), "VK VA", "Wi")
-    for M, x in (("LW", -1), ("LX", 0)): iota(T[M][:, TAB:TAB + V], [[0, V]], x, 0, "m3", M, V)
+    join(P[2][:, 192:384], T.ICF, "LY", "LZ", 0, "ICF", "P2")
+    ts(T.ICU[:, 0:192], P[2][:, 192:384], -8191.75, None, A.add, None, "P2", "ICU", 192)
+    send("i", "ICU")
 
-    dma("s", [(T.CP[:, 384:576], T.r0[:])], "r0 m0", "CPn", ext=[("a0", short_all)])
-    cp(T.NH[:, 0:192], T.CP[:, 384:576], "CPn", "NH0", 192)
-    tt(T.NH[:, 192:384], T.CP[:, 384:576], T.NH[:, 0:192], A.subtract, "CPn NH0", "NH1", 192)
-    dma("s", rows(CH_HI, T.NH[:, 0:192]) + rows(CH_LO, T.NH[:, 192:384]), "NH0 NH1", "Wd")
-    for s in others:
-        dma("s", [(T.F[slot(s + 1), 0:V], T.rf[s])], "mf NH1 s4 ~s", "F%d ~s" % s, ext=[("af%d" % s, arrivals(via, s, True))])
-    for s in others:
-        dma("s", [(T.X[slot(s), :], T.rx[s])], "mx ~s", "X%d ~s" % s, ext=[("ax%d" % s, arrivals(via, s, True))])
-    Fall = " ".join("F%d" % s for s in range(N)) + " "
-    Xall = " ".join("X%d" % s for s in range(N)) + " "
-    mm(ext16(P[3][:, 0:192], "MN", T.W, 0, 192), "Wd Wc Wb Wf Wo MN", "P3")
-    ts(T.NU[:], P[3][:, 0:192], 0.0, None, A.add, None, "P3", "NU", 192)
-    lin(T.NF[:], P[3][:, 0:192], 1.0, -HALF, "P3", "NF", 192)
-    parts2(0, T.NF[:], "NF", 2.0)
-    dma("s", [x for k, ch in enumerate((CH_OK, CH_OA))
-              for x in onward(lambda a, b: T.PG[16 * a + ch:16 * b:16, TAB:TAB + V], lambda a, b: T.r4[a:b, 32 * k:32 * k + 32, :])]
-        + rows(CH_K, T.r4[:, 64:96, :]) + rows(CH_A, T.r4[:, 96:128, :]) + rows(CH_OK, T.VK[:, 0:192]) + rows(CH_OA, T.VK[:, 192:384]),
-        Xall + "r4 m4 m2 VK VA", Tall + "Wb Wo", ext=[("a4", short_all)])
-    dma("s", [(T.FA[p, 192 * h:192 * h + 192], T.r2[r, 64 * h:64 * h + 64, :]) for h in range(2) for p, r in ((slice(16, 128), slice(0, 7)), (slice(0, 16), 7))],
-        "r2 m2", "FA", ext=[("a2", short_all)])
-    tt(T.NI[:], T.FA[:, 0:192], T.FA[:, 192:384], A.max, "FA", "NI", 192)
-    ts(T.LU[:], T.NI[:], -4096.0, 0.0, A.add, A.max, "NI", "LU0 LU1 LU2", 192)
-    ts(P[4][:, 0:192], T.NI[:], -4096.0 - HALF, -HALF, A.add, A.max, "NI", "P4", 192)
-    act(T.EM[:], T.FA[:], AF.Sign, "FA", "EM", 384)
-    dma("s", [(T.ICF[:, 192 * h:192 * h + 192], T.r3[:, 64 * h:64 * h + 64, :]) for h in range(2)], "r3 m3", "ICF", ext=[("a3", short_all)])
-    tt(T.ICF[:, 0:192], T.ICF[:, 0:192], T.ICF[:, 192:384], A.max, "ICF", "ICF", 192)
-    ts(T.ICU[:], T.ICF[:, 0:192], -8191.75, None, A.add, None, "ICF", "ICU", 192)
+    op("v", 3 * cyc(64), "a0", "NH", lambda q: [q.tensor_scalar(T.NH[:, 64 * j:64 * j + 64], T.N0[:, :, 16 * j:16 * j + 16], -HALF, None, A.add) for j in range(3)])
+    for h in range(2):
+        c = slice(64 * h, 64 * h + 64)
+        for j in range(3): mm([(P[3][c, j:192:3], T.NH[c, 64 * j:64 * j + 64], T.YF[c, c], 4 * 64)], "NH YF", "P3")
+    ts(T.NU[:], P[3][:, 0:192], HALF, None, A.add, None, "P3", "NU0 NU1", 192)
+    scl(T.NF[:], P[3][:, 0:192], 1.0, "P3", "NF0 NF1", 192)
+    parts2(T.HN[:, 0:192], T.HN[:, 192:384], 0, P[3][:, 0:192], "P3", 1.0)
+
+    def pair(ch, src, o=0):
+        return rows(ch, src[0], o) + rows(ch + 1, src[1], o)
+    own = (T.VK[:, 0:192], T.VK[:, 400:592])
+    con = lambda t: (T.KC[:, 384 * t - 384:384 * t - 192], T.KC[:, 384 * t - 192:384 * t])
 
     for t in range(1, TV + 1):
         s0 = S * t % V
         cs = s0 // 16
         last = t == TV
-        Ft = T.F[:, V * t - V:V * t]
-        if t > 1: Fall = "Ft%d " % t
-        b0, b1 = (t - 1) % 2, t % 2
-        HI, LO, CH, CL = T.HL[:, 384 * b1:384 * b1 + 192], T.HL[:, 384 * b1 + 192:384 * b1 + 384], T.CD[:, 0:192], T.CD[:, 192:384]
-        now = "HI%d LO%d " % (b1, b1 + 4)
+        HI, LO, CH, CL = [T.HL[:, 768 * t - 768 + 192 * k:768 * t - 576 + 192 * k] for k in range(4)]
+        name = [T.HN[:, 768 * t - 768 + 192 * k:768 * t - 576 + 192 * k] for k in range(4)]
+        cut = lambda M, k, a, b, j=None: T[M][:, slice(768 * t - 768 + 192 * k + a + (j or 0), 768 * t - 768 + 192 * k + b, None if j is None else 3)]
+        now, was = "HI%d LO%d " % (t, t + 4), ["av%d " % (t - 1), "av%d aw%d " % (t - 1, t - 1)] if t > 1 else ["HI0 LO4 "] * 2
+        if t == 1: dma("s", pair(CH_K, con(1)) + pair(CH_J, con(1)) + pair(CH_OK, own), "ac1 VK VA", "Wb Wo")
+        elif t == 2: dma("s", pair(CH_K, con(2)) + rows(CH_OK, T.VK[:, 192:384]), "ac2 VK", "Wb Wo")
+        elif t == 3: dma("s", pair(CH_K, con(3)) + pair(CH_OK, con(2)), "ac2 ac3", "Wb Wo")
+        else:
+            dma("s", pair(CH_OK, own) + pair(CH_HI, name[0:2]) + pair(CH_C, name[2:4]), "VK VA " + was[1], "Wo Wd Wc")
+        if t == 2:
+            for o in range(FREE + 16, NONE + 16, 464): iota(T.W[:, o:o + 464], [[0, 464]], 64, 0, "mb1", "Wi", 464)
+            dma("g", pair(CH_J, own, SAME), "VK VA", "Wi")
+            ops[-1]["c"] = 2000.0
+            for h in [x for x in VCH[0] if x not in VCH[1]]: iota(T.FV[:, 512 * h:512 * h + 512], [[1, 512]], 4096 + 512 * h, 0, "mb1", "FV%d" % h, 512)
+        if t == 3:
+            for M, x in (("LW", 0), ("LX", 4095)):
+                for o in range(TAB, TAB + V, 512): iota(T[M][:, o:o + 512], [[0, 512]], x, 0, "mb2", M, 512)
+        if t > 1:
+            for p, (a, b) in enumerate(PARTS):
+                mm([(P[2][:, a:b], y[:], cut("HN", k, a, b), b - a) for k, y in enumerate((T.Y1, T.Y1, T.YN, T.YN))], "Y1 YN " + was[p], "P2")
+                ts(T.NU[:, a:b], P[2][:, a:b], HALF, None, A.add, None, "P2", "NU%d" % p, b - a)
+                scl(T.NF[:, a:b], P[2][:, a:b], 1.0, "P2", "NF%d" % p, b - a)
+        part = lambda j: int(32 * j >= PARTS[1][0])
+        by = lambda x, j: (T.F[:].indirect(T[x][:, 32 * j:32 * j + 32]), "F %s%d" % (x, part(j) if x == "NU" else j // 2))
+        role = lambda j: ("NU", "LU", -1.0) if t == 1 else ("LU", "NU", 1.0)
         for j in range(6):
-            gat("a", T.G2[:, 512 * j:512 * j + 512], Ft.indirect(T.NU[:, 32 * j:32 * j + 32]), Fall + "NU", "G%d" % j, 512)
+            one = role(j)[0]
+            gat("a", T.G2[:, 512 * j:512 * j + 512], by(one, j)[0], by(one, j)[1], "G%d" % j, 512)
+        parts2(HI, LO, t, P[4][:, 0:192], "P4", 1.0)
         if not last:
-            dma("s", [(T.F[16 * t + 16:128, V * t:V * t + V], T.rf[0:7 - t]), (T.F[0:16 * t + 16, V * t:V * t + V], T.rf[7 - t:8])],
-                Fall + Xall + ("FA r4" if t == 1 else "G5"), "Ft%d" % (t + 1), lat=3500.0)
-        tt(T.EQ[:], P[4][:, 0:192], T.NF[:], A.is_equal, "P4 NF", "EQ", 192, 1.0)
-        parts2(b1, P[4][:, 0:192], "P4", 1.0)
-        if not last: dma("s", rows(CH_HI, HI) + rows(CH_LO, LO), now, "Wd")
-        for h in (0, 1):
-            o = P[4][:, 192 - 192 * h:384 - 192 * h]
-            mm([(o, T.Y1[:], (HI, LO)[h], 192), (o, T.YN[:], T.HL[:, 384 * b0 + 192 * h:384 * b0 + 192 * h + 192], 192)]
-               + ([(o, T.Y1[:], (CH, CL)[h], 192)] if t > 1 else []), "YN HI0 HI1 LO4 LO5 Y1 CH CL", "P4")
-        parts = [(ext16(P[2][:, 64 * h:64 * h + 64], "ME", T.NE, 1024 * h, 64), "ME NE%d NE%d" % (2 * h, 2 * h + 1)) for h in range(3)]
-        if t > 1: parts += [(ext16(P[2][:, 64 * h:64 * h + 64], "MF", T.TR, 1024 * h, 64, 1), "MF" + TRall) for h in range(3)]
-        else: parts.append(([(P[2][:, 0:192], T.YE[:], T.EM[:, 192 * h:192 * h + 192], 192) for h in (0, 1)], "YE EM"))
-        parts = group(2, 192, parts, (T.YE[:], T.EQ[:], "YE EQ"))
+            dma("s", pair(CH_HI, (HI, LO)), now, "Wd")
+            send("a%d" % t, now)
+        for p, (a, b) in enumerate(PARTS):
+            tt(T.EQ[:, a:b], P[4][:, a:b], T.NF[:, a:b], A.is_equal, "P4 NF%d" % p, "EQ%d" % p, b - a, 1.0)
+            for h in (0, 1):
+                mm([(P[4][:, 192 - 192 * h + a:192 - 192 * h + b], y[:], cut(M, k + h, a, b), b - a)
+                    for M, k, y in (("HL", 0, T.Y1), ("HN", 0, T.YN), ("HN", 2, T.Y1))[:3 if t > 1 else 2]], "YN Y1 " + now + was[p], "P4")
         for j in range(6):
             c = slice(512 * j, 512 * j + 512)
             b = BANK[t - 1][j]
+            one, two, sgn = role(j)
+            if j in SIZE[t - 1]:
+                gat("a", T.PR[:, c], by(two, j)[0], by(two, j)[1], "PR%d" % j, 512)
+                for y in ("G2", "PR"):
+                    mm([(P[b][:], T.YN[:], T.X[:, V * t - V + 512 * j:V * t - V + 512 * j + 512], 512)], "ax%d YN" % t, "P%d" % b, True, False)
+                    mm([(P[b][:], T.Y1[:], T[y][:, c], 512)], "Y1 %s%d" % (y.strip("2"), j), "P%d" % b, False, True)
+                    act(T["D" if y == "G2" else y][:, c], P[b][:], AF.Abs, "P%d" % b, "%s%d" % ("D" if y == "G2" else y, j), 512)
+                mm([(P[b][:], T.YN[:], T.D[:, c], 512)], "YN D%d" % j, "P%d" % b, True, False)
+                mm([(P[b][:], T.Y1[:], T.PR[:, c], 512)], "Y1 PR%d" % j, "P%d" % b, False, True)
+                ts(T.NE[:, c], P[b][:], 0.0, 0.5, A.is_lt if sgn < 0 else A.is_gt, A.subtract, "P%d" % b, "NE%d" % j, 512)
+                act(T.NE[:, c], P[b][:], AF.Sign, "P%d" % b, "NE%d" % j, 512, bias=-0.5, scale=sgn)
+                either("a")
+                continue
             if j in SIGN[t - 1]:
-                act(T.PR[:, c], Ft.indirect(T.LU[:, 32 * j:32 * j + 32]), AF.Copy, Fall + "LU%d" % (j // 2), "PR%d" % j, 512, 1.56)
+                act(T.PR[:, c], by(two, j)[0], AF.Copy, by(two, j)[1], "PR%d" % j, 512, 1.56)
                 mm([(P[b][:], T.YN[:], T.G2[:, c], 512)], "YN G%d" % j, "P%d" % b, True, False)
                 mm([(P[b][:], T.Y1[:], T.PR[:, c], 512)], "Y1 PR%d" % j, "P%d" % b, False, True)
                 act(T.D[:, c], P[b][:], AF.Sign, "P%d" % b, "D%d" % j, 512)
             else:
-                tt(T.D[:, c], Ft.indirect(T.LU[:, 32 * j:32 * j + 32]), T.G2[:, c], A.subtract, Fall + "LU%d G%d" % (j // 2, j), "D%d" % j, 512, 1.56)
-            x, a = ([(P[b][:], T.YM[:], T.X[:, c], 512)], Xall + "YM"), ([(P[b][:], T.Y1[:], T.D[:, c], 512)], "Y1 D%d" % j)
-            n = ([(P[b][:], T.Y2[:], T.G2[:, c], 512)], "Y2 G%d" % j)
-            if j in SIGN[t - 1]:
-                mm([(P[b][:], T.Y1[:], y[:, c], 512) for y in (T.G2, T.PR)] + x[0], "Y2 G%d Y1 PR%d " % (j, j) + x[1], "P%d" % b)
-            elif t == 1:
+                tt(T.D[:, c], by(two, j)[0], T.G2[:, c], A.subtract, by(two, j)[1] + " G%d" % j, "D%d" % j, 512, 1.56)
+            x = ([(P[b][:], T.Y1[:], T.X[:, V * t - V + 512 * j:V * t - V + 512 * j + 512], 512)], "ax%d Y1" % t)
+            a = ([(P[b][:], T.YH[:], T.D[:, c], 512)], "D%d YH" % j)
+            n = ([(P[b][:], T.YN[:], T.G2[:, c], 512)], "G%d YN" % j)
+            if j in SIGN[t - 1]: n, a = [([(P[b][:], T.YH[:], T[y][:, c], 512)], "%s%d YH" % (y.strip("2"), j)) for y in ("G2", "PR")]
+            if t == 1 and j not in SIGN[0]:
                 for y in group(b, 512, [x, a], n[0][0][1:3] + (n[1],)): y()
             else:
-                mm(x[0] + n[0], n[1] + " " + x[1], "P%d" % b, True, False)
+                mm(x[0], x[1], "P%d" % b, True, False)
+                mm(n[0], n[1], "P%d" % b, False, False)
                 mm(a[0], a[1], "P%d" % b, False, True)
             tt(T.PR[:, c], P[b][:], T.D[:, c], A.mult, "P%d D%d " % (b, j), "PR%d A%d" % (j, b), 512, 1.0)
-            ts(T.NE[:, c], T.PR[:, c], 0.0, 0.5, A.is_lt, A.subtract, "PR%d" % j, "NE%d" % j, 512, 0.5)
-            act(T.NE[:, c], T.PR[:, c], AF.Sign, "PR%d" % j, "NE%d" % j, 512, bias=-0.5, scale=-1.0)
+            ts(T.NE[:, c], T.PR[:, c], 0.0, 0.5, A.is_gt if sgn < 0 else A.is_lt, A.subtract, "PR%d" % j, "NE%d" % j, 512, 0.5)
+            act(T.NE[:, c], T.PR[:, c], AF.Sign, "PR%d" % j, "NE%d" % j, 512, bias=-0.25, scale=-sgn)
             either("a")
-        for x in parts: x()
-        ts(T.FR[:], P[2][:, 0:192], 4096.0, None, A.is_lt, None, "", "FR P2 A2", 192)
-        if not last: dma("s", rows(CH_FR, T.FR[:]) + (rows(CH_OK, T.VK[:, 384:576]) if t == 2 else []), "FR VL", "Wf Wo")
-        tt(CH, P[4][:, 192:384], T.FR[:], A.mult, "P4 FR", "CH", 192, 1.0)
-        tt(CL, P[4][:, 0:192], T.FR[:], A.mult, "P4 FR", "CL", 192, 1.0)
-        four = ((HI, T.Y1), (LO, T.Y1), (CH, T.YN), (CL, T.YN))
+        for p, (a, b) in enumerate(PARTS):
+            hs, k, o = range(a // 64, b // 64), (4, 2)[p], (384, 0)[p]
+            parts = [(ext16(P[k][:, o + 64 * h:o + 64 * h + 64], "ME", T.NE, 1024 * h, 64), "ME NE%d NE%d" % (2 * h, 2 * h + 1)) for h in hs]
+            if t == 1: parts.append(([(P[k][:, o + a:o + b], T.YN[:], T.MK[:, a:b], b - a)], "YN MK"))
+            else: parts += [(ext16(P[k][:, o + 64 * h:o + 64 * h + 64], "MF", T.TR, 1024 * h, 64), "MF" + TRall) for h in hs]
+            for x in group(k, o + b, parts, (T.YE[:], T.EQ[:, a:b], "YE EQ%d" % p), o + a): x()
+            fr = ("FQ", "FR")[p]
+            ts(T.FR[:, a:b], P[k][:, o + a:o + b], 4096.0, None, A.is_lt, None, "", fr + " P%d A%d" % (k, k), b - a)
+            if p and not last: dma("s", rows(CH_FR, T.FR[:]), "FQ FR Wb Wo Wd", "Wf")
+            if last:
+                mm([(P[k][:, o + a:o + b], y[:], x, b - a) for x, y in ((cut("HL", 0, a, b), T.YS), (cut("HL", 1, a, b), T.YR), (T.FR[:, a:b], T.YE))],
+                   "YE YS YR " + now + fr, "P%d" % k)
+                tt(T.RF[:, a:b], P[k][:, o + a:o + b], T.DU3[:, a:b], A.min, "DU3 P%d" % k, "RF%d" % p, b - a, 1.0)
+                ts(T.LO[:, a:b], T.RF[:, a:b], 192 * HALF + TAB, None, A.add, None, "RF%d" % p, " ".join("LO%d" % h for h in hs), b - a)
+            tt(cut("HL", 2, a, b), P[4][:, 192 + a:192 + b], T.FR[:, a:b], A.mult, "P4 " + fr, "CH%d%d" % (t, p), b - a, 1.0)
+            tt(cut("HL", 3, a, b), P[4][:, a:b], T.FR[:, a:b], A.mult, "P4 " + fr, "CL%d%d" % (t, p), b - a, 1.0)
+            if not last: send("eb"[p] + str(t), "CH%d%d CL%d%d" % (t, p, t, p), also="ax%d" % (t + 2) * (p and t + 2 <= TV))
+        new = "CH%d0 CL%d0 CH%d1 CL%d1 " % (t, t, t, t)
         if not last:
-            dma("s", rows(CH_C, CH) + rows(CH_C + 1, CL), "CH CL", "Wc")
-            mm([(P[2][:, 0:192], y[:], x, 192) for x, y in four], "CH CL Y1 YN " + now, "P2")
-            ts(T.NU[:], P[2][:, 0:192], HALF, None, A.add, None, "P2", "NU", 192)
-            scl(T.NF[:], P[2][:, 0:192], 1.0, "P2", "NF", 192)
+            dma("s", pair(CH_C, (CH, CL)), new, "Wc")
             for j in range(3):
                 for h in (2 * j, 2 * j + 1):
-                    gat("a", T.TR[:, 512 * h:512 * h + 512], Wt.indirect(T.ICU[:, 32 * h:32 * h + 32]), WA + "ICU", "TR%d" % h, 512)
-                mm(ext16(P[4][:, 64 * j:64 * j + 64], "MN", T.TR, 1024 * j, 64, 1), "TR%d TR%d MN" % (2 * j, 2 * j + 1), "P4")
+                    o = 192 * t + 32 * h
+                    gat("a", T.TR[:, 512 * h:512 * h + 512], Wt.indirect(T.ICU[:, o:o + 32]), WA + "ai%d" % t, "TR%d" % h, 512)
+                mm(ext16(P[4][:, 64 * j:64 * j + 64], "MN", T.TR, 1024 * j, 64), "TR%d TR%d MN" % (2 * j, 2 * j + 1), "P4")
                 ts(T.LU[:, 64 * j:64 * j + 64], P[4][:, 64 * j:64 * j + 64], HALF, None, A.add, None, "P4", "LU%d" % j, 64)
         else:
-            mm([(P[2][:, 0:192], y[:], x, 192) for x, y in ((HI, T.YS), (LO, T.YR), (T.FR[:], T.YE))], "YE FR YS YR " + now, "P2")
-            tt(T.RF[:], P[2][:, 0:192], T.DU3[:], A.min, "DU3 P2", "RF", 192, 1.0)
-            ts(T.LO[:], T.RF[:], 192 * HALF + TAB, None, A.add, None, "RF", "LO0 LO1 LO2", 192)
-            for j, h in enumerate((0, 2, 4, 5)):
-                act(T.LX[:].indirect(T.LO[:, 32 * h:32 * h + 32]), T.FV[:, 512 * j:512 * j + 512], AF.Silu, "FV%d LO0" % j, "LX", 512, 3.8)
-            for h in [x for x in range(0, 192, VS) if x // 32 in (1, 3)]:
-                ts(T.LW[:].indirect(T.LO[:, h:h + VS]), T.IOT[:, 0:16 * VS], 1.0, 16.0 * h, A.mult, A.add, "IOT LO0", "LW", 16 * VS, 3.8)
+            for h in [x for x in range(6) if x not in VCH[1]]:
+                act(T.LX[:].indirect(T.LO[:, 32 * h:32 * h + 32]), T.FV[:, 512 * h:512 * h + 512], AF.Silu, "FV%d LO%d" % (h, h // 2), "LX", 512, 3.8)
+            for h in [x for x in range(0, 192, VS) if x // 32 in VCH[1]]:
+                ts(T.LW[:].indirect(T.LO[:, h:h + VS]), T.IOT[:, 0:16 * VS], 1.0, 16.0 * h + 1, A.mult, A.add, "IOT LO%d" % (h // 64), "LW", 16 * VS, 3.8)
             dma("s", [(T.FA[:, 0:192], T.LX[0:128:16, TAB:TAB + V])], "LX", "FA")
             ts(T.YP[:], T.FA[:, 0:192], MAG / 16 - 4096, -MAG / 16, A.add, A.add, "FA", "YP", 192)
-            dma("s", [(T.sq[0:N - TV], T.YP[16 * TV:128, :]), (T.sq[N - TV:N], T.YP[0:16 * TV, :])], "YP", "sq")
-            for q in range(N):
-                for b in range(2):
-                    o = P[0][0:96, 32 * q + 16 * b:32 * q + 16 * b + 16]
-                    mm([(o, x[:, b:192:2], y[:, slot(q)], 16) for x, y in four], "Y1 YN CH CL " + now, "P0")
-            act(T.TN[0:96, :], P[0][0:96, 0:256], AF.Identity, "P0", "TN", 256, bias=HALF)
-            dma("s", [(T.sn[q], T.TN[0:96, 32 * q:32 * q + 32]) for q in others], "TN", "sn")
-            dma("s", [(T.yn[rank:rank + 1, :], T.TN[0:96, 32 * rank:32 * rank + 32])], "TN", "yno")
-            send("n", 5000.0)
+            op("g", 1500.0, "YP", "yp", lambda q: [q.dma_start(T.yp[:], T.YP[:])], dma=True, lat=2200.0)
+            for j, b in enumerate((0, 1, 3)):
+                for h in range(2):
+                    mm([(P[b][64 * h:64 * h + 64, 0:64], cut("HL", k, 0, 192, j), y[:, 64 * h:64 * h + 64], 64) for k, y in enumerate((T.Y1, T.Y1, T.YN, T.YN))],
+                       "Y1 YN " + new + now, "P%d" % b)
+                lin(T.TN[:, :, 16 * j:16 * j + 16], P[b][:, 0:64], 1.0, HALF, "P%d" % b, "TN%d" % j, 64)
+            send("n", "TN0 TN1 TN2")
         nt, Fc, HP, HM = 192 - cs, T.FR[:, cs:cs + 1], T.SH[:, 256 * t - 256:256 * t - 128], T.SH[:, 256 * t - 128:256 * t]
+        o, base, UA = UB + 1 - nt, T.U[:, UB:UB + 1], "U Ua Ue "
         mm([(P[6][:, 0:nt], T.SG[:], T.FR[:, cs:192], nt), (P[6][:, 0:1], HM, Fc, 1), (P[6][:, nt:192], T.SG[:], T.FR[:, 0:cs], cs), (P[6][:, 192:193], HP, Fc, 1)],
-           "SG FR SH%d" % t, "P6", pair=True)
-        op("v", cyc(193), "P6 ZER", "U", lambda q: q.tensor_tensor_scan(T.U[:, 0:193], P[6][:, 0:193], T.ZER[:, 0:193], -256.0, A.add, A.min))
-        ts(T.BC[:, 1:cs + 2], T.U[:, nt:193], T.U[:, nt - 1:nt], -256.0, A.subtract, A.add, "U", "BCa", cs + 1)
-        ts(T.BC[:, cs + 2:194], T.U[:, 0:nt], T.U[:, 192:193], T.U[:, nt - 1:nt], A.add, A.subtract, "U", "BCb", nt)
-        mm([(P[6][:, 200:201], strip("MU", k), T.BC[:, 16 * k + 16:16 * k + 17], 1) for k in range(12)], "MU BCa BCb", "P6")
-        mm(ext16(P[7][:, 448:461], "ME", T.BC, 1, 13), "ME BCa BCb", "P7")
-        scl(T.BS[:, 0:13], P[7][:, 448:461], 1.0 / 131072, "P7", "BS", 13)
-        mm([(P[7][:, 0:193], T.Y1[:], T.BC[:, 0:193], 193), (P[7][:, 0:cs + 1], T.TRI[:], T.FR[:, 0:cs + 1], cs + 1),
-            (P[7][:, cs + 1:193], T.TRI[:], T.FR[:, cs:192], nt), (P[7][:, cs + 1:cs + 2], HM, Fc, 1)], "TRI Y1 BCa BCb FR SH%d" % t, "P7")
-        scl(T.CU[:, 0:193], P[7][:, 0:193], 1.0, "P7", "CU", 193)
-        ts(T.L1[:], T.JB[:], P[6][:, 200:201], None, A.is_ge, None, "JB P6", "L1", 256, 0.5)
-        mm(ext16(P[6][:, 256:272], "ME", T.L1, 0, 16), "ME L1", "P6")
-        ts(T.AU[:], P[6][:, 256:272], 1.0 / 8192, None, A.mult, None, "P6", "AU", 16)
-        scl(T.AB[:], P[6][:, 256:272], 16.0, "P6 AU", "AB", 16)
-        tt(T.L2[:], T.BS[:, 0:16].indirect(T.AU[:]), T.JF[:], A.is_le, "BS AU JF", "L2", 256, 1.56)
-        mm(ext16(P[6][:, 0:16], "ME", T.L2, 0, 16) + [(P[6][:, 0:16], T.Y1[:], T.AB[:], 16)], "L2 ME Y1 AB", "P6")
-        ts(T.KU[:], P[6][:, 0:16], 1.0 / 8192, None, A.mult, None, "P6", "KU", 16)
-        scl(T.KB[:, 0:16], P[6][:, 0:16], 1.0 / 8192, "P6 KU", "KB", 16)
-        if last: ts(T.KB[:, 16:32], T.KB[:, 0:16], cs + 0.5, 0.5, A.is_gt, A.subtract, "KB", "KC", 16)
-        else: act(T.KB[:, 16:32], T.KB[:, 0:16], AF.Sign, "KB", "KC", 16, bias=-(cs + 0.5))
+           "SG FQ FR SH%d0 SH%d1" % (t, t), "P6", pair=True)
+        op("v", cyc(193), "P6 ZER", "U Ua", lambda q, o=o: q.tensor_tensor_scan(T.U[:, o:o + 193], P[6][:, 0:193], T.ZER[:, 0:193], -256.0, A.add, A.min))
+        ts(T.U[:, o + 193:UB + 194], T.U[:, o:o + nt], T.U[:, o + 192:o + 193], 256.0, A.add, A.add, "U", "Ua", nt, 0.5)
+        ts(T.KB[:, 16:32], T.VK[:, 384:400], base, T.U[:, o + 192:o + 193], A.add, A.is_ge, "U VK", "KC", 16)
+        mm([(P[6][:, 201:202], T.SG[:], base, 1)], "SG U", "P6")
+        at = [UB + i if i <= cs + 1 else o + i - cs - 2 for i in range(16, 208, 16)]
+        mm([(P[6][:, 200:201], strip("MU", k), T.U[:, i:i + 1], 1) for k, i in enumerate(at)]
+           + [(P[6][:, 200:201], T.SA[:, 128 * t - 128:128 * t], T.U[:, i:i + 1], 1) for i in (o + 192, UB + 194)], "MU U Ue SA%d" % t, "P6")
+        mm([(P[7][:, 448:461], strip("MU", k), T.U[:, UB + 1 + k:UB + 209:16], 13) for k in range(16)], "MU " + UA, "P7")
+        lin(T.BS[:, 0:13], P[7][:, 448:461], -1.0 / 16, base, "P7 U", "BS", 13)
+        mm([(P[7][:, 0:193], T.Y1[:], T.U[:, UB:UB + 193], 193), (P[7][:, 0:cs + 1], T.TRI[:], T.FR[:, 0:cs + 1], cs + 1),
+            (P[7][:, cs + 1:193], T.TRI[:], T.FR[:, cs:192], nt), (P[7][:, cs + 1:cs + 2], HM, Fc, 1)], "TRI Y1 FQ FR SH%d1 " % t + UA, "P7")
+        lin(T.CU[:, 0:193], P[7][:, 0:193], -1.0, base, "P7 U", "CU", 193)
+        ts(T.L1[:], T.JB[:], P[6][:, 201:202], P[6][:, 200:201], A.add, A.is_ge, "JB P6", "L1", 256, 0.5)
+        at = P[6][:, 256:272]
+        mm(ext16(at, "MV", T.L1, 0, 16), "MV L1", "P6")
+        ts(T.AU[:], at, 0.0, None, A.add, None, "P6", "AU", 16)
+        scl(T.KB[:, 32:48], at, 16.0, "P6 AU", "AB", 16)
+        tt(T.L2[:], T.BS[:, 0:16].indirect(T.AU[:]), T.JF[:], A.is_ge, "BS AU JF", "L2", 256, 1.56)
+        mm(ext16(at, "MU", T.L2, 0, 16) + [(at, T.Y1[:], T.KB[:, 32:48], 16)], "L2 MU Y1 AB", "P6")
+        ts(T.KU[:], at, 0.0, None, A.add, None, "P6", "KU", 16)
+        scl(T.KB[:, 0:16], at, 1.0, "P6 KU", "KB", 16)
         tt(T.SE[:], T.CU[:, 0:194].indirect(T.KU[:]), T.TAU[:], A.is_equal, "CU KU TAU", "SE", 256, 1.56)
-        mm(ext16(P[6][:, 0:16], "MS", T.SE, 0, 16) + [(P[6][:, 0:16], T.Y1[:], T.KB[:, 0:16], 16), (P[6][:, 0:16], (T.YN if last else T.YH)[:], T.KB[:, 16:32], 16)],
-           "MS SE Y1 YH YN KB KC", "P6")
-        ts(T.RU[:], P[6][:, 0:16], 4095.5, float(V), A.add, A.min, "P6", "RU", 16)
+        mm(ext16(at, "MS", T.SE, 0, 16) + [(at, T.Y1[:], T.KB[:, 0:16], 16), (at, T.YN[:], T.KB[:, 16:32], 16)], "MS SE Y1 YN KB KC", "P6")
+        ts(T.RU[:], at, 4096.0, float(V), A.add, A.min, "P6", "RU", 16)
         gat("a", T.Z[:], Wt.indirect(T.RU[:]), WA + "RU", "Z", 256)
         mm([(P[7][:, 0:256], T.BCN[:], T.Z[:], 256)], "BCN Z", "P7")
         mm(ext16(P[6][:, 0:16], "MN", T.Z, 0, 16), "MN Z", "P6")
         if not last: ts(T.NLU[:, 0:16], P[6][:, 0:16], HALF, None, A.add, None, "P6", "NLU", 16)
         lin(T.NL[:], P[6][:, 0:16], 1.0, HALF, "P6", "NL", 16)
         ts(T.NB[:], P[7][:, 0:256], HALF, None, A.add, None, "P7", "NB", 256)
-        tb, TB = 3584 * ((t - 1) % 2), (Tall, " U0 ")[(t - 1) % 2]
         if not last:
             mm(ext16(P[6][:, 16:32], "MX", T.Z, 0, 16), "MX Z", "P6")
             tt(T.RT[:, 16:32], P[6][:, 16:32], T.DU3[:, 0:16], A.min, "P6 DU3", "RX", 16, 1.0)
             cp(T.NLU[:, 16:32], T.RT[:, 16:32], "RX", "NPU", 16)
-            gat("a", T.O[:], T.PG[:, tb + TAB:tb + TAB + V + 16].indirect(T.NLU[:, 0:16]), TB + "NLU", "O", 256)
+            gat("a", T.O[:], T.PG[:, TAB:TAB + V + 16].indirect(T.NLU[:, 0:16]), Tall + "NLU", "O", 256)
             for k in range(t):
                 wide = t == 3 and k == 0
-                mm(ext16(P[6][:, 0:16], "MA" if k else "MP", T.O, 0, 16, 1 if k else 1 - t), "O MA MP", "P6")
+                mm(ext16(P[6][:, 0:16], "MA" if k == 1 else "MP", T.O, 0, 16), "O MA MP", "P6")
                 ts(T.OU[:], P[6][:, 0:16], float(NONE if wide else FREE), None, A.min, None, "P6", "OU", 16)
                 gat("a", T.O[:], (T.W[:, 0:NONE + 16] if wide else Wt).indirect(T.OU[:]), WA + "OU" + (" Wi" if wide else ""), "O", 256)
             parts = [([(P[7][:, 0:256], T.DO[:], T.O[:], 256)], "DO O"), ([(P[7][:, 0:256], T.DZ[:], T.Z[:], 256)], "DZ Z")]
@@ -830,13 +846,17 @@ def build(g, core, rank, T, topo, via, vib):
             mm(ext16(P[6][:, 0:16], "MR", T.Z, 0, 16), "MR Z", "P6")
             ts(T.OU[:], P[6][:, 0:16], 192 * HALF, None, A.add, None, "P6", "OU", 16)
             gat("a", T.O[:], T.LW[:, TAB:TAB + V].indirect(T.OU[:]), "LW OU", "O", 256)
-            gat("a", T.O1[:], T.LX[:, TAB:TAB + V].indirect(T.OU[:]), "LX OU", "O1", 256)
+            ts(T.O1[:], T.LX[:, TAB:TAB + V].indirect(T.OU[:]), -4096.0, None, A.add, None, "LX OU", "O1", 256, 1.56)
+            act(T.O1[:], T.LX[:, TAB:TAB + V].indirect(T.OU[:]), AF.Identity, "LX OU", "O1", 256, 1.56, bias=-4096.0)
+            either("a")
             parts = [([(P[7][:, 0:256], T.DL[:], T.O[:], 256)], "DL O"), ([(P[7][:, 0:256], T.DL[:], T.O1[:], 256)], "DL O1"),
                      ([(P[7][:, 0:256], T.DX[:], T.Z[:], 256)], "DX Z")]
             mm([(P[3][:, 0:256], T.BCV[:], T.Z[:], 256)], "BCV Z", "P3")
-            lin(T.VAL[:], P[3][:, 0:256], 1.0, -float(SAME // 192), "P3", "VAL", 256)
-        for m in range(16):
-            ts(T.E[:, m, 0:256 - 16 * m], T.NB[:, 16 * m:256], T.NL[:, m:m + 1], None, A.is_equal, None, "NB NL", "E%d" % m, 256 - 16 * m, 0.5)
+            lin(T.VAL[:], P[3][:, 0:256], 1.0, 1.0, "P3", "VAL", 256)
+        for h in range(0, 16, 3):
+            ms_ = range(h, min(h + 3, 16))
+            op("v", sum(cyc(256 - 16 * m, 0.5) for m in ms_), "NB NL", " ".join("E%d" % m for m in ms_),
+               lambda q, ms_=ms_: [q.tensor_scalar(T.E[:, m, 0:256 - 16 * m], T.NB[:, 16 * m:256], T.NL[:, m:m + 1], None, A.is_equal) for m in ms_])
         for h in range(5):
             parts.append(([(P[7][:, 16 * m + 16:256], T.TWO[:], T.E[:, m, 16:256 - 16 * m], 240 - 16 * m) for m in range(3 * h, 3 * h + 3)],
                           " ".join("E%d" % m for m in range(3 * h, 3 * h + 3)) + " TWO"))
@@ -845,25 +865,19 @@ def build(g, core, rank, T, topo, via, vib):
         act(T.WI[:], P[7][:, 0:256], AF.Sign, "", "WI P7 A7", 256, scale=-1.0)
         if not last:
             tt(T.TR[:, 0:3440].indirect(T.NLU[:, 16:32]), T.Z[:], T.WI[:], A.add, "Z WI NPU", TRall, 256, 3.8)
+        if t == TV - 1: continue
         if last:
             mm(ext16(P[6][:, 0:16], "MR", T.Z, 0, 16), "Z MR", "P6", True, False)
             mm(ext16(P[6][:, 0:16], "MF", T.WI, 0, 16), "MF WI", "P6", False, True)
             tt(T.RT[:, 0:16], P[6][:, 0:16], T.DU2[:, 16:32], A.max, "P6 DU2", "RT", 16, 1.0)
-            ts(T.QU[:], T.RT[:, 0:16], TAB - BIG + 192 * HALF, None, A.add, None, "RT", "QU", 16)
-        elif t < TV - 1:
-            mm(ext16(P[7][:, 0:16], "MF", T.WI, 0, 16), "MF WI", "P7")
-            tt(T.RF[:, 0:16], P[7][:, 0:16], T.NL[:], A.add, "P7 NL", "RF", 16, 1.0)
-            tt(T.RT[:, 0:16], T.RF[:, 0:16], T.DU2[:, 0:16], A.max, "RF DU2", "RT", 16)
-            ts(T.QU[:], T.RT[:, 0:16], float(TAB - BIG), None, A.add, None, "RT", "QU", 16)
-            cp(T.PG[:, tb:tb + TAB + V].indirect(T.QU[:]), T.Z[:], "Z QU", TB, 256, 3.8)
-            tn = 3584 - tb
-            dma("s", [x for ch in (CH_OK, CH_OA) for x in onward(lambda a, b: T.PG[16 * a + ch:16 * b:16, tn + TAB:tn + TAB + V],
-                                                                 lambda a, b: T.PG[16 * a + ch:16 * b:16, tb + TAB:tb + TAB + V])],
-                TB, (Tall, " U0 ")[t % 2])
+        else:
+            mm(ext16(P[6][:, 0:16], "MF", T.WI, 0, 16), "MF WI", "P6")
+            tt(T.RT[:, 32:48], P[6][:, 0:16], T.NL[:], A.add, "P6 NL", "RG", 16, 1.0)
+            tt(T.RT[:, 0:16], T.RT[:, 32:48], T.DU2[:, 0:16], A.max, "RG DU2", "RT", 16)
+        ts(T.QU[:], T.RT[:, 0:16], TAB - BIG + 192 * HALF * last, None, A.add, None, "RT", "QU", 16)
+        if not last: cp(T.PG[:, 0:TAB + V].indirect(T.QU[:]), T.Z[:], "Z QU", Tall, 256, 3.8)
 
     cp(T.LW[:, 0:TAB + V].indirect(T.QU[:]), T.VAL[:], "VAL QU", "LW", 256, 3.8)
-    dma("s", [(T.sp[0:N - TV], T.LW[16 * TV:128:16, TAB:TAB + V]), (T.sp[N - TV:N], T.LW[0:16 * TV:16, TAB:TAB + V])], "LW", "sp")
-    send("p", 5000.0, " sq")
-    dma("s", [(T.yn[a:b, :], T.rn[a:b]) for a, b in ((0, rank), (rank + 1, N)) if b > a], "sp mn yno", "yn", ext=[("an", short_all)])
-    dma("s", [(T.yp[:], T.rp[:])], "yn mp", "yp", ext=[("ap", short_all + arrivals(vib, rank, False))])
+    op("g", 500.0, "LW yp", "yp", lambda q: [q.dma_start(T.yp[:], T.LW[0:128:16, TAB:TAB + V], accum_op=A.add, max_dma_last_dim=4096)], dma=True, lat=2600.0)
+    dma("s", [(T.yn[4 * h:4 * h + 4, :], T.rn[:, 64 * h:64 * h + 64, :]) for h in range(2)], "an FA", "yn", lat=5000.0)
     return ops

import math
import numpy as np
from concourse.bass import DstId, RemoteDMATransfer
from concourse.mybir import AluOpType as A, ActivationFunctionType as AF, AxisListType as AX

N, V, S, TV = 8, 3072, 745, 4
FREE, SAME, NONE, TAB, LWN, BIG = 3088, 3264, 6336, 384, 5520, 524288
HALF, MAG = 7.5, 1.5 * 2 ** 27
f32, bf, i32, u16 = "float32", "bfloat16", "int32", "uint16"


def _sb(n, d):
    return ("sbuf", [128, n], d)


LATE = {"y": 0.0, "0": 8500.0, "x": 12000.0, "c": 7000.0, "i": 6200.0, "a": 6200.0, "e": 6200.0, "b": 6200.0, "n": 6500.0}
PARTS = ((0, 64), (64, 192))
SCRATCH = {"s0": ("dram", [4, 128, 48], i32), "h0": ("dram", [128, 48], i32), "sx": ("dram", [4, 128, V // 4], bf), "hx": ("dram", [128, V // 4], bf), "hy": ("dram", [128, V // 4], bf),
           "hc": ("dram", [128, 384], bf), "hi": ("dram", [128, 192], u16), "ka": ("dram", [TV - 1, 128, 192], bf),
           "ke": ("dram", [TV - 1, 128, PARTS[0][1]], bf), "kb": ("dram", [TV - 1, 128, 192 - PARTS[0][1]], bf), "hn": ("dram", [128, 48], f32), "rn": ("dram", [4, 128, 48], f32)}
STRIPS = ["MP", "MN", "ME", "MU", "MV", "MA", "MF", "MS", "MX", "MR"]
SQUARE = ["Y1", "YE", "YH", "YR", "YN", "YS", "SG", "SN", "TRI", "BCN", "POW", "TWO", "DO", "DZ", "DX", "DL", "BCV"]
UB = max(192 - S * _t % V // 16 for _t in range(1, TV + 1)) - 1
SCRATCH.update({
    "X": _sb(TV * V, bf), "F": _sb(V, bf), "G2": _sb(V, bf), "D": _sb(V, bf), "PR": _sb(V, bf), "NE": _sb(V, bf),
    "W": _sb(NONE + 16, bf), "TR": _sb(3440, bf), "PG": _sb(3584, bf),
    "RHO": _sb(2048, f32), "FV": _sb(V, f32), "LW": _sb(LWN, f32), "LX": _sb(LWN, f32), "LY": _sb(V, f32), "LZ": _sb(V, f32),
    "E": ("sbuf", [128, 16, 256], bf),
    "PK": _sb(8, i32), "CC": _sb(8, f32), "CT": _sb(16, f32), "IOT": _sb(512, f32), "TM2": _sb(64, f32), "MM": _sb(len(STRIPS) * 144, bf),
    "YF": _sb(128, f32),
    "ZER": _sb(720, bf), "JB": _sb(256, bf), "JF": _sb(256, f32), "TAU": _sb(256, f32), "THR": _sb(256, bf),
    "DU2": _sb(32, f32), "DU3": _sb(192, f32), "SH": _sb(1024, bf), "SA": _sb(512, bf), "VK": _sb(592, bf),
    "CP": _sb(384, i32), "N0": ("sbuf", [128, 4, 48], i32), "IA": _sb(768, i32), "KA": _sb(768, bf), "NH": _sb(192, f32), "RP": _sb(384, u16),
    "FA": _sb(384, f32), "RF": _sb(192, f32),
    "ICF": _sb(384, f32), "ICU": _sb(192 * TV, u16), "KC": _sb(384 * (TV - 1), bf), "HN": _sb(768 * TV, bf),
    "NF": _sb(192, f32), "NU": _sb(192, u16), "LU": _sb(192, u16), "LO": _sb(192, u16),
    "EQ": _sb(192, bf), "O1": _sb(256, bf), "OU": _sb(16, u16),
    "HL": _sb(768 * TV, bf), "FR": _sb(192, bf), "MK": _sb(192, bf),
    "U": _sb(UB + 215, bf), "CU": _sb(200, f32), "BS": _sb(16, f32),
    "L1": _sb(256, bf), "L2": _sb(256, bf), "SE": _sb(256, bf), "AU": _sb(16, u16), "KU": _sb(16, u16), "KB": _sb(48, bf),
    "RT": _sb(48, f32), "RU": _sb(16, u16), "Z": _sb(256, bf), "O": _sb(256, bf),
    "NB": _sb(256, u16), "NLU": _sb(32, u16), "WI": _sb(256, bf), "VAL": _sb(256, f32), "NL": _sb(16, f32),
    "QU": _sb(16, u16), "YP": _sb(192, f32), "TN": ("sbuf", [128, 4, 48], f32),
})
for _m in SQUARE:
    SCRATCH[_m] = _sb(128, bf)
for _b in range(8):
    SCRATCH["P%d" % _b] = ("psum", [128, 512], f32)
NDMA = 72
LATER = range(1, TV)
SEMAPHORES = (["cv", "ca", "cp", "cg", "loc", "h0", "hx", "hy", "hc", "hi", "hn", "a0", "an", "ax%d" % TV] + [m + str(t) for m in ("ha", "he", "hb", "ax", "ac", "ai", "av", "aw") for t in LATER]
              + ["d%d" % k for k in range(NDMA)])
CH_HI, CH_LO, CH_FR, CH_E, CH_K, CH_A, CH_D, CH_OK, CH_OA, CH_X, CH_Y, CH_C, CH_J = 0, 1, 2, 3, 4, 5, 6, 8, 9, 10, 11, 12, 14
CY, PEC, FIX, LAT = 0.9, 0.45, 55.0, 110.0


def routes(T, topo):
    out = []
    for c in T.cores:
        port = [x for x in topo.cores_of(c) if x != c and all(topo.may_write(x, d) for d in T.cores)]
        by = [[x for x in port if topo.die(x) == y] for y in sorted(set(topo.die(x) for x in port))]
        out.append([l[0] for l in by] + [l[1] for l in by])
    return out


def messages(T):
    half = lambda k, t: (t, T.X[:, V * t - V + V // 4 * k:V * t - V + V // 4 * (k + 1)], "ax%d" % t)
    l = {"0": [(k, T.s0[k], T.h0[:], [(1, T.N0[:, k, :], "a0")]) for k in range(4)],
         "x": [(k, T.sx[k], T.hx[:], [half(k, 1), half(k, 2)]) for k in range(4)],
         "c": [(3, T.KA[:, 0:384], T.hc[:], [(t, T.KC[:, 384 * t - 384:384 * t], "ac%d" % t) for t in LATER])],
         "y": [(k, T.sx[2 + k], T.hy[:], []) for k in range(2)],
         "i": [(2, T.ICU[:, 0:192], T.hi[:], [(t, T.ICU[:, 192 * t:192 * t + 192], "ai%d" % t) for t in LATER])]}
    for t in LATER:
        for m, first, o, (a, b), sem in (("a", 2, 0, (0, 192), "av"), ("e", 2, 384, PARTS[0], "av"), ("b", 0, 384, PARTS[1], "aw")):
            c = [768 * t - 768 + o + 192 * k for k in range(2)]
            l[m + str(t)] = [(first + k, T.HL[:, c[k] + a:c[k] + b], T["k" + m][t - 1], [(1, T.HN[:, c[k] + 768 + a:c[k] + 768 + b], sem + str(t))]) for k in range(2)]
        if t + 2 <= TV: l["x%d" % t] = [(k % 2, None, T["hxhy"[k & 2:][:2]][:], [half(k, t + 2)]) for k in range(4)]
    l["n"] = [(k, T.TN[:, k, :], T.hn[:], [(-TV, T.rn[k], "an")]) for k in range(4)]
    return l


def bits(l):
    return sum(1 << e for e in l)


def helper(g, core, T, topo, ports):
    sent = 0
    for s in [s for s in range(N) if core in ports[s]]:
        for m, l in messages(T).items():
            for k, src, here, to in l:
                if ports[s][k] != core: continue
                if src is not None: g.wait_ge(T.sem["h" + m], len(topo.engines(T.cores[s], core)) // len(l))
                for back, dst, sem in to:
                    d = T.cores[(s - back) % N]
                    rid, pid = topo.addr(d, core)
                    g.remote_dma(dst, here, T.sem[sem], T.sem.loc, pid, rid, topo.mask(core, d))
                    sent += len(topo.engines(core, d))
    if sent: g.wait_ge(T.sem.loc, sent)


def rank_program(g, core, T, topo):
    ports = routes(T, topo)
    rank = T.rank_of(core)
    if rank is None:
        helper(g, core, T, topo, ports)
        return
    ops = build(g, core, rank, T, topo, ports)
    emit(g, T, ops)


PLAN = {}
CASES = [{"far": 1.0, "wide": 1.0, "dma": 1.0, "wake": 1.0, "weight": 1.5},
         {"gather": 1.3, "scatter": 1.55, "far": 0.75, "wide": 0.75, "dma": 0.75, "wake": 0.9, "weight": 1.5},
         {"gather": 0.85, "scatter": 0.8, "tensor": 1.1, "far": 1.45, "wide": 1.4, "dma": 1.2, "wake": 2.5, "weight": 2.0},
         {"gather": 1.1, "scatter": 0.7, "far": 1.8, "wide": 1.4, "dma": 1.0, "wake": 1.2, "weight": 2.0},
         {"gather": 0.78, "scatter": 1.45, "far": 0.85, "wide": 0.9, "dma": 0.85, "wake": 1.2}]
ROUNDS = [((0, 1, 2, 3, 4), 650, 18.0), ((0, 1, 2, 3, 4), 400, 7.0)]
MOVES, WINDOW, NEAR, SOON, URGE = 1200, 70, 400.0, 0.05, 150.0
NA, VS, VCH = 3, 16, ((1, 3, 5), (3, 5))
SPAN = (0.0, 1.0)
SIGN = [(3,), (), (), ()]
SIZE = [(5,), (5,), (5,), (5,)]
BANK = [(0, 1, 5, 6, 3, 7), (0, 1, 3, 5, 0, 1), (0, 1, 3, 5, 0, 1), (0, 1, 3, 5, 0, 1)]


FIRST = [{"v": "ZER YP Wd IA0 IA1 PW KAc Wt Wu IA2 IA3 RP KAp FV2 PU LY T1 LY+ FC0 FC1 LO0 LO1 T4 LW FC2 LW+ LO2 PV LW++ NH LY++ NU0 OH G0 LU0 NF0 D0 D1 P4 "
               "ICU HI1 HI0 LO5 LO4 EQ0 c2 D2 EQ1 PR0 PR1 D4 NE1 PR2 PR3+ PR4 FQ NE5 CH10 c4 CL10 c3 PW2 THR FR",
          "a": "MP FV4 MA FV0 LZ T2 T3 T0 T5 LZ+ LX LX+ LX++ LZ++ G1 G2 G3 MK PR3 G5 G4 D3 D5 PR5 NE0 PR5+ NE2 NE3 NE4 DZ DO BCN",
          "p": "YR.Y1+ YR.Y1 T2.T3 T0.T1 T4.T5 NH.YF NH.YF+ NH.YF++ NH.YF+++ NH.YF++++ NH.YF+++++ FA.YF G1.YN G0.YN G2.YN ICF.YF D0.YH YN.G3 D1.YH Y1.PR3 "
               "ax1.YN ax1.Y1++ ax1.Y1 YN.Y1 Y1.G5 YN.Y1+ ax1.Y1+ G4.YN D2.YH YN.Y1++ ax1.Y1++++ YN.Y1+++ ax1.Y1+++ ax1.YN+ G3.YH Y1.PR5 PR3.YH YE.EQ0 D4.YH "
               "ME.NE0 YN.D5 YN.MK Y1.PR5+ YE.EQ1 YN.MK+ ME.NE2 ME.NE4"},
         {"v": "CH1 U CL1 Ua KC L1 T0- AU L2 TR0 KU SE TR4 LU0 RU Z LU1 NLU NB E3 E12 RX LU2 E6 E0 HI OU NPU NU0 LO D0 E15 EQ0 OU+ E9 D1 PR0 NU1 OU++ PR1 "
               "EQ1 D4 D2 TR0+ D3 PR4 FQ RG CH0 RF0 PR2 CL0 LO0 PR3 NE3 RT QU FR",
          "a": "BS CU AB TR1 TR2 KB TR3 TR5 G1 NL O G3 G0 O+ NF0 G2 O++ G5 G4 O+++ NF1 NE0 NE1 WI D5 PR5 PR5+ NE4 NE5 NE2",
          "p": "ax.Y1+++ SG.FQ ax.Y1+ SG.U MU.U MU.U+ MV.L1 TRI.Y1 ax.Y1 ax.Y1++ L2.MU TR0.TR1 MS.SE TR2.TR3 MN.Z BCN.Z TR4.TR5 MX.Z YH.THR G1.YN E3.E4 O.MA "
               "E6.E7 Y1.YN G3.YN G0.YN E0.E1 O.MA+ DZ.Z D0.YH YN.Y1 G2.YN YN.Y1+ E12.E13 Y1.YN+ O.MA++ D1.YH E9.E10 ax.Y1++++ G4.YN POW.E0 DO.O ax.YN YN.Y1++ "
               "Y1.G5 YN.Y1+++ YE.EQ0 D4.YH ME.NE0 ax.YN+ MF.WI D2.YH Y1.PR5 YE.EQ1 MF.TR0 D3.YH YN.D5 Y1.PR5+ YE.YS MF.TR0++ MF.TR0+ ME.NE4 ME.NE2"},
         {"v": "CH1 CL1 RF1 U LO1 Ua KC TN1 TN2 TN0 L1 LW BS AU L2 CU LW+ KU SE LW++ RU Z LW+++ NB E9 E0 OU E3 YP E6 E12 E15 RT QU LW++++",
          "a": "LX LX+ AB LX++ KB LX+++ NL O1 O VAL WI",
          "p": "YE.YS SG.FQ Y1.YN++ Y1.YN++++ Y1.YN+++ Y1.YN Y1.YN+++++ SG.U Y1.YN+ MU.U MU.U+ MV.L1 TRI.Y1 L2.MU MS.SE BCN.Z MN.Z BCV.Z YH.THR MR.Z DX.Z "
               "E9.E10 E0.E1 E3.E4 DL.O1 E6.E7 DL.O E12.E13 POW.E0 Z.MR MF.WI"}]


def labels(ops):
    out, seen, s = [], {}, 0
    for o in ops:
        w = "" if o["dma"] or o["e"] == "g" else ".".join(o["r"][:2]) if o["e"] == "p" else o["w"][0]
        if s and (w[:2] in ("CH", "CL", "HI", "ax") or w[:2] == "LO" and int(w[2]) > 3): w = w[:2] + w[3:]
        seen[(s, w)] = seen.get((s, w), -1) + 1
        out.append((s, w + "+" * seen[(s, w)]))
        s += w == "FR"
    return out


def listed(ops, alt):
    out = {e: [] for e in "vap"}
    for i, (s, w) in enumerate(labels(ops)):
        for z, x in ((s + 1, w + "-"), (s, w))[s == 0:]:
            hit = [(e, l.split().index(x)) for e, l in FIRST[(z > 0) + (z >= TV)].items() if e in alt[i] and x in l.split() and z <= TV]
            if hit:
                out[hit[0][0]].append((z, hit[0][1], i))
                break
    return {e: [x[2] for x in sorted(l)] for e, l in out.items()}


def first_order(ops, pre, post, alt):
    n = len(ops)
    eng, qs = [o["e"] for o in ops], listed(ops, alt)
    home = {i: e for e in qs for i in qs[e]}
    q, nxt = [0.0] * n, {x: y for l in qs.values() for x, y in zip(l, l[1:])}
    for _ in range(60):
        for i in range(n - 1, -1, -1):
            q[i] = alt[i][home.get(i, eng[i])] + max([q[j] + x for j, x in post[i]] + [ops[i]["lat"], q[nxt[i]] if i in nxt else 0.0])
    fin, free, left = [0.0] * n, {e: 0.0 for e in "vapgs"}, [len(x) for x in pre]
    ready, order = set(i for i in range(n) if not left[i]), []
    while ready:
        c = []
        for i in [x for x in ready if x not in home or qs[home[x]][0] == x] or ready:
            t = max([ops[i]["t0"]] + [fin[d] + x for d, x in pre[i]])
            f, e = min((max(t, free[e]) + alt[i][e], e) for e in (home[i] if i in home else alt[i]))
            c.append((f - alt[i][e], i, f, e))
        t = min(c)[0] + URGE
        _, i, f, eng[i] = max((q[x[1]],) + x[1:] for x in c if x[0] <= t)
        if i in home: qs[home[i]].remove(i)
        fin[i] = free[eng[i]] = f
        ready.discard(i)
        order.append(i)
        for j, _ in post[i]:
            left[j] -= 1
            if not left[j]: ready.add(j)
    return order, eng


def schedule(ops):
    n = len(ops)
    alt = [{e: o["alt"][e][0] for e in sorted(o["alt"])} if "alt" in o else {o["e"]: o["c"]} for o in ops]
    pre = [[(d, (0.0 if ops[d]["e"] == o["e"] == "p" else LAT) + (0.0 if ops[d]["rem"] and o["e"] == "g" or d == o["soft"] else ops[d]["lat"])) for d in o["dep"]] for o in ops]
    post = [[] for _ in ops]
    for i in range(n):
        for d, x in pre[i]: post[d].append((i, x))
    head, tail = [o["t0"] for o in ops], [o["lat"] for o in ops]
    every = [([c.get(o["g"], 1.0) for o in ops],
              [[(d, x * (c["wide"] if "mx" in ops[d]["w"] else c.get("early", 1.0) * c["far"] if ops[d]["rem"] and ops[d]["w"][1][:2] == "me" else c["far"] if ops[d]["rem"] else c["dma"] if ops[d]["dma"] else c["wake"]))
                for d, x in pre[i]] for i in range(n)]) for c in CASES]
    order, eng = first_order(ops, pre, post, alt)
    rnd = np.random.default_rng(1)

    def whole(cases):
        res = []
        for mul, before in cases:
            fin, q, last, up = [0.0] * n, list(tail), {}, [-1] * n
            for i in order:
                t, u = head[i], last.get(eng[i], -1)
                if u >= 0 and fin[u] > t: t = fin[u]
                for d, x in before[i]:
                    if fin[d] + x > t: t = fin[d] + x
                fin[i], last[eng[i]], up[i] = t + alt[i][eng[i]] * mul[i], i, u
            for i in reversed(order):
                t = q[i] + alt[i][eng[i]] * mul[i]
                if up[i] >= 0 and t > q[up[i]]: q[up[i]] = t
                for d, x in before[i]:
                    if t + x > q[d]: q[d] = t + x
            res.append((max(fin[i] + q[i] for i in range(n)), fin, q))
        return res

    def window(cases, norm, res, a, b, heat):
        win = order[a:b]
        m, loc, early, L = len(win), {i: k for k, i in enumerate(win)}, set(order[:a]), []
        for (mul, before), (end, fin, q) in zip(cases, res):
            h, tl = [max([head[i]] + [fin[d] + x for d, x in before[i] if d not in loc]) for i in win], [tail[i] for i in win]
            e0, e1, by = {e: 0.0 for e in "vapgs"}, {e: 0.0 for e in "vapgs"}, 0.0
            for i in order[:a]: e0[eng[i]] = fin[i]
            for j in reversed(order[b:]):
                e1[eng[j]] = t = q[j] + alt[j][eng[j]] * mul[j]
                by = max(by, head[j] + t)
                for d, x in before[j]:
                    if d in loc: tl[loc[d]] = max(tl[loc[d]], t + x)
                    elif d in early: by = max(by, fin[d] + x + t)
            L.append((h, tl, e0, e1, by, [[(loc[d], x) for d, x in before[i] if d in loc] for i in win], [mul[i] for i in win]))
        npre, direct = [len(x) for x in L[0][5]], [set(d for d, _ in x) for x in L[0][5]]
        sc = [[loc[j] for j, _ in post[i] if j in loc] for i in win]
        en, co = [eng[i] for i in win], [alt[i][eng[i]] for i in win]
        seq = {e: [k for k in range(m) if en[k] == e] for e in "vapgs"}

        def times():
            up, down, left = [-1] * m, [-1] * m, list(npre)
            for l in seq.values():
                for x, y in zip(l, l[1:]):
                    up[y], down[x] = x, y
                    left[y] += 1
            o = [k for k in range(m) if not left[k]]
            for k in o:
                for j in sc[k]:
                    left[j] -= 1
                    if not left[j]: o.append(j)
                j = down[k]
                if j >= 0:
                    left[j] -= 1
                    if not left[j]: o.append(j)
            if len(o) < m: return None
            tot, out = 0.0, []
            for (h, tl, e0, e1, by, bf_, mul), z in zip(L, norm):
                f, end = [0.0] * m, by
                for k in o:
                    u = up[k]
                    t = f[u] if u >= 0 else e0[en[k]]
                    if h[k] > t: t = h[k]
                    for d, x in bf_[k]:
                        if f[d] + x > t: t = f[d] + x
                    f[k] = t = t + co[k] * mul[k]
                    if t + tl[k] > end: end = t + tl[k]
                for e, l in seq.items(): end = max(end, (f[l[-1]] if l else e0[e]) + e1[e])
                tot += (end + SOON * sum(f) / m) / z
                out.append((end, f))
            return tot, out, o, up

        def longest(x):
            s = int(rnd.integers(len(L)))
            h, tl, e0, e1, by, bf_, mul = L[s]
            (end, f), q = x[1][s], list(tl)
            for e, l in seq.items():
                if l: q[l[-1]] = max(q[l[-1]], e1[e])
            for k in reversed(x[2]):
                t = q[k] + co[k] * mul[k]
                if x[3][k] >= 0 and t > q[x[3][k]]: q[x[3][k]] = t
                for d, y in bf_[k]:
                    if t + y > q[d]: q[d] = t + y
            return [k for k in range(m) if f[k] + q[k] > end - NEAR] or list(range(m)), f
        now, cr = times(), None
        for r in rnd.random((MOVES, 6)).tolist():
            if cr is None or r[5] < 0.05: cr, f = longest(now)
            v = cr[int(r[0] * len(cr))] if r[5] < 0.9 else int(r[0] * m)
            o = e = en[v]
            l, al = seq[o], alt[win[v]]
            k = p = l.index(v)
            if len(al) > 1 and r[1] < 0.4:
                e = [x for x in al if x != o][int(r[1] * 2.5 * (len(al) - 1))]
                k = sum(f[y] <= f[v] - co[v] for y in seq[e])
                k = max(0, min(k + int(r[2] * 4) - 1, len(seq[e])))
            elif r[1] > 0.7:
                if r[3] < 0.5:
                    while k > 0 and l[k - 1] not in direct[v]: k -= 1
                else:
                    while k + 1 < len(l) and v not in direct[l[k + 1]]: k += 1
                k = p + int(round((k - p) * r[2] ** 2))
                if k == p: continue
            else:
                k = p + (1 + int(-math.log(1 - r[2]) * 1.5)) * (1 if r[3] < 0.5 else -1)
                if k < 0 or k >= len(l) or any(y in direct[v] or v in direct[y] for y in l[min(p, k):max(p, k) + 1]): continue
            l.pop(p)
            seq[e].insert(k, v)
            en[v], co[v] = e, al[e]
            x = times()
            if x and x[0] - now[0] <= -heat * math.log(1.0 - r[4]): now, cr = x, None
            else:
                seq[e].pop(k)
                l.insert(p, v)
                en[v], co[v] = o, al[o]
        order[a:b] = [win[k] for k in now[2]]
        for k, i in enumerate(win): eng[i] = en[k]
    for which, rounds, heat in ROUNDS:
        cases, nc = [every[k] for k in which], len(which)
        norm = [x[0] for x in whole(cases)]
        norm = [x / norm[0] * sum(CASES[j].get("weight", 1.0) for j in which) / CASES[k].get("weight", 1.0) for x, k in zip(norm, which)]
        best = None
        for sw in range(rounds + 1):
            res = whole(cases)
            tot = sum(x[0] / z for x, z in zip(res, norm))
            if best is None or tot < best[0]: best = (tot, list(order), list(eng), res)
            if sw == rounds: break
            order.sort(key=lambda i: res[0][1][i] - alt[i][eng[i]] * cases[0][0][i])
            a = int(rnd.integers(int(SPAN[0] * n) - WINDOW // 2, int(SPAN[1] * n) - WINDOW // 2))
            window(cases, norm, res, max(0, a), min(n, a + WINDOW), heat * (1.02 - sw / rounds))
        order[:], eng[:] = best[1], best[2]
    return best[3], order, eng


def emit(g, T, ops):
    lastw, readers = {}, {}
    for i, o in enumerate(ops):
        dep = set()
        for r in o["r"]:
            if r in lastw: dep.add(lastw[r])
        for w in o["w"]:
            if w in lastw: dep.add(lastw[w])
            dep.update(readers.get(w, []))
        dep.discard(i)
        o["soft"] = lastw.get("~" + o["e"]) if "~" + o["e"] in o["r"] else None
        for r in o["r"]: readers.setdefault(r, []).append(i)
        for w in o["w"]:
            lastw[w] = i
            readers[w] = []
        o["dep"] = sorted(dep)
    if "order" not in PLAN:
        PLAN["order"] = schedule(ops)
    for i, e in enumerate(PLAN["order"][2]):
        if "alt" in ops[i]: ops[i]["e"], ops[i]["f"] = e, ops[i]["alt"][e][1]
    order = PLAN["order"][1]
    Q = {"v": g.vector, "a": g.scalar, "p": g.tensor, "g": g, "s": g.sync}
    cnt = {"v": 0, "a": 0, "p": 0, "g": 0}
    tok, seen, nd, alltok = {}, {}, 0, {}
    for i in order:
        o = ops[i]
        q = Q[o["e"]]
        need = {}
        for d in o["dep"]:
            if tok[d] is None or d == o["soft"] or (o["e"] == "p" and ops[d]["e"] == "p"): continue
            s, v = tok[d]
            need[s] = max(need.get(s, 0), v)
        for s, v in o["ext"]:
            need[s] = max(need.get(s, 0), v)
            alltok[s] = v
        for s in sorted(need):
            if seen.get((o["e"], s), 0) < need[s]:
                q.wait_ge(T.sem[s], need[s])
                seen[(o["e"], s)] = need[s]
        ins = o["f"](q)
        if o["rem"]:
            tok[i] = None
        elif o["dma"]:
            s = "d%d" % nd
            nd += 1
            for x in ins: x.then_inc(T.sem[s], 16)
            tok[i] = (s, 16 * len(ins))
            alltok[s] = 16 * len(ins)
        else:
            for x in ins if isinstance(ins, list) else [ins]:
                cnt[o["e"]] += 1
                x.then_inc(T.sem["c" + o["e"]], 1)
            tok[i] = ("c" + o["e"], cnt[o["e"]])
            alltok["c" + o["e"]] = cnt[o["e"]]
    for o in ops:
        if o["rem"]: alltok["loc"] = alltok.get("loc", 0) + o["rem"]
    for s in sorted(alltok):
        if not any(seen.get((e, s), 0) >= alltok[s] for e in Q):
            g.wait_ge(T.sem[s], alltok[s])


def build(g, core, rank, T, topo, ports):
    ops, kind, gate = [], [""], [""]
    MSG, landed = messages(T), {}
    for l in MSG.values():
        for k, _, _, to in l:
            for back, _, sem in to: landed[sem] = landed.get(sem, 0) + len(topo.engines(ports[(rank + back) % N][k], core))

    def op(e, c, r, w, f, dma=False, lat=0.0, t0=0.0, rem=0):
        r, w = (r + (gate[0] if e == "g" and not rem else "")).split(), w.split()
        w = w + [x for x in r if x[0] == "P" and x[1:].isdigit()]
        ops.append({"g": "tensor" if e == "p" else kind[0] if e in "va" and not dma else "", "e": e, "c": c, "r": r, "w": w, "f": f, "dma": dma,
                    "lat": lat, "ext": [] if rem else [(x, landed[x]) for x in r if x in landed], "t0": t0, "rem": rem})

    def cyc(n, k=1.0):
        kind[0] = {1.56: "gather", 3.8: "scatter"}.get(k, "")
        return FIX + max(64.0, n * k) * CY

    def ts(out, in0, s1, s2, o0, o1, r, w, n, k=1.0):
        if o1 is None: op("v", cyc(n, k), r, w, lambda q: q.tensor_scalar(out, in0, s1, None, o0))
        else: op("v", cyc(n, k), r, w, lambda q: q.tensor_scalar(out, in0, s1, s2, o0, o1))

    def tt(out, a, b, o, r, w, n, k=2.0):
        op("v", cyc(n, k), r, w, lambda q: q.tensor_tensor(out, a, b, o))

    def cp(out, a, r, w, n, k=1.0):
        op("v", cyc(n, k), r, w, lambda q: q.tensor_copy(out, a))

    def ms(out, val, w, n, k=1.0):
        op("v", cyc(n, k), "", w, lambda q: q.memset(out, val))

    def red(out, a, o, r, w, n):
        op("v", cyc(n), r, w, lambda q: q.tensor_reduce(out, a, AX.X, o))

    def act(out, a, fn, r, w, n, k=1.0, bias=None, scale=None):
        kw = {}
        if bias is not None: kw["bias"] = bias
        if scale is not None: kw["scale"] = scale
        op("a", cyc(n, k), r, w, lambda q: q.activation(out, a, fn, **kw))

    def either(e, n=2):
        l = [ops.pop() for _ in range(n)]
        o = dict([x for x in l if x["e"] == e][0], alt={x["e"]: (x["c"], x["f"]) for x in l})
        o["r"] = sorted(set(y for x in l for y in x["r"] if y not in ("m0", "mx")))
        ops.append(o)

    def lin(out, a, scale, bias, r, w, n, k=1.0):
        ts(out, a, scale, bias, A.mult, A.add, r, w, n, k)
        act(out, a, AF.Identity, r, w, n, scale=scale, bias=bias)
        either("a")

    def gat(e, out, win, r, w, n):
        cp(out, win, r, w, n, 1.56)
        act(out, win, AF.Copy, r, w, n, 1.56)
        either(e)

    def scl(out, a, x, r, w, n):
        ts(out, a, x, None, A.mult, None, r, w, n)
        act(out, a, AF.Copy, r, w, n, scale=x)
        either("a")

    def mm(l, r, w, start=True, stop=True, pair=False):
        def f(q):
            for j, (o, a, b, _) in enumerate(l):
                x = q.matmul(o, a, b, j != 1 if pair else start and j == 0, j != 0 if pair else stop and j == len(l) - 1)
            return x
        op("p", sum(max(64, x[3]) for x in l) * PEC + 30.0, r, w, f, lat=40.0)

    def group(bank, n, parts, first, lo=0):
        a, b, r = first
        mm([(P[bank][:, lo:n], a, b, n - lo)], r, "P%d A%d" % (bank, bank), True, False)
        left = [len(parts)]

        def one(l):
            def f(q):
                left[0] -= 1
                for j, (o, a, b, _) in enumerate(l):
                    x = q.matmul(o, a, b, False, left[0] == 0 and j == len(l) - 1)
                return x
            return f
        return [lambda l=l, r=r: op("p", sum(max(64, x[3]) for x in l) * PEC + 30.0, r + " A%d" % bank, "", one(l), lat=40.0) for l, r in parts]

    def dma(e, l, r, w, lat=1800.0, t0=0.0):
        op(e, 70.0 * len(l), r, w, lambda q: [q.dma_start(o, a) for o, a in l], dma=True, lat=lat, t0=t0)

    def iota(out, pat, base, cm, r, w, n, fl=True):
        if fl: op("g", 140 + 2 * n * CY, r, w, lambda q: q.iota(out, pat, base, cm, allow_small_or_imprecise_dtypes=True))
        else: op("g", 140 + 2 * n * CY, r, w, lambda q: q.iota(out, pat, base, cm))

    def sel(out, a, pat, cmp, fill, base, cm, r, w, n):
        op("g", 180 + 2 * n * CY, r, w, lambda q: q.affine_select(out, a, pat, cmp, fill, base, cm))

    def picks(out, wts, w, reps=1, wide=1):
        pat = [p for p in ([0, reps], [16, 8], [0, wide]) if p[1] > 1]
        for ch, x in wts: sel(out, out, pat, A.not_equal, float(x), ch, -1, w, w, 8 * reps * wide)

    def inslot(out, w, reps=1, wide=1, top=15):
        for s, b in ((-1, 0), (1, top)):
            sel(out, out, [p for p in ([0, reps], [16 * s, 8], [0, wide]) if p[1] > 1], A.is_ge, 0.0, b, -s, w, w, 8 * reps * wide)

    def diag(l):
        for M, x in l: sel(T[M][:], T.ZER[:, 0:128], [[1, 128]], A.not_equal, x, 0, -1, "ZER", M, 128)

    def strip(M, k):
        o = 144 * STRIPS.index(M) + 15 - k
        return T.MM[:, o:o + 128]

    def ext16(out, M, src, lo, n):
        return [(out, strip(M, k), src[:, lo + k:lo + 16 * n:16], n) for k in range(16)]

    def rows(ch, src, o=0):
        return [(T.W[ch:128:16, o:o + V], src)]

    def slot(q):
        return slice(16 * (q % N), 16 * (q % N) + 16)

    def parts2(hi, lo, b, src, r, k):
        ts(hi, src, MAG, -MAG, A.add, A.add, r, "HI%d" % b, 192)
        tt(lo, src, hi, A.subtract, r + " HI%d" % b, "LO%d" % (b + 4), 192, k)

    P = [T["P%d" % b] for b in range(8)]

    def send(m, r, c=500.0, also=""):
        l, tr = MSG[m], []
        mine = topo.engines(core, ports[rank][0])
        n = len(mine) // len(l)
        for j, (k, src, there, _) in enumerate(l):
            rid, pid = topo.addr(ports[rank][k], core)
            tr.append(RemoteDMATransfer(dst_ids=[DstId(rid=rid, pnc=pid)], dma_engine_mask=bits(mine[n * j:n * j + n]), remote_sem=T.sem["h" + m], dst=there, src=src))
        op("g", c, r + " gq", "gq m%s %s " % (m, also) + " ".join(x[2] for x in l[0][3]), lambda q: q.remote_dma_fused(tr, local_sem=T.sem.loc),
           rem=len(mine), lat=LATE[m[0]] + 500.0 - c)

    dma("s", [(T.CP[:, 0:192], T.cc[:])], "", "CPc")
    dma("a", [(T.s0[:, 64 * h:64 * h + 64, :], T.nm[4 * h:4 * h + 4, :]) for h in range(2)] + [(T.CP[:, 192:384], T.pl[:])], "", "s0 CPp ~a")
    dma("a", [(T.sx[k], T.tx[:, V // 4 * k:V // 4 * k + V // 4]) for k in range(4)], "~a", "sx", lat=3500.0, t0=250.0)
    dma("s", [(T.F[:], T.fo[:])], "", "F", lat=3500.0, t0=5500.0)

    col = lambda j: T.CC[:, j:j + 1]
    ms(T.ZER[:], 0.0, "ZER", 720, 0.5)
    ms(T.W[:, 0:V], 0.0, "Wd Wc Wb Wf Wo", V, 0.5)
    ms(T.W[:, V:FREE], 255.0, "Wt", 16)
    ms(T.W[:, FREE:FREE + 16], 64.0, "Wu", 16)
    ms(T.YP[:], 0.0, "YP", 192)
    diag((("Y1", 1.0), ("YR", 192.0)))
    iota(T.IOT[:], [[1, 512]], 0, 0, "", "IOT", 512)
    iota(T.RHO[:, 0:512], [[1, 32], [192, 16]], 8192, 0, "", "RHO0", 512)
    send("0", "s0 Y1 YR IOT", 2500.0)
    send("x", "sx")
    ts(T.IA[:, 0:192], T.CP[:, 0:192], 15, None, A.bitwise_and, None, "CPc", "IA0", 192)
    ts(T.IA[:, 192:384], T.CP[:, 0:192], 4, None, A.logical_shift_right, None, "CPc", "IA1", 192)
    cp(T.KA[:, 0:384], T.IA[:, 0:384], "IA0 IA1", "KAc", 384)
    send("c", "KAc", also="mx")
    iota(T.DU3[:], [[0, 6], [16, 32]], V, 1, "", "DU3", 192)
    gate[0] = " mx"
    iota(T.DU2[:], [[-int(192 * HALF), 2], [16, 16]], BIG - TAB, 1, "", "DU2", 32)
    diag((("YE", 262144.0), ("YH", -0.5), ("YN", -1.0), ("YS", 1.0 / 16)))
    sel(T.YF[:], T.YP[:, 0:128], [[1, 128]], A.not_equal, 1.0, 0, -1, "YP", "YF", 128)
    nms = ((CH_HI, 1), (CH_LO, 1), (CH_C, -1), (CH_C + 1, -1))
    for h in [x for x in range(6) if x not in VCH[0]]:
        c = T.FV[:, 512 * h:512 * h + 512]
        if h: lin(c, T.IOT[:], 1.0, 4096.0 + 512 * h, "IOT", "FV%d" % h, 512)
        else:
            act(c, T.IOT[:], AF.Silu, "IOT", "FV0", 512, bias=4096.0)
            ops[-1]["c"] += 1300.0
    for h in range(2): act(T.MM[:, 720 * h:720 * h + 720], T.ZER[:], AF.Copy, "ZER", " ".join(STRIPS[5 * h:5 * h + 5]), 720)
    for M, wts in (("MA", ((CH_J, 192), (CH_J + 1, 1))), ("MN", nms), ("MP", ((CH_OK, 192), (CH_OA, 1))),
                   ("MF", ((CH_FR, -BIG), (CH_E, BIG // 2), (CH_D, BIG // 2), (CH_D + 1, BIG // 2), (CH_Y, 3 * BIG // 2))), ("MX", ((CH_K, 1), (CH_A, 16))),
                   ("MR", ((CH_HI, 1.0 / 16), (CH_LO, 192), (CH_C, -1.0 / 16), (CH_C + 1, -192))),
                   ("ME", 8192), ("MU", 1), ("MV", 1), ("MS", None)):
        o = 144 * STRIPS.index(M)
        gate[0] = "" if M == "MP" else " mx"
        c = T.MM[:, o + 15:o + 143:16]
        if M == "MS": iota(c, [[-V, 8]], -4096, 192, M, M, 8)
        elif M in ("ME", "MU", "MV"): iota(c, [[0, 8]], wts, 0, M, M, 8)
        if M in ("ME", "MU", "MV", "MS"): inslot(c, M, 1, 1, 11 if M == "MV" else 15)
        else: picks(c, wts, M)
    for j, wts in enumerate((((CH_E, 8),), ((CH_FR, 8), (CH_Y, 8), (CH_D, -1), (CH_D + 1, -1)))):
        c = T.CT[:, 8 * j:8 * j + 8]
        iota(c, [[0, 8]], 0, 0, "", "CT%d" % j, 8)
        picks(c, wts, "CT%d" % j)
        red(col(2 + j), c, A.add, "CT%d" % j, "c%d" % (2 + j), 8)
    iota(T.VK[:, 0:384], [[SAME // 192, 2], [0, 192]], 0, 1, "", "VK", 384)
    iota(T.VK[:, 384:400], [[16, 16]], 0, 1, "", "VJ", 16)
    dma("s", [(T.VK[slot(q), 0:400], T.VK[slot(0), 0:400]) for q in range(1, N)], "VK VJ", "VK")
    iota(T.VK[:, 400:592], [[1, 192]], 0, 0, "", "VA", 192)
    cK = T.VK[:, 0:1]
    iota(T.SG[:], [[0, 128]], 1, 0, "", "SG", 128)
    inslot(T.SG[:], "SG", 1, 16)
    sel(T.TRI[:], T.SG[:], [[1, 128]], A.is_gt, 0.0, 0, -1, "SG", "TRI", 128)
    sel(T.TRI[:], T.TRI[:], [[1, 128]], A.not_equal, 512.0, 0, -1, "TRI", "TRI", 128)
    for l in (("TWO", "POW", "DO", "DZ"), ("DX", "DL", "BCV")): dma("s", [(T[M][:], T.ZER[:, 0:128]) for M in l], "ZER F", " ".join(l))
    o = 144 * STRIPS.index("MN")
    red(col(4), T.MM[:, o + 15:o + 143:16], A.add, "MN", "c4", 8)
    lin(T.BCN[:], T.SG[:], col(4), 0.0, "SG c4", "BCN", 128, 0.5)
    iota(T.TWO[:, CH_E:128:16], [[0, 8]], 2, 0, "TWO", "TWO", 8)
    inslot(T.TWO[:, CH_E:128:16], "TWO")
    o = 144 * STRIPS.index("MN")
    for M, h in (("DO", 0), ("DZ", 1)):
        sel(T[M][:, CH_D + h:128:16], T.MM[:, o + 15:o + 143:16], [[0, 8]], A.is_ge, 0.0, 0, 0, "MN " + M, M, 8)
        if M == "DO": picks(T.DO[:, CH_D:128:16], ((CH_FR, 8192),), M)
        lin(T[M][:, CH_D + 1 - h:128:16], T[M][:, CH_D + h:128:16], -1.0, 0.0, M, M, 8)
    for M in ("DZ", "DX"): picks(T[M][:, CH_E:128:16], ((CH_X, 8),), M)
    picks(T.DL[:, CH_D:128:16], ((0, 1),), "DL")
    picks(T.BCV[:, 0:128:16], ((CH_OK, 1), (CH_OA, 16)), "BCV")
    ms(T.TM2[:, 16:32], 0.5, "PW", 16)
    op("v", cyc(16), "PW ZER", "PV", lambda q: q.tensor_tensor_scan(T.TM2[:, 48:64], T.TM2[:, 16:32], T.ZER[:, 0:16], 2.0, A.mult, A.add))
    ts(T.TM2[:, 0:16], T.IOT[:, 0:16], cK, None, A.is_equal, None, "IOT VK", "OH", 16)
    tt(T.TM2[:, 32:48], T.TM2[:, 48:64], T.TM2[:, 0:16], A.mult, "PV OH", "PW2", 16)
    red(col(1), T.TM2[:, 32:48], A.max, "PW2", "c1", 16)
    lin(T.POW[:, CH_E:128:16], T.TWO[:, CH_E:128:16], col(1), 0.0, "TWO POW c1", "POW", 8)
    lin(T.THR[:, 0:16], T.TM2[:, 48:64], col(2), col(3), "PV c2 c3", "THR", 16)
    for n in (16, 32, 64, 128): sel(T.THR[:, n:2 * n], T.THR[:, 0:n], [[0, n]], A.is_ge, 0.0, 0, 0, "THR", "THR", n)
    iota(T.JB[:], [[16, 256]], 0, 0, "", "JB", 256)
    iota(T.JF[:], [[-1, 256]], 0, 0, "", "JF", 256)
    iota(T.TAU[:], [[-1, 256]], -512, 0, "", "TAU", 256)
    iota(T.SN[:], [[0, 128]], -1, 0, "", "SN", 128)
    inslot(T.SN[:], "SN", 1, 16)
    for t in range(1, TV + 1):
        for h, M in enumerate(("SG", "SN")):
            sel(T.SH[:, 256 * t - 256 + 128 * h:256 * t - 128 + 128 * h], T[M][:], [[16, 8], [0, 16]], A.is_gt, 0.0, S * t % 16, -1, M, "SH%d%d" % (t, h), 128)
        sel(T.SA[:, 128 * t - 128:128 * t], T.SG[:], [[0, 8], [16, 16]], A.is_ge, 0.0, 14 - S * t % V // 16, 0, "SG", "SA%d" % t, 128)
    iota(T.U[:, UB + 194:UB + 215], [[0, 21]], 256, 0, "", "Ue", 21)
    iota(T.BS[:], [[0, 16]], 0, 0, "", "BS", 16)
    iota(T.CU[:, 192:200], [[0, 8]], 0, 0, "", "CU", 8)
    iota(T.PG[:, TAB + V:TAB + V + 16], [[0, 16]], 0, 0, "", "Tt", 16)
    for j in range(1, NA): iota(T.RHO[:, 512 * j:512 * j + 512], [[1, 32], [192, 16]], 8192 + 32 * j, 0, "", "RHO%d" % j, 512)

    dma("s", rows(CH_OK, T.KA[:, 0:192]) + rows(CH_OA, T.KA[:, 192:384]), "KAc", "Wo")
    dma("s", [(T.LZ[0:128:16, 0:V], T.YP[:])], "YP", "LZ")
    dma("s", [(T.LW[0:128:16, 0:V], T.YP[:]), (T.LX[0:128:16, 0:V], T.YP[:])], "YP KAc", "LW LX")
    dma("s", [(T.LY[0:128:16, 0:V], T.YP[:])], "YP KAc", "LY")
    ts(T.IA[:, 384:576], T.CP[:, 192:384], 15, None, A.bitwise_and, None, "CPp", "IA2", 192)
    ts(T.IA[:, 576:768], T.CP[:, 192:384], 4, None, A.logical_shift_right, None, "CPp", "IA3", 192)
    cp(T.KA[:, 384:768], T.IA[:, 384:768], "IA2 IA3", "KAp", 384)
    for h in (1, 0):
        c = slice(192 * h, 192 * h + 192)
        mm([(P[3 + h][:, c], T.YR[:], T.KA[:, 384 * h:384 * h + 192], 192),
            (P[3 + h][:, c], T.Y1[:], T.KA[:, 384 * h + 192:384 * h + 384], 192)], "YR Y1 " + ("KAc", "KAp")[h], "P%d" % (3 + h))
        ts(T.RP[:, c], P[3 + h][:, c], float(FREE), None, A.min, None, "P%d" % (3 + h), ("RP", "PU")[h], 192)

    Wt, WA = T.W[:, 0:FREE + 16], "Wd Wc Wb Wf Wo Wt Wu "
    Tall = " T0 T1 T2 T3 T4 T5 Tt "
    TRall = " TR0 TR1 TR2 TR3 TR4 TR5 "
    for j in range(6):
        gat("av"[j % 2], T.PG[:, TAB + 512 * j:TAB + 512 * j + 512], Wt.indirect(T.RP[:, 192 + 32 * j:224 + 32 * j]), WA + "PU", "T%d" % j, 512)
    for j in range(3):
        c = slice(64 * j, 64 * j + 64)
        b = 5 + j % 2
        mm(ext16(P[b][:, c], "MP", T.PG, TAB + 1024 * j, 64), "T%d T%d MP" % (2 * j, 2 * j + 1), "P%d" % b)
        tt(T.RF[:, c], P[b][:, c], T.DU3[:, c], A.min, "P%d DU3" % b, "FC%d" % j, 64, 1.0)
        cp(T.LO[:, c], T.RF[:, c], "FC%d" % j, "LO%d" % j, 64)
    for h in range(6):
        if h in VCH[0]: ts(T.LW[:].indirect(T.LO[:, 32 * h:32 * h + 32]), T.IOT[:], 1.0, 4096.0 + 512 * h, A.mult, A.add, "IOT LO%d" % (h // 2), "LW", 512, 3.8)
        else: act(T.LX[:].indirect(T.LO[:, 32 * h:32 * h + 32]), T.FV[:, 512 * h:512 * h + 512], AF.Silu, "FV%d LO%d" % (h, h // 2), "LX", 512, 3.8)

    def join(out, dst, a, b, lo, w, bank):
        dma("s", [(dst[:, 192 * h:192 * h + 192], T[x][0:128:16, lo:lo + V]) for h, x in enumerate((a, b))], a + " " + b, w)
        mm([(out, T.YF[:], dst[:, 192 * h:192 * h + 192], 4 * 192) for h in range(2)], w + " YF", bank)
    send("y", "F")
    join(P[4][:, 192:384], T.FA, "LW", "LX", 0, "FA", "P4")
    ops[-2]["r"].append("my")
    ts(T.LU[:], P[4][:, 192:384], -4095.75, 0.0, A.add, A.max, "P4", "LU0 LU1 LU2", 192)
    act(T.MK[:], P[4][:, 192:384], AF.Relu, "P4", "MK", 192, scale=-256.0, bias=float(BIG))
    ts(P[4][:, 0:192], T.LU[:], -HALF, None, A.add, None, "LU0 LU1 LU2", "P4", 192)
    for j in range(6):
        if j < NA: act(T.LZ[:].indirect(T.RP[:, 32 * j:32 * j + 32]), T.RHO[:, 512 * j:512 * j + 512], AF.Silu, "RHO%d RP" % j, "LZ", 512, 3.8)
        else: ts(T.LY[:, 0:V].indirect(T.RP[:, 32 * j:32 * j + 32]), T.RHO[:, 0:512], 1.0, 32.0 * j, A.mult, A.add, "RHO0 RP", "LY", 512, 3.8)
    join(P[2][:, 192:384], T.ICF, "LY", "LZ", 0, "ICF", "P2")
    ts(T.ICU[:, 0:192], P[2][:, 192:384], -8191.75, None, A.add, None, "P2", "ICU", 192)
    send("i", "ICU")

    op("v", 3 * cyc(64), "a0", "NH", lambda q: [q.tensor_scalar(T.NH[:, 64 * j:64 * j + 64], T.N0[:, :, 16 * j:16 * j + 16], -HALF, None, A.add) for j in range(3)])
    for h in range(2):
        c = slice(64 * h, 64 * h + 64)
        for j in range(3): mm([(P[3][c, j:192:3], T.NH[c, 64 * j:64 * j + 64], T.YF[c, c], 4 * 64)], "NH YF", "P3")
    ts(T.NU[:], P[3][:, 0:192], HALF, None, A.add, None, "P3", "NU0 NU1", 192)
    scl(T.NF[:], P[3][:, 0:192], 1.0, "P3", "NF0 NF1", 192)
    parts2(T.HN[:, 0:192], T.HN[:, 192:384], 0, P[3][:, 0:192], "P3", 1.0)

    def pair(ch, src, o=0):
        return rows(ch, src[0], o) + rows(ch + 1, src[1], o)
    own = (T.VK[:, 0:192], T.VK[:, 400:592])
    con = lambda t: (T.KC[:, 384 * t - 384:384 * t - 192], T.KC[:, 384 * t - 192:384 * t])

    for t in range(1, TV + 1):
        s0 = S * t % V
        cs = s0 // 16
        last = t == TV
        HI, LO, CH, CL = [T.HL[:, 768 * t - 768 + 192 * k:768 * t - 576 + 192 * k] for k in range(4)]
        name = [T.HN[:, 768 * t - 768 + 192 * k:768 * t - 576 + 192 * k] for k in range(4)]
        cut = lambda M, k, a, b, j=None: T[M][:, slice(768 * t - 768 + 192 * k + a + (j or 0), 768 * t - 768 + 192 * k + b, None if j is None else 3)]
        now, was = "HI%d LO%d " % (t, t + 4), ["av%d " % (t - 1), "av%d aw%d " % (t - 1, t - 1)] if t > 1 else ["HI0 LO4 "] * 2
        if t == 1: dma("s", pair(CH_K, con(1)) + pair(CH_J, con(1)) + pair(CH_OK, own), "ac1 VK VA", "Wb Wo")
        elif t == 2: dma("s", pair(CH_K, con(2)) + rows(CH_OK, T.VK[:, 192:384]), "ac2 VK", "Wb Wo")
        elif t == 3: dma("s", pair(CH_K, con(3)) + pair(CH_OK, con(2)), "ac2 ac3", "Wb Wo")
        else:
            dma("s", pair(CH_OK, own) + pair(CH_HI, name[0:2]) + pair(CH_C, name[2:4]), "VK VA " + was[1], "Wo Wd Wc")
        if t == 2:
            for o in range(FREE + 16, NONE + 16, 464): iota(T.W[:, o:o + 464], [[0, 464]], 64, 0, "mb1", "Wi", 464)
            dma("g", pair(CH_J, own, SAME), "VK VA", "Wi")
            ops[-1]["c"] = 2000.0
            for h in [x for x in VCH[0] if x not in VCH[1]]: iota(T.FV[:, 512 * h:512 * h + 512], [[1, 512]], 4096 + 512 * h, 0, "mb1", "FV%d" % h, 512)
        if t == 3:
            for M, x in (("LW", 0), ("LX", 4095)):
                for o in range(TAB, TAB + V, 512): iota(T[M][:, o:o + 512], [[0, 512]], x, 0, "mb2", M, 512)
        if t > 1:
            for p, (a, b) in enumerate(PARTS):
                mm([(P[2][:, a:b], y[:], cut("HN", k, a, b), b - a) for k, y in enumerate((T.Y1, T.Y1, T.YN, T.YN))], "Y1 YN " + was[p], "P2")
                ts(T.NU[:, a:b], P[2][:, a:b], HALF, None, A.add, None, "P2", "NU%d" % p, b - a)
                scl(T.NF[:, a:b], P[2][:, a:b], 1.0, "P2", "NF%d" % p, b - a)
        part = lambda j: int(32 * j >= PARTS[1][0])
        by = lambda x, j: (T.F[:].indirect(T[x][:, 32 * j:32 * j + 32]), "F %s%d" % (x, part(j) if x == "NU" else j // 2))
        role = lambda j: ("NU", "LU", -1.0) if t == 1 else ("LU", "NU", 1.0)
        for j in range(6):
            one = role(j)[0]
            gat("a", T.G2[:, 512 * j:512 * j + 512], by(one, j)[0], by(one, j)[1], "G%d" % j, 512)
        parts2(HI, LO, t, P[4][:, 0:192], "P4", 1.0)
        if not last:
            dma("s", pair(CH_HI, (HI, LO)), now, "Wd")
            send("a%d" % t, now)
        for p, (a, b) in enumerate(PARTS):
            tt(T.EQ[:, a:b], P[4][:, a:b], T.NF[:, a:b], A.is_equal, "P4 NF%d" % p, "EQ%d" % p, b - a, 1.0)
            for h in (0, 1):
                mm([(P[4][:, 192 - 192 * h + a:192 - 192 * h + b], y[:], cut(M, k + h, a, b), b - a)
                    for M, k, y in (("HL", 0, T.Y1), ("HN", 0, T.YN), ("HN", 2, T.Y1))[:3 if t > 1 else 2]], "YN Y1 " + now + was[p], "P4")
        for j in range(6):
            c = slice(512 * j, 512 * j + 512)
            b = BANK[t - 1][j]
            one, two, sgn = role(j)
            if j in SIZE[t - 1]:
                gat("a", T.PR[:, c], by(two, j)[0], by(two, j)[1], "PR%d" % j, 512)
                for y in ("G2", "PR"):
                    mm([(P[b][:], T.YN[:], T.X[:, V * t - V + 512 * j:V * t - V + 512 * j + 512], 512)], "ax%d YN" % t, "P%d" % b, True, False)
                    mm([(P[b][:], T.Y1[:], T[y][:, c], 512)], "Y1 %s%d" % (y.strip("2"), j), "P%d" % b, False, True)
                    act(T["D" if y == "G2" else y][:, c], P[b][:], AF.Abs, "P%d" % b, "%s%d" % ("D" if y == "G2" else y, j), 512)
                mm([(P[b][:], T.YN[:], T.D[:, c], 512)], "YN D%d" % j, "P%d" % b, True, False)
                mm([(P[b][:], T.Y1[:], T.PR[:, c], 512)], "Y1 PR%d" % j, "P%d" % b, False, True)
                ts(T.NE[:, c], P[b][:], 0.0, 0.5, A.is_lt if sgn < 0 else A.is_gt, A.subtract, "P%d" % b, "NE%d" % j, 512)
                act(T.NE[:, c], P[b][:], AF.Sign, "P%d" % b, "NE%d" % j, 512, bias=-0.5, scale=sgn)
                either("a")
                continue
            if j in SIGN[t - 1]:
                act(T.PR[:, c], by(two, j)[0], AF.Copy, by(two, j)[1], "PR%d" % j, 512, 1.56)
                mm([(P[b][:], T.YN[:], T.G2[:, c], 512)], "YN G%d" % j, "P%d" % b, True, False)
                mm([(P[b][:], T.Y1[:], T.PR[:, c], 512)], "Y1 PR%d" % j, "P%d" % b, False, True)
                act(T.D[:, c], P[b][:], AF.Sign, "P%d" % b, "D%d" % j, 512)
            else:
                tt(T.D[:, c], by(two, j)[0], T.G2[:, c], A.subtract, by(two, j)[1] + " G%d" % j, "D%d" % j, 512, 1.56)
            x = ([(P[b][:], T.Y1[:], T.X[:, V * t - V + 512 * j:V * t - V + 512 * j + 512], 512)], "ax%d Y1" % t)
            a = ([(P[b][:], T.YH[:], T.D[:, c], 512)], "D%d YH" % j)
            n = ([(P[b][:], T.YN[:], T.G2[:, c], 512)], "G%d YN" % j)
            if j in SIGN[t - 1]: n, a = [([(P[b][:], T.YH[:], T[y][:, c], 512)], "%s%d YH" % (y.strip("2"), j)) for y in ("G2", "PR")]
            if t == 1 and j not in SIGN[0]:
                for y in group(b, 512, [x, a], n[0][0][1:3] + (n[1],)): y()
            else:
                mm(x[0], x[1], "P%d" % b, True, False)
                mm(n[0], n[1], "P%d" % b, False, False)
                mm(a[0], a[1], "P%d" % b, False, True)
            tt(T.PR[:, c], P[b][:], T.D[:, c], A.mult, "P%d D%d " % (b, j), "PR%d A%d" % (j, b), 512, 1.0)
            ts(T.NE[:, c], T.PR[:, c], 0.0, 0.5, A.is_gt if sgn < 0 else A.is_lt, A.subtract, "PR%d" % j, "NE%d" % j, 512, 0.5)
            act(T.NE[:, c], T.PR[:, c], AF.Sign, "PR%d" % j, "NE%d" % j, 512, bias=-0.25, scale=-sgn)
            either("a")
        for p, (a, b) in enumerate(PARTS):
            hs, k, o = range(a // 64, b // 64), (4, 2)[p], (384, 0)[p]
            parts = [(ext16(P[k][:, o + 64 * h:o + 64 * h + 64], "ME", T.NE, 1024 * h, 64), "ME NE%d NE%d" % (2 * h, 2 * h + 1)) for h in hs]
            if t == 1: parts.append(([(P[k][:, o + a:o + b], T.YN[:], T.MK[:, a:b], b - a)], "YN MK"))
            else: parts += [(ext16(P[k][:, o + 64 * h:o + 64 * h + 64], "MF", T.TR, 1024 * h, 64), "MF" + TRall) for h in hs]
            for x in group(k, o + b, parts, (T.YE[:], T.EQ[:, a:b], "YE EQ%d" % p), o + a): x()
            fr = ("FQ", "FR")[p]
            ts(T.FR[:, a:b], P[k][:, o + a:o + b], 4096.0, None, A.is_lt, None, "", fr + " P%d A%d" % (k, k), b - a)
            if p and not last: dma("s", rows(CH_FR, T.FR[:]), "FQ FR Wb Wo Wd", "Wf")
            if last:
                mm([(P[k][:, o + a:o + b], y[:], x, b - a) for x, y in ((cut("HL", 0, a, b), T.YS), (cut("HL", 1, a, b), T.YR), (T.FR[:, a:b], T.YE))],
                   "YE YS YR " + now + fr, "P%d" % k)
                tt(T.RF[:, a:b], P[k][:, o + a:o + b], T.DU3[:, a:b], A.min, "DU3 P%d" % k, "RF%d" % p, b - a, 1.0)
                ts(T.LO[:, a:b], T.RF[:, a:b], 192 * HALF + TAB, None, A.add, None, "RF%d" % p, " ".join("LO%d" % h for h in hs), b - a)
            tt(cut("HL", 2, a, b), P[4][:, 192 + a:192 + b], T.FR[:, a:b], A.mult, "P4 " + fr, "CH%d%d" % (t, p), b - a, 1.0)
            tt(cut("HL", 3, a, b), P[4][:, a:b], T.FR[:, a:b], A.mult, "P4 " + fr, "CL%d%d" % (t, p), b - a, 1.0)
            if not last: send("eb"[p] + str(t), "CH%d%d CL%d%d" % (t, p, t, p), also="ax%d" % (t + 2) * (p and t + 2 <= TV))
        new = "CH%d0 CL%d0 CH%d1 CL%d1 " % (t, t, t, t)
        if not last:
            dma("s", pair(CH_C, (CH, CL)), new, "Wc")
            for j in range(3):
                for h in (2 * j, 2 * j + 1):
                    o = 192 * t + 32 * h
                    gat("a", T.TR[:, 512 * h:512 * h + 512], Wt.indirect(T.ICU[:, o:o + 32]), WA + "ai%d" % t, "TR%d" % h, 512)
                mm(ext16(P[4][:, 64 * j:64 * j + 64], "MN", T.TR, 1024 * j, 64), "TR%d TR%d MN" % (2 * j, 2 * j + 1), "P4")
                ts(T.LU[:, 64 * j:64 * j + 64], P[4][:, 64 * j:64 * j + 64], HALF, None, A.add, None, "P4", "LU%d" % j, 64)
        else:
            for h in [x for x in range(6) if x not in VCH[1]]:
                act(T.LX[:].indirect(T.LO[:, 32 * h:32 * h + 32]), T.FV[:, 512 * h:512 * h + 512], AF.Silu, "FV%d LO%d" % (h, h // 2), "LX", 512, 3.8)
            for h in [x for x in range(0, 192, VS) if x // 32 in VCH[1]]:
                ts(T.LW[:].indirect(T.LO[:, h:h + VS]), T.IOT[:, 0:16 * VS], 1.0, 16.0 * h + 1, A.mult, A.add, "IOT LO%d" % (h // 64), "LW", 16 * VS, 3.8)
            dma("s", [(T.FA[:, 0:192], T.LX[0:128:16, TAB:TAB + V])], "LX", "FA")
            ts(T.YP[:], T.FA[:, 0:192], MAG / 16 - 4096, -MAG / 16, A.add, A.add, "FA", "YP", 192)
            op("g", 1500.0, "YP", "yp", lambda q: [q.dma_start(T.yp[:], T.YP[:])], dma=True, lat=2200.0)
            for j, b in enumerate((0, 1, 3)):
                for h in range(2):
                    mm([(P[b][64 * h:64 * h + 64, 0:64], cut("HL", k, 0, 192, j), y[:, 64 * h:64 * h + 64], 64) for k, y in enumerate((T.Y1, T.Y1, T.YN, T.YN))],
                       "Y1 YN " + new + now, "P%d" % b)
                lin(T.TN[:, :, 16 * j:16 * j + 16], P[b][:, 0:64], 1.0, HALF, "P%d" % b, "TN%d" % j, 64)
            send("n", "TN0 TN1 TN2")
        nt, Fc, HP, HM = 192 - cs, T.FR[:, cs:cs + 1], T.SH[:, 256 * t - 256:256 * t - 128], T.SH[:, 256 * t - 128:256 * t]
        o, base, UA = UB + 1 - nt, T.U[:, UB:UB + 1], "U Ua Ue "
        mm([(P[6][:, 0:nt], T.SG[:], T.FR[:, cs:192], nt), (P[6][:, 0:1], HM, Fc, 1), (P[6][:, nt:192], T.SG[:], T.FR[:, 0:cs], cs), (P[6][:, 192:193], HP, Fc, 1)],
           "SG FQ FR SH%d0 SH%d1" % (t, t), "P6", pair=True)
        op("v", cyc(193), "P6 ZER", "U Ua", lambda q, o=o: q.tensor_tensor_scan(T.U[:, o:o + 193], P[6][:, 0:193], T.ZER[:, 0:193], -256.0, A.add, A.min))
        ts(T.U[:, o + 193:UB + 194], T.U[:, o:o + nt], T.U[:, o + 192:o + 193], 256.0, A.add, A.add, "U", "Ua", nt, 0.5)
        ts(T.KB[:, 16:32], T.VK[:, 384:400], base, T.U[:, o + 192:o + 193], A.add, A.is_ge, "U VK", "KC", 16)
        mm([(P[6][:, 201:202], T.SG[:], base, 1)], "SG U", "P6")
        at = [UB + i if i <= cs + 1 else o + i - cs - 2 for i in range(16, 208, 16)]
        mm([(P[6][:, 200:201], strip("MU", k), T.U[:, i:i + 1], 1) for k, i in enumerate(at)]
           + [(P[6][:, 200:201], T.SA[:, 128 * t - 128:128 * t], T.U[:, i:i + 1], 1) for i in (o + 192, UB + 194)], "MU U Ue SA%d" % t, "P6")
        mm([(P[7][:, 448:461], strip("MU", k), T.U[:, UB + 1 + k:UB + 209:16], 13) for k in range(16)], "MU " + UA, "P7")
        lin(T.BS[:, 0:13], P[7][:, 448:461], -1.0 / 16, base, "P7 U", "BS", 13)
        mm([(P[7][:, 0:193], T.Y1[:], T.U[:, UB:UB + 193], 193), (P[7][:, 0:cs + 1], T.TRI[:], T.FR[:, 0:cs + 1], cs + 1),
            (P[7][:, cs + 1:193], T.TRI[:], T.FR[:, cs:192], nt), (P[7][:, cs + 1:cs + 2], HM, Fc, 1)], "TRI Y1 FQ FR SH%d1 " % t + UA, "P7")
        lin(T.CU[:, 0:193], P[7][:, 0:193], -1.0, base, "P7 U", "CU", 193)
        ts(T.L1[:], T.JB[:], P[6][:, 201:202], P[6][:, 200:201], A.add, A.is_ge, "JB P6", "L1", 256, 0.5)
        at = P[6][:, 256:272]
        mm(ext16(at, "MV", T.L1, 0, 16), "MV L1", "P6")
        ts(T.AU[:], at, 0.0, None, A.add, None, "P6", "AU", 16)
        scl(T.KB[:, 32:48], at, 16.0, "P6 AU", "AB", 16)
        tt(T.L2[:], T.BS[:, 0:16].indirect(T.AU[:]), T.JF[:], A.is_ge, "BS AU JF", "L2", 256, 1.56)
        mm(ext16(at, "MU", T.L2, 0, 16) + [(at, T.Y1[:], T.KB[:, 32:48], 16)], "L2 MU Y1 AB", "P6")
        ts(T.KU[:], at, 0.0, None, A.add, None, "P6", "KU", 16)
        scl(T.KB[:, 0:16], at, 1.0, "P6 KU", "KB", 16)
        tt(T.SE[:], T.CU[:, 0:194].indirect(T.KU[:]), T.TAU[:], A.is_equal, "CU KU TAU", "SE", 256, 1.56)
        mm(ext16(at, "MS", T.SE, 0, 16) + [(at, T.Y1[:], T.KB[:, 0:16], 16), (at, T.YN[:], T.KB[:, 16:32], 16)], "MS SE Y1 YN KB KC", "P6")
        ts(T.RU[:], at, 4096.0, float(V), A.add, A.min, "P6", "RU", 16)
        gat("a", T.Z[:], Wt.indirect(T.RU[:]), WA + "RU", "Z", 256)
        mm([(P[7][:, 0:256], T.BCN[:], T.Z[:], 256)], "BCN Z", "P7")
        mm(ext16(P[6][:, 0:16], "MN", T.Z, 0, 16), "MN Z", "P6")
        if not last: ts(T.NLU[:, 0:16], P[6][:, 0:16], HALF, None, A.add, None, "P6", "NLU", 16)
        lin(T.NL[:], P[6][:, 0:16], 1.0, HALF, "P6", "NL", 16)
        ts(T.NB[:], P[7][:, 0:256], HALF, None, A.add, None, "P7", "NB", 256)
        if not last:
            mm(ext16(P[6][:, 16:32], "MX", T.Z, 0, 16), "MX Z", "P6")
            tt(T.RT[:, 16:32], P[6][:, 16:32], T.DU3[:, 0:16], A.min, "P6 DU3", "RX", 16, 1.0)
            cp(T.NLU[:, 16:32], T.RT[:, 16:32], "RX", "NPU", 16)
            gat("a", T.O[:], T.PG[:, TAB:TAB + V + 16].indirect(T.NLU[:, 0:16]), Tall + "NLU", "O", 256)
            for k in range(t):
                wide = t == 3 and k == 0
                mm(ext16(P[6][:, 0:16], "MA" if k == 1 else "MP", T.O, 0, 16), "O MA MP", "P6")
                ts(T.OU[:], P[6][:, 0:16], float(NONE if wide else FREE), None, A.min, None, "P6", "OU", 16)
                gat("a", T.O[:], (T.W[:, 0:NONE + 16] if wide else Wt).indirect(T.OU[:]), WA + "OU" + (" Wi" if wide else ""), "O", 256)
            parts = [([(P[7][:, 0:256], T.DO[:], T.O[:], 256)], "DO O"), ([(P[7][:, 0:256], T.DZ[:], T.Z[:], 256)], "DZ Z")]
        else:
            mm(ext16(P[6][:, 0:16], "MR", T.Z, 0, 16), "MR Z", "P6")
            ts(T.OU[:], P[6][:, 0:16], 192 * HALF, None, A.add, None, "P6", "OU", 16)
            gat("a", T.O[:], T.LW[:, TAB:TAB + V].indirect(T.OU[:]), "LW OU", "O", 256)
            ts(T.O1[:], T.LX[:, TAB:TAB + V].indirect(T.OU[:]), -4096.0, None, A.add, None, "LX OU", "O1", 256, 1.56)
            act(T.O1[:], T.LX[:, TAB:TAB + V].indirect(T.OU[:]), AF.Identity, "LX OU", "O1", 256, 1.56, bias=-4096.0)
            either("a")
            parts = [([(P[7][:, 0:256], T.DL[:], T.O[:], 256)], "DL O"), ([(P[7][:, 0:256], T.DL[:], T.O1[:], 256)], "DL O1"),
                     ([(P[7][:, 0:256], T.DX[:], T.Z[:], 256)], "DX Z")]
            mm([(P[3][:, 0:256], T.BCV[:], T.Z[:], 256)], "BCV Z", "P3")
            lin(T.VAL[:], P[3][:, 0:256], 1.0, 1.0, "P3", "VAL", 256)
        for h in range(0, 16, 3):
            ms_ = range(h, min(h + 3, 16))
            op("v", sum(cyc(256 - 16 * m, 0.5) for m in ms_), "NB NL", " ".join("E%d" % m for m in ms_),
               lambda q, ms_=ms_: [q.tensor_scalar(T.E[:, m, 0:256 - 16 * m], T.NB[:, 16 * m:256], T.NL[:, m:m + 1], None, A.is_equal) for m in ms_])
        for h in range(5):
            parts.append(([(P[7][:, 16 * m + 16:256], T.TWO[:], T.E[:, m, 16:256 - 16 * m], 240 - 16 * m) for m in range(3 * h, 3 * h + 3)],
                          " ".join("E%d" % m for m in range(3 * h, 3 * h + 3)) + " TWO"))
        parts.append(([(P[7][:, 0:256], T.POW[:], T.E[:, :, 0:16], 256)], "POW " + " ".join("E%d" % m for m in range(16))))
        for x in group(7, 256, parts, (T.YH[:], T.THR[:], "YH THR")): x()
        act(T.WI[:], P[7][:, 0:256], AF.Sign, "", "WI P7 A7", 256, scale=-1.0)
        if not last:
            tt(T.TR[:, 0:3440].indirect(T.NLU[:, 16:32]), T.Z[:], T.WI[:], A.add, "Z WI NPU", TRall, 256, 3.8)
        if t == TV - 1: continue
        if last:
            mm(ext16(P[6][:, 0:16], "MR", T.Z, 0, 16), "Z MR", "P6", True, False)
            mm(ext16(P[6][:, 0:16], "MF", T.WI, 0, 16), "MF WI", "P6", False, True)
            tt(T.RT[:, 0:16], P[6][:, 0:16], T.DU2[:, 16:32], A.max, "P6 DU2", "RT", 16, 1.0)
        else:
            mm(ext16(P[6][:, 0:16], "MF", T.WI, 0, 16), "MF WI", "P6")
            tt(T.RT[:, 32:48], P[6][:, 0:16], T.NL[:], A.add, "P6 NL", "RG", 16, 1.0)
            tt(T.RT[:, 0:16], T.RT[:, 32:48], T.DU2[:, 0:16], A.max, "RG DU2", "RT", 16)
        ts(T.QU[:], T.RT[:, 0:16], TAB - BIG + 192 * HALF * last, None, A.add, None, "RT", "QU", 16)
        if not last: cp(T.PG[:, 0:TAB + V].indirect(T.QU[:]), T.Z[:], "Z QU", Tall, 256, 3.8)

    cp(T.LW[:, 0:TAB + V].indirect(T.QU[:]), T.VAL[:], "VAL QU", "LW", 256, 3.8)
    op("g", 500.0, "LW yp", "yp", lambda q: [q.dma_start(T.yp[:], T.LW[0:128:16, TAB:TAB + V], accum_op=A.add, max_dma_last_dim=4096)], dma=True, lat=2600.0)
    dma("s", [(T.yn[4 * h:4 * h + 4, :], T.rn[:, 64 * h:64 * h + 64, :]) for h in range(2)], "an FA", "yn", lat=5000.0)
    return ops
